import numpy as np, ml_dtypes
CORES = [9,25,41,57]
N = 4
BF = ml_dtypes.bfloat16
V, M, T = 512, 1, 3
WIN = N * V
HI = WIN // 16
B = V // M
H = (N, 8, 16, V)
def sized(u, hi):
    return np.where(u < 0, -1.0, 1.0) * np.clip(np.abs(u), 0.125, hi)
def draw(rng):
    return {"x": np.minimum((rng.random(H) * rng.choice(np.array([8, 16, 16, 24]), (N, 8, 1, V))).astype(np.int64), 15),
            "u": sized(rng.standard_normal(H, dtype=np.float32) * np.exp2(rng.integers(-1, 1, (N, 8, 16, 1))), 3.0),
            "w": (rng.random(H) * rng.choice(np.array([4, 8, 12, 16]), (N, 8, 1, V))).astype(np.int64),
            "ag": rng.choice(np.array([0, 1, 2, 3, 3, 3]), H), "s": rng.integers(0, WIN, H), "p": rng.integers(0, WIN, H),
            "j": rng.integers(0, HI, (N, 8, 16, WIN)), "tb": rng.integers(30, 110, (N, 8, 16)), "te": rng.integers(40, 200, (N, 8, 16))}
def pack(d):
    o = {}
    o["x0"] = d["x"].reshape(N, 128, V).astype(np.float32).astype(BF)
    o["u0"] = d["u"].reshape(N, 128, V).astype(np.float32)
    o["s0"] = d["s"].reshape(N, 128, V).astype(np.int32)
    o["p0"] = d["p"].reshape(N, 128, V).astype(np.int32)
    o["w0"] = d["w"].reshape(N, 128, V).astype(np.float32).astype(BF)
    o["ag"] = d["ag"].reshape(N, 128, V).astype(np.float32).astype(BF)
    o["ax"] = d["j"].reshape(N, 128, WIN).astype(np.float32).astype(BF)
    o["th"] = np.stack([d["tb"], d["te"]], axis=-1).reshape(N, 128, 2).astype(np.int32)
    return o
def ends(rng, lo, hi, shape, share):
    e = np.where(rng.random(shape) < 0.5, lo, hi)
    return np.where(rng.random(shape) < share, e, rng.integers(lo, hi + 1, shape))
def setup_inputs(rng):
    return pack(draw(rng))
def setup_inputs_spread(rng):
    d = draw(rng); c = (N, 8, 1, V)
    d["u"] = sized(d["u"] * np.exp2(rng.integers(-1, 2, c)), 8.0)
    d["x"] = np.minimum((np.exp2(4 * rng.random(H)) - 1).astype(np.int64) + rng.integers(0, 4, c), 15)
    d["w"] = np.minimum(np.exp2(4 * rng.random(H)).astype(np.int64), 15) * (rng.random(H) > 0.1)
    d["tb"] = rng.integers(0, 241, (N, 8, 16)); d["te"] = rng.integers(0, 241, (N, 8, 16))
    return pack(d)
def setup_inputs_ends(rng):
    d = draw(rng)
    d["x"] = ends(rng, 0, 15, H, 1.0)
    d["w"] = 15 * (rng.random(H) < rng.choice(np.array([0.0, 0.1, 0.2, 1.0]), (N, 8, 1, V))).astype(np.int64)
    d["ag"] = ends(rng, 0, 3, H, 0.8)
    d["s"] = ends(rng, 0, WIN - 1, H, 0.7); d["p"] = ends(rng, 0, WIN - 1, H, 0.7)
    d["j"] = ends(rng, 0, HI - 1, (N, 8, 16, WIN), 0.7)
    d["tb"] = ends(rng, 0, 240, (N, 8, 16), 0.8); d["te"] = ends(rng, 0, 240, (N, 8, 16), 0.8)
    d["u"] = np.where(rng.random(H) < 0.5, -1.0, 1.0) * np.where(rng.random(H) < 0.5, 0.125, 8.0)
    d["u"][:, ::2, :, V - 2:] = 8.0; d["u"][:, 1::2, :, V - 2:] = -8.0
    low = np.where(rng.permutation(8) < 4, 0, 15)[:, None, None]
    d["x"][0, :, :, :16] = low; d["w"][0, :, :, :16] = low
    d["x"][N - 1, :, :, V - 32:] = 15; d["w"][N - 1, :, :, V - 32:] = 15
    d["x"][:, :, :, V - 2:] = 15; d["w"][:, :, :, V - 2:] = 15
    d["ag"][:, :, :, V - 1] = 0; d["p"][:, :, :, V - 1] = WIN - 1
    d["ag"][:, :, :, V - 2] = 3; d["s"][:, :, :, V - 2] = WIN - 1
    d["x"][:, :, :, V - 3] = 0; d["w"][:, :, :, V - 3] = 0; d["ag"][:, :, :, V - 3] = 0
    d["te"][:, 7, 15] = 240; d["te"][:, 7, 0] = 0; d["tb"][:, 7, 15] = 240; d["tb"][:, 7, 0] = 0
    return pack(d)
def setup_inputs_corners(rng):
    d = draw(rng)
    lev = np.broadcast_to(rng.choice(np.array([0, 3, 6, 11, 15]), (N, 8, 1, V)), H)
    d["x"][:, ::2] = lev[:, ::2]
    many = rng.choice(np.array([0, 1, 2, 3, 4, 5, 6, 7, 8, 9, 15, 16]), (N, 8, 1, V))
    many[:, 3] = 16; many[::2, 4] = 0
    live = np.argsort(rng.random(H), axis=2) < many
    age = rng.integers(0, 3, H); age[:, 0] = 2; age[:, 1] = 0; age[:, 2] = 1
    d["ag"] = np.where(live, age, 3)
    d["w"] = rng.choice(np.array([0, 0, 0, 1, 1, 4, 11, 12, 15]), H)
    own = np.arange(N)[:, None, None, None] * V + np.arange(V)
    for k in ("s", "p"):
        c = rng.integers(0, 6, H)
        d[k] = np.where(c == 0, own, np.where(c == 1, 0, np.where(c == 2, WIN - 1, d[k])))
    for q in range(N):
        m = (8, 4, 0, 7, 1, 6, 3, 2)[q]
        d["te"][q] = np.where(rng.permutation(8) < m, 0, 240)[:, None]
    d["tb"] = rng.choice(np.array([0, 1, 60, 100, 239, 240]), (N, 8, 16))
    return pack(d)
def setup_inputs_crowd(rng):
    d = draw(rng); o = rng.permutation(8); z = rng.integers(0, WIN, 8); h = (N, 16, V)
    for i in range(4):
        g = int(o[i]); q = int(z[g]) // V; v = int(z[g]) % V
        d["s"][:, g] = z[g]; d["p"][:, g] = z[g]; d["ag"][:, g] = rng.integers(0, 3, h)
        d["x"][q, g, :, v] = rng.integers(4, 16, 16); d["w"][q, g, :, v] = 8
        if i >= 2:
            one = np.arange(16)[:, None] == rng.integers(0, 16, (N, 1, V))
            d["p"][:, g] = np.where(one, rng.integers(0, WIN, h), z[g]); d["s"][:, g] = np.where(one, rng.integers(0, WIN, h), z[g])
    g = int(o[4]); few = rng.integers(0, WIN, 4)
    d["s"][:, g] = rng.choice(few, h); d["p"][:, g] = rng.choice(few, h)
    keep = d["te"][1].copy(); d["te"][:] = 0; d["te"][:, int(o[7]), 1::2] = 240; d["te"][1] = keep
    return pack(d)
def setup_inputs_calm(rng):
    d = draw(rng); turn = int(rng.integers(0, 4))
    for q in range(N):
        d["te"][q] = np.where(rng.permutation(8) < q % 4, 0, 240)[:, None]
    d["ag"] = np.broadcast_to(((np.arange(8) + turn) % 4)[None, :, None, None], H).copy()
    lev = np.broadcast_to(rng.choice(np.array([3, 6, 9, 12]), (N, 8, 1, V)), H)
    d["x"][:, 1::2] = lev[:, 1::2]
    d["tb"] = rng.choice(np.array([0, 40, 80]), (N, 8, 16))
    return pack(d)
def check_ranges(d):
    bad = []
    for k, lo, hi in (("x0", 0, 15), ("s0", 0, WIN - 1), ("p0", 0, WIN - 1), ("w0", 0, 15), ("ag", 0, 3), ("ax", 0, HI - 1), ("th", 0, 240), ("u0", -8, 8)):
        v = np.asarray(d[k]).astype(np.float64)
        if not (np.min(v) >= lo and np.max(v) <= hi): bad.append("range of " + k)
        if k != "u0" and np.any(v != np.floor(v)): bad.append("whole numbers of " + k)
        if k == "u0" and not np.min(np.abs(v)) >= 0.125: bad.append("least size of " + k)
    return bad
def reference(x0, u0, s0, p0, w0, ag, ax, th):
    X, W, A = [a.astype(np.float32).astype(np.int64).reshape(H) for a in (x0, w0, ag)]
    S, P = [a.astype(np.int64).reshape(H) for a in (s0, p0)]
    U = u0.astype(np.float64).reshape(H); J = ax.astype(np.float32).astype(np.int64).reshape(N, 8, 16, WIN)
    tb = th[:, :, 0].astype(np.int64).reshape(N, 8, 16, 1); te = th[:, :, 1].astype(np.int64).reshape(N, 8, 16, 1)
    gi = np.arange(8)[:, None, None, None]; ii = np.arange(16)[None, :, None, None]; K = np.arange(16)[:, None]
    for t in range(T):
        a = (t % M) * B; b = a + B
        XA = X.transpose(1, 2, 0, 3).reshape(8, 16, WIN); UA = U.transpose(1, 2, 0, 3).reshape(8, 16, WIN)
        s = S[..., a:b]; p = P[..., a:b]; e = W[..., a:b]; age = A[..., a:b]
        live = age < 3
        C = np.where(live, p, s)
        w = e * (4 - np.where(live, age, 0))
        c = np.zeros((N, 8, 16, B), np.int64); sx = np.zeros((N, 8, 16, B), np.int64); su = np.zeros((N, 8, 16, B))
        for r in range(N):
            ix = C[r][:, None]; wr = w[r][:, None]
            XC = XA[gi, ii, ix]
            c[r] = np.sum(np.minimum(XC, X[r][:, :, None, a:b]), axis=1)
            sx[r] = np.sum(wr * XC, axis=2)
            su[r] = np.sum(wr * UA[gi, ii, ix], axis=2)
        nx = np.minimum(sx >> 8, 15)
        nu = np.tanh(su * 2.0 ** -11 + 0.5 * U[..., a:b] + 0.0625 * (X[..., a:b] - 8))
        strong = np.sum(nx, axis=2, keepdims=True) >= te
        n = np.sum(strong.astype(np.int64), axis=1, keepdims=True)
        key = np.where(live, 16 * c + 15 - K, -1)
        before = np.sum((key[:, :, :, None] > key[:, :, None]).astype(np.int64), axis=2)
        cap = live & strong & (before < n)
        fresh = ~live & (c >= tb)
        q = (C + 16 * np.take_along_axis(J, C, 3) + K) & (WIN - 1)
        s2 = np.where(cap, p, s); e2 = np.where(cap, np.minimum(e + 4, 15), e); p2 = np.where(fresh, q, p)
        a2 = np.where(cap, 3, np.where(live, age + 1, np.where(fresh, 0, 3)))
        S[..., a:b] = s2; W[..., a:b] = e2; P[..., a:b] = p2; A[..., a:b] = a2; X[..., a:b] = nx; U[..., a:b] = nu
    Y = np.where(A < 3, P, S)
    return {"yx": X.reshape(N, 128, V).astype(np.float32), "yu": U.reshape(N, 128, V).astype(np.float32), "yc": Y.reshape(N, 128, V).astype(np.float32), "yw": (16 * A + W).reshape(N, 128, V).astype(np.float32)}

def check_inputs(d):
    bad = list(check_ranges(d))
    if not bad:
        for name, y in reference(**d).items():
            for q in range(N):
                v = np.abs(np.asarray(y[q], np.float64)); s = np.sqrt(np.mean(v * v))
                if v.max() > 6 * s or s < 2.0 ** -3: bad.append('%s of rank %d is uneven or too small' % (name, q))
    return bad

@@ -1,0 +1,590 @@
+from concourse.bass import DstId, RemoteDMATransfer
+from concourse.mybir import AluOpType, ActivationFunctionType
+
+A = AluOpType
+F = ActivationFunctionType
+V, NR, STEPS = 512, 4, 3
+CW, NCH = 128, 4
+HW = 256
+CFG = {
+    "sends": [[0], [1], [2], [3]],
+    "gv": "",
+    "gw": 64,
+    "pesum": [(), (), ()],
+    "j0": "avav", "j1": "aaaa",
+    "order": "0X0 0X1 0x0 0c0 0X2 0U0 0x1 0c1 0U1 0u0 0U2 0u1 0XU3 0s0 0xu2 0xu3 0c2 0c3 1XU0 0s1 "
+             "1XU1 1xu0 0j0 1XU2 1xu1 1c0 1c1 1d0 1XU3 1xu2 1s0 1xu3 1c2 1c3 2XU0 1d1 1s1 "
+             "2XU1 2xu0 2c0 2X2 2xu1 2c1 2X3 2d0 2s0 2c2 2U2 2x2 2c3 2U3 2x3 2d1 2s1 2u2 2u3",
+    "sid": "a", "wv": True,
+    "seed": 0, "noise": 700.0, "rounds": 160, "mix": 0.0,
+}
+PRM = {"cy": 1.0, "pe": 0.55, "gc": 1.56, "link": 16.0, "lat": 2500.0, "sync": 120.0}
+
+bf, f32, f16, i32, u16 = "bfloat16", "float32", "float16", "int32", "uint16"
+SCRATCH = {}
+
+
+def _buf(name, cols, dt, where="sbuf"):
+    SCRATCH[name] = (where, [128, cols], dt)
+
+
+for _t in range(STEPS):
+    _buf("tx%d" % _t, NR * V, bf)
+    _buf("tu%d" % _t, NR * V, f32)
+    _buf("off%d" % _t, V, u16)
+for _j in range(NCH):
+    _buf("xc%d" % _j, 16 * CW, bf)
+    _buf("uc%d" % _j, 16 * CW, f32)
+    _buf("mn%d" % _j, 16 * CW, bf)
+    _buf("px%d" % _j, 16 * CW, f16)
+for _j in range(2):
+    _buf("pu%d" % _j, 16 * CW, f32)
+    _buf("sc%d" % _j, 16 * CW, f32)
+    _buf("sg%d" % _j, 8 * HW, bf)
+    for _n in ("bb", "la", "ww", "wt", "ga"):
+        _buf("%s%d" % (_n, _j), V, bf)
+    _buf("cc%d" % _j, V, f32)
+    _buf("dd%d" % _j, V, f32)
+for _n, _c, _d in [
+        ("jt", NR * V, bf), ("si", V, i32), ("pi", V, i32), ("ab", V, bf), ("ti", 4, i32),
+        ("offs", V, u16), ("offn", V, u16), ("le", V, f32), ("n1", V, f32), ("g1", V, f32), ("g2", V, f32),
+        ("tmp", V, f32), ("tm2", V, f32), ("live", V, bf), ("dead", V, bf), ("yy", V, bf), ("xo", V, bf), ("uo", V, f32), ("wo", V, f32),
+        ("ck", V, bf), ("ph", V, bf), ("ss", V, bf), ("rr", V, bf), ("ones", HW, bf), ("msk", 1024, bf), ("thf", 4, f32),
+        ("ci", 144, bf), ("cm", 128, bf), ("cb", 128, bf), ("ia", 16, i32), ("ib", 16, i32), ("ic", 16, i32), ("fa", 16, f32), ("ks", 16, f32),
+        ("mk", 16, f32), ("mk16", 16, f32), ("tb", 16, f32), ("col", 16, f32),
+        ("bo", 128, bf), ("ee", 144, bf), ("ff", 2048, bf), ("dg", 2048, bf), ("sh", 2048, bf), ("n32", 128, bf), ("nm", 128, bf),
+        ("kd", 128, bf), ("ih", 128, f16), ("i1", 128, f32), ("ik", 128, f32), ("sid", 128 * 13, bf)]:
+    _buf(_n, _c, _d)
+for _n in ("w0b", "w1b", "xb", "cbk", "hb", "ub", "m0", "m1"):
+    _buf(_n, 512, f32, "psum")
+SCALES = [1.0, -1.0, 128.0, 64.0, 2.0, -2.0, -3.0, 4.0, -4.0, 0.5, -1.5, -16.0, 2.5]
+
+ENG = ("g", "pe", "dve", "act", "sp")
+NDMA = 24
+SEMAPHORES = ["q_" + e for e in ENG] + ["d%d" % i for i in range(NDMA)] + ["sent"] + \
+             ["ax%d" % t for t in range(STEPS)] + ["au%d" % t for t in range(STEPS)]
+
+
+SPREAD = [{}, {"gc": 1.15, "link": 10.0}, {"gc": 2.0, "link": 24.0, "lat": 3500.0}, {"pe": 0.45, "sync": 250.0}, {"pe": 0.7, "cy": 0.9, "link": 22.0}]
+KEPT = {}
+
+
+def order_nodes(nodes, others):
+    n = len(nodes)
+    SYNC = PRM["sync"]
+    cost = [x["cost"] for x in nodes]
+    fwd, bwd = [[] for _ in range(n)], [[] for _ in range(n)]
+    for i, x in enumerate(nodes):
+        for d in sorted(x["hard"] | x["soft"]):
+            gap = nodes[d]["lat"] + SYNC if d in x["hard"] else 0.0
+            fwd[i].append((d, gap))
+            bwd[d].append((i, gap))
+
+    def place(before, after, pr, first):
+        left = [len(b) for b in before]
+        ready = [i for i in range(n) if left[i] == 0]
+        st, busy, seq = [0.0] * n, {}, []
+        while ready:
+            i = max(ready, key=lambda c: pr[c])
+            ready.remove(i)
+            t = max([st[d] + cost[d] + gap for d, gap in before[i]] + [first[i]])
+            line = busy.setdefault(nodes[i]["eng"], [])
+            k = 0
+            while k < len(line) and t + cost[i] > line[k][0]:
+                t = max(t, line[k][1])
+                k += 1
+            line.insert(k, (t, t + cost[i]))
+            st[i] = t
+            seq.append(i)
+            for s, _g in after[i]:
+                left[s] -= 1
+                if left[s] == 0:
+                    ready.append(s)
+        return st, seq
+
+    pr = [0.0] * n
+    for i in range(n - 1, -1, -1):
+        pr[i] = cost[i] + max([pr[s] + gap for s, gap in bwd[i]] + [nodes[i]["lat"]])
+    pr = [CFG["mix"] * pr[i] - 100.0 * i for i in range(n)]
+    z = CFG["seed"]
+    best = None
+    for rnd in range(CFG["rounds"]):
+        if rnd % 4 == 0 and best is not None:
+            pr = [-s for s in best[1]]
+            for i in range(n):
+                z = (z * 1103515245 + 12345) % 2147483648
+                pr[i] += CFG["noise"] * (1 + rnd // 4 % 3) * z / 2147483648
+        st, seq = place(fwd, bwd, pr, [0.0] * n)
+        at = {i: k for k, i in enumerate(seq)}
+        order = sorted(range(n), key=lambda i: (st[i], at[i]))
+        end = sum(replay(o, order, sy) for o, sy in others)
+        if best is None or end < best[0]:
+            best = (end, st, order)
+        back, _s = place(bwd, fwd, [st[i] + cost[i] for i in range(n)], [x["lat"] for x in nodes])
+        pr = [back[i] + cost[i] for i in range(n)]
+    for i, x in enumerate(nodes):
+        x["st"], x["end"] = best[1][i], best[1][i] + cost[i] + x["lat"]
+    return best[2]
+
+
+def replay(nodes, order, sync):
+    free, end = {}, [0.0] * len(nodes)
+    for i in order:
+        x = nodes[i]
+        st = max([free.get(x["eng"], 0.0)] + [end[d] + sync for d in x["hard"]])
+        free[x["eng"]] = st + x["cost"]
+        end[i] = st + x["cost"] + x["lat"]
+    return max(end)
+
+
+def plan(g, core, T, topo):
+    sets = [(build(g, core, T, topo, dict(PRM, **m))[0], dict(PRM, **m)["sync"]) for m in SPREAD]
+    nodes, ncalls, neng = build(g, core, T, topo, PRM)
+    if "order" not in KEPT:
+        KEPT["order"] = order_nodes(nodes, sets)
+        KEPT["st"] = [x["st"] for x in nodes]
+    for x, s in zip(nodes, KEPT["st"]):
+        x["st"] = s
+    return nodes, KEPT["order"], ncalls, neng
+
+
+def build(g, core, T, topo, PRM):
+    rank = T.rank_of(core)
+    CY, PEC, GC = PRM["cy"], PRM["pe"], PRM["gc"]
+    nodes = []
+    lastw, readers, bankt = {}, {}, {}
+    ve, ac, pe = g.vector, g.scalar, g.tensor
+
+    def node(eng, cost, fn, r=(), w=(), banks=(), lat=0.0, kind="c", name=""):
+        i = len(nodes)
+        hard, soft = set(), set()
+
+        def dep(d, raw):
+            if raw or nodes[d]["eng"] != eng or nodes[d]["kind"] != "c" or kind != "c":
+                hard.add(d)
+            else:
+                soft.add(d)
+        for k in r:
+            if k in lastw:
+                dep(lastw[k], True)
+        for k in w:
+            if k in lastw:
+                dep(lastw[k], True)
+            for d in readers.get(k, ()):
+                dep(d, True)
+        for b in banks:
+            for d in bankt.get(b, {}).values():
+                dep(d, False)
+            bankt.setdefault(b, {})[eng] = i
+        for k in r:
+            readers.setdefault(k, []).append(i)
+        for k in w:
+            lastw[k] = i
+            readers[k] = []
+        nodes.append({"eng": eng, "cost": cost, "lat": lat, "fn": fn, "hard": hard, "soft": soft - hard, "kind": kind, "name": name})
+        return i
+
+    def dve(n, cyc, fn, r, w, banks=(), name=""):
+        node("dve", 60 + max(64, n * cyc) * CY, fn, r, w, banks, name=name)
+
+    def act(out, in_, func, n, r, w, banks=(), cyc=1.0, name="", **kw):
+        node("act", 70 + max(64, n * cyc) * CY, lambda: ac.activation(out, in_, func, **kw), r, w, banks, name=name)
+
+    def tt(out, a, b, op, n, cyc, r, w, banks=(), name=""):
+        dve(n, cyc, lambda: ve.tensor_tensor(out, a, b, op), r, w, banks, name)
+
+    def ts(out, a, s1, s2, op0, op1, n, cyc, r, w, banks=(), name=""):
+        if op1 is None:
+            dve(n, cyc, lambda: ve.tensor_scalar(out, a, s1, None, op0), r, w, banks, name)
+        else:
+            dve(n, cyc, lambda: ve.tensor_scalar(out, a, s1, s2, op0, op1), r, w, banks, name)
+
+    def cp(out, a, n, cyc, r, w, banks=(), name=""):
+        dve(n, cyc, lambda: ve.tensor_copy(out, a), r, w, banks, name)
+
+    def mm(items, r, w, bank, name=""):
+        def fn():
+            last = None
+            for o, l, x, s0, s1, _c in items:
+                last = pe.matmul(o, l, x, s0, s1)
+            return last
+        node("pe", 30 + sum(max(64, it[5]) * PEC for it in items), fn, r, w, (bank,), lat=100.0, name=name)
+
+    def acc(out, terms, n, r, w, bank, name=""):
+        mm([(out, l, x, i == 0, i == len(terms) - 1, n * c) for i, (l, x, c) in enumerate(terms)], r, w, bank, name)
+
+    def dma(q, out, in_, kb, r, w, name=""):
+        eng = {"sp": g.sync, "act": g.scalar, "g": g}[q]
+        node(q, 1000.0 if q == "g" else 100.0, lambda: eng.dma_start(out, in_), r, w, lat=1800.0 + kb * 6.0, kind="d", name=name)
+
+    def sid(s):
+        k = SCALES.index(s)
+        return T.sid[:, 128 * k:128 * (k + 1)]
+
+    def blk(t, k):
+        return t[:, 128 * k:128 * (k + 1)]
+
+    own = rank * V
+    peers = [T.cores[(rank + d) % NR] for d in range(1, NR)]
+    mask = topo.mask(core, peers[0])
+    for p in peers:
+        mask &= topo.mask(core, p)
+    neng = bin(mask).count("1")
+    ids = [DstId(rid=topo.addr(p)[0], pnc=topo.addr(p)[1]) for p in peers]
+    ncalls = {}
+
+    def send(kind, t, c0, c1, keys, kb):
+        ap = T["t%s%d" % (kind, t)][:, own + c0:own + c1]
+        sem = T.sem["a%s%d" % (kind, t)]
+        ncalls[(kind, t)] = ncalls.get((kind, t), 0) + 1
+
+        def fn():
+            g.remote_dma_fused([RemoteDMATransfer(dst_ids=ids, dma_engine_mask=mask, remote_sem=sem, srcs=[ap], dsts=[ap] * len(ids))],
+                               local_sem=T.sem.sent)
+        node("g", 600.0, fn, keys, [("wire", kind, t, c0)], kind="r", name="send")
+        node("link", 500.0 + kb * 3 * PRM["link"], None, [("wire", kind, t, c0)], [("land", kind, t, c0)], lat=PRM["lat"], kind="l")
+        return ("land", kind, t, c0)
+
+    def arrive(kind, t, lands):
+        node("arr", 0.0, (kind, t), lands, [("arr", kind, t)], kind="a")
+
+    allx = lambda t: [("tx", t, j) for j in range(NCH)]
+    allu = lambda t: [("tu", t, j) for j in range(NCH)]
+    dma("sp", T.tx0[:, own:own + V], T.x0[:], 128, [], allx(0))
+    dma("act", T.tu0[:, own:own + V], T.u0[:], 256, [], allu(0))
+    dma("sp", T.si[:], T.s0[:], 256, [], ["si"])
+    dma("act", T.jt[:], T.ax[:], 512, [], ["jt"])
+    dma("sp", T.ab[:], T.ag[:], 128, [], ["ab"])
+    dma("sp", T.pi[:], T.p0[:], 256, [], ["pi"])
+    dma("sp", T.ww0[:], T.w0[:], 128, [], [("ww", 0, 0), ("ww", 0, 1)])
+    dma("sp", T.ti[:, 0:2], T.th[:], 1, [], ["ti"])
+    arrive("x", 0, [send("x", 0, 0, V, allx(0), 128)])
+    arrive("u", 0, [send("u", 0, 0, V, allu(0), 256)])
+
+    def iota(out, pat, base, cm, n, key, small=True):
+        if small:
+            node("g", 130 + 2 * n * CY, lambda: g.iota(out, pat, base, cm, allow_small_or_imprecise_dtypes=True), [], [key])
+        else:
+            node("g", 130 + 2 * n * CY, lambda: g.iota(out, pat, base, cm), [], [key])
+    iota(T.ia[:], [[-1, 16]], 16, 1, 16, "ia", False)
+    iota(T.ci[:], [[1, 144]], 0, 0, 144, "ci")
+    iota(T.cm[:], [[0, 8], [1, 16]], 0, 0, 128, "cm")
+    iota(T.cb[:], [[16, 8], [0, 16]], 16, 0, 128, "cb")
+    ts(T.ib[:], T.ia[:], 15, None, A.bitwise_and, None, 16, 1, ["ia"], ["ib"])
+    ts(T.ic[:], T.ia[:], 240, None, A.bitwise_and, None, 16, 1, ["ia"], ["ic"])
+    cp(T.fa[:], T.ib[:], 16, 1, ["ib"], ["fa"])
+    cp(T.col[:], T.ic[:], 16, 1, ["ic"], ["col"])
+    p16, pb16 = T.fa[:, 0:1], T.col[:, 0:1]
+    ts(T.ks[:], T.fa[:], pb16, -16.0, A.add, A.add, 16, 1, ["fa", "col"], ["ks"])
+    ts(T.mk[:], T.fa[:], 0.0, None, A.is_equal, None, 16, 1, ["fa"], ["mk"])
+    ts(T.mk16[:], T.fa[:], 0.0, 16.0, A.is_equal, A.mult, 16, 1, ["fa"], ["mk16"])
+    ts(T.tmp[:, 0:16], T.ci[:, 0:16], p16, 16.0, A.add, A.is_ge, 16, 1, ["ci", "fa"], ["tmp"])
+    ts(T.tb[:], T.tmp[:, 0:16], -0.5, None, A.add, None, 16, 1, ["tmp"], ["tb"])
+    ts(T.bo[:], T.cb[:], pb16, None, A.is_equal, None, 128, .5, ["cb", "col"], ["bo"])
+    ts(T.ee[:], T.ci[:], pb16, None, A.is_equal, None, 144, .5, ["ci", "col"], ["ee"])
+    cI = T.ci[:, 0:128]
+    k0 = T.ks[:, 0:1]
+    for k, s in enumerate(SCALES):
+        if s == 1.0 or CFG["sid"] == "v":
+            ts(sid(s), cI, k0, s, A.is_equal, A.mult, 128, .5, ["ci", "ks"], [("sid", s)])
+        else:
+            act(sid(s), sid(1.0), F.Identity, 128, [("sid", 1.0)], [("sid", s)], scale=s)
+    ts(T.ih[:], cI, k0, None, A.is_equal, None, 128, .5, ["ci", "ks"], ["ih"])
+    ts(T.i1[:], cI, k0, None, A.is_equal, None, 128, 1, ["ci", "ks"], ["i1"])
+    ts(T.ik[:], cI, k0, 1024.0, A.is_equal, A.mult, 128, 1, ["ci", "ks"], ["ik"])
+    ts(T.kd[:], cI, k0, p16, A.is_equal, A.mult, 128, .5, ["ci", "ks", "fa"], ["kd"])
+    ts(T.nm[:], T.cm[:], p16, None, A.is_equal, None, 128, .5, ["cm", "fa"], ["nm"])
+    ts(T.rr[:, 0:128], cI, k0, 32.0, A.is_equal, A.mult, 128, .5, ["ci", "ks"], [("rr", 0)])
+    tt(T.n32[:], T.nm[:], T.rr[:, 0:128], A.add, 128, 2, ["nm", ("rr", 0)], ["n32"])
+    for k in range(16):
+        ts(blk(T.ff, k), T.bo[:], T.mk[:, k:k + 1], None, A.mult, None, 128, .5, ["bo", "mk"], [("ff", k)])
+        act(blk(T.dg, k), sid(1.0), F.Identity, 128, [("sid", 1.0), "mk16"], [("dg", k)], scale=T.mk16[:, k:k + 1])
+    sh = T.sh[:, 128:2048]
+    node("g", 130 + 2 * 1920 * CY, lambda: g.iota(sh, [[0, 1920]], 0, 0, allow_small_or_imprecise_dtypes=True), [("wire", "u", 0, 0)], ["sh"])
+    for pat, op, fill, base, cm in (([[-1, 15], [-16, 8], [-1, 16]], A.not_equal, 1.0, -1, 1), ([[-1, 15], [-16, 8], [-1, 16]], A.not_equal, 1.0, 15, 1),
+                                    ([[0, 15], [-16, 8], [0, 16]], A.is_ge, 0.0, 0, 1), ([[0, 15], [16, 8], [0, 16]], A.is_ge, 0.0, 15, -1),
+                                    ([[0, 15], [-1, 128]], A.not_equal, -1.0, 0, 1)):
+        node("g", 170 + 2 * 1920 * CY, lambda pat=pat, op=op, fill=fill, base=base, cm=cm: g.affine_select(sh, sh, pat, op, fill, base, cm), ["sh"], ["sh"])
+    dve(HW, .5, lambda: ve.memset(T.ones[:], 1.0), [], ["ones"])
+    dve(1024, .5, lambda: ve.memset(T.msk[:], 1.0), [], ["msk0"])
+    dve(64, 1, lambda: ve.memset(T.msk[:, 0:1024:16], 0.0), ["msk0"], ["msk"])
+    ts(T.thf[:, 0:1], T.ti[:, 0:1], -1.0, 128.5, A.mult, A.add, 1, 1, ["ti"], ["thq"])
+    ts(T.thf[:, 1:2], T.ti[:, 1:2], -1.0, 0.5, A.mult, A.add, 1, 1, ["ti"], ["thb"])
+
+    hs = lambda h: slice(h * HW, (h + 1) * HW)
+    lo, hi = slice(0, HW), slice(HW, 2 * HW)
+
+    def weights(b, h):
+        s = hs(h)
+        acc(T.m1[:, lo], [(sid(1.0), T["bb%d" % b][:, s], 1), (sid(-1.5), T["la%d" % b][:, s], 1), (sid(2.5), T.ones[:], 1)],
+            HW, [("bb", b, h), ("la", b, h), "ones", ("sid", 1.0), ("sid", -1.5), ("sid", 2.5)], ["m1lo"], "m1", "m")
+        tt(T["wt%d" % b][:, s], T["ww%d" % b][:, s], T.m1[:, lo], A.mult, HW, 1, [("ww", b, h), "m1lo"], [("wt", b, h)], ["m1"], "w")
+
+    def jump(off, offkey, base, basekeys, bank, engines):
+        ps = T[bank]
+        for j in range(NCH):
+            dst, src = T["mn%d" % j][:], T.jt[:].indirect(off[:, j * CW:(j + 1) * CW])
+            wk = [("mn", j, r) for r in range(4)]
+            if engines[j] == "v":
+                cp(dst, src, 16 * CW, GC, ["jt", offkey], wk, name="jg")
+            else:
+                act(dst, src, F.Copy, 16 * CW, ["jt", offkey], wk, cyc=GC, name="jg")
+            acc(ps[:, j * CW:(j + 1) * CW], [(blk(T.dg, k), T["mn%d" % j][:, k:16 * CW:16], 1) for k in range(16)] + [(T.kd[:], T.ones[:, 0:CW], 1)],
+                CW, wk + [("dg", k) for k in range(16)] + ["kd", "ones"], [bank + ("lo" if j < 2 else "hi")], bank, "jd")
+        pk = [bank + "lo", bank + "hi"]
+        tt(T.tmp[:], base, ps[:], A.add, V, 1, basekeys + pk, ["tmp"], [bank], "j1")
+        ts(T.tm2[:], T.tmp[:], float(NR * V), -float(NR * V), A.is_ge, A.mult, V, 1, ["tmp"], ["tm2"], name="j2")
+        tt(ps[:], T.tm2[:], ps[:], A.add, V, 1, ["tm2"] + pk, pk, [bank], "j3")
+
+    both = lambda n, b: [(n, b, 0), (n, b, 1)]
+    cp(T.offs[:], T.si[:], V, 1, ["si"], ["offs"])
+    act(T.bb0[:], T.ab[:], F.Identity, V, ["ab"], both("bb", 0), scale=-1.0, bias=3.0)
+    act(T.la0[:], T.ab[:], F.Sign, V, ["ab"], both("la", 0), scale=-1.0, bias=2.5)
+    ts(T.live[:], T.ab[:], 2.5, None, A.is_lt, None, V, .5, ["ab"], ["live"])
+    act(T.dead[:], T.ab[:], F.Relu, V, ["ab"], ["dead"], bias=-2.0)
+    cp(T.ub[:], T.pi[:], V, 1, ["pi"], ["ub"], ["ub"])
+    tt(T.ub[:], T.ub[:], T.si[:], A.subtract, V, 1, ["ub", "si"], ["ub"], ["ub"])
+    tt(T.ub[:], T.ub[:], T.live[:], A.mult, V, 1, ["ub", "live"], ["ub"], ["ub"])
+    tt(T.cc0[:], T.ub[:], T.si[:], A.add, V, 1, ["si", "ub"], both("cc", 0), ["ub"])
+    cp(T.off0[:], T.cc0[:], V, 1, both("cc", 0), both("off", 0))
+    act(T.le[:], T.ub[:], F.Copy, V, ["ub"], ["le"], ["ub"])
+    weights(0, 0)
+    weights(0, 1)
+    jump(T.offs, "offs", T.si[:], ["si"], "m0", CFG["j0"])
+    m0k, m1k = ["m0lo", "m0hi"], ["m1lo", "m1hi"]
+    tt(T.m1[:], T.m0[:], T.dead[:], A.mult, V, 1, m0k + ["dead"], m1k, ["m0", "m1"])
+    tt(T.n1[:], T.m1[:], T.cc0[:], A.add, V, 1, both("cc", 0) + m1k, ["n1"], ["m1"])
+    cp(T.offn[:], T.n1[:], V, 1, ["n1"], ["offn"])
+    tt(T.dd0[:], T.m1[:], T.le[:], A.subtract, V, 1, m1k + ["le"], both("dd", 0), ["m1"])
+    tt(T.g2[:], T.m0[:], T.dd0[:], A.subtract, V, 1, m0k + both("dd", 0), ["g2"], ["m0"])
+
+    def second_jump():
+        jump(T.offn, "offn", T.n1[:], ["n1"], "m1", CFG["j1"])
+        tt(T.g1[:], T.m1[:], T.dd0[:], A.subtract, V, 1, m1k + both("dd", 0), ["g1"], ["m1"])
+
+    turn = [0]
+
+    gathered = set()
+
+    def chunk(t, j, what):
+        b, h, last = t % 2, j // 2, t == STEPS - 1
+        GW = CFG["gw"]
+        tx, tu, off = T["tx%d" % t], T["tu%d" % t], T["off%d" % t]
+        xc, uc, mn, px = T["xc%d" % j], T["uc%d" % j], T["mn%d" % j], T["px%d" % j]
+        pu, sc = T["pu%d" % (j % 2)], T["sc%d" % (j % 2)]
+        cs = slice(j * CW, (j + 1) * CW)
+        os_ = slice(own + j * CW, own + (j + 1) * CW)
+        ng = CW // GW
+        for nm, tab, dst, al in (("x", tx, xc, allx), ("u", tu, uc, allu)):
+            if (nm, t, j) in gathered or nm not in what.replace("c", "x").lower():
+                continue
+            gathered.add((nm, t, j))
+            for q in range(ng):
+                o_, i_ = dst[:, q * 16 * GW:(q + 1) * 16 * GW], tab[:].indirect(off[:, j * CW + q * GW:j * CW + (q + 1) * GW])
+                rk, wk = al(t) + [("arr", nm, t), ("off", t, h)], [(nm + "c", j, q)]
+                if "%d%s%d%d" % (t, nm, j, q) in CFG["gv"]:
+                    cp(o_, i_, 16 * GW, GC, rk, wk, name="g" + nm)
+                else:
+                    act(o_, i_, F.Copy, 16 * GW, rk, wk, cyc=GC, name="g" + nm)
+        if what in ("X", "U", "XU"):
+            return
+        xk, uk = [("xc", j, q) for q in range(ng)], [("uc", j, q) for q in range(ng)]
+        for r in range(4 if what != "c" else 0):
+            bank = "w%db" % (turn[0] % 2)
+            turn[0] += 1
+            ps = T[bank]
+            mm([(ps[:, m:512:4], blk(T.ff, r + 4 * m), T["wt%d" % b][:, cs], True, True, CW) for m in range(4)],
+               [("wt", b, h)] + [("ff", r + 4 * m) for m in range(4)], [bank], bank, "wrep")
+            if "x" in what:
+                tt(px[:, r * 512:(r + 1) * 512], xc[:, r:2048:4], ps[:], A.mult, 512, 1, xk + [bank], [("px", j, r)], [bank], "xm")
+            if "u" in what:
+                tt(pu[:, r:2048:4], uc[:, r:2048:4], ps[:], A.mult, 512, 1, uk + [bank], [("pu", j % 2, r)], [bank], "um")
+        if "x" in what:
+            acc(T.hb[:, 0:CW], [(T.ih[:], px[:, (k % 4) * 512 + k // 4:(k % 4 + 1) * 512:4], 1) for k in range(16)], CW,
+                [("px", j, r) for r in range(4)] + ["ih"], ["hb"], "hb", "h")
+            act(T.yy[:, cs], T.hb[:, 0:CW], F.Identity, CW, ["hb"], [("yy", j)], ["hb"], scale=1.0 / 256, bias=160.0 - 255.0 / 512, name="y")
+            nx = T.xo[:, cs] if last else T["tx%d" % (t + 1)][:, os_]
+            ts(nx, T.yy[:, cs], -160.0, 15.0, A.add, A.min, CW, .5, [("yy", j)], [("tx", t + 1, j)], name="X")
+        if "u" in what:
+            pk = [("pu", j % 2, r) for r in range(4)]
+            if j not in CFG["pesum"][t]:
+                for q in range(2):
+                    s = slice(q * 1024, (q + 1) * 1024)
+                    dve(1024, 1, lambda s=s: ve.tensor_tensor_scan(sc[:, s], T.msk[:], pu[:, s], 0.0, A.mult, A.add), pk + ["msk"], [("sc", j % 2, q)], name="scan")
+                terms, rk = [(T.i1[:], sc[:, 15:2048:16], 4)], [("sc", j % 2, 0), ("sc", j % 2, 1)]
+            if j in CFG["pesum"][t]:
+                mm([(T.ub[:, 0:CW], T.ik[:], tu[:, os_], True, False, 4 * CW), (T.ub[:, 0:CW], sid(128.0), tx[:, os_], False, False, CW)],
+                   [("tu", t, j), ("tx", t, j), "ik", ("sid", 128.0)], [("ub", -1)], "ub", "arg")
+                for k in range(0, 16, 2):
+                    ks = [(k + i) // 4 + 4 * ((k + i) % 4) for i in range(2)]
+                    mm([(T.ub[:, 0:CW], T.i1[:], pu[:, q:2048:16], False, q == 15, 4 * CW) for q in ks],
+                       [pk[k // 4], "i1"], ["ub"] if k == 14 else [("ub", k)], "ub", "sum")
+            else:
+                acc(T.ub[:, 0:CW], [(T.ik[:], tu[:, os_], 4), (sid(128.0), tx[:, os_], 1)] + terms, CW,
+                    rk + [("tu", t, j), ("tx", t, j), "i1", "ik", ("sid", 128.0)], ["ub"], "ub", "arg")
+            nu = T.uo[:, cs] if last else T["tu%d" % (t + 1)][:, os_]
+            act(nu, T.ub[:, 0:CW], F.Tanh, CW, ["ub"], [("tu", t + 1, j)], ["ub"], scale=2.0 ** -11, bias=-0.5, name="tanh")
+            if last:
+                dma("sp", T.yu[:, cs], nu, 64, [("tu", t + 1, j)], [])
+        if what != "c":
+            return
+        mm([(T.xb[:, m:512:4], sid(1.0), tx[:, os_], True, True, CW) for m in range(4)], [("tx", t, j), ("sid", 1.0)], ["xb"], "xb", "xrep")
+        for r in range(4):
+            tt(mn[:, r * 512:(r + 1) * 512], xc[:, r:2048:4], T.xb[:], A.min, 512, 1, xk + ["xb"], [("mn", j, r)], ["xb"], "min")
+        acc(T.cbk[:, (j % 2) * CW:(j % 2 + 1) * CW],
+            [(sid(128.0), T["la%d" % b][:, cs], 1)] +
+            [(T.ee[:, 16 - k:144 - k], mn[:, (k % 4) * 512 + k // 4:(k % 4 + 1) * 512:4], 1) for k in range(16)], CW,
+            [("mn", j, r) for r in range(4)] + ["ee", ("la", b, h), ("sid", 128.0)], [("cbk", j % 2)], "cbk", "c")
+
+    def slots(t, h):
+        b, n, last = t % 2, 1 - t % 2, t == STEPS - 1
+        s = hs(h)
+        la, bb, ww, cc, dd, ga, sg = (T["la%d" % b][:, s], T["bb%d" % b][:, s], T["ww%d" % b][:, s], T["cc%d" % b][:, s],
+                                      T["dd%d" % b][:, s], T["ga%d" % b][:, s], T["sg%d" % h])
+        ck = [("cbk", 0), ("cbk", 1)]
+        act(T.ck[:, s], T.cbk[:, lo], F.Identity, HW, ck, [("ck", h)], ["cbk"], bias=-128.0, name="ck")
+        act(T.ph[:, s], T.cbk[:, lo], F.Sign, HW, ck + ["thq"], [("ph", h)], ["cbk"], bias=T.thf[:, 0:1], name="ph")
+        nx = T.xo[:, s] if last else T["tx%d" % (t + 1)][:, own + h * HW:own + (h + 1) * HW]
+        for q in range(4):
+            bank = "m%d" % (q % 2)
+            mm([(T[bank][:, sl], blk(T.sh, 1 + 2 * q + i), T.ck[:, s], True, True, HW) for i, sl in enumerate((lo, hi))],
+               [("ck", h), "sh"], [bank + "lo", bank + "hi"], bank, "diff")
+            for i, sl in enumerate((lo, hi)):
+                sn = 1 + 2 * q + i
+                act(sg[:, (sn - 1) * HW:sn * HW], T[bank][:, sl], F.Sign, HW, [bank + ("lo", "hi")[i], "tb"], [("sg", h, sn)], [bank],
+                    bias=T.tb[:, sn:sn + 1], name="sgn")
+        acc(T.m0[:, hi], [(T.bo[:], nx, 1)], HW, [("tx", t + 1, 2 * h), ("tx", t + 1, 2 * h + 1), "bo"], ["m0hi"], "m0", "E")
+        act(T.ss[:, s], T.m0[:, hi], F.Sign, HW, ["m0hi", "thb"], [("ss", h)], ["m0"], bias=T.thf[:, 1:2], name="ss")
+        acc(T.m1[:, lo], [(sid(64.0), la, 1)] + [(blk(T.sh, 16 - sn) if sn < 8 else sid(-1.0), sg[:, (sn - 1) * HW:sn * HW], 1) for sn in range(1, 9)] +
+            [(T.n32[:], T.ss[:, s], 1)], HW,
+            [("sg", h, sn) for sn in range(1, 9)] + [("ss", h), ("la", b, h), "sh", "n32", ("sid", 64.0), ("sid", -1.0)], ["m1lo"], "m1", "V")
+        act(ga, T.m1[:, lo], F.Sign, HW, ["m1lo"], [("ga", t, h)], ["m1"], bias=-104.0, name="ga")
+        base = [("bb", b, h), ("ga", t, h), ("ph", h), ("la", b, h)]
+        acc(T.m0[:, hi], [(sid(-2.0), bb, 1), (sid(1.0), T.ph[:, s], 1), (sid(1.0), la, 1), (sid(-3.0), ga, 1)], HW,
+            base + [("sid", x) for x in (-2.0, 1.0, -3.0)], ["m0hi"], "m0", "u")
+        acc(T.m0[:, lo], [(sid(2.0), bb, 1), (sid(4.0), T.ph[:, s], 1), (sid(-4.0), la, 1), (sid(-3.0), ga, 1)], HW,
+            base + [("sid", x) for x in (2.0, 4.0, -4.0, -3.0)], ["m0lo"], "m0", "t")
+        acc(T.m1[:, lo], [(sid(1.0), ww, 1), (sid(2.0), ga, 1)], HW, [("ww", b, h), ("ga", t, h), ("sid", 1.0), ("sid", 2.0)], ["m1lo"], "m1", "W")
+        act(T.m0[:, hi], T.m0[:, hi], F.Relu, HW, ["m0hi"], ["m0hi"], ["m0"], bias=-2.0, name="sw")
+        act(T["bb%d" % n][:, s], T.m0[:, lo], F.Relu, HW, ["m0lo"], [("bb", n, h)], ["m0"], scale=0.5, bias=-2.5, name="b")
+        if not last:
+            act(T["la%d" % n][:, s], T.m0[:, lo], F.Sign, HW, ["m0lo"], [("la", n, h)], ["m0"], scale=0.5, bias=-3.0, name="la")
+        nw = T["ww%d" % n][:, s]
+        if CFG["wv"]:
+            ts(nw, T.m1[:, lo], 2.0, 15.0, A.add, A.min, HW, 1, ["m1lo"], [("ww", n, h)], ["m1"], "W")
+        else:
+            act(T.rr[:, s], T.m1[:, lo], F.Relu, HW, ["m1lo"], [("rr", h)], ["m1"], scale=-1.0, bias=13.0, name="rr")
+            act(nw, T.rr[:, s], F.Identity, HW, [("rr", h)], [("ww", n, h)], scale=-1.0, bias=15.0, name="W")
+        tt(T.m0[:, lo], dd, T.m0[:, hi], A.mult, HW, 1, [("dd", b, h), "m0hi"], ["m0lo"], ["m0"], "dl")
+        tt(T["cc%d" % n][:, s], cc, T.m0[:, lo], A.add, HW, 1, [("cc", b, h), "m0lo"], [("cc", n, h)], ["m0"], "C")
+        if last:
+            acc(T.m1[:, hi], [(sid(1.0), nw, 1), (sid(-16.0), T["bb%d" % n][:, s], 1)], HW,
+                [("ww", n, h), ("bb", n, h), ("sid", 1.0), ("sid", -16.0)], ["m1hi"], "m1", "yw")
+            act(T.wo[:, s], T.m1[:, hi], F.Identity, HW, ["m1hi"], [("wo", h)], ["m1"], bias=48.0, name="yw")
+            dma("sp", T.yw[:, s], T.wo[:, s], 128, [("wo", h)], [])
+            dma("sp", T.yc[:, s], T["cc%d" % n][:, s], 128, [("cc", n, h)], [])
+            dma("g", T.yx[:, s], T.xo[:, s], 128, [("tx", t + 1, 2 * h), ("tx", t + 1, 2 * h + 1)], [])
+            return
+        cp(T["off%d" % (t + 1)][:, s], T["cc%d" % n][:, s], HW, 1, [("cc", n, h)], [("off", t + 1, h)], name="off")
+        tt(T.m0[:, hi], T.g2[:, s], T.m0[:, hi], A.mult, HW, 1, ["g2", "m0hi"], ["m0hi"], ["m0"], "d1")
+        tt(T["dd%d" % n][:, s], dd, T.m0[:, hi], A.add, HW, 1, [("dd", b, h), "m0hi"], [("dd", n, h)], ["m0"], "d2")
+        weights(n, h)
+
+    def captured(t, h):
+        b, n, s = t % 2, 1 - t % 2, hs(h)
+        nd = T["dd%d" % n][:, s]
+        acc(T.m1[:, hi], [(sid(0.5), T.ones[:], 1), (sid(0.5), T["ga%d" % b][:, s], 1)], HW, ["ones", ("ga", t, h), ("sid", 0.5)], ["m1hi"], "m1", "cap")
+        tt(T.m1[:, hi], T.g1[:, s], T.m1[:, hi], A.mult, HW, 1, ["g1", "m1hi"], ["m1hi"], ["m1"], "d3")
+        tt(nd, nd, T.m1[:, hi], A.add, HW, 1, [("dd", n, h), "m1hi"], [("dd", n, h)], ["m1"], "d4")
+
+    lands = {}
+    for part in CFG["order"].split():
+        if True:
+            t, what, j = int(part[0]), part[1:-1], int(part[-1])
+            if what == "s":
+                slots(t, j)
+            elif what == "d":
+                captured(t - 1, j)
+            elif what == "j":
+                second_jump()
+            else:
+                chunk(t, j, what)
+            for kind in "xu":
+                for grp in CFG["sends"]:
+                    if t < STEPS - 1 and kind in what and grp[-1] == j:
+                        ld = lands.setdefault((kind, t), [])
+                        ld.append(send(kind, t + 1, grp[0] * CW, (j + 1) * CW, [("t" + kind, t + 1, i) for i in grp],
+                                       (32 if kind == "x" else 64) * len(grp)))
+                        if len(ld) == len(CFG["sends"]):
+                            arrive(kind, t + 1, ld)
+    return nodes, ncalls, neng
+
+
+def emit(g, T, nodes, order, ncalls, neng):
+    Q = {"g": g, "pe": g.tensor, "dve": g.vector, "act": g.scalar, "sp": g.sync}
+    real = lambda x: x["kind"] in "cdr"
+    pos, clock, cnt = {}, {e: {} for e in Q}, {e: 0 for e in Q}
+    done, waits, need = {}, {}, set()
+    for i in order:
+        x = nodes[i]
+        if x["kind"] == "a":
+            done[i] = {("a",) + x["fn"]: 1}
+            pos[i] = (("a",) + x["fn"], 1)
+            continue
+        if not real(x):
+            continue
+        ck = clock[x["eng"]]
+        ws = []
+        for d in sorted(x["hard"], key=lambda d: -nodes[d]["st"]):
+            if nodes[d]["kind"] == "r":
+                continue
+            k, v = pos[d]
+            if ck.get(k, 0) >= v:
+                continue
+            ws.append(d)
+            need.add(d)
+            for kk, vv in done[d].items():
+                if ck.get(kk, 0) < vv:
+                    ck[kk] = vv
+        waits[i] = ws
+        if x["kind"] == "c":
+            cnt[x["eng"]] += 1
+            pos[i] = (x["eng"], cnt[x["eng"]])
+        else:
+            pos[i] = (("d", i), 1)
+        done[i] = dict(ck)
+        done[i][pos[i][0]] = pos[i][1]
+    sem, val, nd, nsent = {}, {e: 0 for e in Q}, 0, 0
+    tail = []
+    for i in order:
+        x = nodes[i]
+        if x["kind"] == "a":
+            sem[i] = (T.sem["a%s%d" % x["fn"]], ncalls[x["fn"]] * neng * (NR - 1))
+            continue
+        if not real(x):
+            continue
+        q = Q[x["eng"]]
+        for d in waits[i]:
+            q.wait_ge(sem[d][0], sem[d][1])
+        ins = x["fn"]()
+        if x["kind"] == "r":
+            nsent += neng
+        elif x["kind"] == "d":
+            sem[i] = (T.sem["d%d" % nd], 16)
+            nd += 1
+            ins.then_inc(sem[i][0], 16)
+            if i not in need:
+                tail.append((q, sem[i]))
+        elif i in need:
+            val[x["eng"]] += 1
+            sem[i] = (T.sem["q_" + x["eng"]], val[x["eng"]])
+            ins.then_inc(sem[i][0], 1)
+    g.wait_ge(T.sem.sent, nsent)
+    for q, s in tail:
+        q.wait_ge(s[0], s[1])
+
+
+def rank_program(g, core, T, topo):
+    if T.rank_of(core) is None:
+        return
+    emit(g, T, *plan(g, core, T, topo))

@@ -8,17 +8,19 @@ CW, NCH = 128, 4
 HW = 256
 CFG = {
     "sends": [[0], [1], [2], [3]],
-    "gv": "",
+    "gv": "1x01 2x01 2u01 1u01",
     "gw": 64,
-    "pesum": [(), (), ()],
+    "pesum": [(0,), (0,), (0,)],
     "j0": "avav", "j1": "aaaa",
-    "order": "0X0 0X1 0x0 0c0 0X2 0U0 0x1 0c1 0U1 0u0 0U2 0u1 0XU3 0s0 0xu2 0xu3 0c2 0c3 1XU0 0s1 "
-             "1XU1 1xu0 0j0 1XU2 1xu1 1c0 1c1 1d0 1XU3 1xu2 1s0 1xu3 1c2 1c3 2XU0 1d1 1s1 "
-             "2XU1 2xu0 2c0 2X2 2xu1 2c1 2X3 2d0 2s0 2c2 2U2 2x2 2c3 2U3 2x3 2d1 2s1 2u2 2u3",
-    "sid": "a", "wv": True,
-    "seed": 0, "noise": 700.0, "rounds": 160, "mix": 0.0,
+    "order": "0X0 0X1 0x0 0c0 0X2 0U0 0c1 0U1 0u0 0U2 0xu1 0XU3 0s0 0xu2 0xu3 0c2 0c3 1XU0 0j0 0s1 "
+             "1XU1 1xu0 1XU2 1xu1 1c0 1c1 1d0 1XU3 1xu2 1s0 1xu3 1c2 1c3 2XU0 1d1 1s1 "
+             "2XU1 2xu0 2c0 2X2 2xu1 2c1 2X3 2d0 2s0 2c2 2U2 2xu2 2c3 2U3 2x3 2d1 2s1 2u3",
+    "fold": [(0, 1, 2), (0, 1, 2), (0, 1, 2)],
+    "cut": 128, "relay": "u0 u1 u2",
+    "sid": "v", "wv": True, "hbank": "cbk",
+    "seed": 0, "noise": 1500.0, "rounds": 550, "window": 15000.0, "wbanks": 2, "mix": 0.0,
 }
-PRM = {"cy": 1.0, "pe": 0.55, "gc": 1.56, "link": 16.0, "lat": 2500.0, "sync": 120.0}
+PRM = {"cy": 0.88, "pe": 0.44, "gc": 1.56, "link": 13.0, "lat": 2500.0, "sync": 80.0, "fx": 30.0, "fold": 6000.0}
 
 bf, f32, f16, i32, u16 = "bfloat16", "float32", "float16", "int32", "uint16"
 SCRATCH = {}
@@ -39,7 +41,7 @@ for _j in range(NCH):
     _buf("px%d" % _j, 16 * CW, f16)
 for _j in range(2):
     _buf("pu%d" % _j, 16 * CW, f32)
-    _buf("sc%d" % _j, 16 * CW, f32)
+    _buf(("sc", "pu2")[_j], 16 * CW, f32)
     _buf("sg%d" % _j, 8 * HW, bf)
     for _n in ("bb", "la", "ww", "wt", "ga"):
         _buf("%s%d" % (_n, _j), V, bf)
@@ -49,7 +51,7 @@ for _n, _c, _d in [
         ("jt", NR * V, bf), ("si", V, i32), ("pi", V, i32), ("ab", V, bf), ("ti", 4, i32),
         ("offs", V, u16), ("offn", V, u16), ("le", V, f32), ("n1", V, f32), ("g1", V, f32), ("g2", V, f32),
         ("tmp", V, f32), ("tm2", V, f32), ("live", V, bf), ("dead", V, bf), ("yy", V, bf), ("xo", V, bf), ("uo", V, f32), ("wo", V, f32),
-        ("ck", V, bf), ("ph", V, bf), ("ss", V, bf), ("rr", V, bf), ("ones", HW, bf), ("msk", 1024, bf), ("thf", 4, f32),
+        ("ck", V, bf), ("ph", V, bf), ("ss", V, bf), ("rr", V, bf), ("ones", HW, bf), ("msk", 1024, bf), ("msk8", 1024, bf), ("thf", 4, f32),
         ("ci", 144, bf), ("cm", 128, bf), ("cb", 128, bf), ("ia", 16, i32), ("ib", 16, i32), ("ic", 16, i32), ("fa", 16, f32), ("ks", 16, f32),
         ("mk", 16, f32), ("mk16", 16, f32), ("tb", 16, f32), ("col", 16, f32),
         ("bo", 128, bf), ("ee", 144, bf), ("ff", 2048, bf), ("dg", 2048, bf), ("sh", 2048, bf), ("n32", 128, bf), ("nm", 128, bf),
@@ -60,12 +62,14 @@ for _n in ("w0b", "w1b", "xb", "cbk", "hb", "ub", "m0", "m1"):
 SCALES = [1.0, -1.0, 128.0, 64.0, 2.0, -2.0, -3.0, 4.0, -4.0, 0.5, -1.5, -16.0, 2.5]
 
 ENG = ("g", "pe", "dve", "act", "sp")
-NDMA = 24
-SEMAPHORES = ["q_" + e for e in ENG] + ["d%d" % i for i in range(NDMA)] + ["sent"] + \
+NDMA = 32
+SEMAPHORES = ["q_" + e for e in ENG] + ["d%d" % i for i in range(NDMA)] + ["sent"] + ["h%d" % i for i in range(12)] + \
              ["ax%d" % t for t in range(STEPS)] + ["au%d" % t for t in range(STEPS)]
 
 
-SPREAD = [{}, {"gc": 1.15, "link": 10.0}, {"gc": 2.0, "link": 24.0, "lat": 3500.0}, {"pe": 0.45, "sync": 250.0}, {"pe": 0.7, "cy": 0.9, "link": 22.0}]
+SPREAD = [{}, {"gc": 1.15, "link": 10.0, "cy": 0.83, "pe": 0.42}, {"gc": 2.0, "link": 20.0, "lat": 3500.0, "cy": 1.1, "pe": 0.55},
+          {"sync": 200.0, "fx": 60.0, "link": 30.0, "lat": 4500.0}, {"cy": 1.2, "pe": 0.7, "gc": 1.3}, {"link": 35.0, "lat": 3500.0, "fold": 9000.0},
+          {"pe": 0.8, "cy": 0.95}]
 KEPT = {}
 
 
@@ -109,11 +113,14 @@ def order_nodes(nodes, others):
     z = CFG["seed"]
     best = None
     for rnd in range(CFG["rounds"]):
-        if rnd % 4 == 0 and best is not None:
+        if rnd % 2 == 0 and rnd >= 8:
             pr = [-s for s in best[1]]
+            z = (z * 1103515245 + 12345) % 2147483648
+            t0 = (max(best[1]) + 10000.0) * z / 2147483648 - 10000.0
             for i in range(n):
-                z = (z * 1103515245 + 12345) % 2147483648
-                pr[i] += CFG["noise"] * (1 + rnd // 4 % 3) * z / 2147483648
+                if t0 < best[1][i] < t0 + CFG["window"]:
+                    z = (z * 1103515245 + 12345) % 2147483648
+                    pr[i] += CFG["noise"] * (1 + rnd // 2 % 4) * (z / 2147483648 - 0.5)
         st, seq = place(fwd, bwd, pr, [0.0] * n)
         at = {i: k for k, i in enumerate(seq)}
         order = sorted(range(n), key=lambda i: (st[i], at[i]))
@@ -146,6 +153,37 @@ def plan(g, core, T, topo):
     for x, s in zip(nodes, KEPT["st"]):
         x["st"] = s
     return nodes, KEPT["order"], ncalls, neng
+
+
+def relayed():
+    out = [("u", 0, CFG["cut"], V)]
+    for t in range(1, STEPS):
+        out += [(k[0], t, int(k[1]) * CW, (int(k[1]) + 1) * CW) for k in CFG["relay"].split()]
+    return out
+
+
+def helper_of(core, T, topo):
+    return [c for c in topo.cores_of(core) if topo.die(c) != topo.die(core) and T.rank_of(c) is None
+            and all(topo.may_write(c, p) for p in T.cores)][0]
+
+
+def way_out(src, rank, T, topo):
+    peers = [T.cores[(rank + d) % NR] for d in range(1, NR)]
+    mask = topo.mask(src, peers[0])
+    for p in peers:
+        mask &= topo.mask(src, p)
+    return mask, [DstId(rid=topo.addr(p)[0], pnc=topo.addr(p)[1]) for p in peers]
+
+
+def hand_on(g, core, rank, T, topo):
+    mask, ids = way_out(core, rank, T, topo)
+    neng = bin(mask).count("1")
+    for k, (kind, t, c0, c1) in enumerate(relayed()):
+        ap = T["t%s%d" % (kind, t)][:, rank * V + c0:rank * V + c1]
+        g.wait_ge(T.sem["h%d" % k], neng)
+        g.remote_dma_fused([RemoteDMATransfer(dst_ids=ids, dma_engine_mask=mask, remote_sem=T.sem["a%s%d" % (kind, t)], srcs=[ap], dsts=[ap] * len(ids))],
+                           local_sem=T.sem.sent)
+    g.wait_ge(T.sem.sent, neng * len(relayed()))
 
 
 def build(g, core, T, topo, PRM):
@@ -185,10 +223,10 @@ def build(g, core, T, topo, PRM):
         return i
 
     def dve(n, cyc, fn, r, w, banks=(), name=""):
-        node("dve", 60 + max(64, n * cyc) * CY, fn, r, w, banks, name=name)
+        node("dve", PRM["fx"] + max(64, n * cyc) * CY, fn, r, w, banks, name=name)
 
     def act(out, in_, func, n, r, w, banks=(), cyc=1.0, name="", **kw):
-        node("act", 70 + max(64, n * cyc) * CY, lambda: ac.activation(out, in_, func, **kw), r, w, banks, name=name)
+        node("act", PRM["fx"] + 15 + max(64, n * cyc) * CY, lambda: ac.activation(out, in_, func, **kw), r, w, banks, name=name)
 
     def tt(out, a, b, op, n, cyc, r, w, banks=(), name=""):
         dve(n, cyc, lambda: ve.tensor_tensor(out, a, b, op), r, w, banks, name)
@@ -225,18 +263,24 @@ def build(g, core, T, topo, PRM):
         return t[:, 128 * k:128 * (k + 1)]
 
     own = rank * V
-    peers = [T.cores[(rank + d) % NR] for d in range(1, NR)]
-    mask = topo.mask(core, peers[0])
-    for p in peers:
-        mask &= topo.mask(core, p)
+    mask, ids = way_out(core, rank, T, topo)
     neng = bin(mask).count("1")
-    ids = [DstId(rid=topo.addr(p)[0], pnc=topo.addr(p)[1]) for p in peers]
+    aid = helper_of(core, T, topo)
+    near = topo.mask(core, aid) & ~mask
+    assert bin(near).count("1") == neng and bin(way_out(aid, rank, T, topo)[0]).count("1") == neng
     ncalls = {}
 
     def send(kind, t, c0, c1, keys, kb):
         ap = T["t%s%d" % (kind, t)][:, own + c0:own + c1]
         sem = T.sem["a%s%d" % (kind, t)]
         ncalls[(kind, t)] = ncalls.get((kind, t), 0) + 1
+        if (kind, t, c0, c1) in relayed():
+            hs_ = T.sem["h%d" % relayed().index((kind, t, c0, c1))]
+            node("g", 600.0, lambda: g.remote_dma(ap, ap, hs_, T.sem.sent, topo.addr(aid)[1], topo.addr(aid)[0], near),
+                 keys, [("wire", kind, t, c0), "turn"], kind="r", name="relay")
+            node("hop", 300.0 + kb * 8.0, None, [("wire", kind, t, c0)], [("hop", kind, t, c0)], lat=PRM["lat"] + 600.0, kind="l")
+            node("link2", 500.0 + kb * 3 * PRM["link"], None, [("hop", kind, t, c0)], [("land", kind, t, c0), "turn2"], lat=PRM["lat"], kind="l")
+            return ("land", kind, t, c0)
 
         def fn():
             g.remote_dma_fused([RemoteDMATransfer(dst_ids=ids, dma_engine_mask=mask, remote_sem=sem, srcs=[ap], dsts=[ap] * len(ids))],
@@ -259,7 +303,8 @@ def build(g, core, T, topo, PRM):
     dma("sp", T.ww0[:], T.w0[:], 128, [], [("ww", 0, 0), ("ww", 0, 1)])
     dma("sp", T.ti[:, 0:2], T.th[:], 1, [], ["ti"])
     arrive("x", 0, [send("x", 0, 0, V, allx(0), 128)])
-    arrive("u", 0, [send("u", 0, 0, V, allu(0), 256)])
+    cut = CFG["cut"]
+    arrive("u", 0, [send("u", 0, cut, V, allu(0), (V - cut) // 2), send("u", 0, 0, cut, allu(0), cut // 2)])
 
     def iota(out, pat, base, cm, n, key, small=True):
         if small:
@@ -308,6 +353,8 @@ def build(g, core, T, topo, PRM):
     dve(HW, .5, lambda: ve.memset(T.ones[:], 1.0), [], ["ones"])
     dve(1024, .5, lambda: ve.memset(T.msk[:], 1.0), [], ["msk0"])
     dve(64, 1, lambda: ve.memset(T.msk[:, 0:1024:16], 0.0), ["msk0"], ["msk"])
+    dve(1024, .5, lambda: ve.memset(T.msk8[:], 1.0), [], ["msk80"])
+    dve(128, 1, lambda: ve.memset(T.msk8[:, 0:1024:8], 0.0), ["msk80"], ["msk8"])
     ts(T.thf[:, 0:1], T.ti[:, 0:1], -1.0, 128.5, A.mult, A.add, 1, 1, ["ti"], ["thq"])
     ts(T.thf[:, 1:2], T.ti[:, 1:2], -1.0, 0.5, A.mult, A.add, 1, 1, ["ti"], ["thb"])
 
@@ -371,7 +418,8 @@ def build(g, core, T, topo, PRM):
         GW = CFG["gw"]
         tx, tu, off = T["tx%d" % t], T["tu%d" % t], T["off%d" % t]
         xc, uc, mn, px = T["xc%d" % j], T["uc%d" % j], T["mn%d" % j], T["px%d" % j]
-        pu, sc = T["pu%d" % (j % 2)], T["sc%d" % (j % 2)]
+        pu, sc = T["pu%d" % (j % 3)], T.sc
+        folded = j in CFG["fold"][t]
         cs = slice(j * CW, (j + 1) * CW)
         os_ = slice(own + j * CW, own + (j + 1) * CW)
         ng = CW // GW
@@ -390,7 +438,7 @@ def build(g, core, T, topo, PRM):
             return
         xk, uk = [("xc", j, q) for q in range(ng)], [("uc", j, q) for q in range(ng)]
         for r in range(4 if what != "c" else 0):
-            bank = "w%db" % (turn[0] % 2)
+            bank = ("w0b", "w1b", "hb")[turn[0] % CFG["wbanks"]]
             turn[0] += 1
             ps = T[bank]
             mm([(ps[:, m:512:4], blk(T.ff, r + 4 * m), T["wt%d" % b][:, cs], True, True, CW) for m in range(4)],
@@ -398,24 +446,39 @@ def build(g, core, T, topo, PRM):
             if "x" in what:
                 tt(px[:, r * 512:(r + 1) * 512], xc[:, r:2048:4], ps[:], A.mult, 512, 1, xk + [bank], [("px", j, r)], [bank], "xm")
             if "u" in what:
-                tt(pu[:, r:2048:4], uc[:, r:2048:4], ps[:], A.mult, 512, 1, uk + [bank], [("pu", j % 2, r)], [bank], "um")
+                po = pu[:, r // 2 * 1024 + r % 2:(r // 2 + 1) * 1024:2] if folded else pu[:, r:2048:4]
+                tt(po, uc[:, r:2048:4], ps[:], A.mult, 512, 1, uk + [bank], [("pu", j % 3, r)] + ([("pu", j % 3, "all")] if r == 0 else []), [bank], "um")
         if "x" in what:
-            acc(T.hb[:, 0:CW], [(T.ih[:], px[:, (k % 4) * 512 + k // 4:(k % 4 + 1) * 512:4], 1) for k in range(16)], CW,
-                [("px", j, r) for r in range(4)] + ["ih"], ["hb"], "hb", "h")
-            act(T.yy[:, cs], T.hb[:, 0:CW], F.Identity, CW, ["hb"], [("yy", j)], ["hb"], scale=1.0 / 256, bias=160.0 - 255.0 / 512, name="y")
+            hn = "hb" if CFG["wbanks"] == 2 else CFG["hbank"]
+            hp = T[hn][:, 3 * CW:4 * CW]
+            acc(hp, [(T.ih[:], px[:, (k % 4) * 512 + k // 4:(k % 4 + 1) * 512:4], 1) for k in range(16)], CW,
+                [("px", j, r) for r in range(4)] + ["ih"], ["hacc"], hn, "h")
+            act(T.yy[:, cs], hp, F.Identity, CW, ["hacc"], [("yy", j)], [hn], scale=1.0 / 256, bias=160.0 - 255.0 / 512, name="y")
             nx = T.xo[:, cs] if last else T["tx%d" % (t + 1)][:, os_]
             ts(nx, T.yy[:, cs], -160.0, 15.0, A.add, A.min, CW, .5, [("yy", j)], [("tx", t + 1, j)], name="X")
         if "u" in what:
-            pk = [("pu", j % 2, r) for r in range(4)]
-            if j not in CFG["pesum"][t]:
+            pk = [("pu", j % 3, r) for r in range(4)]
+            if folded:
+                node("g", 1000.0, lambda: g.dma_start(pu[:, 0:1024], pu[:, 1024:2048], accum_op=A.add), pk, pk[0:2],
+                     lat=PRM["fold"], kind="d", name="fold")
+            if j in CFG["pesum"][t]:
+                pass
+            elif folded:
+                s = slice(j % 2 * 1024, (j % 2 + 1) * 1024)
+                dve(1024, 1, lambda: ve.tensor_tensor_scan(sc[:, s], T.msk8[:], pu[:, 0:1024], 0.0, A.mult, A.add), pk + ["msk8"], [("sc", j % 2)], name="scan")
+                terms, rk = [(T.i1[:], sc[:, s.start + 7:s.stop:8], 4)], [("sc", j % 2)]
+            else:
                 for q in range(2):
                     s = slice(q * 1024, (q + 1) * 1024)
-                    dve(1024, 1, lambda s=s: ve.tensor_tensor_scan(sc[:, s], T.msk[:], pu[:, s], 0.0, A.mult, A.add), pk + ["msk"], [("sc", j % 2, q)], name="scan")
-                terms, rk = [(T.i1[:], sc[:, 15:2048:16], 4)], [("sc", j % 2, 0), ("sc", j % 2, 1)]
+                    dve(1024, 1, lambda s=s: ve.tensor_tensor_scan(sc[:, s], T.msk[:], pu[:, s], 0.0, A.mult, A.add), pk + ["msk"], [("sc", q)], name="scan")
+                terms, rk = [(T.i1[:], sc[:, 15:2048:16], 4)], [("sc", 0), ("sc", 1)]
             if j in CFG["pesum"][t]:
                 mm([(T.ub[:, 0:CW], T.ik[:], tu[:, os_], True, False, 4 * CW), (T.ub[:, 0:CW], sid(128.0), tx[:, os_], False, False, CW)],
                    [("tu", t, j), ("tx", t, j), "ik", ("sid", 128.0)], [("ub", -1)], "ub", "arg")
-                for k in range(0, 16, 2):
+                for k in range(0, 8 if folded else 0, 2):
+                    mm([(T.ub[:, 0:CW], T.i1[:], pu[:, q:1024:8], False, q == 7, 4 * CW) for q in (k, k + 1)],
+                       pk + ["i1"], ["ub"] if k == 6 else [("ub", k)], "ub", "sum")
+                for k in range(0, 0 if folded else 16, 2):
                     ks = [(k + i) // 4 + 4 * ((k + i) % 4) for i in range(2)]
                     mm([(T.ub[:, 0:CW], T.i1[:], pu[:, q:2048:16], False, q == 15, 4 * CW) for q in ks],
                        [pk[k // 4], "i1"], ["ub"] if k == 14 else [("ub", k)], "ub", "sum")
@@ -586,5 +649,8 @@ def emit(g, T, nodes, order, ncalls, neng):
 
 def rank_program(g, core, T, topo):
     if T.rank_of(core) is None:
+        for rank, c in enumerate(T.cores):
+            if helper_of(c, T, topo) == core:
+                hand_on(g, core, rank, T, topo)
         return
     emit(g, T, *plan(g, core, T, topo))

@@ -1,28 +1,30 @@
+import math
 from concourse.bass import DstId, RemoteDMATransfer
 from concourse.mybir import AluOpType, ActivationFunctionType
 
 A = AluOpType
 F = ActivationFunctionType
 V, NR, STEPS = 512, 4, 3
-CW, NCH = 128, 4
 HW = 256
+BL = 4 * HW
+QW = 128
+BIG = 4096.0
 CFG = {
-    "sends": [[0], [1], [2], [3]],
-    "gv": "1x01 2x01 2u01 1u01",
-    "gw": 64,
-    "pesum": [(0,), (0,), (0,)],
-    "j0": "avav", "j1": "aaaa",
-    "order": "0X0 0X1 0x0 0c0 0X2 0U0 0c1 0U1 0u0 0U2 0xu1 0XU3 0s0 0xu2 0xu3 0c2 0c3 1XU0 0j0 0s1 "
-             "1XU1 1xu0 1XU2 1xu1 1c0 1c1 1d0 1XU3 1xu2 1s0 1xu3 1c2 1c3 2XU0 1d1 1s1 "
-             "2XU1 2xu0 2c0 2X2 2xu1 2c1 2X3 2d0 2s0 2c2 2U2 2xu2 2c3 2U3 2x3 2d1 2s1 2u3",
-    "fold": [(0, 1, 2), (0, 1, 2), (0, 1, 2)],
-    "cut": 128, "relay": "u0 u1 u2",
-    "sid": "v", "wv": True, "hbank": "cbk",
-    "seed": 0, "noise": 1500.0, "rounds": 550, "window": 15000.0, "wbanks": 2, "mix": 0.0,
+    "min": "vv vv vv",
+    "jump": "aaaa aaaa aaaa aaaa",
+    "fin": "1ss hsss 1ss hsss 1ss hsss",
+    "pieces": "X02 x24 U02 u24",
+    "order": "0w0 0w1 0X0 0c0 0x0 0X1 0x1 0c1 0j0 0s0 0U0 0u0 1w0 0j1 0s1 0U1 0u1 1w1 "
+             "1X0 1c0 1x0 1X1 1x1 1c1 1j0 1s0 1U0 1u0 2w0 1j1 1s1 1U1 1u1 2w1 "
+             "2X0 2c0 2x0 2X1 2c1 2x1 2s0 2U0 2u0 2s1 2U1 2u1",
+    "cut": 128, "hbank": "ub",
+    "due": {"X": (0, 8), "x": (1, 9), "c": (2, 10), "w": (-15, -5), "s": (-5, -4), "U": (18, 23), "u": (0, 0), "j": (6, 14)},
+    "period": 29.0, "seed": 1, "rounds": 300, "temp": 200.0, "swaps": 40000, "heat": 500.0,
 }
-PRM = {"cy": 0.88, "pe": 0.44, "gc": 1.56, "link": 13.0, "lat": 2500.0, "sync": 80.0, "fx": 30.0, "fold": 6000.0}
+PRM = {"cy": 0.88, "pe": 0.44, "gc": 1.56, "link": 13.0, "lat": 2500.0, "sync": 80.0, "fx": 30.0, "dr": 3.0, "dl": 2000.0}
 
 bf, f32, f16, i32, u16 = "bfloat16", "float32", "float16", "int32", "uint16"
+ND = f16
 SCRATCH = {}
 
 
@@ -30,108 +32,71 @@ def _buf(name, cols, dt, where="sbuf"):
     SCRATCH[name] = (where, [128, cols], dt)
 
 
+SCALES = [1.0, -1.0, 256.0, 128.0, 2.0, 3.0, -3.0, -4.0, -1.5, -16.0, BIG, -BIG, -2 * BIG, BIG / 2, -BIG / 2, 1.5 * BIG]
 for _t in range(STEPS):
     _buf("tx%d" % _t, NR * V, bf)
     _buf("tu%d" % _t, NR * V, f32)
     _buf("off%d" % _t, V, u16)
-for _j in range(NCH):
-    _buf("xc%d" % _j, 16 * CW, bf)
-    _buf("uc%d" % _j, 16 * CW, f32)
-    _buf("mn%d" % _j, 16 * CW, bf)
-    _buf("px%d" % _j, 16 * CW, f16)
+    _buf("ga%d" % _t, V, bf)
 for _j in range(2):
-    _buf("pu%d" % _j, 16 * CW, f32)
-    _buf(("sc", "pu2")[_j], 16 * CW, f32)
+    _buf("xc%d" % _j, 4 * BL, bf)
+    _buf("mn%d" % _j, 4 * BL, bf)
+    _buf("px%d" % _j, 4 * BL, f16)
+    _buf("pu%d" % _j, 4 * BL, f32)
+    _buf("wp%d" % _j, BL, bf)
+    _buf("wr%d" % _j, 4 * BL, bf)
+    _buf("wr%d" % (2 + _j), 4 * BL, bf)
+    _buf("sc%d" % _j, BL, f32)
     _buf("sg%d" % _j, 8 * HW, bf)
-    for _n in ("bb", "la", "ww", "wt", "ga"):
+    for _n in ("bb", "lv", "ww"):
         _buf("%s%d" % (_n, _j), V, bf)
-    _buf("cc%d" % _j, V, f32)
-    _buf("dd%d" % _j, V, f32)
+    _buf("cc%d" % _j, V, ND)
+    _buf("q%d" % _j, V, ND)
 for _n, _c, _d in [
         ("jt", NR * V, bf), ("si", V, i32), ("pi", V, i32), ("ab", V, bf), ("ti", 4, i32),
-        ("offs", V, u16), ("offn", V, u16), ("le", V, f32), ("n1", V, f32), ("g1", V, f32), ("g2", V, f32),
-        ("tmp", V, f32), ("tm2", V, f32), ("live", V, bf), ("dead", V, bf), ("yy", V, bf), ("xo", V, bf), ("uo", V, f32), ("wo", V, f32),
-        ("ck", V, bf), ("ph", V, bf), ("ss", V, bf), ("rr", V, bf), ("ones", HW, bf), ("msk", 1024, bf), ("msk8", 1024, bf), ("thf", 4, f32),
-        ("ci", 144, bf), ("cm", 128, bf), ("cb", 128, bf), ("ia", 16, i32), ("ib", 16, i32), ("ic", 16, i32), ("fa", 16, f32), ("ks", 16, f32),
-        ("mk", 16, f32), ("mk16", 16, f32), ("tb", 16, f32), ("col", 16, f32),
-        ("bo", 128, bf), ("ee", 144, bf), ("ff", 2048, bf), ("dg", 2048, bf), ("sh", 2048, bf), ("n32", 128, bf), ("nm", 128, bf),
-        ("kd", 128, bf), ("ih", 128, f16), ("i1", 128, f32), ("ik", 128, f32), ("sid", 128 * 13, bf)]:
+        ("offs", V, u16), ("sf", V, ND), ("pf", V, ND), ("r1", V, ND), ("r2", V, ND), ("md", V, bf), ("nw", V, bf),
+        ("yy", V, bf), ("xo", V, bf), ("uo", V, f32), ("wo", V, f32), ("co", V, f32),
+        ("ck", V, bf), ("nq", V, bf), ("ss", V, bf), ("ones", HW, bf), ("msk", BL, bf), ("thf", 4, f32), ("thq", 8, bf),
+        ("ci", 144, bf), ("cm", 128, bf), ("cb", 128, bf), ("cg", 128, bf), ("ia", 16, i32), ("ib", 16, i32), ("ic", 16, i32), ("fa", 16, f32),
+        ("ks", 16, f32), ("mk16", 16, f32), ("tb", 16, f32), ("col", 16, f32), ("tmp", 16, f32), ("m4", 4, f32), ("k12", 4, f32),
+        ("bo", 128, bf), ("ee", 144, bf), ("ne", 144, bf), ("dg", 2048, bf), ("sh", 2048, bf), ("n32", 128, bf), ("nm", 128, bf),
+        ("kd", 128, bf), ("nih", 128, f16), ("ino", 128, ND), ("inn", 128, ND), ("ni1", 128, f32), ("ik", 128, f32), ("pw", 4 * 144, ND),
+        ("gm", 512, bf), ("sid", 128 * len(SCALES), bf)]:
     _buf(_n, _c, _d)
-for _n in ("w0b", "w1b", "xb", "cbk", "hb", "ub", "m0", "m1"):
+for _n in ("xb0", "xb1", "cbk", "ub", "m0", "m1", "m2", "m3"):
     _buf(_n, 512, f32, "psum")
-SCALES = [1.0, -1.0, 128.0, 64.0, 2.0, -2.0, -3.0, 4.0, -4.0, 0.5, -1.5, -16.0, 2.5]
 
 ENG = ("g", "pe", "dve", "act", "sp")
-NDMA = 32
-SEMAPHORES = ["q_" + e for e in ENG] + ["d%d" % i for i in range(NDMA)] + ["sent"] + ["h%d" % i for i in range(12)] + \
+NDMA = 72
+SEMAPHORES = ["q_" + e for e in ENG] + ["d%d" % i for i in range(NDMA)] + ["sent"] + ["h%d" % i for i in range(16)] + \
              ["ax%d" % t for t in range(STEPS)] + ["au%d" % t for t in range(STEPS)]
 
 
-SPREAD = [{}, {"gc": 1.15, "link": 10.0, "cy": 0.83, "pe": 0.42}, {"gc": 2.0, "link": 20.0, "lat": 3500.0, "cy": 1.1, "pe": 0.55},
-          {"sync": 200.0, "fx": 60.0, "link": 30.0, "lat": 4500.0}, {"cy": 1.2, "pe": 0.7, "gc": 1.3}, {"link": 35.0, "lat": 3500.0, "fold": 9000.0},
-          {"pe": 0.8, "cy": 0.95}]
+SPREAD = [{}, {"gc": 1.15, "link": 10.0, "cy": 0.83, "pe": 0.42}, {"gc": 1.9, "link": 20.0, "lat": 3500.0, "cy": 1.0, "pe": 0.7},
+          {"link": 25.0, "lat": 4000.0, "dr": 6.0, "dl": 3000.0, "sync": 150.0, "fx": 50.0}]
+WEIGHT = [3, 1, 1, 1]
 KEPT = {}
 
 
-def order_nodes(nodes, others):
-    n = len(nodes)
-    SYNC = PRM["sync"]
-    cost = [x["cost"] for x in nodes]
-    fwd, bwd = [[] for _ in range(n)], [[] for _ in range(n)]
+def dispatch(nodes, after, count, pr):
+    left, ready = list(count), [0.0] * len(nodes)
+    pend, free = {x["eng"]: [] for x in nodes}, {x["eng"]: 0.0 for x in nodes}
     for i, x in enumerate(nodes):
-        for d in sorted(x["hard"] | x["soft"]):
-            gap = nodes[d]["lat"] + SYNC if d in x["hard"] else 0.0
-            fwd[i].append((d, gap))
-            bwd[d].append((i, gap))
-
-    def place(before, after, pr, first):
-        left = [len(b) for b in before]
-        ready = [i for i in range(n) if left[i] == 0]
-        st, busy, seq = [0.0] * n, {}, []
-        while ready:
-            i = max(ready, key=lambda c: pr[c])
-            ready.remove(i)
-            t = max([st[d] + cost[d] + gap for d, gap in before[i]] + [first[i]])
-            line = busy.setdefault(nodes[i]["eng"], [])
-            k = 0
-            while k < len(line) and t + cost[i] > line[k][0]:
-                t = max(t, line[k][1])
-                k += 1
-            line.insert(k, (t, t + cost[i]))
-            st[i] = t
-            seq.append(i)
-            for s, _g in after[i]:
-                left[s] -= 1
-                if left[s] == 0:
-                    ready.append(s)
-        return st, seq
-
-    pr = [0.0] * n
-    for i in range(n - 1, -1, -1):
-        pr[i] = cost[i] + max([pr[s] + gap for s, gap in bwd[i]] + [nodes[i]["lat"]])
-    pr = [CFG["mix"] * pr[i] - 100.0 * i for i in range(n)]
-    z = CFG["seed"]
-    best = None
-    for rnd in range(CFG["rounds"]):
-        if rnd % 2 == 0 and rnd >= 8:
-            pr = [-s for s in best[1]]
-            z = (z * 1103515245 + 12345) % 2147483648
-            t0 = (max(best[1]) + 10000.0) * z / 2147483648 - 10000.0
-            for i in range(n):
-                if t0 < best[1][i] < t0 + CFG["window"]:
-                    z = (z * 1103515245 + 12345) % 2147483648
-                    pr[i] += CFG["noise"] * (1 + rnd // 2 % 4) * (z / 2147483648 - 0.5)
-        st, seq = place(fwd, bwd, pr, [0.0] * n)
-        at = {i: k for k, i in enumerate(seq)}
-        order = sorted(range(n), key=lambda i: (st[i], at[i]))
-        end = sum(replay(o, order, sy) for o, sy in others)
-        if best is None or end < best[0]:
-            best = (end, st, order)
-        back, _s = place(bwd, fwd, [st[i] + cost[i] for i in range(n)], [x["lat"] for x in nodes])
-        pr = [back[i] + cost[i] for i in range(n)]
-    for i, x in enumerate(nodes):
-        x["st"], x["end"] = best[1][i], best[1][i] + cost[i] + x["lat"]
-    return best[2]
+        if left[i] == 0:
+            pend[x["eng"]].append(i)
+    st, order = [0.0] * len(nodes), []
+    while len(order) < len(nodes):
+        t, e = min((max(free[e], min(ready[i] for i in l)), e) for e, l in pend.items() if l)
+        i = max((j for j in pend[e] if ready[j] <= t), key=lambda j: pr[j])
+        pend[e].remove(i)
+        st[i], free[e] = t, t + nodes[i]["cost"]
+        order.append(i)
+        for j, gap in after[i]:
+            ready[j] = max(ready[j], t + gap)
+            left[j] -= 1
+            if left[j] == 0:
+                pend[nodes[j]["eng"]].append(j)
+    return st, order
 
 
 def replay(nodes, order, sync):
@@ -144,12 +109,128 @@ def replay(nodes, order, sync):
     return max(end)
 
 
+def order_nodes(sets):
+    nodes, sync = sets[0]
+    after, count, groups, pr = [[] for _ in nodes], [0] * len(nodes), {}, []
+    for i, x in enumerate(nodes):
+        for d in sorted(x["hard"] | x["soft"]):
+            after[d].append((i, nodes[d]["cost"] + (nodes[d]["lat"] + sync if d in x["hard"] else 0.0)))
+            count[i] += 1
+        p = x["part"]
+        for k in (p, p + " " + x["name"], p + " " + x["eng"]):
+            groups.setdefault(k, []).append(i)
+        due = int(p[0]) * CFG["period"] + CFG["due"][p[1]][int(p[2])] if p[0].isdigit() else {"load": -100, "const": -50, "init0": -58, "init1": -40}[p]
+        pr.append(-1000.0 * due - i)
+    keys, z = list(groups), [CFG["seed"]]
+
+    def rnd():
+        z[0] = (z[0] * 1103515245 + 12345) % 2147483648
+        return (z[0] + 0.5) / 2147483648
+
+    def judge(pr):
+        st, order = dispatch(nodes, after, count, pr)
+        return sum(w * replay(o, order, sy) for w, (o, sy) in zip(WEIGHT, sets)) / sum(WEIGHT), st, order
+    best = cur = judge(pr)
+    for it in range(CFG["rounds"]):
+        new = list(pr)
+        for _ in range((1, 1, 2, 3)[int(4 * rnd())]):
+            d = (rnd() + rnd() + rnd() - 1.5) * (2000.0, 6000.0, 16000.0)[int(3 * rnd())]
+            for i in groups[keys[int(len(keys) * rnd())]]:
+                new[i] += d
+        got = judge(new)
+        if got[0] < cur[0] - CFG["temp"] * (1 - it / CFG["rounds"]) * math.log(rnd()):
+            cur, pr = got, new
+            if got[0] < best[0]:
+                best = got
+    return polish(sets, best[2], rnd)
+
+
+def polish(sets, order, rnd):
+    nodes = sets[0][0]
+    n, anc, hard = len(nodes), [], []
+    for x in nodes:
+        keep, cover = [], 0
+        for d in sorted(x["hard"], reverse=True):
+            if not cover >> d & 1:
+                keep.append(d)
+            cover |= anc[d] | 1 << d
+        anc.append(cover)
+        hard.append(keep)
+    names = sorted({x["eng"] for x in nodes})
+    eng = [names.index(x["eng"]) for x in nodes]
+    pre = [x["hard"] | x["soft"] for x in nodes]
+    tabs = [([x["cost"] for x in o], [x["lat"] + sy for x in o]) for o, sy in sets]
+    pick = [tab for w, tab in zip(WEIGHT, tabs) for _ in range(w)]
+
+    def run(order, cost, lat):
+        free, end = [0.0] * len(names), [0.0] * n
+        for i in order:
+            e = eng[i]
+            st = free[e]
+            for d in hard[i]:
+                if end[d] > st:
+                    st = end[d]
+            free[e] = st = st + cost[i]
+            end[i] = st + lat[i]
+        return end
+
+    def chain(order, cost, lat):
+        end, last, ahead, pairs = run(order, cost, lat), {}, {}, []
+        for i in order:
+            ahead[i], last[eng[i]] = last.get(eng[i]), i
+        i = end.index(max(end))
+        while i is not None:
+            d = max(hard[i], key=lambda d: end[d], default=None)
+            p = ahead[i]
+            if p is not None and (d is None or end[p] - lat[p] >= end[d]):
+                pairs.append((p, i))
+                d = p
+            i = d
+        return pairs
+
+    def swap(order, a, b):
+        ia, ib = order.index(a), order.index(b)
+        need, engs, preds = [b], set(), set(pre[b])
+        for x in reversed(order[ia:ib]):
+            if x in preds or eng[x] in engs:
+                if x == a:
+                    return None
+                need.append(x)
+                engs.add(eng[x])
+                preds |= pre[x]
+        return order[:ia] + need[::-1] + [x for x in order[ia:ib] if x not in need] + order[ib + 1:]
+
+    def judge(o):
+        return sum(w * max(run(o, *tab)) for w, tab in zip(WEIGHT, tabs)) / sum(WEIGHT)
+    cur, pairs = judge(order), None
+    best = (cur, order)
+    for it in range(CFG["swaps"]):
+        if pairs is None or rnd() < 0.1:
+            pairs = chain(order, *pick[int(len(pick) * rnd())])
+        a, b = pairs[int(len(pairs) * rnd())]
+        new, back = swap(order, a, b), rnd() < 0.5
+        if new is None:
+            continue
+        for _ in range((0, 0, 1, 2, 3, 5)[int(6 * rnd())]):
+            k = new.index(b if back else a)
+            near = [x for x in (new[max(0, k - 60):k][::-1] if back else new[k + 1:k + 60]) if eng[x] == eng[a]]
+            more = near and (swap(new, near[0], b) if back else swap(new, a, near[0]))
+            if not more:
+                break
+            new = more
+        v = judge(new)
+        if v < cur - CFG["heat"] * (1 - it / CFG["swaps"]) * math.log(rnd()):
+            cur, order, pairs = v, new, None
+            if v < best[0]:
+                best = (v, new)
+    end = run(best[1], *tabs[0])
+    return best[0], [end[i] - tabs[0][0][i] - tabs[0][1][i] for i in range(n)], best[1]
+
+
 def plan(g, core, T, topo):
-    sets = [(build(g, core, T, topo, dict(PRM, **m))[0], dict(PRM, **m)["sync"]) for m in SPREAD]
     nodes, ncalls, neng = build(g, core, T, topo, PRM)
     if "order" not in KEPT:
-        KEPT["order"] = order_nodes(nodes, sets)
-        KEPT["st"] = [x["st"] for x in nodes]
+        _end, KEPT["st"], KEPT["order"] = order_nodes([(build(g, core, T, topo, dict(PRM, **m))[0], dict(PRM, **m)["sync"]) for m in SPREAD])
     for x, s in zip(nodes, KEPT["st"]):
         x["st"] = s
     return nodes, KEPT["order"], ncalls, neng
@@ -157,8 +238,10 @@ def plan(g, core, T, topo):
 
 def relayed():
     out = [("u", 0, CFG["cut"], V)]
-    for t in range(1, STEPS):
-        out += [(k[0], t, int(k[1]) * CW, (int(k[1]) + 1) * CW) for k in CFG["relay"].split()]
+    for part in CFG["order"].split():
+        for k in CFG["pieces"].split():
+            if k[0].isupper() and part[1] == k[0].lower() and int(part[2]) == (int(k[2]) - 1) // 2 and int(part[0]) < STEPS - 1:
+                out.append((part[1], int(part[0]) + 1, int(k[1]) * QW, int(k[2]) * QW))
     return out
 
 
@@ -189,11 +272,12 @@ def hand_on(g, core, rank, T, topo):
 def build(g, core, T, topo, PRM):
     rank = T.rank_of(core)
     CY, PEC, GC = PRM["cy"], PRM["pe"], PRM["gc"]
-    nodes = []
+    NC = 4 if ND == f32 else 1
+    nodes, here = [], ["load"]
     lastw, readers, bankt = {}, {}, {}
     ve, ac, pe = g.vector, g.scalar, g.tensor
 
-    def node(eng, cost, fn, r=(), w=(), banks=(), lat=0.0, kind="c", name=""):
+    def node(eng, cost, fn, r=(), w=(), banks=(), lat=0.0, kind="c", name="", of=None):
         i = len(nodes)
         hard, soft = set(), set()
 
@@ -219,7 +303,8 @@ def build(g, core, T, topo, PRM):
         for k in w:
             lastw[k] = i
             readers[k] = []
-        nodes.append({"eng": eng, "cost": cost, "lat": lat, "fn": fn, "hard": hard, "soft": soft - hard, "kind": kind, "name": name})
+        nodes.append({"eng": eng, "cost": cost, "lat": lat, "fn": fn, "hard": hard, "soft": soft - hard, "kind": kind, "name": name,
+                      "of": i if of is None else of, "part": here[0]})
         return i
 
     def dve(n, cyc, fn, r, w, banks=(), name=""):
@@ -251,13 +336,21 @@ def build(g, core, T, topo, PRM):
     def acc(out, terms, n, r, w, bank, name=""):
         mm([(out, l, x, i == 0, i == len(terms) - 1, n * c) for i, (l, x, c) in enumerate(terms)], r, w, bank, name)
 
-    def dma(q, out, in_, kb, r, w, name=""):
-        eng = {"sp": g.sync, "act": g.scalar, "g": g}[q]
-        node(q, 1000.0 if q == "g" else 100.0, lambda: eng.dma_start(out, in_), r, w, lat=1800.0 + kb * 6.0, kind="d", name=name)
-
     def sid(s):
         k = SCALES.index(s)
         return T.sid[:, 128 * k:128 * (k + 1)]
+
+    def lin(out, terms, n, w, bank, name="", more=(), mk=()):
+        acc(out, list(more) + [(sid(s), x, 1) for s, x, _k in terms], n,
+            list(mk) + [k for _s, _x, k in terms] + [("sid", s) for s, _x, _k in terms], w, bank, name)
+
+    def dma(q, pairs, kb, r, w, name="", add=False):
+        eng = {"sp": g.sync, "act": g.scalar, "g": g}[q]
+        kw = {"accum_op": A.add} if add else {}
+        i = node(q, (1000.0 if q == "g" else 100.0) * len(pairs), lambda: [eng.dma_start(o, x, **kw) for o, x in pairs], r, w,
+                 lat=PRM["dl"] / 2, kind="d", name=name)
+        node("dma", kb * PRM["dr"], None, list(r) + list(w), list(w) + [("dma", i)], lat=PRM["dl"] / 2, kind="l", name=name, of=i)
+        nodes[-1]["hard"].add(i)
 
     def blk(t, k):
         return t[:, 128 * k:128 * (k + 1)]
@@ -270,7 +363,8 @@ def build(g, core, T, topo, PRM):
     assert bin(near).count("1") == neng and bin(way_out(aid, rank, T, topo)[0]).count("1") == neng
     ncalls = {}
 
-    def send(kind, t, c0, c1, keys, kb):
+    def send(kind, t, c0, c1):
+        kb, keys = (c1 - c0) // (4 if kind == "x" else 2), [("t" + kind, t, j) for j in range(c0 // HW, (c1 - 1) // HW + 1)]
         ap = T["t%s%d" % (kind, t)][:, own + c0:own + c1]
         sem = T.sem["a%s%d" % (kind, t)]
         ncalls[(kind, t)] = ncalls.get((kind, t), 0) + 1
@@ -278,7 +372,7 @@ def build(g, core, T, topo, PRM):
             hs_ = T.sem["h%d" % relayed().index((kind, t, c0, c1))]
             node("g", 600.0, lambda: g.remote_dma(ap, ap, hs_, T.sem.sent, topo.addr(aid)[1], topo.addr(aid)[0], near),
                  keys, [("wire", kind, t, c0), "turn"], kind="r", name="relay")
-            node("hop", 300.0 + kb * 8.0, None, [("wire", kind, t, c0)], [("hop", kind, t, c0)], lat=PRM["lat"] + 600.0, kind="l")
+            node("dma", 300.0 + kb * 2 * PRM["dr"], None, [("wire", kind, t, c0)], [("hop", kind, t, c0)], lat=PRM["lat"] + 600.0, kind="l")
             node("link2", 500.0 + kb * 3 * PRM["link"], None, [("hop", kind, t, c0)], [("land", kind, t, c0), "turn2"], lat=PRM["lat"], kind="l")
             return ("land", kind, t, c0)
 
@@ -286,31 +380,34 @@ def build(g, core, T, topo, PRM):
             g.remote_dma_fused([RemoteDMATransfer(dst_ids=ids, dma_engine_mask=mask, remote_sem=sem, srcs=[ap], dsts=[ap] * len(ids))],
                                local_sem=T.sem.sent)
         node("g", 600.0, fn, keys, [("wire", kind, t, c0)], kind="r", name="send")
-        node("link", 500.0 + kb * 3 * PRM["link"], None, [("wire", kind, t, c0)], [("land", kind, t, c0)], lat=PRM["lat"], kind="l")
+        node("dma", 500.0 + kb * 3 * PRM["link"], None, [("wire", kind, t, c0)], [("land", kind, t, c0)], lat=PRM["lat"], kind="l")
         return ("land", kind, t, c0)
+
+    def sends(kind, t, h):
+        return [send(kind, t, int(k[1]) * QW, int(k[2]) * QW) for k in CFG["pieces"].split() if k[0].lower() == kind and (int(k[2]) - 1) // 2 == h]
 
     def arrive(kind, t, lands):
         node("arr", 0.0, (kind, t), lands, [("arr", kind, t)], kind="a")
 
-    allx = lambda t: [("tx", t, j) for j in range(NCH)]
-    allu = lambda t: [("tu", t, j) for j in range(NCH)]
-    dma("sp", T.tx0[:, own:own + V], T.x0[:], 128, [], allx(0))
-    dma("act", T.tu0[:, own:own + V], T.u0[:], 256, [], allu(0))
-    dma("sp", T.si[:], T.s0[:], 256, [], ["si"])
-    dma("act", T.jt[:], T.ax[:], 512, [], ["jt"])
-    dma("sp", T.ab[:], T.ag[:], 128, [], ["ab"])
-    dma("sp", T.pi[:], T.p0[:], 256, [], ["pi"])
-    dma("sp", T.ww0[:], T.w0[:], 128, [], [("ww", 0, 0), ("ww", 0, 1)])
-    dma("sp", T.ti[:, 0:2], T.th[:], 1, [], ["ti"])
-    arrive("x", 0, [send("x", 0, 0, V, allx(0), 128)])
-    cut = CFG["cut"]
-    arrive("u", 0, [send("u", 0, cut, V, allu(0), (V - cut) // 2), send("u", 0, 0, cut, allu(0), cut // 2)])
+    both = lambda *n: [n + (0,), n + (1,)]
+    four = lambda *n: [n + (j,) for j in range(4)]
+    dma("sp", [(T.tx0[:, own:own + V], T.x0[:])], 128, [], both("tx", 0), "x")
+    dma("act", [(T.tu0[:, own:own + V], T.u0[:])], 256, [], both("tu", 0), "u")
+    dma("sp", [(T.si[:], T.s0[:])], 256, [], ["si"], "s")
+    dma("sp", [(T.pi[:], T.p0[:])], 256, [], ["pi"], "p")
+    dma("sp", [(T.ab[:], T.ag[:])], 128, [], ["ab"], "a")
+    dma("sp", [(T.ww0[:], T.w0[:])], 128, [], both("ww", 0), "w")
+    dma("sp", [(T.ti[:, 0:2], T.th[:])], 1, [], ["ti"], "t")
+    dma("act", [(T.jt[:], T.ax[:])], 512, [], ["jt"], "j")
+    arrive("x", 0, [send("x", 0, 0, V)])
+    arrive("u", 0, [send("u", 0, CFG["cut"], V), send("u", 0, 0, CFG["cut"])])
 
     def iota(out, pat, base, cm, n, key, small=True):
         if small:
             node("g", 130 + 2 * n * CY, lambda: g.iota(out, pat, base, cm, allow_small_or_imprecise_dtypes=True), [], [key])
         else:
             node("g", 130 + 2 * n * CY, lambda: g.iota(out, pat, base, cm), [], [key])
+    here[0] = "const"
     iota(T.ia[:], [[-1, 16]], 16, 1, 16, "ia", False)
     iota(T.ci[:], [[1, 144]], 0, 0, 144, "ci")
     iota(T.cm[:], [[0, 8], [1, 16]], 0, 0, 128, "cm")
@@ -321,265 +418,248 @@ def build(g, core, T, topo, PRM):
     cp(T.col[:], T.ic[:], 16, 1, ["ic"], ["col"])
     p16, pb16 = T.fa[:, 0:1], T.col[:, 0:1]
     ts(T.ks[:], T.fa[:], pb16, -16.0, A.add, A.add, 16, 1, ["fa", "col"], ["ks"])
-    ts(T.mk[:], T.fa[:], 0.0, None, A.is_equal, None, 16, 1, ["fa"], ["mk"])
     ts(T.mk16[:], T.fa[:], 0.0, 16.0, A.is_equal, A.mult, 16, 1, ["fa"], ["mk16"])
-    ts(T.tmp[:, 0:16], T.ci[:, 0:16], p16, 16.0, A.add, A.is_ge, 16, 1, ["ci", "fa"], ["tmp"])
-    ts(T.tb[:], T.tmp[:, 0:16], -0.5, None, A.add, None, 16, 1, ["tmp"], ["tb"])
-    ts(T.bo[:], T.cb[:], pb16, None, A.is_equal, None, 128, .5, ["cb", "col"], ["bo"])
-    ts(T.ee[:], T.ci[:], pb16, None, A.is_equal, None, 144, .5, ["ci", "col"], ["ee"])
+    ts(T.tmp[:], T.ci[:, 0:16], p16, 16.0, A.add, A.is_ge, 16, 1, ["ci", "fa"], ["tmp"])
+    ts(T.tb[:], T.tmp[:], -0.5, None, A.add, None, 16, 1, ["tmp"], ["tb"])
+    ts(T.m4[:], T.fa[:, 0:16:4], 3.5, None, A.is_lt, None, 4, 1, ["fa"], ["m4"])
+    ts(T.k12[:], T.ks[:, 0:16:4], 12.0, None, A.add, None, 4, 1, ["ks"], ["k12"])
+    ts(T.bo[:], T.cb[:], pb16, None, A.is_equal, None, 128, .5, ["cb", "col"], ["bo"], name="bo")
+    ts(T.ee[:], T.ci[:], pb16, None, A.is_equal, None, 144, .5, ["ci", "col"], ["ee"], name="ee")
+    if "a" in CFG["min"]:
+        ts(T.ne[:], T.ci[:], pb16, -1.0, A.is_equal, A.mult, 144, .5, ["ci", "col"], ["ne"], name="ee")
     cI = T.ci[:, 0:128]
     k0 = T.ks[:, 0:1]
-    for k, s in enumerate(SCALES):
-        if s == 1.0 or CFG["sid"] == "v":
-            ts(sid(s), cI, k0, s, A.is_equal, A.mult, 128, .5, ["ci", "ks"], [("sid", s)])
-        else:
-            act(sid(s), sid(1.0), F.Identity, 128, [("sid", 1.0)], [("sid", s)], scale=s)
-    ts(T.ih[:], cI, k0, None, A.is_equal, None, 128, .5, ["ci", "ks"], ["ih"])
-    ts(T.i1[:], cI, k0, None, A.is_equal, None, 128, 1, ["ci", "ks"], ["i1"])
-    ts(T.ik[:], cI, k0, 1024.0, A.is_equal, A.mult, 128, 1, ["ci", "ks"], ["ik"])
-    ts(T.kd[:], cI, k0, p16, A.is_equal, A.mult, 128, .5, ["ci", "ks", "fa"], ["kd"])
-    ts(T.nm[:], T.cm[:], p16, None, A.is_equal, None, 128, .5, ["cm", "fa"], ["nm"])
-    ts(T.rr[:, 0:128], cI, k0, 32.0, A.is_equal, A.mult, 128, .5, ["ci", "ks"], [("rr", 0)])
-    tt(T.n32[:], T.nm[:], T.rr[:, 0:128], A.add, 128, 2, ["nm", ("rr", 0)], ["n32"])
+    for s in SCALES:
+        ts(sid(s), cI, k0, s, A.is_equal, A.mult, 128, .5, ["ci", "ks"], [("sid", s)], name="sid")
+    for out, s, key in ((T.nih, -1.0, "nih"), (T.ino, 1.0, "ino"), (T.inn, -1.0, "inn"), (T.ni1, -1.0, "ni1"), (T.ik, 1024.0, "ik"), (T.kd, p16, "kd")):
+        ts(out[:], cI, k0, s, A.is_equal, A.mult, 128, 1, ["ci", "ks", "fa"], [key], name=key)
+    for kh in range(4):
+        ts(T.pw[:, 144 * kh:144 * (kh + 1)], T.ci[:], T.k12[:, kh:kh + 1], T.m4[:, kh:kh + 1], A.is_equal, A.mult, 144, .5, ["ci", "k12", "m4"], [("pw", kh)], name="pw")
+    ts(T.nm[:], T.cm[:], p16, None, A.is_equal, None, 128, .5, ["cm", "fa"], ["nm"], name="n32")
+    ts(T.yy[:, 0:128], cI, k0, 32.0, A.is_equal, A.mult, 128, .5, ["ci", "ks"], [("yy", 0)], name="n32")
+    tt(T.n32[:], T.nm[:], T.yy[:, 0:128], A.add, 128, 2, ["nm", ("yy", 0)], ["n32"], name="n32")
     for k in range(16):
-        ts(blk(T.ff, k), T.bo[:], T.mk[:, k:k + 1], None, A.mult, None, 128, .5, ["bo", "mk"], [("ff", k)])
-        act(blk(T.dg, k), sid(1.0), F.Identity, 128, [("sid", 1.0), "mk16"], [("dg", k)], scale=T.mk16[:, k:k + 1])
+        act(blk(T.dg, k), sid(1.0), F.Identity, 128, [("sid", 1.0), "mk16"], [("dg", k)], scale=T.mk16[:, k:k + 1], name="dg")
+    iota(T.cg[:], [[16, 8], [0, 4], [4, 4]], 16, 0, 128, "cg")
+    cp(T.tmp[:], T.ia[:], 16, 1, ["ia"], ["tmp"])
+    for kl in range(4):
+        ts(blk(T.gm, kl), T.cg[:], T.tmp[:, kl:kl + 1], None, A.is_equal, None, 128, .5, ["cg", "tmp"], [("gm", kl)], name="gm")
+    for s in range(1, 16):
+        ts(blk(T.sh, s), cI, T.ks[:, s:s + 1], None, A.is_equal, None, 128, .5, ["ci", "ks"], [("sh", s)], name="sh")
     sh = T.sh[:, 128:2048]
-    node("g", 130 + 2 * 1920 * CY, lambda: g.iota(sh, [[0, 1920]], 0, 0, allow_small_or_imprecise_dtypes=True), [("wire", "u", 0, 0)], ["sh"])
-    for pat, op, fill, base, cm in (([[-1, 15], [-16, 8], [-1, 16]], A.not_equal, 1.0, -1, 1), ([[-1, 15], [-16, 8], [-1, 16]], A.not_equal, 1.0, 15, 1),
-                                    ([[0, 15], [-16, 8], [0, 16]], A.is_ge, 0.0, 0, 1), ([[0, 15], [16, 8], [0, 16]], A.is_ge, 0.0, 15, -1),
-                                    ([[0, 15], [-1, 128]], A.not_equal, -1.0, 0, 1)):
-        node("g", 170 + 2 * 1920 * CY, lambda pat=pat, op=op, fill=fill, base=base, cm=cm: g.affine_select(sh, sh, pat, op, fill, base, cm), ["sh"], ["sh"])
-    dve(HW, .5, lambda: ve.memset(T.ones[:], 1.0), [], ["ones"])
-    dve(1024, .5, lambda: ve.memset(T.msk[:], 1.0), [], ["msk0"])
-    dve(64, 1, lambda: ve.memset(T.msk[:, 0:1024:16], 0.0), ["msk0"], ["msk"])
-    dve(1024, .5, lambda: ve.memset(T.msk8[:], 1.0), [], ["msk80"])
-    dve(128, 1, lambda: ve.memset(T.msk8[:, 0:1024:8], 0.0), ["msk80"], ["msk8"])
-    ts(T.thf[:, 0:1], T.ti[:, 0:1], -1.0, 128.5, A.mult, A.add, 1, 1, ["ti"], ["thq"])
-    ts(T.thf[:, 1:2], T.ti[:, 1:2], -1.0, 0.5, A.mult, A.add, 1, 1, ["ti"], ["thb"])
+    node("g", 170 + 2 * 1920 * CY, lambda: g.affine_select(sh, sh, [[0, 15], [-1, 128]], A.not_equal, -1.0, 0, 1),
+         [("sh", s) for s in range(1, 16)] + [("wire", "u", 0, 0)], ["sh"], name="sh")
+    dve(HW, .5, lambda: ve.memset(T.ones[:], 1.0), [], ["ones"], name="ones")
+    dve(BL, .5, lambda: ve.memset(T.msk[:], 1.0), [], ["msk0"], name="msk")
+    dve(HW, .5, lambda: ve.memset(T.msk[:, 0:BL:4], 0.0), ["msk0"], ["msk"], name="msk")
+    ts(T.thq[:, 0:1], T.ti[:, 0:1], -256.0, None, A.add, None, 1, 1, ["ti"], ["thq"], name="th")
+    ts(T.thf[:, 1:2], T.ti[:, 1:2], -1.0, 0.5, A.mult, A.add, 1, 1, ["ti"], ["thb"], name="th")
 
     hs = lambda h: slice(h * HW, (h + 1) * HW)
+    mine = lambda h: slice(own + h * HW, own + (h + 1) * HW)
     lo, hi = slice(0, HW), slice(HW, 2 * HW)
-
-    def weights(b, h):
-        s = hs(h)
-        acc(T.m1[:, lo], [(sid(1.0), T["bb%d" % b][:, s], 1), (sid(-1.5), T["la%d" % b][:, s], 1), (sid(2.5), T.ones[:], 1)],
-            HW, [("bb", b, h), ("la", b, h), "ones", ("sid", 1.0), ("sid", -1.5), ("sid", 2.5)], ["m1lo"], "m1", "m")
-        tt(T["wt%d" % b][:, s], T["ww%d" % b][:, s], T.m1[:, lo], A.mult, HW, 1, [("ww", b, h), "m1lo"], [("wt", b, h)], ["m1"], "w")
-
-    def jump(off, offkey, base, basekeys, bank, engines):
-        ps = T[bank]
-        for j in range(NCH):
-            dst, src = T["mn%d" % j][:], T.jt[:].indirect(off[:, j * CW:(j + 1) * CW])
-            wk = [("mn", j, r) for r in range(4)]
-            if engines[j] == "v":
-                cp(dst, src, 16 * CW, GC, ["jt", offkey], wk, name="jg")
-            else:
-                act(dst, src, F.Copy, 16 * CW, ["jt", offkey], wk, cyc=GC, name="jg")
-            acc(ps[:, j * CW:(j + 1) * CW], [(blk(T.dg, k), T["mn%d" % j][:, k:16 * CW:16], 1) for k in range(16)] + [(T.kd[:], T.ones[:, 0:CW], 1)],
-                CW, wk + [("dg", k) for k in range(16)] + ["kd", "ones"], [bank + ("lo" if j < 2 else "hi")], bank, "jd")
-        pk = [bank + "lo", bank + "hi"]
-        tt(T.tmp[:], base, ps[:], A.add, V, 1, basekeys + pk, ["tmp"], [bank], "j1")
-        ts(T.tm2[:], T.tmp[:], float(NR * V), -float(NR * V), A.is_ge, A.mult, V, 1, ["tmp"], ["tm2"], name="j2")
-        tt(ps[:], T.tm2[:], ps[:], A.add, V, 1, ["tm2"] + pk, pk, [bank], "j3")
-
-    both = lambda n, b: [(n, b, 0), (n, b, 1)]
-    cp(T.offs[:], T.si[:], V, 1, ["si"], ["offs"])
-    act(T.bb0[:], T.ab[:], F.Identity, V, ["ab"], both("bb", 0), scale=-1.0, bias=3.0)
-    act(T.la0[:], T.ab[:], F.Sign, V, ["ab"], both("la", 0), scale=-1.0, bias=2.5)
-    ts(T.live[:], T.ab[:], 2.5, None, A.is_lt, None, V, .5, ["ab"], ["live"])
-    act(T.dead[:], T.ab[:], F.Relu, V, ["ab"], ["dead"], bias=-2.0)
-    cp(T.ub[:], T.pi[:], V, 1, ["pi"], ["ub"], ["ub"])
-    tt(T.ub[:], T.ub[:], T.si[:], A.subtract, V, 1, ["ub", "si"], ["ub"], ["ub"])
-    tt(T.ub[:], T.ub[:], T.live[:], A.mult, V, 1, ["ub", "live"], ["ub"], ["ub"])
-    tt(T.cc0[:], T.ub[:], T.si[:], A.add, V, 1, ["si", "ub"], both("cc", 0), ["ub"])
-    cp(T.off0[:], T.cc0[:], V, 1, both("cc", 0), both("off", 0))
-    act(T.le[:], T.ub[:], F.Copy, V, ["ub"], ["le"], ["ub"])
-    weights(0, 0)
-    weights(0, 1)
-    jump(T.offs, "offs", T.si[:], ["si"], "m0", CFG["j0"])
-    m0k, m1k = ["m0lo", "m0hi"], ["m1lo", "m1hi"]
-    tt(T.m1[:], T.m0[:], T.dead[:], A.mult, V, 1, m0k + ["dead"], m1k, ["m0", "m1"])
-    tt(T.n1[:], T.m1[:], T.cc0[:], A.add, V, 1, both("cc", 0) + m1k, ["n1"], ["m1"])
-    cp(T.offn[:], T.n1[:], V, 1, ["n1"], ["offn"])
-    tt(T.dd0[:], T.m1[:], T.le[:], A.subtract, V, 1, m1k + ["le"], both("dd", 0), ["m1"])
-    tt(T.g2[:], T.m0[:], T.dd0[:], A.subtract, V, 1, m0k + both("dd", 0), ["g2"], ["m0"])
-
-    def second_jump():
-        jump(T.offn, "offn", T.n1[:], ["n1"], "m1", CFG["j1"])
-        tt(T.g1[:], T.m1[:], T.dd0[:], A.subtract, V, 1, m1k + both("dd", 0), ["g1"], ["m1"])
-
+    one = T.ones[:]
+    block = lambda buf, kh: buf[:, kh * BL:(kh + 1) * BL]
+    slot = lambda buf, k: buf[:, k // 4 * BL + k % 4:(k // 4 + 1) * BL:4]
+    listed = lambda off, h, kh: off[:, h * HW + 64 * kh:h * HW + 64 * (kh + 1)]
+    pair = lambda h: ("m%d" % (2 * h), "m%d" % (2 * h + 1))
     turn = [0]
 
-    gathered = set()
+    def weights(b, h):
+        s, m1 = hs(h), pair(h)[1]
+        lin(T[m1][:, lo], [(-1.0, T["bb%d" % b][:, s], ("bb", b, h)), (3.0, T["lv%d" % b][:, s], ("lv", b, h)), (-4.0, one, "ones")], HW, [m1 + "lo"], m1, "m")
+        tt(T.nw[:, s], T["ww%d" % b][:, s], T[m1][:, lo], A.mult, HW, 1, [("ww", b, h), m1 + "lo"], [("nw", h)], [m1], "w")
 
-    def chunk(t, j, what):
-        b, h, last = t % 2, j // 2, t == STEPS - 1
-        GW = CFG["gw"]
-        tx, tu, off = T["tx%d" % t], T["tu%d" % t], T["off%d" % t]
-        xc, uc, mn, px = T["xc%d" % j], T["uc%d" % j], T["mn%d" % j], T["px%d" % j]
-        pu, sc = T["pu%d" % (j % 3)], T.sc
-        folded = j in CFG["fold"][t]
-        cs = slice(j * CW, (j + 1) * CW)
-        os_ = slice(own + j * CW, own + (j + 1) * CW)
-        ng = CW // GW
-        for nm, tab, dst, al in (("x", tx, xc, allx), ("u", tu, uc, allu)):
-            if (nm, t, j) in gathered or nm not in what.replace("c", "x").lower():
-                continue
-            gathered.add((nm, t, j))
-            for q in range(ng):
-                o_, i_ = dst[:, q * 16 * GW:(q + 1) * 16 * GW], tab[:].indirect(off[:, j * CW + q * GW:j * CW + (q + 1) * GW])
-                rk, wk = al(t) + [("arr", nm, t), ("off", t, h)], [(nm + "c", j, q)]
-                if "%d%s%d%d" % (t, nm, j, q) in CFG["gv"]:
-                    cp(o_, i_, 16 * GW, GC, rk, wk, name="g" + nm)
+    def offsets(names, key, off, offkey, h):
+        m0 = pair(h)[0]
+        mm([(T[m0][:, HW + 64 * kh:HW + 64 * (kh + 1)], T.pw[:, 144 * kh + 12 - 4 * vl:144 * kh + 140 - 4 * vl],
+             names[:, h * HW + vl:(h + 1) * HW:4], vl == 0, vl == 3, 64 * NC) for kh in range(4) for vl in range(4)],
+           [key] + four("pw"), [m0 + "hi"], m0, "perm")
+        cp(off[:, hs(h)], T[m0][:, hi], HW, 1, [m0 + "hi"], [offkey], [m0], "off")
+
+    def jump(t, h):
+        off, offkey, n = (T.off1, ("off", 1, h), h) if t else (T.offs, ("offs", h), 2 + h)
+        for kh in range(4):
+            out, src = block(T["wr%d" % n], kh), T.jt[:].indirect(listed(off, h, kh))
+            if CFG["jump"].split()[2 * t + h][kh] == "v":
+                cp(out, src, BL, GC, ["jt", offkey], [("wr", n, kh)], name="jg")
+            else:
+                act(out, src, F.Copy, BL, ["jt", offkey], [("wr", n, kh)], cyc=GC, name="jg")
+
+    def jumped(t, h, bank):
+        base, basekey, n = (T.cc1, ("cc", 1, h), h) if t else (T.sf, "sf", 2 + h)
+        s, ps = hs(h), T[bank][:, hi]
+        for kh in range(4):
+            mm([(ps, T.ino[:], base[:, s], True, False, HW * NC), (ps, T.kd[:], one, False, False, HW)] * (kh == 0) +
+               [(ps, blk(T.dg, k), slot(T["wr%d" % n], k), False, k == 15, HW) for k in range(4 * kh, 4 * kh + 4)],
+               [("wr", n, kh), "kd", "ones", "ino", basekey] + [("dg", k) for k in range(4 * kh, 4 * kh + 4)], [bank + "lo", bank + "hi"], bank, "jd")
+        ts(T.md[:, s], ps, float(NR * V), -float(NR * V), A.is_ge, A.mult, HW, 1, [bank + "hi"], [("md", h)], [bank], "j1")
+        tt(T["q%d" % t][:, s], T.md[:, s], ps, A.add, HW, 1, [("md", h), bank + "hi"], [("q", t, h)], [bank], "j2")
+
+    here[0] = "init0"
+    cp(T.sf[:], T.si[:], V, 1, ["si"], ["sf"])
+    cp(T.pf[:], T.pi[:], V, 1, ["pi"], ["pf"])
+    ts(T.bb0[:], T.ab[:], -1.0, 3.0, A.mult, A.add, V, .5, ["ab"], both("bb", 0))
+    ts(T.lv0[:], T.ab[:], 2.5, None, A.is_lt, None, V, .5, ["ab"], both("lv", 0))
+    for h in range(2):
+        here[0] = "init%d" % h
+        s, m0 = hs(h), pair(h)[0]
+        lin(T[m0][:, lo], [(-BIG, T.lv0[:, s], ("lv", 0, h)), (BIG, one, "ones")], HW, [m0 + "lo"], m0, "N", [(T.inn[:], T.pf[:, s], NC)], ["inn", "pf"])
+        tt(T.r1[:, s], T.sf[:, s], T[m0][:, lo], A.min, HW, 1, ["sf", m0 + "lo"], [("r1", h)], [m0], "r")
+        act(T.cc0[:, s], T.r1[:, s], F.Abs, HW, [("r1", h)], [("cc", 0, h)], name="abs")
+        offsets(T.cc0, ("cc", 0, h), T.off0, ("off", 0, h), h)
+        offsets(T.sf, "sf", T.offs, ("offs", h), h)
+        weights(0, h)
+
+    def spread_weights(t, h):
+        n = 2 * (t % 2) + h
+        wr, wp = T["wr%d" % n], T["wp%d" % h]
+        for i, bank in enumerate(pair(h)):
+            bk = [bank + "lo", bank + "hi"]
+            mm([(T[bank][:, kl:512:4], blk(T.gm, kl), T.nw[:, h * HW + i * QW:h * HW + (i + 1) * QW], True, True, QW) for kl in range(4)],
+               [("nw", h)] + four("gm"), bk, bank, "wrep")
+            act(wp[:, 512 * i:512 * (i + 1)], T[bank][:], F.Copy, 512, bk, [("wp", h, i)], [bank], name="wc")
+        dma("sp", [(wr[q:128:4, :], wp[:]) for q in range(4)], 1024, both("wp", h), four("wr", n), "wdma")
+
+    def gather_x(t, h):
+        for kh in range(4):
+            act(block(T["xc%d" % h], kh), T["tx%d" % t][:].indirect(listed(T["off%d" % t], h, kh)), F.Copy, BL,
+                both("tx", t) + [("arr", "x", t), ("off", t, h)], [("xc", h, kh)], cyc=GC, name="gx")
+
+    def new_x(t, h):
+        n, last, hb = 2 * (t % 2) + h, t == STEPS - 1, CFG["hbank"]
+        xc, px, wr = T["xc%d" % h], T["px%d" % h], T["wr%d" % n]
+        for kh in range(4):
+            dve(BL, .5, lambda kh=kh: ve.tensor_tensor_scan(block(px, kh), block(xc, kh), block(wr, kh), 0.0, A.max, A.mult),
+                [("xc", h, kh), ("wr", n, kh)], [("px", h, kh)], name="xm")
+            mm([(T[hb][:, hi], T.nih[:], slot(px, k), k == 0, k == 15, HW) for k in range(4 * kh, 4 * kh + 4)],
+               [("px", h, kh), "nih"], [hb + "lo", hb + "hi"], hb, "h")
+        act(T.yy[:, hs(h)], T[hb][:, hi], F.Identity, HW, [hb + "hi"], [("yy", h)], [hb], scale=1.0 / 256, bias=160.0 - 255.0 / 512, name="y")
+        nx = T.xo[:, hs(h)] if last else T["tx%d" % (t + 1)][:, mine(h)]
+        ts(nx, T.yy[:, hs(h)], -160.0, 15.0, A.add, A.min, HW, .5, [("yy", h)], [("tx", t + 1, h)], name="X")
+        if last:
+            dma("g", [(T.yx[:, hs(h)], nx)], 128, [("tx", t + 1, h)], [])
+        return [] if last else sends("x", t + 1, h)
+
+    def matches(t, h):
+        b, xc, mn, tx = t % 2, T["xc%d" % h], T["mn%d" % h], T["tx%d" % t]
+        scalar = CFG["min"].split()[t][h] == "a"
+        spread_x = lambda ps, i, start: [(ps[:, m:512:4], sid(1.0), tx[:, own + h * HW + i * QW:own + h * HW + (i + 1) * QW], start, start or m == 3, QW)
+                                         for m in range(4)]
+        for i in range(0 if scalar else 2):
+            mm(spread_x(T["xb%d" % i], i, True), [("tx", t, h), ("sid", 1.0)], ["xb%d" % i], "xb%d" % i, "xrep")
+        for kh in range(4):
+            for i in range(2):
+                s, bank = slice(kh * BL + 512 * i, kh * BL + 512 * (i + 1)), "xb%d" % i
+                if scalar:
+                    mm([(T[bank][:], sid(-1.0), xc[:, s], True, False, 512)] + spread_x(T[bank], i, False),
+                       [("xc", h, kh), ("tx", t, h), ("sid", 1.0), ("sid", -1.0)], [bank], bank, "xd")
+                    act(mn[:, s], T[bank][:], F.Relu, 512, [bank], [("mn", h, kh, i)], [bank], name="relu")
                 else:
-                    act(o_, i_, F.Copy, 16 * GW, rk, wk, cyc=GC, name="g" + nm)
-        if what in ("X", "U", "XU"):
-            return
-        xk, uk = [("xc", j, q) for q in range(ng)], [("uc", j, q) for q in range(ng)]
-        for r in range(4 if what != "c" else 0):
-            bank = ("w0b", "w1b", "hb")[turn[0] % CFG["wbanks"]]
-            turn[0] += 1
-            ps = T[bank]
-            mm([(ps[:, m:512:4], blk(T.ff, r + 4 * m), T["wt%d" % b][:, cs], True, True, CW) for m in range(4)],
-               [("wt", b, h)] + [("ff", r + 4 * m) for m in range(4)], [bank], bank, "wrep")
-            if "x" in what:
-                tt(px[:, r * 512:(r + 1) * 512], xc[:, r:2048:4], ps[:], A.mult, 512, 1, xk + [bank], [("px", j, r)], [bank], "xm")
-            if "u" in what:
-                po = pu[:, r // 2 * 1024 + r % 2:(r // 2 + 1) * 1024:2] if folded else pu[:, r:2048:4]
-                tt(po, uc[:, r:2048:4], ps[:], A.mult, 512, 1, uk + [bank], [("pu", j % 3, r)] + ([("pu", j % 3, "all")] if r == 0 else []), [bank], "um")
-        if "x" in what:
-            hn = "hb" if CFG["wbanks"] == 2 else CFG["hbank"]
-            hp = T[hn][:, 3 * CW:4 * CW]
-            acc(hp, [(T.ih[:], px[:, (k % 4) * 512 + k // 4:(k % 4 + 1) * 512:4], 1) for k in range(16)], CW,
-                [("px", j, r) for r in range(4)] + ["ih"], ["hacc"], hn, "h")
-            act(T.yy[:, cs], hp, F.Identity, CW, ["hacc"], [("yy", j)], [hn], scale=1.0 / 256, bias=160.0 - 255.0 / 512, name="y")
-            nx = T.xo[:, cs] if last else T["tx%d" % (t + 1)][:, os_]
-            ts(nx, T.yy[:, cs], -160.0, 15.0, A.add, A.min, CW, .5, [("yy", j)], [("tx", t + 1, j)], name="X")
-        if "u" in what:
-            pk = [("pu", j % 3, r) for r in range(4)]
-            if folded:
-                node("g", 1000.0, lambda: g.dma_start(pu[:, 0:1024], pu[:, 1024:2048], accum_op=A.add), pk, pk[0:2],
-                     lat=PRM["fold"], kind="d", name="fold")
-            if j in CFG["pesum"][t]:
-                pass
-            elif folded:
-                s = slice(j % 2 * 1024, (j % 2 + 1) * 1024)
-                dve(1024, 1, lambda: ve.tensor_tensor_scan(sc[:, s], T.msk8[:], pu[:, 0:1024], 0.0, A.mult, A.add), pk + ["msk8"], [("sc", j % 2)], name="scan")
-                terms, rk = [(T.i1[:], sc[:, s.start + 7:s.stop:8], 4)], [("sc", j % 2)]
+                    tt(mn[:, s], xc[:, s], T[bank][:], A.min, 512, 1, [("xc", h, kh), bank], [("mn", h, kh, i)], [bank], "min")
+            mm([(T.cbk[:, lo], sid(256.0), T["lv%d" % b][:, hs(h)], True, False, HW)] * (kh == 0) +
+               [(T.cbk[:, lo], T.bo[:], tx[:, mine(h)], False, False, HW)] * (kh == 0 and scalar) +
+               [(T.cbk[:, lo], (T.ne if scalar else T.ee)[:, 16 - k:144 - k], slot(mn, k), False, k == 15, HW) for k in range(4 * kh, 4 * kh + 4)],
+               both("mn", h, kh) + ["ee", "ne", "bo", ("tx", t, h), ("lv", b, h), ("sid", 256.0)], ["cbklo", "cbkhi"], "cbk", "c")
+        act(T.ck[:, hs(h)], T.cbk[:, lo], F.Identity, HW, ["cbklo"], [("ck", h)], ["cbk"], bias=-256.0, name="ck")
+        ts(T.nq[:, hs(h)], T.ck[:, hs(h)], T.thq[:, 0:1], None, A.is_lt, None, HW, .5, [("ck", h), "thq"], [("nq", h)], name="nq")
+
+    FOLDS = {"0": ([], [0, 1, 2, 3]), "h": ([(0, 1)], [0, 2, 3]), "1": ([(0, 1), (2, 3)], [0, 2]), "2": ([(0, 1), (2, 3), (0, 2)], [0]),
+             "c": ([(0, 1), (0, 2)], [0, 3])}
+
+    def gather_u(t, h):
+        n, pu = 2 * (t % 2) + h, T["pu%d" % h]
+        for kh in range(4):
+            tt(block(pu, kh), T["tu%d" % t][:].indirect(listed(T["off%d" % t], h, kh)), block(T["wr%d" % n], kh), A.mult, BL, GC,
+               both("tu", t) + [("arr", "u", t), ("off", t, h), ("wr", n, kh)], [("pu", h, kh)], name="gu")
+        for a, c in FOLDS[CFG["fin"].split()[2 * t + h][0]][0]:
+            dma("g", [(block(pu, a), block(pu, c))], 1024, [("pu", h, c)], [("pu", h, a)], "fold", True)
+
+    def new_u(t, h):
+        last, fin, pu, up = t == STEPS - 1, CFG["fin"].split()[2 * t + h], T["pu%d" % h], T.ub[:, lo]
+        left = FOLDS[fin[0]][1]
+        for kh, who in zip(left, fin[1:]):
+            if who == "s":
+                turn[0] += 1
+                sc = T["sc%d" % (turn[0] % 2)]
+                dve(BL, 1, lambda sc=sc, kh=kh: ve.tensor_tensor_scan(sc[:], T.msk[:], block(pu, kh), 0.0, A.mult, A.add),
+                    [("pu", h, kh), "msk"], [("sc", turn[0] % 2)], name="scan")
+                terms, key = [slot(sc, 3)], ("sc", turn[0] % 2)
             else:
-                for q in range(2):
-                    s = slice(q * 1024, (q + 1) * 1024)
-                    dve(1024, 1, lambda s=s: ve.tensor_tensor_scan(sc[:, s], T.msk[:], pu[:, s], 0.0, A.mult, A.add), pk + ["msk"], [("sc", q)], name="scan")
-                terms, rk = [(T.i1[:], sc[:, 15:2048:16], 4)], [("sc", 0), ("sc", 1)]
-            if j in CFG["pesum"][t]:
-                mm([(T.ub[:, 0:CW], T.ik[:], tu[:, os_], True, False, 4 * CW), (T.ub[:, 0:CW], sid(128.0), tx[:, os_], False, False, CW)],
-                   [("tu", t, j), ("tx", t, j), "ik", ("sid", 128.0)], [("ub", -1)], "ub", "arg")
-                for k in range(0, 8 if folded else 0, 2):
-                    mm([(T.ub[:, 0:CW], T.i1[:], pu[:, q:1024:8], False, q == 7, 4 * CW) for q in (k, k + 1)],
-                       pk + ["i1"], ["ub"] if k == 6 else [("ub", k)], "ub", "sum")
-                for k in range(0, 0 if folded else 16, 2):
-                    ks = [(k + i) // 4 + 4 * ((k + i) % 4) for i in range(2)]
-                    mm([(T.ub[:, 0:CW], T.i1[:], pu[:, q:2048:16], False, q == 15, 4 * CW) for q in ks],
-                       [pk[k // 4], "i1"], ["ub"] if k == 14 else [("ub", k)], "ub", "sum")
-            else:
-                acc(T.ub[:, 0:CW], [(T.ik[:], tu[:, os_], 4), (sid(128.0), tx[:, os_], 1)] + terms, CW,
-                    rk + [("tu", t, j), ("tx", t, j), "i1", "ik", ("sid", 128.0)], ["ub"], "ub", "arg")
-            nu = T.uo[:, cs] if last else T["tu%d" % (t + 1)][:, os_]
-            act(nu, T.ub[:, 0:CW], F.Tanh, CW, ["ub"], [("tu", t + 1, j)], ["ub"], scale=2.0 ** -11, bias=-0.5, name="tanh")
-            if last:
-                dma("sp", T.yu[:, cs], nu, 64, [("tu", t + 1, j)], [])
-        if what != "c":
-            return
-        mm([(T.xb[:, m:512:4], sid(1.0), tx[:, os_], True, True, CW) for m in range(4)], [("tx", t, j), ("sid", 1.0)], ["xb"], "xb", "xrep")
-        for r in range(4):
-            tt(mn[:, r * 512:(r + 1) * 512], xc[:, r:2048:4], T.xb[:], A.min, 512, 1, xk + ["xb"], [("mn", j, r)], ["xb"], "min")
-        acc(T.cbk[:, (j % 2) * CW:(j % 2 + 1) * CW],
-            [(sid(128.0), T["la%d" % b][:, cs], 1)] +
-            [(T.ee[:, 16 - k:144 - k], mn[:, (k % 4) * 512 + k // 4:(k % 4 + 1) * 512:4], 1) for k in range(16)], CW,
-            [("mn", j, r) for r in range(4)] + ["ee", ("la", b, h), ("sid", 128.0)], [("cbk", j % 2)], "cbk", "c")
+                terms, key = [slot(pu, 4 * kh + kl) for kl in range(4)], ("pu", h, kh)
+            mm([(up, T.ik[:], T["tu%d" % t][:, mine(h)], True, False, 4 * HW), (up, sid(128.0), T["tx%d" % t][:, mine(h)], False, False, HW)] * (kh == 0) +
+               [(up, T.ni1[:], x, False, kh == left[-1] and i == len(terms) - 1, 4 * HW) for i, x in enumerate(terms)],
+               [key, ("tu", t, h), ("tx", t, h), "ik", "ni1", ("sid", 128.0)], ["ublo", "ubhi"], "ub", "arg")
+        nu = T.uo[:, hs(h)] if last else T["tu%d" % (t + 1)][:, mine(h)]
+        act(nu, up, F.Tanh, HW, ["ublo"], [("tu", t + 1, h)], ["ub"], scale=2.0 ** -11, bias=-0.5, name="tanh")
+        if last:
+            dma("sp", [(T.yu[:, hs(h)], nu)], 128, [("tu", t + 1, h)], [])
+        return [] if last else sends("u", t + 1, h)
 
     def slots(t, h):
         b, n, last = t % 2, 1 - t % 2, t == STEPS - 1
         s = hs(h)
-        la, bb, ww, cc, dd, ga, sg = (T["la%d" % b][:, s], T["bb%d" % b][:, s], T["ww%d" % b][:, s], T["cc%d" % b][:, s],
-                                      T["dd%d" % b][:, s], T["ga%d" % b][:, s], T["sg%d" % h])
-        ck = [("cbk", 0), ("cbk", 1)]
-        act(T.ck[:, s], T.cbk[:, lo], F.Identity, HW, ck, [("ck", h)], ["cbk"], bias=-128.0, name="ck")
-        act(T.ph[:, s], T.cbk[:, lo], F.Sign, HW, ck + ["thq"], [("ph", h)], ["cbk"], bias=T.thf[:, 0:1], name="ph")
+        lv, bb, ww, ga = [(T["%s%d" % (x, i)][:, s], (x, i, h)) for x, i in (("lv", b), ("bb", b), ("ww", b), ("ga", t))]
+        nq, on, sg = (T.nq[:, s], ("nq", h)), (one, "ones"), T["sg%d" % h]
         nx = T.xo[:, s] if last else T["tx%d" % (t + 1)][:, own + h * HW:own + (h + 1) * HW]
         for q in range(4):
-            bank = "m%d" % (q % 2)
+            bank = pair(h)[q % 2]
             mm([(T[bank][:, sl], blk(T.sh, 1 + 2 * q + i), T.ck[:, s], True, True, HW) for i, sl in enumerate((lo, hi))],
                [("ck", h), "sh"], [bank + "lo", bank + "hi"], bank, "diff")
             for i, sl in enumerate((lo, hi)):
                 sn = 1 + 2 * q + i
                 act(sg[:, (sn - 1) * HW:sn * HW], T[bank][:, sl], F.Sign, HW, [bank + ("lo", "hi")[i], "tb"], [("sg", h, sn)], [bank],
                     bias=T.tb[:, sn:sn + 1], name="sgn")
-        acc(T.m0[:, hi], [(T.bo[:], nx, 1)], HW, [("tx", t + 1, 2 * h), ("tx", t + 1, 2 * h + 1), "bo"], ["m0hi"], "m0", "E")
-        act(T.ss[:, s], T.m0[:, hi], F.Sign, HW, ["m0hi", "thb"], [("ss", h)], ["m0"], bias=T.thf[:, 1:2], name="ss")
-        acc(T.m1[:, lo], [(sid(64.0), la, 1)] + [(blk(T.sh, 16 - sn) if sn < 8 else sid(-1.0), sg[:, (sn - 1) * HW:sn * HW], 1) for sn in range(1, 9)] +
-            [(T.n32[:], T.ss[:, s], 1)], HW,
-            [("sg", h, sn) for sn in range(1, 9)] + [("ss", h), ("la", b, h), "sh", "n32", ("sid", 64.0), ("sid", -1.0)], ["m1lo"], "m1", "V")
-        act(ga, T.m1[:, lo], F.Sign, HW, ["m1lo"], [("ga", t, h)], ["m1"], bias=-104.0, name="ga")
-        base = [("bb", b, h), ("ga", t, h), ("ph", h), ("la", b, h)]
-        acc(T.m0[:, hi], [(sid(-2.0), bb, 1), (sid(1.0), T.ph[:, s], 1), (sid(1.0), la, 1), (sid(-3.0), ga, 1)], HW,
-            base + [("sid", x) for x in (-2.0, 1.0, -3.0)], ["m0hi"], "m0", "u")
-        acc(T.m0[:, lo], [(sid(2.0), bb, 1), (sid(4.0), T.ph[:, s], 1), (sid(-4.0), la, 1), (sid(-3.0), ga, 1)], HW,
-            base + [("sid", x) for x in (2.0, 4.0, -4.0, -3.0)], ["m0lo"], "m0", "t")
-        acc(T.m1[:, lo], [(sid(1.0), ww, 1), (sid(2.0), ga, 1)], HW, [("ww", b, h), ("ga", t, h), ("sid", 1.0), ("sid", 2.0)], ["m1lo"], "m1", "W")
-        act(T.m0[:, hi], T.m0[:, hi], F.Relu, HW, ["m0hi"], ["m0hi"], ["m0"], bias=-2.0, name="sw")
-        act(T["bb%d" % n][:, s], T.m0[:, lo], F.Relu, HW, ["m0lo"], [("bb", n, h)], ["m0"], scale=0.5, bias=-2.5, name="b")
+        m0, m1 = pair(h)
+        acc(T[m0][:, hi], [(T.bo[:], nx, 1)], HW, [("tx", t + 1, h), "bo"], [m0 + "hi"], m0, "E")
+        act(T.ss[:, s], T[m0][:, hi], F.Sign, HW, [m0 + "hi", "thb"], [("ss", h)], [m0], bias=T.thf[:, 1:2], name="ss")
+        lin(T[m1][:, lo], [(128.0,) + lv, (-1.0, sg[:, 7 * HW:8 * HW], ("sg", h, 8))], HW, [m1 + "lo"], m1, "V",
+            [(blk(T.sh, 16 - sn), sg[:, (sn - 1) * HW:sn * HW], 1) for sn in range(1, 8)] + [(T.n32[:], T.ss[:, s], 1)],
+            [("sg", h, sn) for sn in range(1, 8)] + [("ss", h), "sh", "n32"])
+        act(ga[0], T[m1][:, lo], F.Sign, HW, [m1 + "lo"], [ga[1]], [m1], bias=-168.0, name="ga")
+        tag = [(BIG,) + lv, (BIG,) + nq]
+        lapse = (T.sf, "sf", [(BIG,) + bb, (-2 * BIG,) + lv, (BIG / 2,) + ga, (1.5 * BIG,) + on], m1)
         if not last:
-            act(T["la%d" % n][:, s], T.m0[:, lo], F.Sign, HW, ["m0lo"], [("la", n, h)], ["m0"], scale=0.5, bias=-3.0, name="la")
-        nw = T["ww%d" % n][:, s]
-        if CFG["wv"]:
-            ts(nw, T.m1[:, lo], 2.0, 15.0, A.add, A.min, HW, 1, ["m1lo"], [("ww", n, h)], ["m1"], "W")
+            jumped(t, h, m0)
+            ways = [(T["q%d" % t], ("q", t, h), tag, m0), lapse]
         else:
-            act(T.rr[:, s], T.m1[:, lo], F.Relu, HW, ["m1lo"], [("rr", h)], ["m1"], scale=-1.0, bias=13.0, name="rr")
-            act(nw, T.rr[:, s], F.Identity, HW, [("rr", h)], [("ww", n, h)], scale=-1.0, bias=15.0, name="W")
-        tt(T.m0[:, lo], dd, T.m0[:, hi], A.mult, HW, 1, [("dd", b, h), "m0hi"], ["m0lo"], ["m0"], "dl")
-        tt(T["cc%d" % n][:, s], cc, T.m0[:, lo], A.add, HW, 1, [("cc", b, h), "m0lo"], [("cc", n, h)], ["m0"], "C")
+            ever = [(T["ga%d" % i][:, s], ("ga", i, h)) for i in range(2)]
+            ways = [(T.q0, ("q", 0, h), tag + [(BIG / 2,) + x for x in ever] + [(BIG,) + on], m0),
+                    (T.q1, ("q", 1, h), tag + [(-BIG / 2,) + x for x in ever], m0), lapse]
+        cur = (T["cc%d" % b][:, s], ("cc", b, h))
+        for i, (name, key, terms, bank) in enumerate(ways):
+            lin(T[bank][:, hi], terms, HW, [bank + "hi"], bank, "N", [(T.inn[:], name[:, s], NC)], ["inn", key])
+            out = (T["r%d" % (1 + i % 2)][:, s], ("r%d" % (1 + i % 2), h))
+            tt(out[0], cur[0], T[bank][:, hi], A.min, HW, 1, [cur[1], bank + "hi"], [out[1]], [bank], "r")
+            cur = out
+        nc = T.co[:, s] if last else T["cc%d" % n][:, s]
+        act(nc, cur[0], F.Abs, HW, [cur[1]], [("cc", n, h)], name="abs")
+        lin(T[m0][:, lo], [(1.0,) + bb, (-1.5,) + ga, (-4.0,) + lv, (-3.0,) + nq], HW, [m0 + "lo"], m0, "t")
+        lin(T[m1][:, lo], [(1.0,) + ww, (2.0,) + ga], HW, [m1 + "lo"], m1, "W")
+        nb, nw = T["bb%d" % n][:, s], T["ww%d" % n][:, s]
+        act(nb, T[m0][:, lo], F.Relu, HW, [m0 + "lo"], [("bb", n, h)], [m0], bias=1.5, name="b")
+        ts(nw, T[m1][:, lo], 2.0, 15.0, A.add, A.min, HW, 1, [m1 + "lo"], [("ww", n, h)], [m1], "W")
         if last:
-            acc(T.m1[:, hi], [(sid(1.0), nw, 1), (sid(-16.0), T["bb%d" % n][:, s], 1)], HW,
-                [("ww", n, h), ("bb", n, h), ("sid", 1.0), ("sid", -16.0)], ["m1hi"], "m1", "yw")
-            act(T.wo[:, s], T.m1[:, hi], F.Identity, HW, ["m1hi"], [("wo", h)], ["m1"], bias=48.0, name="yw")
-            dma("sp", T.yw[:, s], T.wo[:, s], 128, [("wo", h)], [])
-            dma("sp", T.yc[:, s], T["cc%d" % n][:, s], 128, [("cc", n, h)], [])
-            dma("g", T.yx[:, s], T.xo[:, s], 128, [("tx", t + 1, 2 * h), ("tx", t + 1, 2 * h + 1)], [])
+            lin(T[m1][:, hi], [(1.0, nw, ("ww", n, h)), (-16.0, nb, ("bb", n, h))], HW, [m1 + "hi"], m1, "yw")
+            act(T.wo[:, s], T[m1][:, hi], F.Identity, HW, [m1 + "hi"], [("wo", h)], [m1], bias=48.0, name="yw")
+            dma("sp", [(T.yw[:, s], T.wo[:, s])], 128, [("wo", h)], [])
+            dma("sp", [(T.yc[:, s], nc)], 128, [("cc", n, h)], [])
             return
-        cp(T["off%d" % (t + 1)][:, s], T["cc%d" % n][:, s], HW, 1, [("cc", n, h)], [("off", t + 1, h)], name="off")
-        tt(T.m0[:, hi], T.g2[:, s], T.m0[:, hi], A.mult, HW, 1, ["g2", "m0hi"], ["m0hi"], ["m0"], "d1")
-        tt(T["dd%d" % n][:, s], dd, T.m0[:, hi], A.add, HW, 1, [("dd", b, h), "m0hi"], [("dd", n, h)], ["m0"], "d2")
+        offsets(T["cc%d" % n], ("cc", n, h), T["off%d" % (t + 1)], ("off", t + 1, h), h)
+        ts(T["lv%d" % n][:, s], nb, 1.0, None, A.min, None, HW, .5, [("bb", n, h)], [("lv", n, h)], name="lv")
         weights(n, h)
-
-    def captured(t, h):
-        b, n, s = t % 2, 1 - t % 2, hs(h)
-        nd = T["dd%d" % n][:, s]
-        acc(T.m1[:, hi], [(sid(0.5), T.ones[:], 1), (sid(0.5), T["ga%d" % b][:, s], 1)], HW, ["ones", ("ga", t, h), ("sid", 0.5)], ["m1hi"], "m1", "cap")
-        tt(T.m1[:, hi], T.g1[:, s], T.m1[:, hi], A.mult, HW, 1, ["g1", "m1hi"], ["m1hi"], ["m1"], "d3")
-        tt(nd, nd, T.m1[:, hi], A.add, HW, 1, [("dd", n, h), "m1hi"], [("dd", n, h)], ["m1"], "d4")
 
     lands = {}
     for part in CFG["order"].split():
-        if True:
-            t, what, j = int(part[0]), part[1:-1], int(part[-1])
-            if what == "s":
-                slots(t, j)
-            elif what == "d":
-                captured(t - 1, j)
-            elif what == "j":
-                second_jump()
-            else:
-                chunk(t, j, what)
-            for kind in "xu":
-                for grp in CFG["sends"]:
-                    if t < STEPS - 1 and kind in what and grp[-1] == j:
-                        ld = lands.setdefault((kind, t), [])
-                        ld.append(send(kind, t + 1, grp[0] * CW, (j + 1) * CW, [("t" + kind, t + 1, i) for i in grp],
-                                       (32 if kind == "x" else 64) * len(grp)))
-                        if len(ld) == len(CFG["sends"]):
-                            arrive(kind, t + 1, ld)
+        t, what, j = int(part[0]), part[1], int(part[2])
+        here[0] = part
+        if what in "xu":
+            ld = lands.setdefault((what, t), [])
+            ld.append({"x": new_x, "u": new_u}[what](t, j))
+            if len(ld) == 2 and t < STEPS - 1:
+                arrive(what, t + 1, sum(ld, []))
+        else:
+            {"w": spread_weights, "X": gather_x, "U": gather_u, "c": matches, "s": slots, "j": jump}[what](t, j)
     return nodes, ncalls, neng
 
 
@@ -598,7 +678,7 @@ def emit(g, T, nodes, order, ncalls, neng):
             continue
         ck = clock[x["eng"]]
         ws = []
-        for d in sorted(x["hard"], key=lambda d: -nodes[d]["st"]):
+        for d in sorted({nodes[d]["of"] for d in x["hard"]}, key=lambda d: (-nodes[d]["st"], d)):
             if nodes[d]["kind"] == "r":
                 continue
             k, v = pos[d]
@@ -633,9 +713,10 @@ def emit(g, T, nodes, order, ncalls, neng):
         if x["kind"] == "r":
             nsent += neng
         elif x["kind"] == "d":
-            sem[i] = (T.sem["d%d" % nd], 16)
+            sem[i] = (T.sem["d%d" % nd], 16 * len(ins))
             nd += 1
-            ins.then_inc(sem[i][0], 16)
+            for one in ins:
+                one.then_inc(sem[i][0], 16)
             if i not in need:
                 tail.append((q, sem[i]))
         elif i in need:

@@ -1,6 +1,6 @@
 import math
 from concourse.bass import DstId, RemoteDMATransfer
-from concourse.mybir import AluOpType, ActivationFunctionType
+from concourse.mybir import AluOpType, ActivationFunctionType, AxisListType
 
 A = AluOpType
 F = ActivationFunctionType
@@ -11,17 +11,21 @@ QW = 128
 BIG = 4096.0
 CFG = {
     "min": "vv vv vv",
-    "jump": "aaaa aaaa aaaa aaaa",
-    "fin": "1ss hsss 1ss hsss 1ss hsss",
-    "pieces": "X02 x24 U02 u24",
-    "order": "0w0 0w1 0X0 0c0 0x0 0X1 0x1 0c1 0j0 0s0 0U0 0u0 1w0 0j1 0s1 0U1 0u1 1w1 "
-             "1X0 1c0 1x0 1X1 1x1 1c1 1j0 1s0 1U0 1u0 2w0 1j1 1s1 1U1 1u1 2w1 "
-             "2X0 2c0 2x0 2X1 2c1 2x1 2s0 2U0 2u0 2s1 2U1 2u1",
-    "cut": 128, "hbank": "ub",
-    "due": {"X": (0, 8), "x": (1, 9), "c": (2, 10), "w": (-15, -5), "s": (-5, -4), "U": (18, 23), "u": (0, 0), "j": (6, 14)},
-    "period": 29.0, "seed": 1, "rounds": 300, "temp": 200.0, "swaps": 40000, "heat": 500.0,
+    "gx": "aaaa aaaa aaaa aaaa aaaa aaaa",
+    "gu": "vvvv vvvv vvvv vvvv vava vava",
+    "jump": "avav aaaa aaaa aaaa",
+    "fin": "1ss 0ssss 1ss 0ssss 1ss 0ssss",
+    "pieces": "X02 x24 U02 u23 u34",
+    "order": "0w0 0w1 0X0 0c0 0x0 0X1 0x1 0c1 0j0 0s0 0U02 0u02 1w0 0j1 0s1 0U23 0u23 0U34 0u34 1w1 "
+             "1X0 1c0 1x0 1X1 1x1 1c1 1j0 1s0 1U02 1u02 2w0 1j1 1s1 1U23 1u23 1U34 1u34 2w1 "
+             "2X0 2c0 2x0 2X1 2c1 2x1 2s0 2U02 2u02 2s1 2U24 2u24",
+    "end": "cbk",
+    "loads": "xUawsp j", "cuts": (192, 512), "first": "xrd", "hbank": "ub", "mod": "v", "lv": "v",
+    "due": {"X": (0, 8), "x": (1, 9), "c": (2, 10), "w": (-15, -5), "s": (-5, -4), "U": (18, 20, 23, 25), "u": (0, 0, 0, 0), "j": (6, 14), "q": (-3, -3)},
+    "early": {"load": -100, "list": -80, "const": 0, "init0": -58, "init1": -55, "0j0": -20, "0j1": 0.5, "0w0": -50, "0w1": -45},
+    "period": 29.0, "seed": 7, "rounds": 300, "temp": 200.0, "swaps": 12000, "heat": 500.0, "more": 30000, "cool": 0.3,
 }
-PRM = {"cy": 0.88, "pe": 0.44, "gc": 1.56, "link": 13.0, "lat": 2500.0, "sync": 80.0, "fx": 30.0, "dr": 3.0, "dl": 2000.0}
+PRM = {"cy": 0.88, "pe": 0.44, "gc": 1.56, "link": 13.0, "lat": 2500.0, "sync": 100.0, "fx": 40.0, "dr": 3.0, "dl": 2000.0, "fl": 2000.0, "share": 0.4}
 
 bf, f32, f16, i32, u16 = "bfloat16", "float32", "float16", "int32", "uint16"
 ND = f16
@@ -32,7 +36,7 @@ def _buf(name, cols, dt, where="sbuf"):
     SCRATCH[name] = (where, [128, cols], dt)
 
 
-SCALES = [1.0, -1.0, 256.0, 128.0, 2.0, 3.0, -3.0, -4.0, -1.5, -16.0, BIG, -BIG, -2 * BIG, BIG / 2, -BIG / 2, 1.5 * BIG]
+SCALES = [1.0, -1.0, 256.0, 128.0, 2.0, 3.0, -3.0, -4.0, -1.5, -16.0, BIG, -BIG, -2 * BIG, BIG / 2, -BIG / 2, 1.5 * BIG, -NR * V / 2]
 for _t in range(STEPS):
     _buf("tx%d" % _t, NR * V, bf)
     _buf("tu%d" % _t, NR * V, f32)
@@ -48,33 +52,35 @@ for _j in range(2):
     _buf("wr%d" % (2 + _j), 4 * BL, bf)
     _buf("sc%d" % _j, BL, f32)
     _buf("sg%d" % _j, 8 * HW, bf)
-    for _n in ("bb", "lv", "ww"):
+    _buf("uc%d" % _j, BL, f32)
+    for _n in ("bb", "lv", "ww", "nw"):
         _buf("%s%d" % (_n, _j), V, bf)
     _buf("cc%d" % _j, V, ND)
     _buf("q%d" % _j, V, ND)
 for _n, _c, _d in [
         ("jt", NR * V, bf), ("si", V, i32), ("pi", V, i32), ("ab", V, bf), ("ti", 4, i32),
-        ("offs", V, u16), ("sf", V, ND), ("pf", V, ND), ("r1", V, ND), ("r2", V, ND), ("md", V, bf), ("nw", V, bf),
+        ("sf", V, ND), ("r1", V, ND), ("r2", V, ND), ("md", V, bf), ("tm2", 16, f32), ("tm3", 4, f32), ("lf", 512, bf),
         ("yy", V, bf), ("xo", V, bf), ("uo", V, f32), ("wo", V, f32), ("co", V, f32),
-        ("ck", V, bf), ("nq", V, bf), ("ss", V, bf), ("ones", HW, bf), ("msk", BL, bf), ("thf", 4, f32), ("thq", 8, bf),
+        ("ck", V, f16), ("nq", V, bf), ("ss", V, bf), ("ones", HW, bf), ("msk", BL, bf), ("thf", 4, f32),
         ("ci", 144, bf), ("cm", 128, bf), ("cb", 128, bf), ("cg", 128, bf), ("ia", 16, i32), ("ib", 16, i32), ("ic", 16, i32), ("fa", 16, f32),
-        ("ks", 16, f32), ("mk16", 16, f32), ("tb", 16, f32), ("col", 16, f32), ("tmp", 16, f32), ("m4", 4, f32), ("k12", 4, f32),
-        ("bo", 128, bf), ("ee", 144, bf), ("ne", 144, bf), ("dg", 2048, bf), ("sh", 2048, bf), ("n32", 128, bf), ("nm", 128, bf),
+        ("ks", 16, f32), ("mk16", 4, f32), ("tb", 1, f32), ("col", 16, f32), ("tmp", 16, f32), ("m4", 4, f32), ("k12", 1, f32),
+        ("bo", 128, bf), ("ee", 144, bf), ("ne", 144, bf), ("dg", 512, bf), ("sh", 2048, bf), ("n32", 128, bf), ("nm", 128, bf),
         ("kd", 128, bf), ("nih", 128, f16), ("ino", 128, ND), ("inn", 128, ND), ("ni1", 128, f32), ("ik", 128, f32), ("pw", 4 * 144, ND),
         ("gm", 512, bf), ("sid", 128 * len(SCALES), bf)]:
     _buf(_n, _c, _d)
-for _n in ("xb0", "xb1", "cbk", "ub", "m0", "m1", "m2", "m3"):
+_buf("xb", BL, f32, "psum")
+for _n in ("cbk", "ub", "m0", "m1", "m2", "m3"):
     _buf(_n, 512, f32, "psum")
 
 ENG = ("g", "pe", "dve", "act", "sp")
-NDMA = 72
-SEMAPHORES = ["q_" + e for e in ENG] + ["d%d" % i for i in range(NDMA)] + ["sent"] + ["h%d" % i for i in range(16)] + \
+NDMA = 48
+SEMAPHORES = ["q_" + e for e in ENG] + ["d%d" % i for i in range(NDMA)] + ["sent"] + ["h%d" % i for i in range(10)] + \
              ["ax%d" % t for t in range(STEPS)] + ["au%d" % t for t in range(STEPS)]
 
 
-SPREAD = [{}, {"gc": 1.15, "link": 10.0, "cy": 0.83, "pe": 0.42}, {"gc": 1.9, "link": 20.0, "lat": 3500.0, "cy": 1.0, "pe": 0.7},
-          {"link": 25.0, "lat": 4000.0, "dr": 6.0, "dl": 3000.0, "sync": 150.0, "fx": 50.0}]
-WEIGHT = [3, 1, 1, 1]
+SPREAD = [{}, {"gc": 1.9, "link": 20.0, "lat": 3500.0, "cy": 1.0, "pe": 0.7},
+          {"link": 22.0, "lat": 3500.0, "dr": 4.5, "dl": 3000.0, "sync": 150.0, "fx": 50.0, "share": 0.7}]
+WEIGHT = [3, 1, 1]
 KEPT = {}
 
 
@@ -119,8 +125,11 @@ def order_nodes(sets):
         p = x["part"]
         for k in (p, p + " " + x["name"], p + " " + x["eng"]):
             groups.setdefault(k, []).append(i)
-        due = int(p[0]) * CFG["period"] + CFG["due"][p[1]][int(p[2])] if p[0].isdigit() else {"load": -100, "const": -50, "init0": -58, "init1": -40}[p]
+        due = CFG["early"][p] if p in CFG["early"] else int(p[0]) * CFG["period"] + CFG["due"][p[1]][int(p[2])]
         pr.append(-1000.0 * due - i)
+    for i in range(len(nodes) - 1, -1, -1):
+        if nodes[i]["part"] == "const":
+            pr[i] = max([pr[j] for j, _gap in after[i]], default=0.0) + 1.0
     keys, z = list(groups), [CFG["seed"]]
 
     def rnd():
@@ -142,10 +151,11 @@ def order_nodes(sets):
             cur, pr = got, new
             if got[0] < best[0]:
                 best = got
-    return polish(sets, best[2], rnd)
+    best = polish(sets, best[2], rnd, CFG["swaps"], CFG["heat"])
+    return polish(sets, best[2], rnd, CFG["more"], CFG["heat"] * CFG["cool"])
 
 
-def polish(sets, order, rnd):
+def polish(sets, order, rnd, swaps, heat):
     nodes = sets[0][0]
     n, anc, hard = len(nodes), [], []
     for x in nodes:
@@ -204,7 +214,7 @@ def polish(sets, order, rnd):
         return sum(w * max(run(o, *tab)) for w, tab in zip(WEIGHT, tabs)) / sum(WEIGHT)
     cur, pairs = judge(order), None
     best = (cur, order)
-    for it in range(CFG["swaps"]):
+    for it in range(swaps):
         if pairs is None or rnd() < 0.1:
             pairs = chain(order, *pick[int(len(pick) * rnd())])
         a, b = pairs[int(len(pairs) * rnd())]
@@ -219,7 +229,7 @@ def polish(sets, order, rnd):
                 break
             new = more
         v = judge(new)
-        if v < cur - CFG["heat"] * (1 - it / CFG["swaps"]) * math.log(rnd()):
+        if v < cur - heat * (1 - it / swaps) * math.log(rnd()):
             cur, order, pairs = v, new, None
             if v < best[0]:
                 best = (v, new)
@@ -237,10 +247,11 @@ def plan(g, core, T, topo):
 
 
 def relayed():
-    out = [("u", 0, CFG["cut"], V)]
+    out = [("u", 0, CFG["cuts"][0], CFG["cuts"][1])] + [("u", 0, CFG["cuts"][1], V)] * ("R" in CFG["first"])
     for part in CFG["order"].split():
         for k in CFG["pieces"].split():
-            if k[0].isupper() and part[1] == k[0].lower() and int(part[2]) == (int(k[2]) - 1) // 2 and int(part[0]) < STEPS - 1:
+            q0, q1 = (int(part[2]), int(part[3])) if len(part) == 4 else (2 * int(part[2]), 2 * int(part[2]) + 2)
+            if k[0].isupper() and part[1] == k[0].lower() and q0 < int(k[2]) <= q1 and int(part[0]) < STEPS - 1:
                 out.append((part[1], int(part[0]) + 1, int(k[1]) * QW, int(k[2]) * QW))
     return out
 
@@ -282,7 +293,7 @@ def build(g, core, T, topo, PRM):
         hard, soft = set(), set()
 
         def dep(d, raw):
-            if raw or nodes[d]["eng"] != eng or nodes[d]["kind"] != "c" or kind != "c":
+            if raw or nodes[d]["eng"] != eng:
                 hard.add(d)
             else:
                 soft.add(d)
@@ -291,7 +302,7 @@ def build(g, core, T, topo, PRM):
                 dep(lastw[k], True)
         for k in w:
             if k in lastw:
-                dep(lastw[k], True)
+                dep(lastw[k], eng != "pe")
             for d in readers.get(k, ()):
                 dep(d, True)
         for b in banks:
@@ -347,9 +358,9 @@ def build(g, core, T, topo, PRM):
     def dma(q, pairs, kb, r, w, name="", add=False):
         eng = {"sp": g.sync, "act": g.scalar, "g": g}[q]
         kw = {"accum_op": A.add} if add else {}
-        i = node(q, (1000.0 if q == "g" else 100.0) * len(pairs), lambda: [eng.dma_start(o, x, **kw) for o, x in pairs], r, w,
-                 lat=PRM["dl"] / 2, kind="d", name=name)
-        node("dma", kb * PRM["dr"], None, list(r) + list(w), list(w) + [("dma", i)], lat=PRM["dl"] / 2, kind="l", name=name, of=i)
+        i = node(q, (1000.0 if q == "g" else 100.0) * len(pairs), lambda: [eng.dma_start(o, x, **kw) for o, x in pairs], r, w, ["fifo" + q] * (here[0] == "load"),
+                 lat=PRM["dl"] / 2 + PRM["fl"] * add, kind="d", name=name)
+        node("dma", kb * PRM["dr"], None, list(r) + list(w), list(w) + [("dma", i)], ["fifo"] * (here[0] == "load"), lat=PRM["dl"] / 2, kind="l", name=name, of=i)
         nodes[-1]["hard"].add(i)
 
     def blk(t, k):
@@ -364,43 +375,49 @@ def build(g, core, T, topo, PRM):
     ncalls = {}
 
     def send(kind, t, c0, c1):
-        kb, keys = (c1 - c0) // (4 if kind == "x" else 2), [("t" + kind, t, j) for j in range(c0 // HW, (c1 - 1) // HW + 1)]
+        unit = HW if kind == "x" else QW
+        kb, keys = (c1 - c0) // (4 if kind == "x" else 2), [("t" + kind, t, j) for j in range(c0 // unit, (c1 - 1) // unit + 1)]
         ap = T["t%s%d" % (kind, t)][:, own + c0:own + c1]
         sem = T.sem["a%s%d" % (kind, t)]
         ncalls[(kind, t)] = ncalls.get((kind, t), 0) + 1
         if (kind, t, c0, c1) in relayed():
             hs_ = T.sem["h%d" % relayed().index((kind, t, c0, c1))]
             node("g", 600.0, lambda: g.remote_dma(ap, ap, hs_, T.sem.sent, topo.addr(aid)[1], topo.addr(aid)[0], near),
-                 keys, [("wire", kind, t, c0), "turn"], kind="r", name="relay")
-            node("dma", 300.0 + kb * 2 * PRM["dr"], None, [("wire", kind, t, c0)], [("hop", kind, t, c0)], lat=PRM["lat"] + 600.0, kind="l")
-            node("link2", 500.0 + kb * 3 * PRM["link"], None, [("hop", kind, t, c0)], [("land", kind, t, c0), "turn2"], lat=PRM["lat"], kind="l")
+                 keys, [("wire", kind, t, c0), "turn"], ["fifog"] * (t == 0), kind="r", name="relay")
+            node("dma", 300.0 + kb * 2 * PRM["dr"], None, [("wire", kind, t, c0)], [("hop", kind, t, c0)], ["fifo"] * (t == 0), lat=PRM["lat"] + 600.0, kind="l")
+            node("link2", 500.0 + kb * 3 * PRM["link"], None, [("hop", kind, t, c0)], [("land", kind, t, c0)], ["turn2"], lat=PRM["lat"], kind="l")
             return ("land", kind, t, c0)
 
         def fn():
             g.remote_dma_fused([RemoteDMATransfer(dst_ids=ids, dma_engine_mask=mask, remote_sem=sem, srcs=[ap], dsts=[ap] * len(ids))],
                                local_sem=T.sem.sent)
-        node("g", 600.0, fn, keys, [("wire", kind, t, c0)], kind="r", name="send")
-        node("dma", 500.0 + kb * 3 * PRM["link"], None, [("wire", kind, t, c0)], [("land", kind, t, c0)], lat=PRM["lat"], kind="l")
+        node("g", 600.0, fn, keys, [("wire", kind, t, c0)], ["fifog"] * (t == 0), kind="r", name="send")
+        node("dma", PRM["share"] * kb * 3 * PRM["link"], None, [("wire", kind, t, c0)], [("hop", kind, t, c0)], ["fifo"] * (t == 0), kind="l")
+        node("link", 500.0 + (1 - PRM["share"]) * kb * 3 * PRM["link"], None, [("hop", kind, t, c0)], [("land", kind, t, c0)], lat=PRM["lat"], kind="l")
         return ("land", kind, t, c0)
 
-    def sends(kind, t, h):
-        return [send(kind, t, int(k[1]) * QW, int(k[2]) * QW) for k in CFG["pieces"].split() if k[0].lower() == kind and (int(k[2]) - 1) // 2 == h]
+    def sends(kind, t, q0, q1):
+        return [send(kind, t, int(k[1]) * QW, int(k[2]) * QW) for k in CFG["pieces"].split() if k[0].lower() == kind and q0 < int(k[2]) <= q1]
 
     def arrive(kind, t, lands):
         node("arr", 0.0, (kind, t), lands, [("arr", kind, t)], kind="a")
 
     both = lambda *n: [n + (0,), n + (1,)]
     four = lambda *n: [n + (j,) for j in range(4)]
-    dma("sp", [(T.tx0[:, own:own + V], T.x0[:])], 128, [], both("tx", 0), "x")
-    dma("act", [(T.tu0[:, own:own + V], T.u0[:])], 256, [], both("tu", 0), "u")
-    dma("sp", [(T.si[:], T.s0[:])], 256, [], ["si"], "s")
-    dma("sp", [(T.pi[:], T.p0[:])], 256, [], ["pi"], "p")
-    dma("sp", [(T.ab[:], T.ag[:])], 128, [], ["ab"], "a")
-    dma("sp", [(T.ww0[:], T.w0[:])], 128, [], both("ww", 0), "w")
-    dma("sp", [(T.ti[:, 0:2], T.th[:])], 1, [], ["ti"], "t")
-    dma("act", [(T.jt[:], T.ax[:])], 512, [], ["jt"], "j")
-    arrive("x", 0, [send("x", 0, 0, V)])
-    arrive("u", 0, [send("u", 0, CFG["cut"], V), send("u", 0, 0, CFG["cut"])])
+    loads = {"x": ([(T.tx0[:, own:own + V], T.x0[:])], 128, both("tx", 0)), "u": ([(T.tu0[:, own:own + V], T.u0[:])], 256, four("tu", 0)),
+             "s": ([(T.si[:], T.s0[:])], 256, ["si"]), "p": ([(T.pi[:], T.p0[:])], 256, ["pi"]), "a": ([(T.ab[:], T.ag[:])], 128, ["ab"]),
+             "w": ([(T.ww0[:], T.w0[:])], 128, both("ww", 0)), "j": ([(T.jt[:], T.ax[:]), (T.ti[:, 0:2], T.th[:])], 512, ["jt", "ti"])}
+    soon, late = CFG["loads"].split()
+    for k in soon:
+        dma("act" if k.isupper() else "sp", loads[k.lower()][0], loads[k.lower()][1], [], loads[k.lower()][2], k)
+    cuts = CFG["cuts"]
+    first = {"x": lambda: send("x", 0, 0, V), "d": lambda: send("u", 0, 0, cuts[0]), "r": lambda: send("u", 0, cuts[0], cuts[1]),
+             "R": lambda: send("u", 0, cuts[1], V)}
+    landed = {k: first[k]() for k in CFG["first"]}
+    arrive("x", 0, [landed.pop("x")])
+    arrive("u", 0, list(landed.values()))
+    for k in late.strip("-"):
+        dma("sp", loads[k][0], loads[k][1], loads[soon[-1].lower()][2], loads[k][2], k)
 
     def iota(out, pat, base, cm, n, key, small=True):
         if small:
@@ -418,41 +435,50 @@ def build(g, core, T, topo, PRM):
     cp(T.col[:], T.ic[:], 16, 1, ["ic"], ["col"])
     p16, pb16 = T.fa[:, 0:1], T.col[:, 0:1]
     ts(T.ks[:], T.fa[:], pb16, -16.0, A.add, A.add, 16, 1, ["fa", "col"], ["ks"])
-    ts(T.mk16[:], T.fa[:], 0.0, 16.0, A.is_equal, A.mult, 16, 1, ["fa"], ["mk16"])
-    ts(T.tmp[:], T.ci[:, 0:16], p16, 16.0, A.add, A.is_ge, 16, 1, ["ci", "fa"], ["tmp"])
-    ts(T.tb[:], T.tmp[:], -0.5, None, A.add, None, 16, 1, ["tmp"], ["tb"])
-    ts(T.m4[:], T.fa[:, 0:16:4], 3.5, None, A.is_lt, None, 4, 1, ["fa"], ["m4"])
-    ts(T.k12[:], T.ks[:, 0:16:4], 12.0, None, A.add, None, 4, 1, ["ks"], ["k12"])
+    ts(T.mk16[:], T.fa[:, 0:16:4], 3.5, 16.0, A.is_lt, A.mult, 4, 1, ["fa"], ["mk16"])
+    ts(T.tb[:], p16, -1.0 / 16, 15.0 / 16 - 384.0, A.mult, A.add, 1, 1, ["fa"], ["tb"])
+    ts(T.ic[:, 0:4], T.ib[:, 0:4], 3, None, A.bitwise_and, None, 4, 1, ["ib", "col"], ["ic"])
+    ts(T.m4[:], T.ic[:, 0:4], 0.0, None, A.is_equal, None, 4, 1, ["ic"], ["m4"])
+    ts(T.ic[:, 4:5], T.ib[:, 0:1], 2, None, A.arith_shift_right, None, 1, 1, ["ib", "col"], ["id"])
+    ts(T.k12[:], T.ic[:, 4:5], pb16, -4.0, A.add, A.add, 1, 1, ["id", "col"], ["k12"])
     ts(T.bo[:], T.cb[:], pb16, None, A.is_equal, None, 128, .5, ["cb", "col"], ["bo"], name="bo")
     ts(T.ee[:], T.ci[:], pb16, None, A.is_equal, None, 144, .5, ["ci", "col"], ["ee"], name="ee")
     if "a" in CFG["min"]:
         ts(T.ne[:], T.ci[:], pb16, -1.0, A.is_equal, A.mult, 144, .5, ["ci", "col"], ["ne"], name="ee")
     cI = T.ci[:, 0:128]
     k0 = T.ks[:, 0:1]
-    for s in SCALES:
-        ts(sid(s), cI, k0, s, A.is_equal, A.mult, 128, .5, ["ci", "ks"], [("sid", s)], name="sid")
-    for out, s, key in ((T.nih, -1.0, "nih"), (T.ino, 1.0, "ino"), (T.inn, -1.0, "inn"), (T.ni1, -1.0, "ni1"), (T.ik, 1024.0, "ik"), (T.kd, p16, "kd")):
-        ts(out[:], cI, k0, s, A.is_equal, A.mult, 128, 1, ["ci", "ks", "fa"], [key], name=key)
+    ts(sid(1.0), cI, k0, None, A.is_equal, None, 128, .5, ["ci", "ks"], [("sid", 1.0)], name="sid")
+    for out, s, key in [(sid(s), s, ("sid", s)) for s in SCALES[1:] if s != -NR * V / 2 or CFG["mod"] == "a"] + \
+            [(T.nih[:], -1.0, "nih"), (T.ino[:], 1.0, "ino"), (T.inn[:], -1.0, "inn"), (T.ni1[:], -1.0, "ni1"), (T.ik[:], 1024.0, "ik"), (T.kd[:], p16, "kd")]:
+        act(out, sid(1.0), F.Identity, 128, [("sid", 1.0), "fa"], [key], scale=s, name="id")
     for kh in range(4):
-        ts(T.pw[:, 144 * kh:144 * (kh + 1)], T.ci[:], T.k12[:, kh:kh + 1], T.m4[:, kh:kh + 1], A.is_equal, A.mult, 144, .5, ["ci", "k12", "m4"], [("pw", kh)], name="pw")
+        ts(T.pw[:, 144 * kh:144 * (kh + 1)], T.ci[:], T.k12[:], T.m4[:, kh:kh + 1], A.is_equal, A.mult, 144, .5, ["ci", "k12", "m4"], [("pw", kh)], name="pw")
     ts(T.nm[:], T.cm[:], p16, None, A.is_equal, None, 128, .5, ["cm", "fa"], ["nm"], name="n32")
     ts(T.yy[:, 0:128], cI, k0, 32.0, A.is_equal, A.mult, 128, .5, ["ci", "ks"], [("yy", 0)], name="n32")
     tt(T.n32[:], T.nm[:], T.yy[:, 0:128], A.add, 128, 2, ["nm", ("yy", 0)], ["n32"], name="n32")
-    for k in range(16):
-        act(blk(T.dg, k), sid(1.0), F.Identity, 128, [("sid", 1.0), "mk16"], [("dg", k)], scale=T.mk16[:, k:k + 1], name="dg")
-    iota(T.cg[:], [[16, 8], [0, 4], [4, 4]], 16, 0, 128, "cg")
+    iota(T.cg[:], [[16, 8], [0, 4], [1, 4]], 16, 0, 128, "cg")
     cp(T.tmp[:], T.ia[:], 16, 1, ["ia"], ["tmp"])
     for kl in range(4):
-        ts(blk(T.gm, kl), T.cg[:], T.tmp[:, kl:kl + 1], None, A.is_equal, None, 128, .5, ["cg", "tmp"], [("gm", kl)], name="gm")
+        act(blk(T.dg, kl), sid(1.0), F.Identity, 128, [("sid", 1.0), "mk16"], [("dg", kl)], scale=T.mk16[:, kl:kl + 1], name="dg")
+        ts(blk(T.gm, kl), T.cg[:], T.tmp[:, 4 * kl:4 * kl + 1], None, A.is_equal, None, 128, .5, ["cg", "tmp"], [("gm", kl)], name="gm")
+    lift = lambda t: 1.0 if t else 8.0
+    LIFTS = sorted({(lift(i // 2), who) for i, who in enumerate(CFG["gu"].split()) if "a" in who})
+    for i, (by, who) in enumerate(LIFTS):
+        col = T.tm2[:, 4 * i:4 * i + 4]
+        for kh in range(4):
+            dve(1, 1, lambda kh=kh, c=col, by=by, who=who, i=i: ve.memset(T.tm2[:, 4 * i + kh:4 * i + kh + 1], by * (who[kh] == "a")), [], [("tm2", i, kh)], name="lf")
+        tt(col, col, T.m4[:], A.mult, 4, 2, four("tm2", i) + ["m4"], four("tm2", i), name="lf")
+        dve(4, 1, lambda c=col, i=i: ve.tensor_reduce(T.tm3[:, i:i + 1], c, AxisListType.X, A.add), four("tm2", i), [("tm3", i)], name="lf")
+        ts(blk(T.lf, i), T.bo[:], T.tm3[:, i:i + 1], None, A.mult, None, 128, .5, ["bo", ("tm3", i)], [("lf", by, who)], name="lf")
     for s in range(1, 16):
         ts(blk(T.sh, s), cI, T.ks[:, s:s + 1], None, A.is_equal, None, 128, .5, ["ci", "ks"], [("sh", s)], name="sh")
     sh = T.sh[:, 128:2048]
     node("g", 170 + 2 * 1920 * CY, lambda: g.affine_select(sh, sh, [[0, 15], [-1, 128]], A.not_equal, -1.0, 0, 1),
-         [("sh", s) for s in range(1, 16)] + [("wire", "u", 0, 0)], ["sh"], name="sh")
+         [("sh", s) for s in range(1, 16)] + [("wire", "u", 0, c) for c in (0,) + cuts] + [("wire", "x", 0, 0)], ["sh"], name="sh")
     dve(HW, .5, lambda: ve.memset(T.ones[:], 1.0), [], ["ones"], name="ones")
-    dve(BL, .5, lambda: ve.memset(T.msk[:], 1.0), [], ["msk0"], name="msk")
-    dve(HW, .5, lambda: ve.memset(T.msk[:, 0:BL:4], 0.0), ["msk0"], ["msk"], name="msk")
-    ts(T.thq[:, 0:1], T.ti[:, 0:1], -256.0, None, A.add, None, 1, 1, ["ti"], ["thq"], name="th")
+    node("g", 130 + 2 * BL * CY, lambda: g.iota(T.msk[:], [[0, BL]], 1, 0, allow_small_or_imprecise_dtypes=True), ["sh"], ["msk"], name="msk")
+    node("g", 170 + 2 * BL * CY, lambda: g.affine_select(T.msk[:], T.msk[:], [[0, HW], [1, 4]], A.not_equal, 0.0, 0, 0), ["msk"], ["msk"], name="msk")
+    cp(T.thf[:, 0:1], T.ti[:, 0:1], 1, 1, ["ti"], ["thq"], name="th")
     ts(T.thf[:, 1:2], T.ti[:, 1:2], -1.0, 0.5, A.mult, A.add, 1, 1, ["ti"], ["thb"], name="th")
 
     hs = lambda h: slice(h * HW, (h + 1) * HW)
@@ -460,15 +486,16 @@ def build(g, core, T, topo, PRM):
     lo, hi = slice(0, HW), slice(HW, 2 * HW)
     one = T.ones[:]
     block = lambda buf, kh: buf[:, kh * BL:(kh + 1) * BL]
-    slot = lambda buf, k: buf[:, k // 4 * BL + k % 4:(k // 4 + 1) * BL:4]
+    slot = lambda buf, k: buf[:, k % 4 * BL + k // 4:(k % 4 + 1) * BL:4]
+    held = lambda kh: range(kh, 16, 4)
     listed = lambda off, h, kh: off[:, h * HW + 64 * kh:h * HW + 64 * (kh + 1)]
     pair = lambda h: ("m%d" % (2 * h), "m%d" % (2 * h + 1))
-    turn = [0]
+    turn = [0, 0]
 
     def weights(b, h):
         s, m1 = hs(h), pair(h)[1]
         lin(T[m1][:, lo], [(-1.0, T["bb%d" % b][:, s], ("bb", b, h)), (3.0, T["lv%d" % b][:, s], ("lv", b, h)), (-4.0, one, "ones")], HW, [m1 + "lo"], m1, "m")
-        tt(T.nw[:, s], T["ww%d" % b][:, s], T[m1][:, lo], A.mult, HW, 1, [("ww", b, h), m1 + "lo"], [("nw", h)], [m1], "w")
+        tt(T["nw%d" % b][:, s], T["ww%d" % b][:, s], T[m1][:, lo], A.mult, HW, 1, [("ww", b, h), m1 + "lo"], [("nw", b, h)], [m1], "w")
 
     def offsets(names, key, off, offkey, h):
         m0 = pair(h)[0]
@@ -478,37 +505,44 @@ def build(g, core, T, topo, PRM):
         cp(off[:, hs(h)], T[m0][:, hi], HW, 1, [m0 + "hi"], [offkey], [m0], "off")
 
     def jump(t, h):
-        off, offkey, n = (T.off1, ("off", 1, h), h) if t else (T.offs, ("offs", h), 2 + h)
+        off, offkey, n = (T.off1, ("off", 1, h), h) if t else (T.off2, ("off", 2, h), 2 + h)
         for kh in range(4):
             out, src = block(T["wr%d" % n], kh), T.jt[:].indirect(listed(off, h, kh))
             if CFG["jump"].split()[2 * t + h][kh] == "v":
                 cp(out, src, BL, GC, ["jt", offkey], [("wr", n, kh)], name="jg")
             else:
                 act(out, src, F.Copy, BL, ["jt", offkey], [("wr", n, kh)], cyc=GC, name="jg")
+        wr = T["wr%d" % n]
+        dma("sp", [(wr[kh:128:4, 0:BL], wr[kh:128:4, kh * BL:(kh + 1) * BL]) for kh in range(1, 4)], 192, four("wr", n)[1:], [("wr", n, 0)], "jdma")
 
-    def jumped(t, h, bank):
+    def jumped(t, h, bank="cbk"):
         base, basekey, n = (T.cc1, ("cc", 1, h), h) if t else (T.sf, "sf", 2 + h)
         s, ps = hs(h), T[bank][:, hi]
-        for kh in range(4):
-            mm([(ps, T.ino[:], base[:, s], True, False, HW * NC), (ps, T.kd[:], one, False, False, HW)] * (kh == 0) +
-               [(ps, blk(T.dg, k), slot(T["wr%d" % n], k), False, k == 15, HW) for k in range(4 * kh, 4 * kh + 4)],
-               [("wr", n, kh), "kd", "ones", "ino", basekey] + [("dg", k) for k in range(4 * kh, 4 * kh + 4)], [bank + "lo", bank + "hi"], bank, "jd")
-        ts(T.md[:, s], ps, float(NR * V), -float(NR * V), A.is_ge, A.mult, HW, 1, [bank + "hi"], [("md", h)], [bank], "j1")
-        tt(T["q%d" % t][:, s], T.md[:, s], ps, A.add, HW, 1, [("md", h), bank + "hi"], [("q", t, h)], [bank], "j2")
+        acc(ps, [(T.ino[:], base[:, s], NC), (T.kd[:], one, 1)] + [(blk(T.dg, kl), slot(T["wr%d" % n], 4 * kl), 1) for kl in range(4)], HW,
+            four("wr", n) + four("dg") + ["kd", "ones", "ino", basekey], [bank + "hi"], bank, "jd")
+        if CFG["mod"] == "v":
+            ts(T.md[:, s], ps, float(NR * V), -float(NR * V), A.is_ge, A.mult, HW, 1, [bank + "hi"], [("md", h)], [bank], "j1")
+            tt(T["q%d" % t][:, s], T.md[:, s], ps, A.add, HW, 1, [("md", h), bank + "hi"], [("q", t, h)], [bank], "j2")
+            return
+        act(T.md[:, s], ps, F.Sign, HW, [bank + "hi"], [("md", h)], [bank], bias=0.5 - NR * V, name="j1")
+        mm([(ps, sid(-NR * V / 2), T.md[:, s], False, True, HW)], [("md", h), ("sid", -NR * V / 2)], [bank + "lo", bank + "hi"], bank, "jm")
+        act(T["q%d" % t][:, s], ps, F.Identity, HW, [bank + "hi"], [("q", t, h)], [bank], bias=-NR * V / 2, name="j2")
 
-    here[0] = "init0"
+    here[0] = "list"
     cp(T.sf[:], T.si[:], V, 1, ["si"], ["sf"])
-    cp(T.pf[:], T.pi[:], V, 1, ["pi"], ["pf"])
+    for h in range(2):
+        offsets(T.sf, "sf", T.off2, ("off", 2, h), h)
+    here[0] = "init0"
+    cp(T.r2[:], T.pi[:], V, 1, ["pi"], both("r2"))
     ts(T.bb0[:], T.ab[:], -1.0, 3.0, A.mult, A.add, V, .5, ["ab"], both("bb", 0))
     ts(T.lv0[:], T.ab[:], 2.5, None, A.is_lt, None, V, .5, ["ab"], both("lv", 0))
     for h in range(2):
         here[0] = "init%d" % h
         s, m0 = hs(h), pair(h)[0]
-        lin(T[m0][:, lo], [(-BIG, T.lv0[:, s], ("lv", 0, h)), (BIG, one, "ones")], HW, [m0 + "lo"], m0, "N", [(T.inn[:], T.pf[:, s], NC)], ["inn", "pf"])
+        lin(T[m0][:, lo], [(-BIG, T.lv0[:, s], ("lv", 0, h)), (BIG, one, "ones")], HW, [m0 + "lo"], m0, "N", [(T.inn[:], T.r2[:, s], NC)], ["inn", ("r2", h)])
         tt(T.r1[:, s], T.sf[:, s], T[m0][:, lo], A.min, HW, 1, ["sf", m0 + "lo"], [("r1", h)], [m0], "r")
         act(T.cc0[:, s], T.r1[:, s], F.Abs, HW, [("r1", h)], [("cc", 0, h)], name="abs")
         offsets(T.cc0, ("cc", 0, h), T.off0, ("off", 0, h), h)
-        offsets(T.sf, "sf", T.offs, ("offs", h), h)
         weights(0, h)
 
     def spread_weights(t, h):
@@ -516,15 +550,19 @@ def build(g, core, T, topo, PRM):
         wr, wp = T["wr%d" % n], T["wp%d" % h]
         for i, bank in enumerate(pair(h)):
             bk = [bank + "lo", bank + "hi"]
-            mm([(T[bank][:, kl:512:4], blk(T.gm, kl), T.nw[:, h * HW + i * QW:h * HW + (i + 1) * QW], True, True, QW) for kl in range(4)],
-               [("nw", h)] + four("gm"), bk, bank, "wrep")
+            mm([(T[bank][:, kl:512:4], blk(T.gm, kl), T["nw%d" % (t % 2)][:, h * HW + i * QW:h * HW + (i + 1) * QW], True, True, QW) for kl in range(4)],
+               [("nw", t % 2, h)] + four("gm"), bk, bank, "wrep")
             act(wp[:, 512 * i:512 * (i + 1)], T[bank][:], F.Copy, 512, bk, [("wp", h, i)], [bank], name="wc")
         dma("sp", [(wr[q:128:4, :], wp[:]) for q in range(4)], 1024, both("wp", h), four("wr", n), "wdma")
 
     def gather_x(t, h):
         for kh in range(4):
-            act(block(T["xc%d" % h], kh), T["tx%d" % t][:].indirect(listed(T["off%d" % t], h, kh)), F.Copy, BL,
-                both("tx", t) + [("arr", "x", t), ("off", t, h)], [("xc", h, kh)], cyc=GC, name="gx")
+            out, src = block(T["xc%d" % h], kh), T["tx%d" % t][:].indirect(listed(T["off%d" % t], h, kh))
+            rk = both("tx", t) + [("arr", "x", t), ("off", t, h)]
+            if CFG["gx"].split()[2 * t + h][kh] == "v":
+                cp(out, src, BL, GC, rk, [("xc", h, kh)], name="gx")
+            else:
+                act(out, src, F.Copy, BL, rk, [("xc", h, kh)], cyc=GC, name="gx")
 
     def new_x(t, h):
         n, last, hb = 2 * (t % 2) + h, t == STEPS - 1, CFG["hbank"]
@@ -532,69 +570,87 @@ def build(g, core, T, topo, PRM):
         for kh in range(4):
             dve(BL, .5, lambda kh=kh: ve.tensor_tensor_scan(block(px, kh), block(xc, kh), block(wr, kh), 0.0, A.max, A.mult),
                 [("xc", h, kh), ("wr", n, kh)], [("px", h, kh)], name="xm")
-            mm([(T[hb][:, hi], T.nih[:], slot(px, k), k == 0, k == 15, HW) for k in range(4 * kh, 4 * kh + 4)],
+            mm([(T[hb][:, hi], T.nih[:], slot(px, k), k == 0, k == 15, HW) for k in held(kh)],
                [("px", h, kh), "nih"], [hb + "lo", hb + "hi"], hb, "h")
         act(T.yy[:, hs(h)], T[hb][:, hi], F.Identity, HW, [hb + "hi"], [("yy", h)], [hb], scale=1.0 / 256, bias=160.0 - 255.0 / 512, name="y")
         nx = T.xo[:, hs(h)] if last else T["tx%d" % (t + 1)][:, mine(h)]
         ts(nx, T.yy[:, hs(h)], -160.0, 15.0, A.add, A.min, HW, .5, [("yy", h)], [("tx", t + 1, h)], name="X")
         if last:
             dma("g", [(T.yx[:, hs(h)], nx)], 128, [("tx", t + 1, h)], [])
-        return [] if last else sends("x", t + 1, h)
+        return [] if last else sends("x", t + 1, 2 * h, 2 * h + 2)
 
     def matches(t, h):
         b, xc, mn, tx = t % 2, T["xc%d" % h], T["mn%d" % h], T["tx%d" % t]
         scalar = CFG["min"].split()[t][h] == "a"
-        spread_x = lambda ps, i, start: [(ps[:, m:512:4], sid(1.0), tx[:, own + h * HW + i * QW:own + h * HW + (i + 1) * QW], start, start or m == 3, QW)
-                                         for m in range(4)]
+        spread_x = lambda i, start: [(T.xb[:, 512 * i + m:512 * (i + 1):4], sid(1.0), tx[:, own + h * HW + i * QW:own + h * HW + (i + 1) * QW],
+                                      start, start or m == 3, QW) for m in range(4)]
         for i in range(0 if scalar else 2):
-            mm(spread_x(T["xb%d" % i], i, True), [("tx", t, h), ("sid", 1.0)], ["xb%d" % i], "xb%d" % i, "xrep")
+            mm(spread_x(i, True), [("tx", t, h), ("sid", 1.0)], ["xb%d" % i], "xb%d" % i, "xrep")
         for kh in range(4):
-            for i in range(2):
-                s, bank = slice(kh * BL + 512 * i, kh * BL + 512 * (i + 1)), "xb%d" % i
-                if scalar:
-                    mm([(T[bank][:], sid(-1.0), xc[:, s], True, False, 512)] + spread_x(T[bank], i, False),
-                       [("xc", h, kh), ("tx", t, h), ("sid", 1.0), ("sid", -1.0)], [bank], bank, "xd")
-                    act(mn[:, s], T[bank][:], F.Relu, 512, [bank], [("mn", h, kh, i)], [bank], name="relu")
-                else:
-                    tt(mn[:, s], xc[:, s], T[bank][:], A.min, 512, 1, [("xc", h, kh), bank], [("mn", h, kh, i)], [bank], "min")
+            for i in range(2 if scalar else 0):
+                s, bank, ps = slice(kh * BL + 512 * i, kh * BL + 512 * (i + 1)), "xb%d" % i, T.xb[:, 512 * i:512 * (i + 1)]
+                mm([(ps, sid(-1.0), xc[:, s], True, False, 512)] + spread_x(i, False),
+                   [("xc", h, kh), ("tx", t, h), ("sid", 1.0), ("sid", -1.0)], [bank], bank, "xd")
+                act(mn[:, s], ps, F.Relu, 512, [bank], [("mn", h, kh, i)], [bank], name="relu")
+            if not scalar:
+                tt(block(mn, kh), block(xc, kh), T.xb[:], A.min, BL, 1, [("xc", h, kh), "xb0", "xb1"], both("mn", h, kh), ["xb0", "xb1"], "min")
             mm([(T.cbk[:, lo], sid(256.0), T["lv%d" % b][:, hs(h)], True, False, HW)] * (kh == 0) +
                [(T.cbk[:, lo], T.bo[:], tx[:, mine(h)], False, False, HW)] * (kh == 0 and scalar) +
-               [(T.cbk[:, lo], (T.ne if scalar else T.ee)[:, 16 - k:144 - k], slot(mn, k), False, k == 15, HW) for k in range(4 * kh, 4 * kh + 4)],
+               [(T.cbk[:, lo], (T.ne if scalar else T.ee)[:, 16 - k:144 - k], slot(mn, k), False, k == 15, HW) for k in held(kh)],
                both("mn", h, kh) + ["ee", "ne", "bo", ("tx", t, h), ("lv", b, h), ("sid", 256.0)], ["cbklo", "cbkhi"], "cbk", "c")
-        act(T.ck[:, hs(h)], T.cbk[:, lo], F.Identity, HW, ["cbklo"], [("ck", h)], ["cbk"], bias=-256.0, name="ck")
-        ts(T.nq[:, hs(h)], T.ck[:, hs(h)], T.thq[:, 0:1], None, A.is_lt, None, HW, .5, [("ck", h), "thq"], [("nq", h)], name="nq")
+        act(T.ck[:, hs(h)], T.cbk[:, lo], F.Identity, HW, ["cbklo", "tb"], [("ck", h)], ["cbk"], bias=T.tb[:], name="ck")
+        act(T.nq[:, hs(h)], T.cbk[:, lo], F.Relu, HW, ["cbklo", "thq"], [("nq", h)], ["cbk"], scale=-1.0, bias=T.thf[:, 0:1], name="nq")
 
-    FOLDS = {"0": ([], [0, 1, 2, 3]), "h": ([(0, 1)], [0, 2, 3]), "1": ([(0, 1), (2, 3)], [0, 2]), "2": ([(0, 1), (2, 3), (0, 2)], [0]),
-             "c": ([(0, 1), (0, 2)], [0, 3])}
+    FOLDS = {"0": ([], [0, 1, 2, 3]), "h": ([(0, 1)], [0, 2, 3]), "1": ([(0, 1), (2, 3)], [0, 2])}
 
-    def gather_u(t, h):
+    def span(q0, q1):
+        h, w = q0 // 2, 512 * (q1 - q0)
+        return h, lambda buf, kh: buf[:, kh * BL + 512 * (q0 % 2):kh * BL + 512 * (q0 % 2) + w], w, lambda kh: [("pu", q, kh) for q in range(q0, q1)]
+
+    def gather_u(t, q0, q1):
+        h, piece, w, keys = span(q0, q1)
         n, pu = 2 * (t % 2) + h, T["pu%d" % h]
+        wr, first = T["wr%d" % n], h * HW + 32 * (q0 % 2)
         for kh in range(4):
-            tt(block(pu, kh), T["tu%d" % t][:].indirect(listed(T["off%d" % t], h, kh)), block(T["wr%d" % n], kh), A.mult, BL, GC,
-               both("tu", t) + [("arr", "u", t), ("off", t, h), ("wr", n, kh)], [("pu", h, kh)], name="gu")
+            src = T["tu%d" % t][:].indirect(T["off%d" % t][:, first + 64 * kh:first + 64 * kh + w // 16])
+            rk = four("tu", t) + [("arr", "u", t), ("off", t, h)]
+            if CFG["gu"].split()[2 * t + h][kh] == "v":
+                tt(piece(pu, kh), src, piece(wr, kh), A.mult, w, GC, rk + [("wr", n, kh)], keys(kh), name="gu")
+                continue
+            turn[1] += 1
+            uc = T["uc%d" % (turn[1] % 2)][:, 0:w]
+            act(uc, src, F.Identity, w, rk, [("uc", turn[1] % 2)], cyc=GC, bias=lift(t), name="gu")
+            dve(w, 1, lambda kh=kh, uc=uc: ve.tensor_tensor_scan(piece(pu, kh), uc, piece(wr, kh), 0.0, A.max, A.mult),
+                [("uc", turn[1] % 2), ("wr", n, kh)], keys(kh), name="um")
         for a, c in FOLDS[CFG["fin"].split()[2 * t + h][0]][0]:
-            dma("g", [(block(pu, a), block(pu, c))], 1024, [("pu", h, c)], [("pu", h, a)], "fold", True)
+            dma("g", [(piece(pu, a), piece(pu, c))], w, keys(c), keys(a), "fold", True)
 
-    def new_u(t, h):
-        last, fin, pu, up = t == STEPS - 1, CFG["fin"].split()[2 * t + h], T["pu%d" % h], T.ub[:, lo]
-        left = FOLDS[fin[0]][1]
+    def new_u(t, q0, q1):
+        h, piece, w, keys = span(q0, q1)
+        last, fin, pu, n = t == STEPS - 1, CFG["fin"].split()[2 * t + h], T["pu%d" % h], w // 4
+        bank = "cbk" if last and q1 == 4 and CFG["end"] == "cbk" else "ub"
+        up, s, os_ = T[bank][:, 0:n], slice(q0 * QW, q1 * QW), slice(own + q0 * QW, own + q1 * QW)
+        left, lifted, made = FOLDS[fin[0]][1], CFG["gu"].split()[2 * t + h], [("tu", t + 1, q) for q in range(q0, q1)]
         for kh, who in zip(left, fin[1:]):
             if who == "s":
                 turn[0] += 1
                 sc = T["sc%d" % (turn[0] % 2)]
-                dve(BL, 1, lambda sc=sc, kh=kh: ve.tensor_tensor_scan(sc[:], T.msk[:], block(pu, kh), 0.0, A.mult, A.add),
-                    [("pu", h, kh), "msk"], [("sc", turn[0] % 2)], name="scan")
-                terms, key = [slot(sc, 3)], ("sc", turn[0] % 2)
+                dve(w, 1, lambda sc=sc, kh=kh: ve.tensor_tensor_scan(sc[:, 0:w], T.msk[:, 0:w], piece(pu, kh), 0.0, A.mult, A.add),
+                    keys(kh) + ["msk"], [("sc", turn[0] % 2)], name="scan")
+                terms, key = [sc[:, 3:w:4]], [("sc", turn[0] % 2)]
             else:
-                terms, key = [slot(pu, 4 * kh + kl) for kl in range(4)], ("pu", h, kh)
-            mm([(up, T.ik[:], T["tu%d" % t][:, mine(h)], True, False, 4 * HW), (up, sid(128.0), T["tx%d" % t][:, mine(h)], False, False, HW)] * (kh == 0) +
-               [(up, T.ni1[:], x, False, kh == left[-1] and i == len(terms) - 1, 4 * HW) for i, x in enumerate(terms)],
-               [key, ("tu", t, h), ("tx", t, h), "ik", "ni1", ("sid", 128.0)], ["ublo", "ubhi"], "ub", "arg")
-        nu = T.uo[:, hs(h)] if last else T["tu%d" % (t + 1)][:, mine(h)]
-        act(nu, up, F.Tanh, HW, ["ublo"], [("tu", t + 1, h)], ["ub"], scale=2.0 ** -11, bias=-0.5, name="tanh")
+                at = kh * BL + 512 * (q0 % 2)
+                terms, key = [pu[:, at + kl:at + w:4] for kl in range(4)], keys(kh)
+            mm([(up, T.ik[:], T["tu%d" % t][:, os_], True, False, 4 * n), (up, sid(128.0), T["tx%d" % t][:, os_], False, False, n)] * (kh == 0) +
+               ([(up, blk(T.lf, LIFTS.index((lift(t), lifted))), T["nw%d" % (t % 2)][:, s], False, False, n)] if kh == 0 and "a" in lifted else []) +
+               [(up, T.ni1[:], x, False, kh == left[-1] and i == len(terms) - 1, 4 * n) for i, x in enumerate(terms)],
+               key + four("tu", t) + [("tx", t, h), "ik", "ni1", ("sid", 128.0), ("nw", t % 2, h), ("lf", lift(t), lifted)],
+               [bank + "lo", bank + "hi"], bank, "arg")
+        nu = T.uo[:, s] if last else T["tu%d" % (t + 1)][:, os_]
+        act(nu, up, F.Tanh, n, [bank + "lo"], made, [bank], scale=2.0 ** -11, bias=-0.5, name="tanh")
         if last:
-            dma("sp", [(T.yu[:, hs(h)], nu)], 128, [("tu", t + 1, h)], [])
-        return [] if last else sends("u", t + 1, h)
+            dma("sp", [(T.yu[:, s], nu)], n // 2, made, [])
+        return [] if last else sends("u", t + 1, q0, q1)
 
     def slots(t, h):
         b, n, last = t % 2, 1 - t % 2, t == STEPS - 1
@@ -606,10 +662,8 @@ def build(g, core, T, topo, PRM):
             bank = pair(h)[q % 2]
             mm([(T[bank][:, sl], blk(T.sh, 1 + 2 * q + i), T.ck[:, s], True, True, HW) for i, sl in enumerate((lo, hi))],
                [("ck", h), "sh"], [bank + "lo", bank + "hi"], bank, "diff")
-            for i, sl in enumerate((lo, hi)):
-                sn = 1 + 2 * q + i
-                act(sg[:, (sn - 1) * HW:sn * HW], T[bank][:, sl], F.Sign, HW, [bank + ("lo", "hi")[i], "tb"], [("sg", h, sn)], [bank],
-                    bias=T.tb[:, sn:sn + 1], name="sgn")
+            act(sg[:, 2 * q * HW:(2 * q + 2) * HW], T[bank][:], F.Sign, 2 * HW, [bank + "lo", bank + "hi"],
+                [("sg", h, 2 * q + 1), ("sg", h, 2 * q + 2)], [bank], name="sgn")
         m0, m1 = pair(h)
         acc(T[m0][:, hi], [(T.bo[:], nx, 1)], HW, [("tx", t + 1, h), "bo"], [m0 + "hi"], m0, "E")
         act(T.ss[:, s], T[m0][:, hi], F.Sign, HW, [m0 + "hi", "thb"], [("ss", h)], [m0], bias=T.thf[:, 1:2], name="ss")
@@ -620,7 +674,8 @@ def build(g, core, T, topo, PRM):
         tag = [(BIG,) + lv, (BIG,) + nq]
         lapse = (T.sf, "sf", [(BIG,) + bb, (-2 * BIG,) + lv, (BIG / 2,) + ga, (1.5 * BIG,) + on], m1)
         if not last:
-            jumped(t, h, m0)
+            if "%dq%d" % (t, h) not in CFG["order"]:
+                jumped(t, h, m0)
             ways = [(T["q%d" % t], ("q", t, h), tag, m0), lapse]
         else:
             ever = [(T["ga%d" % i][:, s], ("ga", i, h)) for i in range(2)]
@@ -646,7 +701,10 @@ def build(g, core, T, topo, PRM):
             dma("sp", [(T.yc[:, s], nc)], 128, [("cc", n, h)], [])
             return
         offsets(T["cc%d" % n], ("cc", n, h), T["off%d" % (t + 1)], ("off", t + 1, h), h)
-        ts(T["lv%d" % n][:, s], nb, 1.0, None, A.min, None, HW, .5, [("bb", n, h)], [("lv", n, h)], name="lv")
+        if CFG["lv"] == "v":
+            ts(T["lv%d" % n][:, s], nb, 1.0, None, A.min, None, HW, .5, [("bb", n, h)], [("lv", n, h)], name="lv")
+        else:
+            act(T["lv%d" % n][:, s], nb, F.Sign, HW, [("bb", n, h)], [("lv", n, h)], name="lv")
         weights(n, h)
 
     lands = {}
@@ -655,11 +713,13 @@ def build(g, core, T, topo, PRM):
         here[0] = part
         if what in "xu":
             ld = lands.setdefault((what, t), [])
-            ld.append({"x": new_x, "u": new_u}[what](t, j))
-            if len(ld) == 2 and t < STEPS - 1:
-                arrive(what, t + 1, sum(ld, []))
+            ld += new_x(t, j) if what == "x" else new_u(t, j, int(part[3]))
+            if len(ld) == CFG["pieces"].lower().count(what):
+                arrive(what, t + 1, ld)
+        elif what == "U":
+            gather_u(t, j, int(part[3]))
         else:
-            {"w": spread_weights, "X": gather_x, "U": gather_u, "c": matches, "s": slots, "j": jump}[what](t, j)
+            {"w": spread_weights, "X": gather_x, "c": matches, "s": slots, "j": jump, "q": jumped}[what](t, j)
     return nodes, ncalls, neng
 
 

@@ -10,22 +10,34 @@ BL = 4 * HW
 QW = 128
 BIG = 4096.0
 CFG = {
-    "min": "vv vv vv",
+    "min": "vvvv vvvv vvvv vvvv vvvv vvvv",
     "gx": "aaaa aaaa aaaa aaaa aaaa aaaa",
-    "gu": "vvvv vvvv vvvv vvvv vava vava",
-    "jump": "avav aaaa aaaa aaaa",
-    "fin": "1ss 0ssss 1ss 0ssss 1ss 0ssss",
-    "pieces": "X02 x24 U02 u23 u34",
-    "order": "0w0 0w1 0X0 0c0 0x0 0X1 0x1 0c1 0j0 0s0 0U02 0u02 1w0 0j1 0s1 0U23 0u23 0U34 0u34 1w1 "
-             "1X0 1c0 1x0 1X1 1x1 1c1 1j0 1s0 1U02 1u02 2w0 1j1 1s1 1U23 1u23 1U34 1u34 2w1 "
-             "2X0 2c0 2x0 2X1 2c1 2x1 2s0 2U02 2u02 2s1 2U24 2u24",
-    "end": "cbk",
-    "loads": "xUawsp j", "cuts": (192, 512), "first": "xrd", "hbank": "ub", "mod": "v", "lv": "v",
-    "due": {"X": (0, 8), "x": (1, 9), "c": (2, 10), "w": (-15, -5), "s": (-5, -4), "U": (18, 20, 23, 25), "u": (0, 0, 0, 0), "j": (6, 14), "q": (-3, -3)},
-    "early": {"load": -100, "list": -80, "const": 0, "init0": -58, "init1": -55, "0j0": -20, "0j1": 0.5, "0w0": -50, "0w1": -45},
-    "period": 29.0, "seed": 7, "rounds": 300, "temp": 200.0, "swaps": 12000, "heat": 500.0, "more": 30000, "cool": 0.3,
+    "gu": {"2U23": "aaaa", "2U34": "aaaa"},
+    "jump": "avav avav aaaa aaaa",
+    "split": {"gx": 2, "jg": 2},
+    "fin": "Fp Fp Pss Pss Fp Fp Pss Pss Fp Fp Pss Pss",
+    "pieces": "X02 x24 U01 u12 U23 u34",
+    "order": "0w0 0w1 0j0 0q0 0j1 0q1 0X0 0c0 0x0 0X1 0x1 0c1 0s0 0U01 0U12 0U23 0U34 1w0 0s1 0u23 0u01 0u34 0u12 1w1 1j0 1q0 1j1 1q1 "
+             "1X0 1c0 1x0 1X1 1x1 1c1 1s0 1U01 1U12 1U23 1U34 2w0 1s1 1u23 1u01 1u34 1u12 2w1 "
+             "2X0 2c0 2x0 2X1 2x1 2c1 2U01 2U12 2U23 2U34 2s0 2s1 2u23 2u01 2u34 2u12",
+    "ubank": "aabb", "qbank": "ua",
+    "ages": "av", "halved": (), "copies": 2, "reads": 1, "table": "aa", "kept": ("gu", "gx"),
+    "loads": "xsj pawu", "cuts": (192, 512), "first": "xrd",
+    "due": {"X": (0, 3), "x": (0, 3), "c": (0, 3), "w": (-28, -25), "s": (0, 3), "U": (0, 1, 2, 3), "u": (0, 3, 6, 9), "j": (0, 3), "q": (0, 3),
+            "a": (20, 23), "y": (0, 0)},
+    "yield": {"gx": 30, "jg": 52, "xm": 40, "min": 41, "gu": 50, "scan": 45, "relu": 29, "um": 53},
+    "early": {"load": -100, "list": -85, "const": 0, "init0": -47, "init1": -45, "0w0": -44, "0w1": -43},
+    "period": 28.0, "seed": 2, "rounds": 4000, "temp": 300.0, "swaps": 16000, "heat": 150.0, "more": 25000, "cool": 0.5,
 }
-PRM = {"cy": 0.88, "pe": 0.44, "gc": 1.56, "link": 13.0, "lat": 2500.0, "sync": 100.0, "fx": 40.0, "dr": 3.0, "dl": 2000.0, "fl": 2000.0, "share": 0.4}
+PRM = {"cy": 0.88, "pe": 0.44, "gc": 1.56, "link": 13.0, "lat": 2500.0, "sync": 100.0, "fx": 40.0, "dr": 3.0, "dl": 2000.0, "fl": 2000.0, "share": 0.4,
+       "fr": 1.0, "short": 2.0, "long": 0.9}
+SPREAD = [{"cy": 1.0, "gc": 1.5, "pe": 0.55}, {"cy": 0.83, "gc": 1.1, "lat": 2000.0, "sync": 70.0, "pe": 0.42},
+          {"cy": 1.245, "gc": 1.95, "pe": 0.75}, {"cy": 0.9, "gc": 1.3, "dr": 3.7, "lat": 3200.0, "link": 22.0, "share": 0.6}]
+WEIGHT = [2, 2, 2, 2]
+SCALE = [1.25, 1.0, 1.72, 1.25]
+REMOTE = {"F": 4, "3": 3, "2": 2}
+LEFT = {"0": [0, 1, 2, 3], "P": [0, 2], "F": [-1], "3": [3, -1], "2": [2, 3, -1]}
+UNDER = " 1y0 " in CFG["order"]
 
 bf, f32, f16, i32, u16 = "bfloat16", "float32", "float16", "int32", "uint16"
 ND = f16
@@ -36,7 +48,7 @@ def _buf(name, cols, dt, where="sbuf"):
     SCRATCH[name] = (where, [128, cols], dt)
 
 
-SCALES = [1.0, -1.0, 256.0, 128.0, 2.0, 3.0, -3.0, -4.0, -1.5, -16.0, BIG, -BIG, -2 * BIG, BIG / 2, -BIG / 2, 1.5 * BIG, -NR * V / 2]
+SCALES = [1.0, -1.0, 256.0, 128.0, 2.0, 3.0, -4.0, -1.5, -16.0, BIG, -BIG, -2 * BIG, BIG / 2, -BIG / 2, 1.5 * BIG, 2.0 ** -19]
 for _t in range(STEPS):
     _buf("tx%d" % _t, NR * V, bf)
     _buf("tu%d" % _t, NR * V, f32)
@@ -44,43 +56,45 @@ for _t in range(STEPS):
     _buf("ga%d" % _t, V, bf)
 for _j in range(2):
     _buf("xc%d" % _j, 4 * BL, bf)
-    _buf("mn%d" % _j, 4 * BL, bf)
-    _buf("px%d" % _j, 4 * BL, f16)
     _buf("pu%d" % _j, 4 * BL, f32)
-    _buf("wp%d" % _j, BL, bf)
+    _buf("wp%d" % _j, HW if CFG["copies"] else BL, bf)
     _buf("wr%d" % _j, 4 * BL, bf)
     _buf("wr%d" % (2 + _j), 4 * BL, bf)
     _buf("sc%d" % _j, BL, f32)
+    _buf("uc%d" % _j, BL // 2, f32)
     _buf("sg%d" % _j, 8 * HW, bf)
-    _buf("uc%d" % _j, BL, f32)
+    if any(how[0] in REMOTE for how in CFG["fin"].split()[2 * _j::4] + CFG["fin"].split()[2 * _j + 1::4]):
+        _buf("fo%d" % _j, BL, f32)
+    if UNDER:
+        _buf("jm%d" % _j, BL, f32)
+    else:
+        _buf("jb%d" % _j, 4 * BL, bf)
     for _n in ("bb", "lv", "ww", "nw"):
         _buf("%s%d" % (_n, _j), V, bf)
     _buf("cc%d" % _j, V, ND)
     _buf("q%d" % _j, V, ND)
 for _n, _c, _d in [
-        ("jt", NR * V, bf), ("si", V, i32), ("pi", V, i32), ("ab", V, bf), ("ti", 4, i32),
-        ("sf", V, ND), ("r1", V, ND), ("r2", V, ND), ("md", V, bf), ("tm2", 16, f32), ("tm3", 4, f32), ("lf", 512, bf),
+        ("mn", 4 * BL, bf), ("px", 4 * BL, f16), ("jt", NR * V, bf), ("si", V, i32), ("pi", V, i32), ("ab", V, bf), ("ti", 4, i32),
+        ("sf", V, ND), ("r1", V, ND), ("r2", V, ND), ("md", V, bf), ("tm2", 16, f32), ("tm3", 4, f32), ("lf", 256, bf), ("bk", 256, bf), ("ba", 256, bf),
         ("yy", V, bf), ("xo", V, bf), ("uo", V, f32), ("wo", V, f32), ("co", V, f32),
         ("ck", V, f16), ("nq", V, bf), ("ss", V, bf), ("ones", HW, bf), ("msk", BL, bf), ("thf", 4, f32),
         ("ci", 144, bf), ("cm", 128, bf), ("cb", 128, bf), ("cg", 128, bf), ("ia", 16, i32), ("ib", 16, i32), ("ic", 16, i32), ("fa", 16, f32),
-        ("ks", 16, f32), ("mk16", 4, f32), ("tb", 1, f32), ("col", 16, f32), ("tmp", 16, f32), ("m4", 4, f32), ("k12", 1, f32),
+        ("ks", 16, f32), ("mk16", 4, f32), ("mk23", 4, f32), ("tb", 1, f32), ("col", 16, f32), ("tmp", 16, f32), ("m4", 4, f32), ("k12", 1, f32), ("k4", 2, f32),
         ("bo", 128, bf), ("ee", 144, bf), ("ne", 144, bf), ("dg", 512, bf), ("sh", 2048, bf), ("n32", 128, bf), ("nm", 128, bf),
         ("kd", 128, bf), ("nih", 128, f16), ("ino", 128, ND), ("inn", 128, ND), ("ni1", 128, f32), ("ik", 128, f32), ("pw", 4 * 144, ND),
-        ("gm", 512, bf), ("sid", 128 * len(SCALES), bf)]:
+        ("gm", 4 * 144, bf), ("sid", 128 * len(SCALES), bf)] + \
+        [("ty", NR * V, f32), ("dy", 512, f32)] * UNDER + [("e2", V, bf), ("wcp", V, bf), ("na", V, bf)] * (" 0a0 " in CFG["order"]):
     _buf(_n, _c, _d)
+for _j in range(2 * STEPS * (CFG["copies"] > 0)):
+    SCRATCH["wd%d" % _j] = ("dram", [8, CFG["copies"], 4 * BL], bf)
 _buf("xb", BL, f32, "psum")
-for _n in ("cbk", "ub", "m0", "m1", "m2", "m3"):
+for _n in ("ua", "ub", "m0", "m1", "m2", "m3"):
     _buf(_n, 512, f32, "psum")
 
 ENG = ("g", "pe", "dve", "act", "sp")
-NDMA = 48
+NDMA = 64
 SEMAPHORES = ["q_" + e for e in ENG] + ["d%d" % i for i in range(NDMA)] + ["sent"] + ["h%d" % i for i in range(10)] + \
-             ["ax%d" % t for t in range(STEPS)] + ["au%d" % t for t in range(STEPS)]
-
-
-SPREAD = [{}, {"gc": 1.9, "link": 20.0, "lat": 3500.0, "cy": 1.0, "pe": 0.7},
-          {"link": 22.0, "lat": 3500.0, "dr": 4.5, "dl": 3000.0, "sync": 150.0, "fx": 50.0, "share": 0.7}]
-WEIGHT = [3, 1, 1]
+             ["%s%d" % (k, i) for k in ("fl", "fh", "afo") for i in range(12)] + ["ax%d" % t for t in range(STEPS)] + ["au%d" % t for t in range(STEPS)]
 KEPT = {}
 
 
@@ -90,19 +104,19 @@ def dispatch(nodes, after, count, pr):
     for i, x in enumerate(nodes):
         if left[i] == 0:
             pend[x["eng"]].append(i)
-    st, order = [0.0] * len(nodes), []
+    order = []
     while len(order) < len(nodes):
         t, e = min((max(free[e], min(ready[i] for i in l)), e) for e, l in pend.items() if l)
-        i = max((j for j in pend[e] if ready[j] <= t), key=lambda j: pr[j])
+        i = max((j for j in pend[e] if ready[j] <= t), key=lambda j: pr[j] if e in ENG else -ready[j])
         pend[e].remove(i)
-        st[i], free[e] = t, t + nodes[i]["cost"]
+        free[e] = t + nodes[i]["cost"]
         order.append(i)
         for j, gap in after[i]:
             ready[j] = max(ready[j], t + gap)
             left[j] -= 1
             if left[j] == 0:
                 pend[nodes[j]["eng"]].append(j)
-    return st, order
+    return order
 
 
 def replay(nodes, order, sync):
@@ -117,41 +131,46 @@ def replay(nodes, order, sync):
 
 def order_nodes(sets):
     nodes, sync = sets[0]
-    after, count, groups, pr = [[] for _ in nodes], [0] * len(nodes), {}, []
+    after, count, parts, kinds, pr = [[] for _ in nodes], [0] * len(nodes), {}, {}, []
     for i, x in enumerate(nodes):
         for d in sorted(x["hard"] | x["soft"]):
             after[d].append((i, nodes[d]["cost"] + (nodes[d]["lat"] + sync if d in x["hard"] else 0.0)))
             count[i] += 1
         p = x["part"]
-        for k in (p, p + " " + x["name"], p + " " + x["eng"]):
-            groups.setdefault(k, []).append(i)
+        if p not in ("const", "load"):
+            parts.setdefault(p, []).append(i)
+            if x["eng"] in ("dve", "act", "pe"):
+                kinds.setdefault(x["name"], []).append(i)
         due = CFG["early"][p] if p in CFG["early"] else int(p[0]) * CFG["period"] + CFG["due"][p[1]][int(p[2])]
-        pr.append(-1000.0 * due - i)
-    for i in range(len(nodes) - 1, -1, -1):
-        if nodes[i]["part"] == "const":
-            pr[i] = max([pr[j] for j, _gap in after[i]], default=0.0) + 1.0
-    keys, z = list(groups), [CFG["seed"]]
+        pr.append(-1000.0 * (due + CFG["yield"].get(x["name"], 0.0)) - i)
+    parts, kinds, z = list(parts.values()), list(kinds.values()), [CFG["seed"]]
+    fixed = [i for i in range(len(nodes) - 1, -1, -1) if nodes[i]["part"] == "const"]
 
     def rnd():
         z[0] = (z[0] * 1103515245 + 12345) % 2147483648
         return (z[0] + 0.5) / 2147483648
 
     def judge(pr):
-        st, order = dispatch(nodes, after, count, pr)
-        return sum(w * replay(o, order, sy) for w, (o, sy) in zip(WEIGHT, sets)) / sum(WEIGHT), st, order
+        for i in fixed:
+            pr[i] = max([pr[j] for j, _gap in after[i]], default=0.0) + 1.0
+        order = dispatch(nodes, after, count, pr)
+        return sum(w * replay(o, order, sy) / s for w, s, (o, sy) in zip(WEIGHT, SCALE, sets)) / sum(WEIGHT), order
     best = cur = judge(pr)
+    KEPT["first"] = best[0]
     for it in range(CFG["rounds"]):
         new = list(pr)
-        for _ in range((1, 1, 2, 3)[int(4 * rnd())]):
-            d = (rnd() + rnd() + rnd() - 1.5) * (2000.0, 6000.0, 16000.0)[int(3 * rnd())]
-            for i in groups[keys[int(len(keys) * rnd())]]:
+        for _ in range((1, 1, 2)[int(3 * rnd())]):
+            d = (-8, -5, -3, -2, -1, 1, 2, 3, 5, 8)[int(10 * rnd())] * 1000.0
+            groups = parts if rnd() < 0.6 else kinds
+            for i in groups[int(len(groups) * rnd())]:
                 new[i] += d
         got = judge(new)
         if got[0] < cur[0] - CFG["temp"] * (1 - it / CFG["rounds"]) * math.log(rnd()):
             cur, pr = got, new
             if got[0] < best[0]:
                 best = got
-    best = polish(sets, best[2], rnd, CFG["swaps"], CFG["heat"])
+    KEPT["mid"] = best[0]
+    best = polish(sets, best[1], rnd, CFG["swaps"], CFG["heat"])
     return polish(sets, best[2], rnd, CFG["more"], CFG["heat"] * CFG["cool"])
 
 
@@ -170,22 +189,30 @@ def polish(sets, order, rnd, swaps, heat):
     eng = [names.index(x["eng"]) for x in nodes]
     pre = [x["hard"] | x["soft"] for x in nodes]
     tabs = [([x["cost"] for x in o], [x["lat"] + sy for x in o]) for o, sy in sets]
-    pick = [tab for w, tab in zip(WEIGHT, tabs) for _ in range(w)]
+    pick = [k for k, w in enumerate(WEIGHT) for _ in range(w)]
+    share = [w / sum(WEIGHT) / scale for w, scale in zip(WEIGHT, SCALE)]
+    rows = {i: (i, eng[i], hard[i]) for i in range(n)}
 
-    def run(order, cost, lat):
-        free, end = [0.0] * len(names), [0.0] * n
-        for i in order:
-            e = eng[i]
+    def run(order, k, at, old):
+        cost, lat = tabs[k]
+        free, end, seen = [0.0] * len(names), list(old), set()
+        for i in reversed(order[:at]):
+            if eng[i] not in seen:
+                seen.add(eng[i])
+                free[eng[i]] = end[i] - lat[i]
+                if len(seen) == len(names):
+                    break
+        for i, e, before in map(rows.get, order[at:]):
             st = free[e]
-            for d in hard[i]:
+            for d in before:
                 if end[d] > st:
                     st = end[d]
             free[e] = st = st + cost[i]
             end[i] = st + lat[i]
         return end
 
-    def chain(order, cost, lat):
-        end, last, ahead, pairs = run(order, cost, lat), {}, {}, []
+    def chain(order, end, lat):
+        last, ahead, pairs = {}, {}, []
         for i in order:
             ahead[i], last[eng[i]] = last.get(eng[i]), i
         i = end.index(max(end))
@@ -193,7 +220,8 @@ def polish(sets, order, rnd, swaps, heat):
             d = max(hard[i], key=lambda d: end[d], default=None)
             p = ahead[i]
             if p is not None and (d is None or end[p] - lat[p] >= end[d]):
-                pairs.append((p, i))
+                if names[eng[i]] in ENG or end[d] <= max(end[x] for x in hard[p]):
+                    pairs.append((p, i))
                 d = p
             i = d
         return pairs
@@ -208,32 +236,38 @@ def polish(sets, order, rnd, swaps, heat):
                 need.append(x)
                 engs.add(eng[x])
                 preds |= pre[x]
-        return order[:ia] + need[::-1] + [x for x in order[ia:ib] if x not in need] + order[ib + 1:]
+        return order[:ia] + need[::-1] + [x for x in order[ia:ib] if x not in need] + order[ib + 1:], ia
 
-    def judge(o):
-        return sum(w * max(run(o, *tab)) for w, tab in zip(WEIGHT, tabs)) / sum(WEIGHT)
-    cur, pairs = judge(order), None
+    ends = [run(order, k, 0, [0.0] * n) for k in range(len(tabs))]
+    cur, pairs = sum(s * max(e) for s, e in zip(share, ends)), None
     best = (cur, order)
     for it in range(swaps):
         if pairs is None or rnd() < 0.1:
-            pairs = chain(order, *pick[int(len(pick) * rnd())])
+            k = pick[int(len(pick) * rnd())]
+            pairs = chain(order, ends[k], tabs[k][1])
         a, b = pairs[int(len(pairs) * rnd())]
-        new, back = swap(order, a, b), rnd() < 0.5
-        if new is None:
+        got, back = swap(order, a, b), rnd() < 0.5
+        if got is None:
             continue
-        for _ in range((0, 0, 1, 2, 3, 5)[int(6 * rnd())]):
+        new, at = got
+        for _ in range((0, 0, 1, 2, 3, 5)[int(6 * rnd())] * (names[eng[a]] in ENG)):
             k = new.index(b if back else a)
             near = [x for x in (new[max(0, k - 60):k][::-1] if back else new[k + 1:k + 60]) if eng[x] == eng[a]]
             more = near and (swap(new, near[0], b) if back else swap(new, a, near[0]))
             if not more:
                 break
-            new = more
-        v = judge(new)
-        if v < cur - heat * (1 - it / swaps) * math.log(rnd()):
-            cur, order, pairs = v, new, None
-            if v < best[0]:
-                best = (v, new)
-    end = run(best[1], *tabs[0])
+            new, at = more[0], min(at, more[1])
+        bar, got, v = cur - heat * (1 - it / swaps) * math.log(rnd()), [], 0.0
+        for k in range(len(tabs)):
+            got.append(run(new, k, at, ends[k]))
+            v += share[k] * (max(got[k]) - max(ends[k]))
+            if cur + v > bar + 600.0:
+                break
+        if len(got) == len(tabs) and cur + v < bar:
+            cur, order, pairs, ends = cur + v, new, None, got
+            if cur < best[0]:
+                best = (cur, new)
+    end = run(best[1], 0, 0, [0.0] * n)
     return best[0], [end[i] - tabs[0][0][i] - tabs[0][1][i] for i in range(n)], best[1]
 
 
@@ -256,9 +290,35 @@ def relayed():
     return out
 
 
+def finish():
+    return dict(zip([p for p in CFG["order"].split() if p[1] == "U"], CFG["fin"].split()))
+
+
+def folded():
+    return [(int(p[0]), int(p[2]), int(p[3]), REMOTE[how[0]]) for p, how in finish().items() if how[0] in REMOTE]
+
+
 def helper_of(core, T, topo):
     return [c for c in topo.cores_of(core) if topo.die(c) != topo.die(core) and T.rank_of(c) is None
             and all(topo.may_write(c, p) for p in T.cores)][0]
+
+
+def mirror_of(core, T, topo):
+    return [c for c in topo.cores_of(core) if topo.die(c) == topo.die(core) and T.rank_of(c) is None and topo.addr(c)[2] != topo.addr(core)[2]][0]
+
+
+def fold_sides(T, t, q0, q1):
+    h, at, w = q0 // 2, 512 * (q0 % 2), 512 * (q1 - q0)
+    return T["pu%d" % h][:, t * BL + at:t * BL + at + w], T["fo%d" % h][:, at:at + w]
+
+
+def hand_back(g, core, home, T, topo):
+    mask = topo.mask(core, home)
+    for k, (t, q0, q1, _n) in enumerate(folded()):
+        there, back = fold_sides(T, t, q0, q1)
+        g.wait_ge(T.sem["fh%d" % k], bin(topo.mask(home, core)).count("1"))
+        g.remote_dma(back, there, T.sem["afo%d" % k], T.sem.sent, topo.addr(home)[1], topo.addr(home)[0], mask)
+    g.wait_ge(T.sem.sent, bin(mask).count("1") * len(folded()))
 
 
 def way_out(src, rank, T, topo):
@@ -283,7 +343,6 @@ def hand_on(g, core, rank, T, topo):
 def build(g, core, T, topo, PRM):
     rank = T.rank_of(core)
     CY, PEC, GC = PRM["cy"], PRM["pe"], PRM["gc"]
-    NC = 4 if ND == f32 else 1
     nodes, here = [], ["load"]
     lastw, readers, bankt = {}, {}, {}
     ve, ac, pe = g.vector, g.scalar, g.tensor
@@ -305,7 +364,7 @@ def build(g, core, T, topo, PRM):
                 dep(lastw[k], eng != "pe")
             for d in readers.get(k, ()):
                 dep(d, True)
-        for b in banks:
+        for b in list(banks) + [(name, eng)] * (name in CFG["kept"]):
             for d in bankt.get(b, {}).values():
                 dep(d, False)
             bankt.setdefault(b, {})[eng] = i
@@ -344,8 +403,8 @@ def build(g, core, T, topo, PRM):
             return last
         node("pe", 30 + sum(max(64, it[5]) * PEC for it in items), fn, r, w, (bank,), lat=100.0, name=name)
 
-    def acc(out, terms, n, r, w, bank, name=""):
-        mm([(out, l, x, i == 0, i == len(terms) - 1, n * c) for i, (l, x, c) in enumerate(terms)], r, w, bank, name)
+    def acc(out, terms, n, r, w, bank, name="", start=True):
+        mm([(out, l, x, start and i == 0, i == len(terms) - 1, n * c) for i, (l, x, c) in enumerate(terms)], r, w, bank, name)
 
     def sid(s):
         k = SCALES.index(s)
@@ -413,11 +472,12 @@ def build(g, core, T, topo, PRM):
     cuts = CFG["cuts"]
     first = {"x": lambda: send("x", 0, 0, V), "d": lambda: send("u", 0, 0, cuts[0]), "r": lambda: send("u", 0, cuts[0], cuts[1]),
              "R": lambda: send("u", 0, cuts[1], V)}
-    landed = {k: first[k]() for k in CFG["first"]}
-    arrive("x", 0, [landed.pop("x")])
-    arrive("u", 0, list(landed.values()))
+    landed = {k: first[k]() for k in CFG["first"] if k == "x" or "u" not in late}
     for k in late.strip("-"):
         dma("sp", loads[k][0], loads[k][1], loads[soon[-1].lower()][2], loads[k][2], k)
+    landed.update({k: first[k]() for k in CFG["first"] if k not in landed})
+    arrive("x", 0, [landed.pop("x")])
+    arrive("u", 0, list(landed.values()))
 
     def iota(out, pat, base, cm, n, key, small=True):
         if small:
@@ -425,6 +485,7 @@ def build(g, core, T, topo, PRM):
         else:
             node("g", 130 + 2 * n * CY, lambda: g.iota(out, pat, base, cm), [], [key])
     here[0] = "const"
+    short = " 0a0 " in CFG["order"]
     iota(T.ia[:], [[-1, 16]], 16, 1, 16, "ia", False)
     iota(T.ci[:], [[1, 144]], 0, 0, 144, "ci")
     iota(T.cm[:], [[0, 8], [1, 16]], 0, 0, 128, "cm")
@@ -436,48 +497,56 @@ def build(g, core, T, topo, PRM):
     p16, pb16 = T.fa[:, 0:1], T.col[:, 0:1]
     ts(T.ks[:], T.fa[:], pb16, -16.0, A.add, A.add, 16, 1, ["fa", "col"], ["ks"])
     ts(T.mk16[:], T.fa[:, 0:16:4], 3.5, 16.0, A.is_lt, A.mult, 4, 1, ["fa"], ["mk16"])
-    ts(T.tb[:], p16, -1.0 / 16, 15.0 / 16 - 384.0, A.mult, A.add, 1, 1, ["fa"], ["tb"])
+    act(T.tb[:], p16, F.Identity, 1, ["fa"], ["tb"], scale=-1.0 / 16, bias=15.0 / 16 - 384.0)
     ts(T.ic[:, 0:4], T.ib[:, 0:4], 3, None, A.bitwise_and, None, 4, 1, ["ib", "col"], ["ic"])
     ts(T.m4[:], T.ic[:, 0:4], 0.0, None, A.is_equal, None, 4, 1, ["ic"], ["m4"])
     ts(T.ic[:, 4:5], T.ib[:, 0:1], 2, None, A.arith_shift_right, None, 1, 1, ["ib", "col"], ["id"])
     ts(T.k12[:], T.ic[:, 4:5], pb16, -4.0, A.add, A.add, 1, 1, ["id", "col"], ["k12"])
     ts(T.bo[:], T.cb[:], pb16, None, A.is_equal, None, 128, .5, ["cb", "col"], ["bo"], name="bo")
     ts(T.ee[:], T.ci[:], pb16, None, A.is_equal, None, 144, .5, ["ci", "col"], ["ee"], name="ee")
-    if "a" in CFG["min"]:
+    sent = [("wire", "u", 0, c) for c in (0,) + cuts] + [("wire", "x", 0, 0)]
+    SHARED = sorted({who for who in CFG["min"].split() if "a" in who})
+    if SHARED:
         ts(T.ne[:], T.ci[:], pb16, -1.0, A.is_equal, A.mult, 144, .5, ["ci", "col"], ["ne"], name="ee")
+    for i, who in enumerate(SHARED):
+        node("g", 170 + 256 * CY, lambda i=i, who=who: g.affine_select(blk(T.bk, i), T.cb[:], [[0, 32], [1, 4]], A.is_ge, 0.0, -who.index("a"), 0),
+             ["cb"] + sent, [("bk", who)])
+        ts(blk(T.ba, i), blk(T.bk, i), pb16, None, A.is_equal, None, 128, .5, [("bk", who), "col"], [("ba", who)], name="ba")
     cI = T.ci[:, 0:128]
     k0 = T.ks[:, 0:1]
     ts(sid(1.0), cI, k0, None, A.is_equal, None, 128, .5, ["ci", "ks"], [("sid", 1.0)], name="sid")
-    for out, s, key in [(sid(s), s, ("sid", s)) for s in SCALES[1:] if s != -NR * V / 2 or CFG["mod"] == "a"] + \
+    for out, s, key in [(sid(s), s, ("sid", s)) for s in SCALES[1:len(SCALES) - (not UNDER)]] + \
             [(T.nih[:], -1.0, "nih"), (T.ino[:], 1.0, "ino"), (T.inn[:], -1.0, "inn"), (T.ni1[:], -1.0, "ni1"), (T.ik[:], 1024.0, "ik"), (T.kd[:], p16, "kd")]:
         act(out, sid(1.0), F.Identity, 128, [("sid", 1.0), "fa"], [key], scale=s, name="id")
     for kh in range(4):
         ts(T.pw[:, 144 * kh:144 * (kh + 1)], T.ci[:], T.k12[:], T.m4[:, kh:kh + 1], A.is_equal, A.mult, 144, .5, ["ci", "k12", "m4"], [("pw", kh)], name="pw")
     ts(T.nm[:], T.cm[:], p16, None, A.is_equal, None, 128, .5, ["cm", "fa"], ["nm"], name="n32")
-    ts(T.yy[:, 0:128], cI, k0, 32.0, A.is_equal, A.mult, 128, .5, ["ci", "ks"], [("yy", 0)], name="n32")
-    tt(T.n32[:], T.nm[:], T.yy[:, 0:128], A.add, 128, 2, ["nm", ("yy", 0)], ["n32"], name="n32")
-    iota(T.cg[:], [[16, 8], [0, 4], [1, 4]], 16, 0, 128, "cg")
-    cp(T.tmp[:], T.ia[:], 16, 1, ["ia"], ["tmp"])
+    node("g", 170 + 256 * CY, lambda: g.affine_select(T.n32[:], T.nm[:], [[-1, 128]], A.not_equal, 33.0, 0, 1), ["nm"] + sent, ["n32"], name="n32")
+    if CFG["copies"]:
+        ts(T.k4[:, 0:1], T.ic[:, 0:1], 4.0, -13.0, A.mult, A.add, 1, 1, ["ic"], ["k4a"])
+        act(T.k4[:, 1:2], T.k4[:, 0:1], F.Identity, 1, ["k4a", "col"], ["k4"], bias=pb16)
+    else:
+        iota(T.cg[:], [[16, 8], [0, 4], [1, 4]], 16, 0, 128, "cg")
+        cp(T.tmp[:], T.ia[:], 16, 1, ["ia"], ["tmp"])
+    if UNDER:
+        ts(T.mk23[:], T.mk16[:], 2.0 ** 19, None, A.mult, None, 4, 1, ["mk16"], ["mk23"])
     for kl in range(4):
         act(blk(T.dg, kl), sid(1.0), F.Identity, 128, [("sid", 1.0), "mk16"], [("dg", kl)], scale=T.mk16[:, kl:kl + 1], name="dg")
-        ts(blk(T.gm, kl), T.cg[:], T.tmp[:, 4 * kl:4 * kl + 1], None, A.is_equal, None, 128, .5, ["cg", "tmp"], [("gm", kl)], name="gm")
-    lift = lambda t: 1.0 if t else 8.0
-    LIFTS = sorted({(lift(i // 2), who) for i, who in enumerate(CFG["gu"].split()) if "a" in who})
-    for i, (by, who) in enumerate(LIFTS):
-        col = T.tm2[:, 4 * i:4 * i + 4]
-        for kh in range(4):
-            dve(1, 1, lambda kh=kh, c=col, by=by, who=who, i=i: ve.memset(T.tm2[:, 4 * i + kh:4 * i + kh + 1], by * (who[kh] == "a")), [], [("tm2", i, kh)], name="lf")
-        tt(col, col, T.m4[:], A.mult, 4, 2, four("tm2", i) + ["m4"], four("tm2", i), name="lf")
-        dve(4, 1, lambda c=col, i=i: ve.tensor_reduce(T.tm3[:, i:i + 1], c, AxisListType.X, A.add), four("tm2", i), [("tm3", i)], name="lf")
-        ts(blk(T.lf, i), T.bo[:], T.tm3[:, i:i + 1], None, A.mult, None, 128, .5, ["bo", ("tm3", i)], [("lf", by, who)], name="lf")
+        if UNDER:
+            act(blk(T.dy, kl), sid(1.0), F.Identity, 128, [("sid", 1.0), "mk23"], [("dy", kl)], scale=T.mk23[:, kl:kl + 1], name="dg")
+        if CFG["copies"]:
+            ts(T.gm[:, 144 * kl:144 * (kl + 1)], T.ci[:], T.k4[:, 1:2], T.mk16[:, kl:kl + 1], A.is_equal, A.mult, 144, .5, ["ci", "k4", "mk16"], [("gm", kl)], name="gm")
+        else:
+            ts(blk(T.gm, kl), T.cg[:], T.tmp[:, 4 * kl:4 * kl + 1], None, A.is_equal, None, 128, .5, ["cg", "tmp"], [("gm", kl)], name="gm")
+    assert all(who == "aaaa" and p[0] != "0" for p, who in CFG["gu"].items())
     for s in range(1, 16):
         ts(blk(T.sh, s), cI, T.ks[:, s:s + 1], None, A.is_equal, None, 128, .5, ["ci", "ks"], [("sh", s)], name="sh")
     sh = T.sh[:, 128:2048]
     node("g", 170 + 2 * 1920 * CY, lambda: g.affine_select(sh, sh, [[0, 15], [-1, 128]], A.not_equal, -1.0, 0, 1),
-         [("sh", s) for s in range(1, 16)] + [("wire", "u", 0, c) for c in (0,) + cuts] + [("wire", "x", 0, 0)], ["sh"], name="sh")
-    dve(HW, .5, lambda: ve.memset(T.ones[:], 1.0), [], ["ones"], name="ones")
+         [("sh", s) for s in range(1, 16)] + sent, ["sh"], name="sh")
+    iota(T.ones[:], [[0, HW]], 1, 0, HW, "ones")
     node("g", 130 + 2 * BL * CY, lambda: g.iota(T.msk[:], [[0, BL]], 1, 0, allow_small_or_imprecise_dtypes=True), ["sh"], ["msk"], name="msk")
-    node("g", 170 + 2 * BL * CY, lambda: g.affine_select(T.msk[:], T.msk[:], [[0, HW], [1, 4]], A.not_equal, 0.0, 0, 0), ["msk"], ["msk"], name="msk")
+    node("g", 170 + 2 * BL * CY, lambda: g.affine_select(T.msk[:], T.msk[:], [[0, QW], [1, 8]], A.not_equal, 0.0, 0, 0), ["msk"], ["msk"], name="msk")
     cp(T.thf[:, 0:1], T.ti[:, 0:1], 1, 1, ["ti"], ["thq"], name="th")
     ts(T.thf[:, 1:2], T.ti[:, 1:2], -1.0, 0.5, A.mult, A.add, 1, 1, ["ti"], ["thb"], name="th")
 
@@ -488,7 +557,6 @@ def build(g, core, T, topo, PRM):
     block = lambda buf, kh: buf[:, kh * BL:(kh + 1) * BL]
     slot = lambda buf, k: buf[:, k % 4 * BL + k // 4:(k % 4 + 1) * BL:4]
     held = lambda kh: range(kh, 16, 4)
-    listed = lambda off, h, kh: off[:, h * HW + 64 * kh:h * HW + 64 * (kh + 1)]
     pair = lambda h: ("m%d" % (2 * h), "m%d" % (2 * h + 1))
     turn = [0, 0]
 
@@ -497,36 +565,73 @@ def build(g, core, T, topo, PRM):
         lin(T[m1][:, lo], [(-1.0, T["bb%d" % b][:, s], ("bb", b, h)), (3.0, T["lv%d" % b][:, s], ("lv", b, h)), (-4.0, one, "ones")], HW, [m1 + "lo"], m1, "m")
         tt(T["nw%d" % b][:, s], T["ww%d" % b][:, s], T[m1][:, lo], A.mult, HW, 1, [("ww", b, h), m1 + "lo"], [("nw", b, h)], [m1], "w")
 
+    def other_weights(t, h):
+        b, s, bank = t % 2, hs(h), pair(h)[0]
+        ts(T.e2[:, s], T["bb%d" % b][:, s], 1.5, None, A.is_gt, None, HW, .5, [("bb", b, h)], [("e2", h)], name="e2")
+        ts(T.wcp[:, s], T["ww%d" % b][:, s], 4.0, 15.0, A.add, A.min, HW, .5, [("ww", b, h)], [("wcp", h)], name="wcp")
+        lin(T[bank][:, hi], [(-1.0, T["bb%d" % b][:, s], ("bb", b, h)), (3.0, T.e2[:, s], ("e2", h)), (1.0, T["lv%d" % b][:, s], ("lv", b, h)), (-4.0, one, "ones")],
+            HW, [bank + "hi"], bank, "m")
+        tt(T.na[:, s], T["ww%d" % b][:, s], T[bank][:, hi], A.mult, HW, 1, [("ww", b, h), bank + "hi"], [("na", h)], [bank], "na")
+
     def offsets(names, key, off, offkey, h):
         m0 = pair(h)[0]
         mm([(T[m0][:, HW + 64 * kh:HW + 64 * (kh + 1)], T.pw[:, 144 * kh + 12 - 4 * vl:144 * kh + 140 - 4 * vl],
-             names[:, h * HW + vl:(h + 1) * HW:4], vl == 0, vl == 3, 64 * NC) for kh in range(4) for vl in range(4)],
+             names[:, h * HW + vl:(h + 1) * HW:4], vl == 0, vl == 3, 64) for kh in range(4) for vl in range(4)],
            [key] + four("pw"), [m0 + "hi"], m0, "perm")
         cp(off[:, hs(h)], T[m0][:, hi], HW, 1, [m0 + "hi"], [offkey], [m0], "off")
 
-    def jump(t, h):
-        off, offkey, n = (T.off1, ("off", 1, h), h) if t else (T.off2, ("off", 2, h), 2 + h)
-        for kh in range(4):
-            out, src = block(T["wr%d" % n], kh), T.jt[:].indirect(listed(off, h, kh))
-            if CFG["jump"].split()[2 * t + h][kh] == "v":
-                cp(out, src, BL, GC, ["jt", offkey], [("wr", n, kh)], name="jg")
+    def gather(who, buf, table, off, h, kh, rk, wk, name):
+        n = CFG["split"][name]
+        for i in range(n):
+            w = BL // n
+            out, at = buf[:, kh * BL + i * w:kh * BL + (i + 1) * w], h * HW + 64 * kh + i * w // 16
+            src = table[:].indirect(off[:, at:at + w // 16])
+            if who == "v":
+                cp(out, src, w, GC, rk, wk[i::n], name=name)
             else:
-                act(out, src, F.Copy, BL, ["jt", offkey], [("wr", n, kh)], cyc=GC, name="jg")
-        wr = T["wr%d" % n]
-        dma("sp", [(wr[kh:128:4, 0:BL], wr[kh:128:4, kh * BL:(kh + 1) * BL]) for kh in range(1, 4)], 192, four("wr", n)[1:], [("wr", n, 0)], "jdma")
+                act(out, src, F.Copy, w, rk, wk[i::n], cyc=GC, name=name)
 
-    def jumped(t, h, bank="cbk"):
-        base, basekey, n = (T.cc1, ("cc", 1, h), h) if t else (T.sf, "sf", 2 + h)
-        s, ps = hs(h), T[bank][:, hi]
-        acc(ps, [(T.ino[:], base[:, s], NC), (T.kd[:], one, 1)] + [(blk(T.dg, kl), slot(T["wr%d" % n], 4 * kl), 1) for kl in range(4)], HW,
-            four("wr", n) + four("dg") + ["kd", "ones", "ino", basekey], [bank + "hi"], bank, "jd")
-        if CFG["mod"] == "v":
-            ts(T.md[:, s], ps, float(NR * V), -float(NR * V), A.is_ge, A.mult, HW, 1, [bank + "hi"], [("md", h)], [bank], "j1")
-            tt(T["q%d" % t][:, s], T.md[:, s], ps, A.add, HW, 1, [("md", h), bank + "hi"], [("q", t, h)], [bank], "j2")
+    def jumps(t, h):
+        if UNDER:
+            return T["wr%d" % (2 + h)], lambda kh: [("wr", 2 + h, kh)] * 2
+        return T["jb%d" % h], lambda kh: both("jb", h, kh)
+
+    def jump(t, h):
+        if t and UNDER:
+            pu, jm = T["pu%d" % h], T["jm%d" % h]
+            dma("sp", [(jm[kh:128:4, :], pu[kh:128:4, kh * BL:(kh + 1) * BL]) for kh in range(4)], 512,
+                [("pu", 2 * h + i, kh) for i in range(2) for kh in range(4)], [("jm", h)], "jdma")
             return
-        act(T.md[:, s], ps, F.Sign, HW, [bank + "hi"], [("md", h)], [bank], bias=0.5 - NR * V, name="j1")
-        mm([(ps, sid(-NR * V / 2), T.md[:, s], False, True, HW)], [("md", h), ("sid", -NR * V / 2)], [bank + "lo", bank + "hi"], bank, "jm")
-        act(T["q%d" % t][:, s], ps, F.Identity, HW, [bank + "hi"], [("q", t, h)], [bank], bias=-NR * V / 2, name="j2")
+        (off, offkey), (jb, keys) = (T.off1, ("off", 1, h)) if t else (T.off2, ("off", 2, h)), jumps(t, h)
+        for kh in range(4):
+            gather(CFG["jump"].split()[2 * t + h][kh], jb, T.jt, off, h, kh, ["jt", offkey], keys(kh), "jg")
+        dma("sp", [(jb[kh:128:4, 0:BL], jb[kh:128:4, kh * BL:(kh + 1) * BL]) for kh in range(1, 4)], 192,
+            [k for kh in range(1, 4) for k in keys(kh)], keys(0), "jdma")
+
+    def jumped(t, h):
+        base, basekey, bank = (T.cc1, ("cc", 1, h), CFG["qbank"]) if t else (T.sf, "sf", "u" + "ab"[h])
+        s, ps = hs(h), T[bank][:, hi]
+        rest, rk = [(T.ino[:], base[:, s], 1), (T.kd[:], one, 1)], ["kd", "ones", "ino", basekey]
+        if t and UNDER:
+            acc(ps, [(blk(T.dy, kl), T["jm%d" % h][:, kl:BL:4], 4) for kl in range(4)], HW, [("jm", h)] + four("dy"), [bank + "lo", bank + "hi"], bank, "jd")
+            ts(T.md[:, s], ps, 1.5 * 2.0 ** 46, -1.5 * 2.0 ** 46, A.add, A.add, HW, 1, [bank + "hi"], [("md", h)], [bank], "j0")
+            acc(ps, [(sid(-1.0), T.md[:, s], 1)] + rest, HW, rk + [("md", h), ("sid", -1.0)], [bank + "lo", bank + "hi"], bank, "jd", False)
+        else:
+            jb, keys = jumps(t, h)
+            acc(ps, rest + [(blk(T.dg, kl), slot(jb, 4 * kl), 1) for kl in range(4)], HW, rk + keys(0) + four("dg"), [bank + "lo", bank + "hi"], bank, "jd")
+        ts(T.md[:, s], ps, float(NR * V), -float(NR * V), A.is_ge, A.mult, HW, 1, [bank + "hi"], [("md", h)], [bank], "j1")
+        tt(T["q%d" % t][:, s], T.md[:, s], ps, A.add, HW, 1, [("md", h), bank + "hi"], [("q", t, h)], [bank], "j2")
+
+    def under(t, _h):
+        for i in range(2):
+            for j in range(2):
+                s = slice(BL * i + 512 * j, BL * i + 512 * (j + 1))
+                acc(T.xb[:, 512 * j:512 * (j + 1)], [(sid(1.0), T["tx%d" % t][:, s], 1), (sid(2.0 ** -19), T.jt[:, s], 1)], 512,
+                    both("tx", t) + [("arr", "x", t), "jt", ("sid", 1.0), ("sid", 2.0 ** -19)], ["xb%d" % j], "xb%d" % j, "ty")
+            if CFG["table"][i] == "v":
+                cp(T.ty[:, BL * i:BL * (i + 1)], T.xb[:], BL, 1, ["xb0", "xb1"], [("ty", i)], ["xb0", "xb1"], "ty")
+            else:
+                act(T.ty[:, BL * i:BL * (i + 1)], T.xb[:], F.Copy, BL, ["xb0", "xb1"], [("ty", i)], ["xb0", "xb1"], name="ty")
 
     here[0] = "list"
     cp(T.sf[:], T.si[:], V, 1, ["si"], ["sf"])
@@ -534,44 +639,63 @@ def build(g, core, T, topo, PRM):
         offsets(T.sf, "sf", T.off2, ("off", 2, h), h)
     here[0] = "init0"
     cp(T.r2[:], T.pi[:], V, 1, ["pi"], both("r2"))
-    ts(T.bb0[:], T.ab[:], -1.0, 3.0, A.mult, A.add, V, .5, ["ab"], both("bb", 0))
-    ts(T.lv0[:], T.ab[:], 2.5, None, A.is_lt, None, V, .5, ["ab"], both("lv", 0))
+    if CFG["ages"][0] == "v":
+        ts(T.bb0[:], T.ab[:], -1.0, 3.0, A.mult, A.add, V, .5, ["ab"], both("bb", 0))
+    else:
+        act(T.bb0[:], T.ab[:], F.Identity, V, ["ab"], both("bb", 0), scale=-1.0, bias=3.0)
+    if CFG["ages"][1] == "v":
+        ts(T.lv0[:], T.ab[:], 2.5, None, A.is_lt, None, V, .5, ["ab"], both("lv", 0))
+    else:
+        act(T.lv0[:], T.ab[:], F.Sign, V, ["ab"], both("lv", 0), scale=-1.0, bias=3.0)
     for h in range(2):
         here[0] = "init%d" % h
         s, m0 = hs(h), pair(h)[0]
-        lin(T[m0][:, lo], [(-BIG, T.lv0[:, s], ("lv", 0, h)), (BIG, one, "ones")], HW, [m0 + "lo"], m0, "N", [(T.inn[:], T.r2[:, s], NC)], ["inn", ("r2", h)])
+        lin(T[m0][:, lo], [(-BIG, T.lv0[:, s], ("lv", 0, h)), (BIG, one, "ones")], HW, [m0 + "lo"], m0, "N", [(T.inn[:], T.r2[:, s], 1)], ["inn", ("r2", h)])
         tt(T.r1[:, s], T.sf[:, s], T[m0][:, lo], A.min, HW, 1, ["sf", m0 + "lo"], [("r1", h)], [m0], "r")
         act(T.cc0[:, s], T.r1[:, s], F.Abs, HW, [("r1", h)], [("cc", 0, h)], name="abs")
         offsets(T.cc0, ("cc", 0, h), T.off0, ("off", 0, h), h)
         weights(0, h)
 
     def spread_weights(t, h):
-        n = 2 * (t % 2) + h
+        n, c, nw = 2 * (t % 2) + h, CFG["copies"], T["nw%d" % (t % 2)]
         wr, wp = T["wr%d" % n], T["wp%d" % h]
-        for i, bank in enumerate(pair(h)):
-            bk = [bank + "lo", bank + "hi"]
-            mm([(T[bank][:, kl:512:4], blk(T.gm, kl), T["nw%d" % (t % 2)][:, h * HW + i * QW:h * HW + (i + 1) * QW], True, True, QW) for kl in range(4)],
-               [("nw", t % 2, h)] + four("gm"), bk, bank, "wrep")
-            act(wp[:, 512 * i:512 * (i + 1)], T[bank][:], F.Copy, 512, bk, [("wp", h, i)], [bank], name="wc")
-        dma("sp", [(wr[q:128:4, :], wp[:]) for q in range(4)], 1024, both("wp", h), four("wr", n), "wdma")
+        if not c:
+            for i, bank in enumerate(pair(h)):
+                bk = [bank + "lo", bank + "hi"]
+                mm([(T[bank][:, kl:512:4], blk(T.gm, kl), nw[:, h * HW + i * QW:h * HW + (i + 1) * QW], True, True, QW) for kl in range(4)],
+                   [("nw", t % 2, h)] + four("gm"), bk, bank, "wrep")
+                act(wp[:, 512 * i:512 * (i + 1)], T[bank][:], F.Copy, 512, bk, [("wp", h, i)], [bank], name="wc")
+            dma("sp", [(wr[q:128:4, :], wp[:]) for q in range(4)], 1024, both("wp", h), four("wr", n), "wdma")
+            return
+        bank, wd = pair(h)[1], T["wd%d" % (2 * t + h)]
+        mm([(T[bank][:, kl:HW:4], T.gm[:, 144 * kl + 3 - vq:144 * kl + 131 - vq], nw[:, h * HW + 64 * vq:h * HW + 64 * (vq + 1)], vq == 0, vq == 3, 64)
+            for kl in range(4) for vq in range(4)], [("nw", t % 2, h)] + four("gm"), [bank + "lo", bank + "hi"], bank, "wrep")
+        act(wp[:], T[bank][:, lo], F.Identity, HW, [bank + "lo"], [("wp", h)], [bank], scale=1.0 / 16, name="wc")
+        dma("sp", [(wd[:, i, :], wp[:]) for i in range(c)], 64 * c * PRM["short"], [("wp", h)], [("wd", t, h)], "wout")
+        for i in range(CFG["reads"]):
+            k = 4 // CFG["reads"]
+            s = slice(i * k * BL, (i + 1) * k * BL)
+            dma("sp", [(wr[q:128:16 // c, s], wd[:, :, s]) for q in range(16 // c)], 256 * k * PRM["long"], [("wd", t, h)], four("wr", n)[i * k:(i + 1) * k], "wdma")
+
+    def gathered(t, h):
+        if t == 1 and UNDER:
+            return T["pu%d" % h], lambda kh: [("pu", 2 * h, kh), ("pu", 2 * h + 1, kh)], 1.0
+        return T["xc%d" % h], lambda kh: both("xc", h, kh), 0.5
 
     def gather_x(t, h):
+        xc, keys, _c = gathered(t, h)
+        table, rk = (T.ty, both("ty")) if t == 1 and UNDER else (T["tx%d" % t], both("tx", t) + [("arr", "x", t)])
         for kh in range(4):
-            out, src = block(T["xc%d" % h], kh), T["tx%d" % t][:].indirect(listed(T["off%d" % t], h, kh))
-            rk = both("tx", t) + [("arr", "x", t), ("off", t, h)]
-            if CFG["gx"].split()[2 * t + h][kh] == "v":
-                cp(out, src, BL, GC, rk, [("xc", h, kh)], name="gx")
-            else:
-                act(out, src, F.Copy, BL, rk, [("xc", h, kh)], cyc=GC, name="gx")
+            gather(CFG["gx"].split()[2 * t + h][kh], xc, table, T["off%d" % t], h, kh, rk + [("off", t, h)], keys(kh), "gx")
 
     def new_x(t, h):
-        n, last, hb = 2 * (t % 2) + h, t == STEPS - 1, CFG["hbank"]
-        xc, px, wr = T["xc%d" % h], T["px%d" % h], T["wr%d" % n]
+        n, last, hb = 2 * (t % 2) + h, t == STEPS - 1, pair(h)[1]
+        (xc, keys, cyc), px, wr = gathered(t, h), T.px, T["wr%d" % n]
         for kh in range(4):
-            dve(BL, .5, lambda kh=kh: ve.tensor_tensor_scan(block(px, kh), block(xc, kh), block(wr, kh), 0.0, A.max, A.mult),
-                [("xc", h, kh), ("wr", n, kh)], [("px", h, kh)], name="xm")
+            dve(BL, cyc, lambda kh=kh: ve.tensor_tensor_scan(block(px, kh), block(xc, kh), block(wr, kh), 0.0, A.max, A.mult),
+                keys(kh) + [("wr", n, kh)], [("px", kh)], name="xm")
             mm([(T[hb][:, hi], T.nih[:], slot(px, k), k == 0, k == 15, HW) for k in held(kh)],
-               [("px", h, kh), "nih"], [hb + "lo", hb + "hi"], hb, "h")
+               [("px", kh), "nih"], [hb + "lo", hb + "hi"], hb, "h")
         act(T.yy[:, hs(h)], T[hb][:, hi], F.Identity, HW, [hb + "hi"], [("yy", h)], [hb], scale=1.0 / 256, bias=160.0 - 255.0 / 512, name="y")
         nx = T.xo[:, hs(h)] if last else T["tx%d" % (t + 1)][:, mine(h)]
         ts(nx, T.yy[:, hs(h)], -160.0, 15.0, A.add, A.min, HW, .5, [("yy", h)], [("tx", t + 1, h)], name="X")
@@ -580,28 +704,29 @@ def build(g, core, T, topo, PRM):
         return [] if last else sends("x", t + 1, 2 * h, 2 * h + 2)
 
     def matches(t, h):
-        b, xc, mn, tx = t % 2, T["xc%d" % h], T["mn%d" % h], T["tx%d" % t]
-        scalar = CFG["min"].split()[t][h] == "a"
+        b, (xc, keys, _c), mn, tx, cb = t % 2, gathered(t, h), T.mn, T["tx%d" % t], pair(h)[0]
+        who = CFG["min"].split()[2 * t + h]
         spread_x = lambda i, start: [(T.xb[:, 512 * i + m:512 * (i + 1):4], sid(1.0), tx[:, own + h * HW + i * QW:own + h * HW + (i + 1) * QW],
-                                      start, start or m == 3, QW) for m in range(4)]
-        for i in range(0 if scalar else 2):
+                                      start and m == 0, m == 3, QW) for m in range(4)]
+        for i in range(2 * (who[0] == "v")):
             mm(spread_x(i, True), [("tx", t, h), ("sid", 1.0)], ["xb%d" % i], "xb%d" % i, "xrep")
         for kh in range(4):
-            for i in range(2 if scalar else 0):
+            for i in range(2 * (who[kh] == "a")):
                 s, bank, ps = slice(kh * BL + 512 * i, kh * BL + 512 * (i + 1)), "xb%d" % i, T.xb[:, 512 * i:512 * (i + 1)]
                 mm([(ps, sid(-1.0), xc[:, s], True, False, 512)] + spread_x(i, False),
-                   [("xc", h, kh), ("tx", t, h), ("sid", 1.0), ("sid", -1.0)], [bank], bank, "xd")
-                act(mn[:, s], ps, F.Relu, 512, [bank], [("mn", h, kh, i)], [bank], name="relu")
-            if not scalar:
-                tt(block(mn, kh), block(xc, kh), T.xb[:], A.min, BL, 1, [("xc", h, kh), "xb0", "xb1"], both("mn", h, kh), ["xb0", "xb1"], "min")
-            mm([(T.cbk[:, lo], sid(256.0), T["lv%d" % b][:, hs(h)], True, False, HW)] * (kh == 0) +
-               [(T.cbk[:, lo], T.bo[:], tx[:, mine(h)], False, False, HW)] * (kh == 0 and scalar) +
-               [(T.cbk[:, lo], (T.ne if scalar else T.ee)[:, 16 - k:144 - k], slot(mn, k), False, k == 15, HW) for k in held(kh)],
-               both("mn", h, kh) + ["ee", "ne", "bo", ("tx", t, h), ("lv", b, h), ("sid", 256.0)], ["cbklo", "cbkhi"], "cbk", "c")
-        act(T.ck[:, hs(h)], T.cbk[:, lo], F.Identity, HW, ["cbklo", "tb"], [("ck", h)], ["cbk"], bias=T.tb[:], name="ck")
-        act(T.nq[:, hs(h)], T.cbk[:, lo], F.Relu, HW, ["cbklo", "thq"], [("nq", h)], ["cbk"], scale=-1.0, bias=T.thf[:, 0:1], name="nq")
-
-    FOLDS = {"0": ([], [0, 1, 2, 3]), "h": ([(0, 1)], [0, 2, 3]), "1": ([(0, 1), (2, 3)], [0, 2])}
+                   [keys(kh)[i], ("tx", t, h), ("sid", 1.0), ("sid", -1.0)], [bank], bank, "xd")
+                act(mn[:, s], ps, F.Relu, 512, [bank], [("mn", kh, i)], [bank], name="relu")
+            for i in range(2 * (who[kh] == "v" and kh in CFG["halved"])):
+                s = slice(kh * BL + 512 * i, kh * BL + 512 * (i + 1))
+                tt(mn[:, s], xc[:, s], T.xb[:, 512 * i:512 * (i + 1)], A.min, 512, 1, [keys(kh)[i], "xb%d" % i], [("mn", kh, i)], ["xb%d" % i], "min")
+            if who[kh] == "v" and kh not in CFG["halved"]:
+                tt(block(mn, kh), block(xc, kh), T.xb[:], A.min, BL, 1, keys(kh) + ["xb0", "xb1"], both("mn", kh), ["xb0", "xb1"], "min")
+            mm([(T[cb][:, lo], sid(256.0), T["lv%d" % b][:, hs(h)], True, False, HW)] * (kh == 0) +
+               ([(T[cb][:, lo], blk(T.ba, SHARED.index(who)), tx[:, mine(h)], False, False, HW)] if kh == 0 and "a" in who else []) +
+               [(T[cb][:, lo], (T.ne if who[kh] == "a" else T.ee)[:, 16 - k:144 - k], slot(mn, k), False, k == 15, HW) for k in held(kh)],
+               both("mn", kh) + ["ee", "ne", ("ba", who), ("tx", t, h), ("lv", b, h), ("sid", 256.0)], [cb + "lo", cb + "hi"], cb, "c")
+        act(T.ck[:, hs(h)], T[cb][:, lo], F.Identity, HW, [cb + "lo", "tb"], [("ck", h)], [cb], bias=T.tb[:], name="ck")
+        act(T.nq[:, hs(h)], T[cb][:, lo], F.Relu, HW, [cb + "lo", "thq"], [("nq", h)], [cb], scale=-1.0, bias=T.thf[:, 0:1], name="nq")
 
     def span(q0, q1):
         h, w = q0 // 2, 512 * (q1 - q0)
@@ -609,42 +734,69 @@ def build(g, core, T, topo, PRM):
 
     def gather_u(t, q0, q1):
         h, piece, w, keys = span(q0, q1)
-        n, pu = 2 * (t % 2) + h, T["pu%d" % h]
+        n, pu, how = 2 * (t % 2) + h, T["pu%d" % h], finish()[here[0]][0]
         wr, first = T["wr%d" % n], h * HW + 32 * (q0 % 2)
         for kh in range(4):
             src = T["tu%d" % t][:].indirect(T["off%d" % t][:, first + 64 * kh:first + 64 * kh + w // 16])
             rk = four("tu", t) + [("arr", "u", t), ("off", t, h)]
-            if CFG["gu"].split()[2 * t + h][kh] == "v":
-                tt(piece(pu, kh), src, piece(wr, kh), A.mult, w, GC, rk + [("wr", n, kh)], keys(kh), name="gu")
-                continue
-            turn[1] += 1
-            uc = T["uc%d" % (turn[1] % 2)][:, 0:w]
-            act(uc, src, F.Identity, w, rk, [("uc", turn[1] % 2)], cyc=GC, bias=lift(t), name="gu")
-            dve(w, 1, lambda kh=kh, uc=uc: ve.tensor_tensor_scan(piece(pu, kh), uc, piece(wr, kh), 0.0, A.max, A.mult),
-                [("uc", turn[1] % 2), ("wr", n, kh)], keys(kh), name="um")
-        for a, c in FOLDS[CFG["fin"].split()[2 * t + h][0]][0]:
-            dma("g", [(piece(pu, a), piece(pu, c))], w, keys(c), keys(a), "fold", True)
+            out = product(q0, kh, how)
+            if CFG["gu"].get(here[0], "vvvv")[kh] == "v":
+                tt(out, src, piece(wr, kh), A.mult, w, GC, rk + [("wr", n, kh)], keys(kh), name="gu")
+            else:
+                turn[1] += 1
+                uc = T["uc%d" % (turn[1] % 2)][:, 0:w]
+                act(uc, src, F.Identity, w, rk, [("uc", turn[1] % 2)], cyc=GC, bias=1.0, name="gu")
+                dve(w, 1, lambda kh=kh, uc=uc, out=out: ve.tensor_tensor_scan(out, uc, piece(wr, kh), 0.0, A.max, A.mult),
+                    [("uc", turn[1] % 2), ("wr", n, kh)], keys(kh), name="um")
+            if kh + 1 == REMOTE.get(how):
+                fold(t, q0, q1, kh + 1)
+
+    def product(q, kh, how):
+        at = 2 * BL * (q % 2)
+        if how == "P":
+            return T["pu%d" % (q // 2)][:, at + BL * (kh // 2) + kh % 2:at + BL * (kh // 2 + 1):2]
+        return T["pu%d" % (q // 2)][:, at + 512 * kh:at + 512 * (kh + 1)]
+
+    def fold(t, q0, q1, n):
+        h, piece, w, keys = span(q0, q1)
+        k, there, to = folded().index((t, q0, q1, n)), fold_sides(T, t, q0, q1)[0], mirror_of(core, T, topo)
+        srcs, rk, fm = [product(q0, kh, "F") for kh in range(n)], [x for kh in range(n) for x in keys(kh)], topo.mask(core, to)
+        wk = [("fo", q) for q in range(q0, q1)]
+        i = node("g", 600.0, lambda: g.remote_dma_fused([RemoteDMATransfer(dst_ids=[DstId(rid=topo.addr(to)[0], pnc=topo.addr(to)[1])], dma_engine_mask=fm,
+                                                                           remote_sem=T.sem["fh%d" % k], srcs=srcs, dsts=[there], alu_op=1)],
+                                                        local_sem=T.sem["fl%d" % k]),
+                 rk + wk, wk, ["turnf"], lat=PRM["lat"] / 2, kind="f", name="fold")
+        nodes[i]["sem"] = (T.sem["fl%d" % k], bin(fm).count("1"))
+        node("dma", n * w / 2 * PRM["dr"] * PRM["fr"], None, rk + wk, [("fw", k)], kind="l", name="fold", of=i, lat=PRM["lat"] / 2)
+        node("dma2", 600.0 + w / 2 * PRM["dr"], None, [("fw", k)], [("fb", k)], kind="l", name="back", lat=PRM["lat"])
+        node("arr", 0.0, ("fo", k), [("fb", k)], wk, kind="a")
+        ncalls[("fo", k)] = bin(topo.mask(to, core)).count("1")
 
     def new_u(t, q0, q1):
         h, piece, w, keys = span(q0, q1)
-        last, fin, pu, n = t == STEPS - 1, CFG["fin"].split()[2 * t + h], T["pu%d" % h], w // 4
-        bank = "cbk" if last and q1 == 4 and CFG["end"] == "cbk" else "ub"
+        name = "%dU%d%d" % (t, q0, q1)
+        last, fin, n, lifted = t == STEPS - 1, finish()[name], w // 4, CFG["gu"].get(name, "vvvv")
+        bank = "u" + CFG["ubank"][q0]
         up, s, os_ = T[bank][:, 0:n], slice(q0 * QW, q1 * QW), slice(own + q0 * QW, own + q1 * QW)
-        left, lifted, made = FOLDS[fin[0]][1], CFG["gu"].split()[2 * t + h], [("tu", t + 1, q) for q in range(q0, q1)]
+        left, made = LEFT[fin[0]], [("tu", t + 1, q) for q in range(q0, q1)]
         for kh, who in zip(left, fin[1:]):
+            pu, at, rk, run = T["pu%d" % h], 2 * BL * (q0 % 2) + 512 * kh, keys(kh), 4
+            if kh < 0:
+                pu, at, rk = T["fo%d" % h], 512 * (q0 % 2), [("fo", q) for q in range(q0, q1)]
+            if fin[0] == "P":
+                rk, run = keys(kh) + keys(kh + 1), 8
             if who == "s":
                 turn[0] += 1
-                sc = T["sc%d" % (turn[0] % 2)]
-                dve(w, 1, lambda sc=sc, kh=kh: ve.tensor_tensor_scan(sc[:, 0:w], T.msk[:, 0:w], piece(pu, kh), 0.0, A.mult, A.add),
-                    keys(kh) + ["msk"], [("sc", turn[0] % 2)], name="scan")
-                terms, key = [sc[:, 3:w:4]], [("sc", turn[0] % 2)]
+                sc, m = T["sc%d" % (turn[0] % 2)], n * run
+                dve(m, 1, lambda sc=sc, m=m, run=run, x=pu[:, at:at + m]: ve.tensor_tensor_scan(sc[:, 0:m], T.msk[:, 0:BL:8 // run], x, 0.0, A.mult, A.add),
+                    rk + ["msk"], [("sc", turn[0] % 2)], name="scan")
+                terms, key = [sc[:, run - 1:m:run]], [("sc", turn[0] % 2)]
             else:
-                at = kh * BL + 512 * (q0 % 2)
-                terms, key = [pu[:, at + kl:at + w:4] for kl in range(4)], keys(kh)
-            mm([(up, T.ik[:], T["tu%d" % t][:, os_], True, False, 4 * n), (up, sid(128.0), T["tx%d" % t][:, os_], False, False, n)] * (kh == 0) +
-               ([(up, blk(T.lf, LIFTS.index((lift(t), lifted))), T["nw%d" % (t % 2)][:, s], False, False, n)] if kh == 0 and "a" in lifted else []) +
+                terms, key = [pu[:, at + kl:at + w:4] for kl in range(4)], rk
+            mm([(up, T.ik[:], T["tu%d" % t][:, os_], True, False, 4 * n), (up, sid(128.0), T["tx%d" % t][:, os_], False, False, n)] * (kh == left[0]) +
+               [(up, T.bo[:], T["nw%d" % (t % 2)][:, s], False, False, n)] * (kh == left[0] and "a" in lifted) +
                [(up, T.ni1[:], x, False, kh == left[-1] and i == len(terms) - 1, 4 * n) for i, x in enumerate(terms)],
-               key + four("tu", t) + [("tx", t, h), "ik", "ni1", ("sid", 128.0), ("nw", t % 2, h), ("lf", lift(t), lifted)],
+               key + four("tu", t) + [("tx", t, h), "ik", "ni1", ("sid", 128.0), ("nw", t % 2, h), "bo"],
                [bank + "lo", bank + "hi"], bank, "arg")
         nu = T.uo[:, s] if last else T["tu%d" % (t + 1)][:, os_]
         act(nu, up, F.Tanh, n, [bank + "lo"], made, [bank], scale=2.0 ** -11, bias=-0.5, name="tanh")
@@ -674,8 +826,6 @@ def build(g, core, T, topo, PRM):
         tag = [(BIG,) + lv, (BIG,) + nq]
         lapse = (T.sf, "sf", [(BIG,) + bb, (-2 * BIG,) + lv, (BIG / 2,) + ga, (1.5 * BIG,) + on], m1)
         if not last:
-            if "%dq%d" % (t, h) not in CFG["order"]:
-                jumped(t, h, m0)
             ways = [(T["q%d" % t], ("q", t, h), tag, m0), lapse]
         else:
             ever = [(T["ga%d" % i][:, s], ("ga", i, h)) for i in range(2)]
@@ -683,29 +833,32 @@ def build(g, core, T, topo, PRM):
                     (T.q1, ("q", 1, h), tag + [(-BIG / 2,) + x for x in ever], m0), lapse]
         cur = (T["cc%d" % b][:, s], ("cc", b, h))
         for i, (name, key, terms, bank) in enumerate(ways):
-            lin(T[bank][:, hi], terms, HW, [bank + "hi"], bank, "N", [(T.inn[:], name[:, s], NC)], ["inn", key])
+            if short and not last and i == 1:
+                lin(T[m0][:, lo], [(-4.0, T.wcp[:, s], ("wcp", h)), (-BIG / 2,) + ga, (BIG / 2,) + on], HW, [m0 + "lo"], m0, "m")
+                tt(T["nw%d" % n][:, s], T.na[:, s], T[m0][:, lo], A.min, HW, 1, [("na", h), m0 + "lo"], [("nw", n, h)], [m0], "w")
+            lin(T[bank][:, hi], terms, HW, [bank + "hi"], bank, "N", [(T.inn[:], name[:, s], 1)], ["inn", key])
             out = (T["r%d" % (1 + i % 2)][:, s], ("r%d" % (1 + i % 2), h))
             tt(out[0], cur[0], T[bank][:, hi], A.min, HW, 1, [cur[1], bank + "hi"], [out[1]], [bank], "r")
             cur = out
         nc = T.co[:, s] if last else T["cc%d" % n][:, s]
         act(nc, cur[0], F.Abs, HW, [cur[1]], [("cc", n, h)], name="abs")
-        lin(T[m0][:, lo], [(1.0,) + bb, (-1.5,) + ga, (-4.0,) + lv, (-3.0,) + nq], HW, [m0 + "lo"], m0, "t")
+        lin(T[m0][:, lo], [(1.0,) + bb, (-1.5,) + ga, (-4.0,) + lv, (-4.0,) + nq], HW, [m0 + "lo"], m0, "t")
         lin(T[m1][:, lo], [(1.0,) + ww, (2.0,) + ga], HW, [m1 + "lo"], m1, "W")
         nb, nw = T["bb%d" % n][:, s], T["ww%d" % n][:, s]
         act(nb, T[m0][:, lo], F.Relu, HW, [m0 + "lo"], [("bb", n, h)], [m0], bias=1.5, name="b")
-        ts(nw, T[m1][:, lo], 2.0, 15.0, A.add, A.min, HW, 1, [m1 + "lo"], [("ww", n, h)], [m1], "W")
+        if not last:
+            ts(nw, T[m1][:, lo], 2.0, 15.0, A.add, A.min, HW, 1, [m1 + "lo"], [("ww", n, h)], [m1], "W")
         if last:
-            lin(T[m1][:, hi], [(1.0, nw, ("ww", n, h)), (-16.0, nb, ("bb", n, h))], HW, [m1 + "hi"], m1, "yw")
-            act(T.wo[:, s], T[m1][:, hi], F.Identity, HW, [m1 + "hi"], [("wo", h)], [m1], bias=48.0, name="yw")
+            act(nw, T[m1][:, lo], F.Relu, HW, [m1 + "lo"], [("ww", n, h)], [m1], scale=-1.0, bias=13.0, name="W")
+            lin(T[m1][:, hi], [(-1.0, nw, ("ww", n, h)), (-16.0, nb, ("bb", n, h))], HW, [m1 + "hi"], m1, "yw")
+            act(T.wo[:, s], T[m1][:, hi], F.Identity, HW, [m1 + "hi"], [("wo", h)], [m1], bias=63.0, name="yw")
             dma("sp", [(T.yw[:, s], T.wo[:, s])], 128, [("wo", h)], [])
             dma("sp", [(T.yc[:, s], nc)], 128, [("cc", n, h)], [])
             return
         offsets(T["cc%d" % n], ("cc", n, h), T["off%d" % (t + 1)], ("off", t + 1, h), h)
-        if CFG["lv"] == "v":
-            ts(T["lv%d" % n][:, s], nb, 1.0, None, A.min, None, HW, .5, [("bb", n, h)], [("lv", n, h)], name="lv")
-        else:
-            act(T["lv%d" % n][:, s], nb, F.Sign, HW, [("bb", n, h)], [("lv", n, h)], name="lv")
-        weights(n, h)
+        ts(T["lv%d" % n][:, s], nb, 1.0, None, A.min, None, HW, .5, [("bb", n, h)], [("lv", n, h)], name="lv")
+        if not short:
+            weights(n, h)
 
     lands = {}
     for part in CFG["order"].split():
@@ -719,13 +872,13 @@ def build(g, core, T, topo, PRM):
         elif what == "U":
             gather_u(t, j, int(part[3]))
         else:
-            {"w": spread_weights, "X": gather_x, "c": matches, "s": slots, "j": jump, "q": jumped}[what](t, j)
+            {"w": spread_weights, "X": gather_x, "c": matches, "s": slots, "j": jump, "q": jumped, "a": other_weights, "y": under}[what](t, j)
     return nodes, ncalls, neng
 
 
 def emit(g, T, nodes, order, ncalls, neng):
     Q = {"g": g, "pe": g.tensor, "dve": g.vector, "act": g.scalar, "sp": g.sync}
-    real = lambda x: x["kind"] in "cdr"
+    real = lambda x: x["kind"] in "cdrf"
     pos, clock, cnt = {}, {e: {} for e in Q}, {e: 0 for e in Q}
     done, waits, need = {}, {}, set()
     for i in order:
@@ -762,7 +915,7 @@ def emit(g, T, nodes, order, ncalls, neng):
     for i in order:
         x = nodes[i]
         if x["kind"] == "a":
-            sem[i] = (T.sem["a%s%d" % x["fn"]], ncalls[x["fn"]] * neng * (NR - 1))
+            sem[i] = (T.sem["a%s%d" % x["fn"]], ncalls[x["fn"]] * (1 if x["fn"][0] == "fo" else neng * (NR - 1)))
             continue
         if not real(x):
             continue
@@ -772,6 +925,10 @@ def emit(g, T, nodes, order, ncalls, neng):
         ins = x["fn"]()
         if x["kind"] == "r":
             nsent += neng
+        elif x["kind"] == "f":
+            sem[i] = x["sem"]
+            if i not in need:
+                tail.append((q, sem[i]))
         elif x["kind"] == "d":
             sem[i] = (T.sem["d%d" % nd], 16 * len(ins))
             nd += 1
@@ -793,5 +950,7 @@ def rank_program(g, core, T, topo):
         for rank, c in enumerate(T.cores):
             if helper_of(c, T, topo) == core:
                 hand_on(g, core, rank, T, topo)
+            if folded() and mirror_of(c, T, topo) == core:
+                hand_back(g, core, c, T, topo)
         return
     emit(g, T, *plan(g, core, T, topo))

@@ -8,36 +8,37 @@ V, NR, STEPS = 512, 4, 3
 HW = 256
 BL = 4 * HW
 QW = 128
+RUN = 12 * QW
 BIG = 4096.0
+LIFT = (8.0, 1.0, 1.0)
 CFG = {
-    "min": "vvvv vvvv vvvv vvvv vvvv vvvv",
+    "min": "vvvv vvvv fffv vvvv ffff vvvv", "xs": "ggg", "spread": "ll Hl Hl", "wrap": "vvvv", "live": "aavv", "abank": "ua ub ua ub",
+    "xm": "22 211 22 211 22 211", "ids": (-1.0, BIG, 3.0, -4.0),
     "gx": "aaaa aaaa aaaa aaaa aaaa aaaa",
     "gu": {"2U23": "aaaa", "2U34": "aaaa"},
-    "jump": "avav avav aaaa aaaa",
-    "split": {"gx": 2, "jg": 2},
-    "fin": "Fp Fp Pss Pss Fp Fp Pss Pss Fp Fp Pss Pss",
-    "pieces": "X02 x24 U01 u12 U23 u34",
-    "order": "0w0 0w1 0j0 0q0 0j1 0q1 0X0 0c0 0x0 0X1 0x1 0c1 0s0 0U01 0U12 0U23 0U34 1w0 0s1 0u23 0u01 0u34 0u12 1w1 1j0 1q0 1j1 1q1 "
-             "1X0 1c0 1x0 1X1 1x1 1c1 1s0 1U01 1U12 1U23 1U34 2w0 1s1 1u23 1u01 1u34 1u12 2w1 "
-             "2X0 2c0 2x0 2X1 2x1 2c1 2U01 2U12 2U23 2U34 2s0 2s1 2u23 2u01 2u34 2u12",
-    "ubank": "aabb", "qbank": "ua",
-    "ages": "av", "halved": (), "copies": 2, "reads": 1, "table": "aa", "kept": ("gu", "gx"),
+    "jump": "avvv avav aaaa aaaa",
+    "split": {"gx": 2, "jg": 1},
+    "pieces": "X02 x24 u01 U12 U23 u34",
+    "order": "0w0 0w1 0j0 0q0 0j1 0q1 0X0 0c0 0x0 0X1 0x1 0c1 0s0 0U01 0U12 0u12 0U23 0U34 1w0 0s1 0u23 0u01 0u34 1w1 1j0 1j1 "
+             "1X0 1c0 1x0 1X1 1x1 1c1 1q0 1q1 1s0 1U01 1U12 1u12 1U23 1U34 2w0 1s1 1u23 1u01 1u34 2w1 "
+             "2X0 2c0 2x0 2X1 2x1 2c1 2U01 2U12 2u12 2U23 2U34 2s0 2s1 2u23 2u01 2u34",
+    "ubank": "abbb abbb abbb", "qbank": "ua ub xb0 xb1",
+    "ages": "aa", "copies": 2, "reads": 2, "behind": (), "kept": ("gu", "gx"),
     "loads": "xsj pawu", "cuts": (192, 512), "first": "xrd",
     "due": {"X": (0, 3), "x": (0, 3), "c": (0, 3), "w": (-28, -25), "s": (0, 3), "U": (0, 1, 2, 3), "u": (0, 3, 6, 9), "j": (0, 3), "q": (0, 3),
             "a": (20, 23), "y": (0, 0)},
     "yield": {"gx": 30, "jg": 52, "xm": 40, "min": 41, "gu": 50, "scan": 45, "relu": 29, "um": 53},
     "early": {"load": -100, "list": -85, "const": 0, "init0": -47, "init1": -45, "0w0": -44, "0w1": -43},
-    "period": 28.0, "seed": 2, "rounds": 4000, "temp": 300.0, "swaps": 16000, "heat": 150.0, "more": 25000, "cool": 0.5,
+    "period": 28.0, "seed": 3, "starts": 2, "rounds": 500, "temp": 300.0, "swaps": 130000, "heat": 180.0, "cool": 0.7,
 }
 PRM = {"cy": 0.88, "pe": 0.44, "gc": 1.56, "link": 13.0, "lat": 2500.0, "sync": 100.0, "fx": 40.0, "dr": 3.0, "dl": 2000.0, "fl": 2000.0, "share": 0.4,
-       "fr": 1.0, "short": 2.0, "long": 0.9}
+       "fr": 1.0, "short": 2.0, "long": 0.9, "cross": 1.5}
+NH = 4
 SPREAD = [{"cy": 1.0, "gc": 1.5, "pe": 0.55}, {"cy": 0.83, "gc": 1.1, "lat": 2000.0, "sync": 70.0, "pe": 0.42},
-          {"cy": 1.245, "gc": 1.95, "pe": 0.75}, {"cy": 0.9, "gc": 1.3, "dr": 3.7, "lat": 3200.0, "link": 22.0, "share": 0.6}]
+          {"cy": 1.2, "gc": 2.05, "pe": 0.65}, {"cy": 0.9, "gc": 1.3, "dr": 3.5, "lat": 3000.0, "link": 18.0, "share": 0.5}]
 WEIGHT = [2, 2, 2, 2]
-SCALE = [1.25, 1.0, 1.72, 1.25]
-REMOTE = {"F": 4, "3": 3, "2": 2}
-LEFT = {"0": [0, 1, 2, 3], "P": [0, 2], "F": [-1], "3": [3, -1], "2": [2, 3, -1]}
-UNDER = " 1y0 " in CFG["order"]
+SCALE = [1.20, 1.01, 1.60, 1.21]
+FLUSH = 1.5 * 2.0 ** 40
 
 bf, f32, f16, i32, u16 = "bfloat16", "float32", "float16", "int32", "uint16"
 ND = f16
@@ -48,7 +49,9 @@ def _buf(name, cols, dt, where="sbuf"):
     SCRATCH[name] = (where, [128, cols], dt)
 
 
-SCALES = [1.0, -1.0, 256.0, 128.0, 2.0, 3.0, -4.0, -1.5, -16.0, BIG, -BIG, -2 * BIG, BIG / 2, -BIG / 2, 1.5 * BIG, 2.0 ** -19]
+SCALES = [1.0, -1.0, 256.0, 128.0, 2.0, 3.0, -4.0, -1.5, -16.0, BIG, -2 * BIG, BIG / 2, -BIG / 2, 1.5 * BIG]
+SHORT = " 0a0 " in CFG["order"]
+SCALES += [-1024.0] * ("a" in CFG["wrap"]) + [-32.0] * SHORT
 for _t in range(STEPS):
     _buf("tx%d" % _t, NR * V, bf)
     _buf("tu%d" % _t, NR * V, f32)
@@ -56,45 +59,47 @@ for _t in range(STEPS):
     _buf("ga%d" % _t, V, bf)
 for _j in range(2):
     _buf("xc%d" % _j, 4 * BL, bf)
-    _buf("pu%d" % _j, 4 * BL, f32)
-    _buf("wp%d" % _j, HW if CFG["copies"] else BL, bf)
+    _buf("wp%d" % _j, HW, bf)
     _buf("wr%d" % _j, 4 * BL, bf)
     _buf("wr%d" % (2 + _j), 4 * BL, bf)
-    _buf("sc%d" % _j, BL, f32)
-    _buf("uc%d" % _j, BL // 2, f32)
+    _buf("sc%d" % _j, RUN, f32)
     _buf("sg%d" % _j, 8 * HW, bf)
-    if any(how[0] in REMOTE for how in CFG["fin"].split()[2 * _j::4] + CFG["fin"].split()[2 * _j + 1::4]):
-        _buf("fo%d" % _j, BL, f32)
-    if UNDER:
-        _buf("jm%d" % _j, BL, f32)
-    else:
-        _buf("jb%d" % _j, 4 * BL, bf)
-    for _n in ("bb", "lv", "ww", "nw"):
+    _buf("mn%d" % _j, 4 * BL, bf)
+    _buf("jb%d" % _j, 4 * BL, bf)
+    if CFG["gu"]:
+        _buf("uc%d" % _j, BL // 2, f32)
+    if "f" in "".join(CFG["min"].split()[_j::2]):
+        _buf("xs%d" % _j, BL, bf)
+    for _n in ("bb", "lv", "nw") + ("ww",) * (_j == 0 or not SHORT):
         _buf("%s%d" % (_n, _j), V, bf)
     _buf("cc%d" % _j, V, ND)
     _buf("q%d" % _j, V, ND)
 for _n, _c, _d in [
-        ("mn", 4 * BL, bf), ("px", 4 * BL, f16), ("jt", NR * V, bf), ("si", V, i32), ("pi", V, i32), ("ab", V, bf), ("ti", 4, i32),
-        ("sf", V, ND), ("r1", V, ND), ("r2", V, ND), ("md", V, bf), ("tm2", 16, f32), ("tm3", 4, f32), ("lf", 256, bf), ("bk", 256, bf), ("ba", 256, bf),
-        ("yy", V, bf), ("xo", V, bf), ("uo", V, f32), ("wo", V, f32), ("co", V, f32),
-        ("ck", V, f16), ("nq", V, bf), ("ss", V, bf), ("ones", HW, bf), ("msk", BL, bf), ("thf", 4, f32),
-        ("ci", 144, bf), ("cm", 128, bf), ("cb", 128, bf), ("cg", 128, bf), ("ia", 16, i32), ("ib", 16, i32), ("ic", 16, i32), ("fa", 16, f32),
-        ("ks", 16, f32), ("mk16", 4, f32), ("mk23", 4, f32), ("tb", 1, f32), ("col", 16, f32), ("tmp", 16, f32), ("m4", 4, f32), ("k12", 1, f32), ("k4", 2, f32),
-        ("bo", 128, bf), ("ee", 144, bf), ("ne", 144, bf), ("dg", 512, bf), ("sh", 2048, bf), ("n32", 128, bf), ("nm", 128, bf),
-        ("kd", 128, bf), ("nih", 128, f16), ("ino", 128, ND), ("inn", 128, ND), ("ni1", 128, f32), ("ik", 128, f32), ("pw", 4 * 144, ND),
+        ("px", 4 * BL, f16), ("jt", NR * V, bf), ("si", V, i32), ("pi", V, i32), ("ab", V, bf), ("ti", 4, i32),
+        ("sf", V, ND), ("r1", V, ND), ("r2", V, ND), ("md", V, bf), ("yy", V, bf),
+        ("ck", V, f16), ("nq", V, bf), ("ss", V, bf), ("ones", HW, bf), ("pf", 2 * BL, f32), ("fo", 512, f32), ("thf", 4, f32),
+        ("ci", 144, bf), ("cm", 128, bf), ("cb", 128, bf), ("ia", 16, i32), ("ib", 16, i32), ("ic", 16, i32), ("fa", 16, f32),
+        ("ks", 16, f32), ("mk16", 4, f32), ("tb", 1, f32), ("col", 16, f32), ("m4", 4, f32), ("k12", 1, f32), ("k4", 4, f32),
+        ("bo", 128, bf), ("ee", 144, bf), ("dg", 512, bf), ("sh", 2048, bf), ("n32", 128, bf), ("nm", 128, bf), ("nil", HW, bf), ("lc", 4, f32), ("bl", 256, bf),
+        ("kd", 128, bf), ("ni1", 128, f32), ("ik", 128, f32), ("pw", 4 * 144, ND),
         ("gm", 4 * 144, bf), ("sid", 128 * len(SCALES), bf)] + \
-        [("ty", NR * V, f32), ("dy", 512, f32)] * UNDER + [("e2", V, bf), ("wcp", V, bf), ("na", V, bf)] * (" 0a0 " in CFG["order"]):
+        [("gn", 4 * 144, bf)] * ("H" in CFG["spread"]) + [("e2", V, bf), ("wcp", V, bf), ("na", V, bf)] * SHORT:
     _buf(_n, _c, _d)
-for _j in range(2 * STEPS * (CFG["copies"] > 0)):
-    SCRATCH["wd%d" % _j] = ("dram", [8, CFG["copies"], 4 * BL], bf)
+for _j in range(2 * STEPS):
+    if "".join(CFG["spread"].split())[_j] == "H":
+        SCRATCH["we%d" % _j] = ("dram", [128, HW], bf)
+    else:
+        SCRATCH["wd%d" % _j] = ("dram", [8, CFG["copies"], 4 * BL], bf)
+_buf("pt", 4 * RUN, f32)
 _buf("xb", BL, f32, "psum")
 for _n in ("ua", "ub", "m0", "m1", "m2", "m3"):
     _buf(_n, 512, f32, "psum")
 
 ENG = ("g", "pe", "dve", "act", "sp")
 NDMA = 64
-SEMAPHORES = ["q_" + e for e in ENG] + ["d%d" % i for i in range(NDMA)] + ["sent"] + ["h%d" % i for i in range(10)] + \
-             ["%s%d" % (k, i) for k in ("fl", "fh", "afo") for i in range(12)] + ["ax%d" % t for t in range(STEPS)] + ["au%d" % t for t in range(STEPS)]
+SEMAPHORES = ["q_" + e for e in ENG] + ["d%d" % i for i in range(NDMA)] + ["sent"] + \
+             ["%s%d" % (k, i) for k in ("fl", "afo") for i in range(12)] + ["ax%d" % t for t in range(STEPS)] + ["au%d" % t for t in range(STEPS)] + \
+             ["%s%d%d" % (k, h, j) for k in ("ml", "am") for h in range(2) for j in range(4)] + ["wl0", "wl1", "aw0", "aw1"]
 KEPT = {}
 
 
@@ -119,7 +124,7 @@ def dispatch(nodes, after, count, pr):
     return order
 
 
-def replay(nodes, order, sync):
+def span_of(nodes, order, sync):
     free, end = {}, [0.0] * len(nodes)
     for i in order:
         x = nodes[i]
@@ -127,6 +132,33 @@ def replay(nodes, order, sync):
         free[x["eng"]] = st + x["cost"]
         end[i] = st + x["cost"] + x["lat"]
     return max(end)
+
+
+def replay(nodes, order, sync):
+    after, left, last = [[] for _ in nodes], [0] * len(nodes), {}
+    for i in order:
+        x = nodes[i]
+        before = x["soft"] if x["eng"] not in ENG else [last[x["eng"]]] if x["eng"] in last else []
+        for d, hard in [(d, True) for d in x["hard"]] + [(d, False) for d in before]:
+            after[d].append((i, hard))
+            left[i] += 1
+        last[x["eng"]] = i
+    ready, start, free, out, end = [0.0] * len(nodes), [0.0] * len(nodes), {}, [], 0.0
+    pend = [(0.0, i) for i in range(len(nodes)) if not left[i]]
+    while pend:
+        t, i = first = min(pend)
+        pend.remove(first)
+        x = nodes[i]
+        start[i] = st = max(t, free.get(x["eng"], 0.0))
+        free[x["eng"]] = st + x["cost"]
+        out.append(i)
+        end = max(end, st + x["cost"] + x["lat"])
+        for j, hard in after[i]:
+            ready[j] = max(ready[j], st + x["cost"] + (x["lat"] + sync if hard else 0.0))
+            left[j] -= 1
+            if not left[j]:
+                pend.append((ready[j], j))
+    return end, out, start
 
 
 def order_nodes(sets):
@@ -154,24 +186,25 @@ def order_nodes(sets):
         for i in fixed:
             pr[i] = max([pr[j] for j, _gap in after[i]], default=0.0) + 1.0
         order = dispatch(nodes, after, count, pr)
-        return sum(w * replay(o, order, sy) / s for w, s, (o, sy) in zip(WEIGHT, SCALE, sets)) / sum(WEIGHT), order
-    best = cur = judge(pr)
-    KEPT["first"] = best[0]
-    for it in range(CFG["rounds"]):
-        new = list(pr)
-        for _ in range((1, 1, 2)[int(3 * rnd())]):
-            d = (-8, -5, -3, -2, -1, 1, 2, 3, 5, 8)[int(10 * rnd())] * 1000.0
-            groups = parts if rnd() < 0.6 else kinds
-            for i in groups[int(len(groups) * rnd())]:
-                new[i] += d
-        got = judge(new)
-        if got[0] < cur[0] - CFG["temp"] * (1 - it / CFG["rounds"]) * math.log(rnd()):
-            cur, pr = got, new
-            if got[0] < best[0]:
-                best = got
-    KEPT["mid"] = best[0]
-    best = polish(sets, best[1], rnd, CFG["swaps"], CFG["heat"])
-    return polish(sets, best[2], rnd, CFG["more"], CFG["heat"] * CFG["cool"])
+        return sum(w * span_of(o, order, sy) / s for w, s, (o, sy) in zip(WEIGHT, SCALE, sets)) / sum(WEIGHT), order
+    def start(pr):
+        best = cur = judge(pr)
+        for it in range(CFG["rounds"]):
+            new = list(pr)
+            for _ in range((1, 1, 2)[int(3 * rnd())]):
+                d = (-8, -5, -3, -2, -1, 1, 2, 3, 5, 8)[int(10 * rnd())] * 1000.0
+                groups = parts if rnd() < 0.6 else kinds
+                for i in groups[int(len(groups) * rnd())]:
+                    new[i] += d
+            got = judge(new)
+            if got[0] < cur[0] - CFG["temp"] * (1 - it / CFG["rounds"]) * math.log(rnd()):
+                cur, pr = got, new
+                if got[0] < best[0]:
+                    best = got
+        return polish(sets, best[1], rnd, CFG["swaps"] // 6, CFG["heat"])
+    got = sorted(start(list(pr)) for _ in range(CFG["starts"]))
+    KEPT["starts"] = [round(x[0]) for x in got]
+    return polish(sets, got[0][2], rnd, CFG["swaps"], CFG["heat"] * CFG["cool"])
 
 
 def polish(sets, order, rnd, swaps, heat):
@@ -187,88 +220,139 @@ def polish(sets, order, rnd, swaps, heat):
         hard.append(keep)
     names = sorted({x["eng"] for x in nodes})
     eng = [names.index(x["eng"]) for x in nodes]
+    queue = [names[e] in ENG for e in eng]
     pre = [x["hard"] | x["soft"] for x in nodes]
+    post, succ = [set() for _ in nodes], [[] for _ in nodes]
+    for i in range(n):
+        for d in pre[i]:
+            post[d].add(i)
+        for d in hard[i]:
+            succ[d].append(i)
     tabs = [([x["cost"] for x in o], [x["lat"] + sy for x in o]) for o, sy in sets]
-    pick = [k for k, w in enumerate(WEIGHT) for _ in range(w)]
+    every = range(len(tabs))
     share = [w / sum(WEIGHT) / scale for w, scale in zip(WEIGHT, SCALE)]
-    rows = {i: (i, eng[i], hard[i]) for i in range(n)}
+    order, pos, ahead, behind = list(order), [0] * n, [n] * (n + 1), [n] * (n + 1)
 
-    def run(order, k, at, old):
+    def link(lo, part, first, final):
+        order[lo:lo + len(part)] = part
+        last = dict(first)
+        for p, i in enumerate(part, lo):
+            pos[i], ahead[i] = p, last[eng[i]]
+            behind[ahead[i]] = last[eng[i]] = i
+        for e, x in final.items():
+            behind[last[e]], ahead[x] = x, last[e]
+
+    def heads(k, lo, end, gone):
         cost, lat = tabs[k]
-        free, end, seen = [0.0] * len(names), list(old), set()
-        for i in reversed(order[:at]):
-            if eng[i] not in seen:
-                seen.add(eng[i])
-                free[eng[i]] = end[i] - lat[i]
-                if len(seen) == len(names):
-                    break
-        for i, e, before in map(rows.get, order[at:]):
-            st = free[e]
-            for d in before:
+        for i in order[lo:]:
+            st = gone[ahead[i]]
+            for d in hard[i]:
                 if end[d] > st:
                     st = end[d]
-            free[e] = st = st + cost[i]
+            gone[i] = st = st + cost[i]
             end[i] = st + lat[i]
-        return end
 
-    def chain(order, end, lat):
-        last, ahead, pairs = {}, {}, []
-        for i in order:
-            ahead[i], last[eng[i]] = last.get(eng[i]), i
-        i = end.index(max(end))
+    def tails(k, hi, tail):
+        cost, lat = tabs[k]
+        for i in order[hi::-1]:
+            q = 0.0
+            for d in succ[i]:
+                if tail[d] > q:
+                    q = tail[d]
+            q += lat[i]
+            if tail[behind[i]] > q:
+                q = tail[behind[i]]
+            tail[i] = q + cost[i]
+
+    def chain(k):
+        end, gone, pairs = ends[k], gones[k], []
+        i = end.index(span[k])
         while i is not None:
             d = max(hard[i], key=lambda d: end[d], default=None)
             p = ahead[i]
-            if p is not None and (d is None or end[p] - lat[p] >= end[d]):
-                if names[eng[i]] in ENG or end[d] <= max(end[x] for x in hard[p]):
+            if p != n and (d is None or gone[p] >= end[d]):
+                if queue[i] or (hard[p] and d is not None and end[d] <= max(end[x] for x in hard[p])):
                     pairs.append((p, i))
                 d = p
             i = d
         return pairs
 
-    def swap(order, a, b):
-        ia, ib = order.index(a), order.index(b)
-        need, engs, preds = [b], set(), set(pre[b])
-        for x in reversed(order[ia:ib]):
-            if x in preds or eng[x] in engs:
-                if x == a:
-                    return None
+    ends, gones, tls = [[[0.0] * (n + 1) for _ in every] for _ in range(3)]
+    best = (1e18, None, None)
+    for it in range(swaps + 1):
+        if it % 1000 == 0 or it == swaps:
+            got = [replay(o, order, sy) for o, sy in sets]
+            v = sum(s * x[0] for s, x in zip(share, got))
+            if v < best[0]:
+                best = (v, got[0][2], got[0][1])
+            if it == swaps:
+                return best
+            none = {e: n for e in set(eng)}
+            link(0, got[int(len(tabs) * rnd())][1], none, none)
+            for k in every:
+                heads(k, 0, ends[k], gones[k])
+                tails(k, n - 1, tls[k])
+            span = [max(e) for e in ends]
+            cur, pairs = sum(s * v for s, v in zip(share, span)), None
+        if pairs is None or rnd() < 0.05:
+            pairs = chain(int(len(tabs) * rnd()))
+        (a, b), back = pairs[int(len(pairs) * rnd())], rnd() < 0.5
+        for _ in range((0, 0, 0, 1, 1, 2, 3, 5)[int(8 * rnd())] * queue[a]):
+            if back and ahead[a] != n:
+                a = ahead[a]
+            if not back and behind[b] != n:
+                b = behind[b]
+        ia, ib = pos[a], pos[b]
+        old = order[ia:ib + 1]
+        mover, stop, rel = (b, a, pre) if back else (a, b, post)
+        need, engs, tied = [mover], set(), set(rel[mover])
+        for x in (old[-2::-1] if back else old[1:]):
+            if x in tied or eng[x] in engs:
                 need.append(x)
                 engs.add(eng[x])
-                preds |= pre[x]
-        return order[:ia] + need[::-1] + [x for x in order[ia:ib] if x not in need] + order[ib + 1:], ia
-
-    ends = [run(order, k, 0, [0.0] * n) for k in range(len(tabs))]
-    cur, pairs = sum(s * max(e) for s, e in zip(share, ends)), None
-    best = (cur, order)
-    for it in range(swaps):
-        if pairs is None or rnd() < 0.1:
-            k = pick[int(len(pick) * rnd())]
-            pairs = chain(order, ends[k], tabs[k][1])
-        a, b = pairs[int(len(pairs) * rnd())]
-        got, back = swap(order, a, b), rnd() < 0.5
-        if got is None:
+                tied |= rel[x]
+        if need[-1] == stop:
             continue
-        new, at = got
-        for _ in range((0, 0, 1, 2, 3, 5)[int(6 * rnd())] * (names[eng[a]] in ENG)):
-            k = new.index(b if back else a)
-            near = [x for x in (new[max(0, k - 60):k][::-1] if back else new[k + 1:k + 60]) if eng[x] == eng[a]]
-            more = near and (swap(new, near[0], b) if back else swap(new, a, near[0]))
-            if not more:
-                break
-            new, at = more[0], min(at, more[1])
-        bar, got, v = cur - heat * (1 - it / swaps) * math.log(rnd()), [], 0.0
-        for k in range(len(tabs)):
-            got.append(run(new, k, at, ends[k]))
-            v += share[k] * (max(got[k]) - max(ends[k]))
-            if cur + v > bar + 600.0:
-                break
-        if len(got) == len(tabs) and cur + v < bar:
-            cur, order, pairs, ends = cur + v, new, None, got
-            if cur < best[0]:
-                best = (cur, new)
-    end = run(best[1], 0, 0, [0.0] * n)
-    return best[0], [end[i] - tabs[0][0][i] - tabs[0][1][i] for i in range(n)], best[1]
+        moved = set(need)
+        rest = [x for x in old if x not in moved]
+        new = need[::-1] + rest if back else rest + need
+        first, final = {eng[x]: ahead[x] for x in reversed(old)}, {eng[x]: behind[x] for x in old}
+        bar, v = cur - heat * (1 - it / swaps) * math.log(rnd()), 0.0
+        for k in every:
+            (cost, lat), end, tail, gone = tabs[k], ends[k], tls[k], gones[k]
+            free, now, est, on = {e: gone[p] for e, p in first.items()}, {}, 0.0, False
+            for i in new:
+                st = free[eng[i]]
+                for d in hard[i]:
+                    y = now[d] if d in now else end[d]
+                    if y > st:
+                        st = y
+                free[eng[i]] = st = st + cost[i]
+                now[i] = st = st + lat[i]
+                if st > est:
+                    est = st
+                for d in succ[i]:
+                    if pos[d] > ib and st + tail[d] > est:
+                        est = st + tail[d]
+                on = on or gone[i] - cost[i] + tail[i] >= span[k] - 1e-6
+            for e, x in final.items():
+                if free[e] + tail[x] > est:
+                    est = free[e] + tail[x]
+            v += share[k] * (est if on or est > span[k] else span[k])
+        if v >= bar:
+            continue
+        link(ia, new, first, final)
+        e2, g2 = [list(e) for e in ends], [list(e) for e in gones]
+        for k in every:
+            heads(k, ia, e2[k], g2[k])
+        s2 = [max(e) for e in e2]
+        v = sum(s * x for s, x in zip(share, s2))
+        if v < bar:
+            cur, ends, gones, span, pairs = v, e2, g2, s2, None
+            for k in every:
+                tails(k, ib, tls[k])
+        else:
+            link(ia, old, first, final)
 
 
 def plan(g, core, T, topo):
@@ -291,11 +375,11 @@ def relayed():
 
 
 def finish():
-    return dict(zip([p for p in CFG["order"].split() if p[1] == "U"], CFG["fin"].split()))
+    return {p: "FTTT"[int(p[2])] for p in CFG["order"].split() if p[1] == "U"}
 
 
 def folded():
-    return [(int(p[0]), int(p[2]), int(p[3]), REMOTE[how[0]]) for p, how in finish().items() if how[0] in REMOTE]
+    return [(int(p[0]), int(p[2]), int(p[3]), 4) for p, how in finish().items() if how == "F"]
 
 
 def helper_of(core, T, topo):
@@ -303,20 +387,66 @@ def helper_of(core, T, topo):
             and all(topo.may_write(c, p) for p in T.cores)][0]
 
 
-def mirror_of(core, T, topo):
-    return [c for c in topo.cores_of(core) if topo.die(c) == topo.die(core) and T.rank_of(c) is None and topo.addr(c)[2] != topo.addr(core)[2]][0]
+def mirror_of(core, T, topo, which=0):
+    return [c for c in topo.cores_of(core) if topo.die(c) == topo.die(core) and T.rank_of(c) is None and topo.addr(c)[2] != topo.addr(core)[2]][which]
+
+
+def spreaders(core, T, topo):
+    taken = [helper_of(core, T, topo), mirror_of(core, T, topo), mirror_of(core, T, topo, 1)]
+    free = [c for c in topo.cores_of(core) if T.rank_of(c) is None and c not in taken]
+    return sorted(free, key=lambda c: topo.addr(c)[2] == topo.addr(core)[2])[:NH]
+
+
+def minned():
+    out = []
+    for part in CFG["order"].split():
+        if part[1] == "c":
+            t, h, run = int(part[0]), int(part[2]), []
+            for kh, who in enumerate(CFG["min"].split()[2 * t + h]):
+                run += [kh] * (who in "fF")
+                if who == "f":
+                    out.append((t, h, kh, run))
+                    run = []
+    return out
+
+
+def min_place(T, t, h, k0, k1, rows=slice(0, 128)):
+    return T[("wr0", "wr1", "wr2", "wr3", "xc0", "xc1")[2 * t + h]][rows, k0 * BL:k1 * BL]
+
+
+def hand_min(g, core, home, T, topo):
+    mask = topo.mask(core, home)
+    for k, (t, h, last, blocks) in enumerate(minned()):
+        g.wait_ge(T.sem["d%d" % k], bin(topo.mask(home, core)).count("1"))
+        g.remote_dma(T["mn%d" % h][:, blocks[0] * BL:(last + 1) * BL], min_place(T, t, h, blocks[0], last + 1), T.sem["am%d%d" % (h, last)], T.sem.sent,
+                     topo.addr(home)[1], topo.addr(home)[0], mask)
+    g.wait_ge(T.sem.sent, bin(mask).count("1") * len(minned()))
+
+
+def hand_spread(g, core, home, j, T, topo):
+    mask, k, rows = topo.mask(core, home), 4 // NH, 128 // NH
+    jobs = [(int(p[0]), int(p[2])) for p in CFG["order"].split() if p[1] == "w" and CFG["spread"].split()[int(p[0])][int(p[2])] == "H"]
+    for t, h in jobs:
+        here, laid = min_place(T, t, h, j * k, (j + 1) * k), T.sem["d%d" % (8 + 2 * t + h)]
+        for i, q in enumerate((g.sync, g.scalar)):
+            q.wait_ge(T.sem["d%d" % (2 * t + h)], bin(topo.mask(home, core)).count("1"))
+            for trial in range(8 * i, 8 * i + 8):
+                q.dma_start(min_place(T, t, h, j * k, (j + 1) * k, slice(trial, 128, 16)), T["we%d" % (2 * t + h)][j * rows:(j + 1) * rows, :]).then_inc(laid, 16)
+        g.wait_ge(laid, 16 * 16)
+        g.remote_dma(T["wr%d" % (2 * (t % 2) + h)][:, j * k * BL:(j + 1) * k * BL], here, T.sem["aw%d" % h], T.sem.sent,
+                     topo.addr(home)[1], topo.addr(home)[0], mask)
+    g.wait_ge(T.sem.sent, bin(mask).count("1") * len(jobs))
 
 
 def fold_sides(T, t, q0, q1):
-    h, at, w = q0 // 2, 512 * (q0 % 2), 512 * (q1 - q0)
-    return T["pu%d" % h][:, t * BL + at:t * BL + at + w], T["fo%d" % h][:, at:at + w]
+    return T.pf[:, 512 * t:512 * (t + 1)], T.fo[:]
 
 
 def hand_back(g, core, home, T, topo):
     mask = topo.mask(core, home)
     for k, (t, q0, q1, _n) in enumerate(folded()):
         there, back = fold_sides(T, t, q0, q1)
-        g.wait_ge(T.sem["fh%d" % k], bin(topo.mask(home, core)).count("1"))
+        g.wait_ge(T.sem["d%d" % k], bin(topo.mask(home, core)).count("1"))
         g.remote_dma(back, there, T.sem["afo%d" % k], T.sem.sent, topo.addr(home)[1], topo.addr(home)[0], mask)
     g.wait_ge(T.sem.sent, bin(mask).count("1") * len(folded()))
 
@@ -334,7 +464,7 @@ def hand_on(g, core, rank, T, topo):
     neng = bin(mask).count("1")
     for k, (kind, t, c0, c1) in enumerate(relayed()):
         ap = T["t%s%d" % (kind, t)][:, rank * V + c0:rank * V + c1]
-        g.wait_ge(T.sem["h%d" % k], neng)
+        g.wait_ge(T.sem["d%d" % k], neng)
         g.remote_dma_fused([RemoteDMATransfer(dst_ids=ids, dma_engine_mask=mask, remote_sem=T.sem["a%s%d" % (kind, t)], srcs=[ap], dsts=[ap] * len(ids))],
                            local_sem=T.sem.sent)
     g.wait_ge(T.sem.sent, neng * len(relayed()))
@@ -343,7 +473,7 @@ def hand_on(g, core, rank, T, topo):
 def build(g, core, T, topo, PRM):
     rank = T.rank_of(core)
     CY, PEC, GC = PRM["cy"], PRM["pe"], PRM["gc"]
-    nodes, here = [], ["load"]
+    nodes, here = [], ["load", []]
     lastw, readers, bankt = {}, {}, {}
     ve, ac, pe = g.vector, g.scalar, g.tensor
 
@@ -364,6 +494,12 @@ def build(g, core, T, topo, PRM):
                 dep(lastw[k], eng != "pe")
             for d in readers.get(k, ()):
                 dep(d, True)
+        for k in here[1]:
+            for d in readers.get(k, ()):
+                dep(d, True)
+        here[1] = []
+        if name == "jg" and eng == "act" and here[0] in CFG["behind"]:
+            soft.add(bankt[("gx", eng)][eng])
         for b in list(banks) + [(name, eng)] * (name in CFG["kept"]):
             for d in bankt.get(b, {}).values():
                 dep(d, False)
@@ -376,6 +512,17 @@ def build(g, core, T, topo, PRM):
         nodes.append({"eng": eng, "cost": cost, "lat": lat, "fn": fn, "hard": hard, "soft": soft - hard, "kind": kind, "name": name,
                       "of": i if of is None else of, "part": here[0]})
         return i
+
+    def join(k):
+        first, part = len(nodes) - k, nodes[len(nodes) - k:]
+        del nodes[first + 1:]
+        nodes[first] = dict(part[0], cost=sum(x["cost"] for x in part), fn=lambda: [x["fn"]() for x in part][-1],
+                            hard=set().union(*[x["hard"] for x in part]), soft={d for x in part for d in x["soft"] if d < first})
+        assert max(nodes[first]["hard"], default=-1) < first
+        for key, i in lastw.items():
+            lastw[key] = min(i, first)
+        for key, l in readers.items():
+            readers[key] = [min(i, first) for i in l]
 
     def dve(n, cyc, fn, r, w, banks=(), name=""):
         node("dve", PRM["fx"] + max(64, n * cyc) * CY, fn, r, w, banks, name=name)
@@ -403,8 +550,8 @@ def build(g, core, T, topo, PRM):
             return last
         node("pe", 30 + sum(max(64, it[5]) * PEC for it in items), fn, r, w, (bank,), lat=100.0, name=name)
 
-    def acc(out, terms, n, r, w, bank, name="", start=True):
-        mm([(out, l, x, start and i == 0, i == len(terms) - 1, n * c) for i, (l, x, c) in enumerate(terms)], r, w, bank, name)
+    def acc(out, terms, n, r, w, bank, name=""):
+        mm([(out, l, x, i == 0, i == len(terms) - 1, n * c) for i, (l, x, c) in enumerate(terms)], r, w, bank, name)
 
     def sid(s):
         k = SCALES.index(s)
@@ -440,7 +587,7 @@ def build(g, core, T, topo, PRM):
         sem = T.sem["a%s%d" % (kind, t)]
         ncalls[(kind, t)] = ncalls.get((kind, t), 0) + 1
         if (kind, t, c0, c1) in relayed():
-            hs_ = T.sem["h%d" % relayed().index((kind, t, c0, c1))]
+            hs_ = T.sem["d%d" % relayed().index((kind, t, c0, c1))]
             node("g", 600.0, lambda: g.remote_dma(ap, ap, hs_, T.sem.sent, topo.addr(aid)[1], topo.addr(aid)[0], near),
                  keys, [("wire", kind, t, c0), "turn"], ["fifog"] * (t == 0), kind="r", name="relay")
             node("dma", 300.0 + kb * 2 * PRM["dr"], None, [("wire", kind, t, c0)], [("hop", kind, t, c0)], ["fifo"] * (t == 0), lat=PRM["lat"] + 600.0, kind="l")
@@ -485,7 +632,7 @@ def build(g, core, T, topo, PRM):
         else:
             node("g", 130 + 2 * n * CY, lambda: g.iota(out, pat, base, cm), [], [key])
     here[0] = "const"
-    short = " 0a0 " in CFG["order"]
+    short = SHORT
     iota(T.ia[:], [[-1, 16]], 16, 1, 16, "ia", False)
     iota(T.ci[:], [[1, 144]], 0, 0, 144, "ci")
     iota(T.cm[:], [[0, 8], [1, 16]], 0, 0, 128, "cm")
@@ -505,48 +652,58 @@ def build(g, core, T, topo, PRM):
     ts(T.bo[:], T.cb[:], pb16, None, A.is_equal, None, 128, .5, ["cb", "col"], ["bo"], name="bo")
     ts(T.ee[:], T.ci[:], pb16, None, A.is_equal, None, 144, .5, ["ci", "col"], ["ee"], name="ee")
     sent = [("wire", "u", 0, c) for c in (0,) + cuts] + [("wire", "x", 0, 0)]
-    SHARED = sorted({who for who in CFG["min"].split() if "a" in who})
-    if SHARED:
-        ts(T.ne[:], T.ci[:], pb16, -1.0, A.is_equal, A.mult, 144, .5, ["ci", "col"], ["ne"], name="ee")
-    for i, who in enumerate(SHARED):
-        node("g", 170 + 256 * CY, lambda i=i, who=who: g.affine_select(blk(T.bk, i), T.cb[:], [[0, 32], [1, 4]], A.is_ge, 0.0, -who.index("a"), 0),
-             ["cb"] + sent, [("bk", who)])
-        ts(blk(T.ba, i), blk(T.bk, i), pb16, None, A.is_equal, None, 128, .5, [("bk", who), "col"], [("ba", who)], name="ba")
     cI = T.ci[:, 0:128]
     k0 = T.ks[:, 0:1]
     ts(sid(1.0), cI, k0, None, A.is_equal, None, 128, .5, ["ci", "ks"], [("sid", 1.0)], name="sid")
-    for out, s, key in [(sid(s), s, ("sid", s)) for s in SCALES[1:len(SCALES) - (not UNDER)]] + \
-            [(T.nih[:], -1.0, "nih"), (T.ino[:], 1.0, "ino"), (T.inn[:], -1.0, "inn"), (T.ni1[:], -1.0, "ni1"), (T.ik[:], 1024.0, "ik"), (T.kd[:], p16, "kd")]:
-        act(out, sid(1.0), F.Identity, 128, [("sid", 1.0), "fa"], [key], scale=s, name="id")
+    dve(HW, .5, lambda: ve.memset(T.nil[:], 0.0), [], ["nil"], name="nil")
+    for out, s, key in [(sid(s), s, ("sid", s)) for s in SCALES[1:]] + [(T.ni1[:], -1.0, "ni1"), (T.ik[:], 1024.0, "ik")]:
+        if s in CFG["ids"] and key != "ni1":
+            act(out, sid(1.0), F.Identity, 128, [("sid", 1.0)], [key], scale=s, name="id")
+        else:
+            node("g", 170 + 256 * CY, lambda out=out, s=s: g.affine_select(out, T.nil[:, 0:128], [[-1, 128]], A.not_equal, s, 0, 1), ["nil"] + sent[-1:], [key], name="id")
+    act(T.kd[:], sid(1.0), F.Identity, 128, [("sid", 1.0), "fa"], ["kd"], scale=p16, name="id")
     for kh in range(4):
         ts(T.pw[:, 144 * kh:144 * (kh + 1)], T.ci[:], T.k12[:], T.m4[:, kh:kh + 1], A.is_equal, A.mult, 144, .5, ["ci", "k12", "m4"], [("pw", kh)], name="pw")
+    join(4)
     ts(T.nm[:], T.cm[:], p16, None, A.is_equal, None, 128, .5, ["cm", "fa"], ["nm"], name="n32")
     node("g", 170 + 256 * CY, lambda: g.affine_select(T.n32[:], T.nm[:], [[-1, 128]], A.not_equal, 33.0, 0, 1), ["nm"] + sent, ["n32"], name="n32")
-    if CFG["copies"]:
+    if "l" in CFG["spread"]:
         ts(T.k4[:, 0:1], T.ic[:, 0:1], 4.0, -13.0, A.mult, A.add, 1, 1, ["ic"], ["k4a"])
         act(T.k4[:, 1:2], T.k4[:, 0:1], F.Identity, 1, ["k4a", "col"], ["k4"], bias=pb16)
-    else:
-        iota(T.cg[:], [[16, 8], [0, 4], [1, 4]], 16, 0, 128, "cg")
-        cp(T.tmp[:], T.ia[:], 16, 1, ["ia"], ["tmp"])
-    if UNDER:
-        ts(T.mk23[:], T.mk16[:], 2.0 ** 19, None, A.mult, None, 4, 1, ["mk16"], ["mk23"])
+    if "H" in CFG["spread"]:
+        k = 4 // NH
+        ts(T.ic[:, 8:9], T.ib[:, 0:1], k - 1, None, A.bitwise_and, None, 1, 1, ["ib", "col"], ["ie"])
+        ts(T.k4[:, 2:3], T.ic[:, 0:1], 32.0, 3.0 - 4 * k, A.mult, A.add, 1, 1, ["ic"], ["k4b"])
+        act(T.k4[:, 3:4], pb16, F.Identity, 1, ["k4b", "col"], ["k4c"], scale=k / 4, bias=T.k4[:, 2:3])
+        ts(T.k4[:, 2:3], T.ic[:, 8:9], -28.0, T.k4[:, 3:4], A.mult, A.add, 1, 1, ["ie", "k4c"], ["k4b"])
     for kl in range(4):
         act(blk(T.dg, kl), sid(1.0), F.Identity, 128, [("sid", 1.0), "mk16"], [("dg", kl)], scale=T.mk16[:, kl:kl + 1], name="dg")
-        if UNDER:
-            act(blk(T.dy, kl), sid(1.0), F.Identity, 128, [("sid", 1.0), "mk23"], [("dy", kl)], scale=T.mk23[:, kl:kl + 1], name="dg")
-        if CFG["copies"]:
-            ts(T.gm[:, 144 * kl:144 * (kl + 1)], T.ci[:], T.k4[:, 1:2], T.mk16[:, kl:kl + 1], A.is_equal, A.mult, 144, .5, ["ci", "k4", "mk16"], [("gm", kl)], name="gm")
-        else:
-            ts(blk(T.gm, kl), T.cg[:], T.tmp[:, 4 * kl:4 * kl + 1], None, A.is_equal, None, 128, .5, ["cg", "tmp"], [("gm", kl)], name="gm")
-    assert all(who == "aaaa" and p[0] != "0" for p, who in CFG["gu"].items())
+    join(4)
+    for how, gm, at, key in (("l", "gm", 1, "k4"), ("H", "gn", 2, "k4b")):
+        if how in CFG["spread"]:
+            for kl in range(4):
+                ts(T[gm][:, 144 * kl:144 * (kl + 1)], T.ci[:], T.k4[:, at:at + 1], T.mk16[:, kl:kl + 1], A.is_equal, A.mult, 144, .5,
+                   ["ci", key, "mk16"], [(gm, kl)], name="gm")
+            join(4)
+    LIFTS = sorted({(LIFT[int(p[0])], who) for p, who in CFG["gu"].items()} - {(1.0, "aaaa")})
+    for i, (lift, who) in enumerate(LIFTS):
+        assert who in ("aaaa", "vvaa", "aavv")
+        ts(T.lc[:, i:i + 1], T.ic[:, 0:1], {"aaaa": -1.0}.get(who, 1.5), lift, A.is_lt if who == "aavv" else A.is_gt, A.mult, 1, 1, ["ic"], [("lc", i)])
+        act(blk(T.bl, i), T.bo[:], F.Identity, 128, ["bo", ("lc", i)], [("bl", lift, who)], scale=T.lc[:, i:i + 1], name="id")
     for s in range(1, 16):
         ts(blk(T.sh, s), cI, T.ks[:, s:s + 1], None, A.is_equal, None, 128, .5, ["ci", "ks"], [("sh", s)], name="sh")
+        if s % 3 == 0:
+            join(3)
     sh = T.sh[:, 128:2048]
     node("g", 170 + 2 * 1920 * CY, lambda: g.affine_select(sh, sh, [[0, 15], [-1, 128]], A.not_equal, -1.0, 0, 1),
          [("sh", s) for s in range(1, 16)] + sent, ["sh"], name="sh")
-    iota(T.ones[:], [[0, HW]], 1, 0, HW, "ones")
-    node("g", 130 + 2 * BL * CY, lambda: g.iota(T.msk[:], [[0, BL]], 1, 0, allow_small_or_imprecise_dtypes=True), ["sh"], ["msk"], name="msk")
-    node("g", 170 + 2 * BL * CY, lambda: g.affine_select(T.msk[:], T.msk[:], [[0, QW], [1, 8]], A.not_equal, 0.0, 0, 0), ["msk"], ["msk"], name="msk")
+    for i, sign in enumerate((1.0, -1.0)):
+        node("g", 130 + 2 * BL * CY, lambda i=i: g.iota(T.pt[:, 2 * RUN * i + 2:2 * RUN * (i + 1):3], [[0, BL]], 0, 0, allow_small_or_imprecise_dtypes=True),
+             sent, [("nought", i)], name="nought")
+    for i, sign in enumerate((1.0, -1.0)):
+        dve(HW, 1, lambda i=i, sign=sign: ve.memset(T.pt[:, 2 * RUN * i + 11:2 * RUN * (i + 1):12], sign * FLUSH), both("nought"), ["flush"][:i], name="flush")
+    join(2)
+    node("act", PRM["fx"] + 15 + HW * CY + 1300.0, lambda: ac.activation(T.ones[:], T.nil[:], F.Tanh, bias=20.0), ["nil"], ["ones"], name="ones")
     cp(T.thf[:, 0:1], T.ti[:, 0:1], 1, 1, ["ti"], ["thq"], name="th")
     ts(T.thf[:, 1:2], T.ti[:, 1:2], -1.0, 0.5, A.mult, A.add, 1, 1, ["ti"], ["thb"], name="th")
 
@@ -558,7 +715,14 @@ def build(g, core, T, topo, PRM):
     slot = lambda buf, k: buf[:, k % 4 * BL + k // 4:(k % 4 + 1) * BL:4]
     held = lambda kh: range(kh, 16, 4)
     pair = lambda h: ("m%d" % (2 * h), "m%d" % (2 * h + 1))
-    turn = [0, 0]
+    turn = [0, 0, 0]
+
+    spare = lambda table, j, s: T[table][:, (own + j * V) % (NR * V) + s.start:(own + j * V) % (NR * V) + s.stop]
+
+    def lent(bank):
+        if bank[0] == "x":
+            return T.xb[:, 512 * int(bank[2]):512 * int(bank[2]) + HW], bank, [bank]
+        return T[bank][:, hi], bank, [bank + "lo", bank + "hi"]
 
     def weights(b, h):
         s, m1 = hs(h), pair(h)[1]
@@ -566,12 +730,13 @@ def build(g, core, T, topo, PRM):
         tt(T["nw%d" % b][:, s], T["ww%d" % b][:, s], T[m1][:, lo], A.mult, HW, 1, [("ww", b, h), m1 + "lo"], [("nw", b, h)], [m1], "w")
 
     def other_weights(t, h):
-        b, s, bank = t % 2, hs(h), pair(h)[0]
+        b, s, (ps, bank, bk) = t % 2, hs(h), lent(CFG["abank"].split()[2 * t + h])
         ts(T.e2[:, s], T["bb%d" % b][:, s], 1.5, None, A.is_gt, None, HW, .5, [("bb", b, h)], [("e2", h)], name="e2")
-        ts(T.wcp[:, s], T["ww%d" % b][:, s], 4.0, 15.0, A.add, A.min, HW, .5, [("ww", b, h)], [("wcp", h)], name="wcp")
-        lin(T[bank][:, hi], [(-1.0, T["bb%d" % b][:, s], ("bb", b, h)), (3.0, T.e2[:, s], ("e2", h)), (1.0, T["lv%d" % b][:, s], ("lv", b, h)), (-4.0, one, "ones")],
-            HW, [bank + "hi"], bank, "m")
-        tt(T.na[:, s], T["ww%d" % b][:, s], T[bank][:, hi], A.mult, HW, 1, [("ww", b, h), bank + "hi"], [("na", h)], [bank], "na")
+        if t == 0:
+            ts(T.wcp[:, s], T.ww0[:, s], -4.0, 7.0, A.add, A.min, HW, .5, [("ww", 0, h)], [("wcp", h)], name="wcp")
+        lin(ps, [(-1.0, T["bb%d" % b][:, s], ("bb", b, h)), (3.0, T.e2[:, s], ("e2", h)), (1.0, T["lv%d" % b][:, s], ("lv", b, h)), (-4.0, one, "ones")],
+            HW, bk, bank, "m")
+        tt(T.na[:, s], T.ww0[:, s], ps, A.mult, HW, 1, [("ww", 0, h)] + bk, [("na", h)], [bank], "na")
 
     def offsets(names, key, off, offkey, h):
         m0 = pair(h)[0]
@@ -592,16 +757,9 @@ def build(g, core, T, topo, PRM):
                 act(out, src, F.Copy, w, rk, wk[i::n], cyc=GC, name=name)
 
     def jumps(t, h):
-        if UNDER:
-            return T["wr%d" % (2 + h)], lambda kh: [("wr", 2 + h, kh)] * 2
         return T["jb%d" % h], lambda kh: both("jb", h, kh)
 
     def jump(t, h):
-        if t and UNDER:
-            pu, jm = T["pu%d" % h], T["jm%d" % h]
-            dma("sp", [(jm[kh:128:4, :], pu[kh:128:4, kh * BL:(kh + 1) * BL]) for kh in range(4)], 512,
-                [("pu", 2 * h + i, kh) for i in range(2) for kh in range(4)], [("jm", h)], "jdma")
-            return
         (off, offkey), (jb, keys) = (T.off1, ("off", 1, h)) if t else (T.off2, ("off", 2, h)), jumps(t, h)
         for kh in range(4):
             gather(CFG["jump"].split()[2 * t + h][kh], jb, T.jt, off, h, kh, ["jt", offkey], keys(kh), "jg")
@@ -609,36 +767,25 @@ def build(g, core, T, topo, PRM):
             [k for kh in range(1, 4) for k in keys(kh)], keys(0), "jdma")
 
     def jumped(t, h):
-        base, basekey, bank = (T.cc1, ("cc", 1, h), CFG["qbank"]) if t else (T.sf, "sf", "u" + "ab"[h])
-        s, ps = hs(h), T[bank][:, hi]
-        rest, rk = [(T.ino[:], base[:, s], 1), (T.kd[:], one, 1)], ["kd", "ones", "ino", basekey]
-        if t and UNDER:
-            acc(ps, [(blk(T.dy, kl), T["jm%d" % h][:, kl:BL:4], 4) for kl in range(4)], HW, [("jm", h)] + four("dy"), [bank + "lo", bank + "hi"], bank, "jd")
-            ts(T.md[:, s], ps, 1.5 * 2.0 ** 46, -1.5 * 2.0 ** 46, A.add, A.add, HW, 1, [bank + "hi"], [("md", h)], [bank], "j0")
-            acc(ps, [(sid(-1.0), T.md[:, s], 1)] + rest, HW, rk + [("md", h), ("sid", -1.0)], [bank + "lo", bank + "hi"], bank, "jd", False)
+        base, basekey = (T.cc1, ("cc", 1, h)) if t else (T.sf, "sf")
+        s, (ps, bank, bk) = hs(h), lent(CFG["qbank"].split()[2 * t + h])
+        rest, rk = [(sid(1.0), base[:, s], 1), (T.kd[:], one, 1)], ["kd", "ones", ("sid", 1.0), basekey]
+        jb, keys = jumps(t, h)
+        rest, rk = rest + [(blk(T.dg, kl), slot(jb, 4 * kl), 1) for kl in range(4)], rk + keys(0) + four("dg")
+        acc(ps, rest, HW, rk, bk, bank, "jd")
+        if CFG["wrap"][2 * t + h] == "v":
+            ts(T.md[:, s], ps, float(NR * V), -float(NR * V), A.is_ge, A.mult, HW, 1, bk, [("md", h)], [bank], "j1")
+            tt(T["q%d" % t][:, s], T.md[:, s], ps, A.add, HW, 1, [("md", h)] + bk, [("q", t, h)], [bank], "j2")
         else:
-            jb, keys = jumps(t, h)
-            acc(ps, rest + [(blk(T.dg, kl), slot(jb, 4 * kl), 1) for kl in range(4)], HW, rk + keys(0) + four("dg"), [bank + "lo", bank + "hi"], bank, "jd")
-        ts(T.md[:, s], ps, float(NR * V), -float(NR * V), A.is_ge, A.mult, HW, 1, [bank + "hi"], [("md", h)], [bank], "j1")
-        tt(T["q%d" % t][:, s], T.md[:, s], ps, A.add, HW, 1, [("md", h), bank + "hi"], [("q", t, h)], [bank], "j2")
-
-    def under(t, _h):
-        for i in range(2):
-            for j in range(2):
-                s = slice(BL * i + 512 * j, BL * i + 512 * (j + 1))
-                acc(T.xb[:, 512 * j:512 * (j + 1)], [(sid(1.0), T["tx%d" % t][:, s], 1), (sid(2.0 ** -19), T.jt[:, s], 1)], 512,
-                    both("tx", t) + [("arr", "x", t), "jt", ("sid", 1.0), ("sid", 2.0 ** -19)], ["xb%d" % j], "xb%d" % j, "ty")
-            if CFG["table"][i] == "v":
-                cp(T.ty[:, BL * i:BL * (i + 1)], T.xb[:], BL, 1, ["xb0", "xb1"], [("ty", i)], ["xb0", "xb1"], "ty")
-            else:
-                act(T.ty[:, BL * i:BL * (i + 1)], T.xb[:], F.Copy, BL, ["xb0", "xb1"], [("ty", i)], ["xb0", "xb1"], name="ty")
+            act(T.md[:, s], ps, F.Sign, HW, bk, [("md", h)], [bank], bias=0.5 - NR * V, name="j1")
+            acc(ps, rest + [(sid(-1024.0), T.md[:, s], 1)], HW, rk + [("md", h), ("sid", -1024.0)], bk, bank, "jd")
+            act(T["q%d" % t][:, s], ps, F.Identity, HW, bk, [("q", t, h)], [bank], bias=-1024.0, name="j2")
 
     here[0] = "list"
     cp(T.sf[:], T.si[:], V, 1, ["si"], ["sf"])
     for h in range(2):
         offsets(T.sf, "sf", T.off2, ("off", 2, h), h)
     here[0] = "init0"
-    cp(T.r2[:], T.pi[:], V, 1, ["pi"], both("r2"))
     if CFG["ages"][0] == "v":
         ts(T.bb0[:], T.ab[:], -1.0, 3.0, A.mult, A.add, V, .5, ["ab"], both("bb", 0))
     else:
@@ -650,8 +797,8 @@ def build(g, core, T, topo, PRM):
     for h in range(2):
         here[0] = "init%d" % h
         s, m0 = hs(h), pair(h)[0]
-        lin(T[m0][:, lo], [(-BIG, T.lv0[:, s], ("lv", 0, h)), (BIG, one, "ones")], HW, [m0 + "lo"], m0, "N", [(T.inn[:], T.r2[:, s], 1)], ["inn", ("r2", h)])
-        tt(T.r1[:, s], T.sf[:, s], T[m0][:, lo], A.min, HW, 1, ["sf", m0 + "lo"], [("r1", h)], [m0], "r")
+        lin(T[m0][:, lo], [(BIG, T.lv0[:, s], ("lv", 0, h)), (-1.0, T.sf[:, s], "sf")], HW, [m0 + "lo"], m0, "N")
+        tt(T.r1[:, s], T.pi[:, s], T[m0][:, lo], A.min, HW, 1, ["pi", m0 + "lo"], [("r1", h)], [m0], "r")
         act(T.cc0[:, s], T.r1[:, s], F.Abs, HW, [("r1", h)], [("cc", 0, h)], name="abs")
         offsets(T.cc0, ("cc", 0, h), T.off0, ("off", 0, h), h)
         weights(0, h)
@@ -659,18 +806,26 @@ def build(g, core, T, topo, PRM):
     def spread_weights(t, h):
         n, c, nw = 2 * (t % 2) + h, CFG["copies"], T["nw%d" % (t % 2)]
         wr, wp = T["wr%d" % n], T["wp%d" % h]
-        if not c:
-            for i, bank in enumerate(pair(h)):
-                bk = [bank + "lo", bank + "hi"]
-                mm([(T[bank][:, kl:512:4], blk(T.gm, kl), nw[:, h * HW + i * QW:h * HW + (i + 1) * QW], True, True, QW) for kl in range(4)],
-                   [("nw", t % 2, h)] + four("gm"), bk, bank, "wrep")
-                act(wp[:, 512 * i:512 * (i + 1)], T[bank][:], F.Copy, 512, bk, [("wp", h, i)], [bank], name="wc")
-            dma("sp", [(wr[q:128:4, :], wp[:]) for q in range(4)], 1024, both("wp", h), four("wr", n), "wdma")
-            return
-        bank, wd = pair(h)[1], T["wd%d" % (2 * t + h)]
-        mm([(T[bank][:, kl:HW:4], T.gm[:, 144 * kl + 3 - vq:144 * kl + 131 - vq], nw[:, h * HW + 64 * vq:h * HW + 64 * (vq + 1)], vq == 0, vq == 3, 64)
-            for kl in range(4) for vq in range(4)], [("nw", t % 2, h)] + four("gm"), [bank + "lo", bank + "hi"], bank, "wrep")
+        bank, gm = pair(h)[1], "gn" if CFG["spread"].split()[t][h] == "H" else "gm"
+        mm([(T[bank][:, kl:HW:4], T[gm][:, 144 * kl + 3 - vq:144 * kl + 131 - vq], nw[:, h * HW + 64 * vq:h * HW + 64 * (vq + 1)], vq == 0, vq == 3, 64)
+            for kl in range(4) for vq in range(4)], [("nw", t % 2, h)] + four(gm), [bank + "lo", bank + "hi"], bank, "wrep")
         act(wp[:], T[bank][:, lo], F.Identity, HW, [bank + "lo"], [("wp", h)], [bank], scale=1.0 / 16, name="wc")
+        if CFG["spread"].split()[t][h] == "H":
+            to, k = spreaders(core, T, topo), 4 // NH
+            wm = topo.mask(core, to[0])
+            ids_ = [DstId(rid=topo.addr(c)[0], pnc=topo.addr(c)[1]) for c in to]
+            i = node("g", 600.0, lambda: g.remote_dma_fused([RemoteDMATransfer(dst_ids=ids_, dma_engine_mask=wm, remote_sem=T.sem["d%d" % (2 * t + h)],
+                                                                               srcs=[wp[:]], dsts=[T["we%d" % (2 * t + h)][:]] * NH)], local_sem=T.sem["wl%d" % h]),
+                     [("wp", h)] + four("wr", n), four("wr", n), ["turnw"], lat=PRM["lat"] / 2, kind="f", name="wsend")
+            ncalls["wl%d" % h] = ncalls.get("wl%d" % h, 0) + bin(wm).count("1")
+            nodes[i]["sem"] = (T.sem["wl%d" % h], ncalls["wl%d" % h])
+            node("dma", 64 * NH * PRM["short"] * PRM["dr"], None, [("wp", h)] + four("wr", n), [("ww", t, h)], kind="l", name="wsend", of=i, lat=PRM["lat"] / 2)
+            node("dmaw", 800.0 + 256 * k * PRM["dr"], None, [("ww", t, h)], [("wx", t, h)], kind="l", name="wrep", lat=PRM["dl"])
+            node("dmaw", 600.0 + 256 * k * PRM["dr"] * PRM["cross"], None, [("wx", t, h)], [("wy", t, h)], kind="l", name="wback", lat=PRM["lat"])
+            ncalls["aw%d" % h] = ncalls.get("aw%d" % h, 0) + sum(bin(topo.mask(c, core)).count("1") for c in to)
+            node("arr", 0.0, ("w", str(h), ncalls["aw%d" % h]), [("wy", t, h)], four("wr", n), kind="a")
+            return
+        wd = T["wd%d" % (2 * t + h)]
         dma("sp", [(wd[:, i, :], wp[:]) for i in range(c)], 64 * c * PRM["short"], [("wp", h)], [("wd", t, h)], "wout")
         for i in range(CFG["reads"]):
             k = 4 // CFG["reads"]
@@ -678,84 +833,113 @@ def build(g, core, T, topo, PRM):
             dma("sp", [(wr[q:128:16 // c, s], wd[:, :, s]) for q in range(16 // c)], 256 * k * PRM["long"], [("wd", t, h)], four("wr", n)[i * k:(i + 1) * k], "wdma")
 
     def gathered(t, h):
-        if t == 1 and UNDER:
-            return T["pu%d" % h], lambda kh: [("pu", 2 * h, kh), ("pu", 2 * h + 1, kh)], 1.0
         return T["xc%d" % h], lambda kh: both("xc", h, kh), 0.5
 
     def gather_x(t, h):
         xc, keys, _c = gathered(t, h)
-        table, rk = (T.ty, both("ty")) if t == 1 and UNDER else (T["tx%d" % t], both("tx", t) + [("arr", "x", t)])
+        table, rk = T["tx%d" % t], both("tx", t) + [("arr", "x", t)]
         for kh in range(4):
             gather(CFG["gx"].split()[2 * t + h][kh], xc, table, T["off%d" % t], h, kh, rk + [("off", t, h)], keys(kh), "gx")
 
     def new_x(t, h):
         n, last, hb = 2 * (t % 2) + h, t == STEPS - 1, pair(h)[1]
         (xc, keys, cyc), px, wr = gathered(t, h), T.px, T["wr%d" % n]
-        for kh in range(4):
-            dve(BL, cyc, lambda kh=kh: ve.tensor_tensor_scan(block(px, kh), block(xc, kh), block(wr, kh), 0.0, A.max, A.mult),
-                keys(kh) + [("wr", n, kh)], [("px", kh)], name="xm")
-            mm([(T[hb][:, hi], T.nih[:], slot(px, k), k == 0, k == 15, HW) for k in held(kh)],
-               [("px", kh), "nih"], [hb + "lo", hb + "hi"], hb, "h")
+        k0 = 0
+        for run in map(int, CFG["xm"].split()[2 * t + h]):
+            s, ks = slice(k0 * BL, (k0 + run) * BL), range(k0, k0 + run)
+            dve(run * BL, cyc, lambda s=s: ve.tensor_tensor_scan(px[:, s], xc[:, s], wr[:, s], 0.0, A.max, A.mult),
+                [x for kh in ks for x in keys(kh) + [("wr", n, kh)]], [("px", kh) for kh in ks], name="xm")
+            for kh in ks:
+                mm([(T[hb][:, hi], sid(-1.0), slot(px, k), k == 0, k == 15, HW) for k in held(kh)],
+                   [("px", kh), ("sid", -1.0)], [hb + "lo", hb + "hi"], hb, "h")
+            k0 += run
         act(T.yy[:, hs(h)], T[hb][:, hi], F.Identity, HW, [hb + "hi"], [("yy", h)], [hb], scale=1.0 / 256, bias=160.0 - 255.0 / 512, name="y")
-        nx = T.xo[:, hs(h)] if last else T["tx%d" % (t + 1)][:, mine(h)]
+        nx = spare("tx1", 1, hs(h)) if last else T["tx%d" % (t + 1)][:, mine(h)]
+        here[1] = [("arr", "x", 1)] * last
         ts(nx, T.yy[:, hs(h)], -160.0, 15.0, A.add, A.min, HW, .5, [("yy", h)], [("tx", t + 1, h)], name="X")
         if last:
             dma("g", [(T.yx[:, hs(h)], nx)], 128, [("tx", t + 1, h)], [])
         return [] if last else sends("x", t + 1, 2 * h, 2 * h + 2)
 
+    def fold_min(t, h, last):
+        k = [m[:3] for m in minned()].index((t, h, last))
+        blocks, to = minned()[k][3], mirror_of(core, T, topo, 1)
+        xc, keys, _c = gathered(t, h)
+        eng = topo.engines(core, to)
+        share = len(eng) // len(blocks)
+        masks = [sum(1 << e for e in eng[i * share:(i + 1) * share]) for i in range(len(blocks))]
+        rk, wk = [x for kh in blocks for x in keys(kh)] + four("xs", h), [("mn", h, kh) for kh in blocks]
+        s = "%d%d" % (h, last)
+        dst = [DstId(rid=topo.addr(to)[0], pnc=topo.addr(to)[1])]
+        i = node("g", 600.0, lambda: g.remote_dma_fused(
+            [RemoteDMATransfer(dst_ids=dst, dma_engine_mask=m, remote_sem=T.sem["d%d" % k], srcs=[block(xc, kh), T["xs%d" % h][:]],
+                               dsts=[min_place(T, t, h, kh, kh + 1)], alu_op=3) for m, kh in zip(masks, blocks)], local_sem=T.sem["ml" + s]),
+            rk + wk, wk, ["turnm"], lat=PRM["lat"] / 2, kind="f", name="fmin")
+        ncalls["ml" + s] = ncalls.get("ml" + s, 0) + len(eng)
+        nodes[i]["sem"] = (T.sem["ml" + s], ncalls["ml" + s])
+        node("dma", len(blocks) * 512 * PRM["dr"] * PRM["fr"], None, rk + wk, [("mw", k)], kind="l", name="fmin", of=i, lat=PRM["lat"] / 2)
+        node("dma3", 600.0 + len(blocks) * 256 * PRM["dr"], None, [("mw", k)], [("mb", k)], kind="l", name="back", lat=PRM["lat"])
+        ncalls["am" + s] = ncalls.get("am" + s, 0) + bin(topo.mask(to, core)).count("1")
+        node("arr", 0.0, ("m", s, ncalls["am" + s]), [("mb", k)], wk, kind="a")
+
     def matches(t, h):
-        b, (xc, keys, _c), mn, tx, cb = t % 2, gathered(t, h), T.mn, T["tx%d" % t], pair(h)[0]
+        b, (xc, keys, _c), tx, cb = t % 2, gathered(t, h), T["tx%d" % t], pair(h)[0]
         who = CFG["min"].split()[2 * t + h]
         spread_x = lambda i, start: [(T.xb[:, 512 * i + m:512 * (i + 1):4], sid(1.0), tx[:, own + h * HW + i * QW:own + h * HW + (i + 1) * QW],
                                       start and m == 0, m == 3, QW) for m in range(4)]
-        for i in range(2 * (who[0] == "v")):
+        mn, xs = T["mn%d" % h], "f" in who and T["xs%d" % h]
+        for i in range(2 * ("v" in who)):
             mm(spread_x(i, True), [("tx", t, h), ("sid", 1.0)], ["xb%d" % i], "xb%d" % i, "xrep")
+        if "f" in who.lower():
+            for kl in range(4):
+                if CFG["xs"][t] == "g":
+                    node("g", 170 + 2 * HW * CY, lambda kl=kl: g.affine_select(xs[:, kl:BL:4], tx[:, mine(h)], [[0, HW]], A.is_ge, 0.0, 0, 0),
+                         [("tx", t, h)], [("xs", h, kl)], name="xs")
+                elif CFG["xs"][t] == "v":
+                    cp(xs[:, kl:BL:4], tx[:, mine(h)], HW, .5, [("tx", t, h)], [("xs", h, kl)], name="xs")
+                else:
+                    act(xs[:, kl:BL:4], tx[:, mine(h)], F.Copy, HW, [("tx", t, h)], [("xs", h, kl)], name="xs")
         for kh in range(4):
-            for i in range(2 * (who[kh] == "a")):
-                s, bank, ps = slice(kh * BL + 512 * i, kh * BL + 512 * (i + 1)), "xb%d" % i, T.xb[:, 512 * i:512 * (i + 1)]
-                mm([(ps, sid(-1.0), xc[:, s], True, False, 512)] + spread_x(i, False),
-                   [keys(kh)[i], ("tx", t, h), ("sid", 1.0), ("sid", -1.0)], [bank], bank, "xd")
-                act(mn[:, s], ps, F.Relu, 512, [bank], [("mn", kh, i)], [bank], name="relu")
-            for i in range(2 * (who[kh] == "v" and kh in CFG["halved"])):
-                s = slice(kh * BL + 512 * i, kh * BL + 512 * (i + 1))
-                tt(mn[:, s], xc[:, s], T.xb[:, 512 * i:512 * (i + 1)], A.min, 512, 1, [keys(kh)[i], "xb%d" % i], [("mn", kh, i)], ["xb%d" % i], "min")
-            if who[kh] == "v" and kh not in CFG["halved"]:
-                tt(block(mn, kh), block(xc, kh), T.xb[:], A.min, BL, 1, keys(kh) + ["xb0", "xb1"], both("mn", kh), ["xb0", "xb1"], "min")
-            mm([(T[cb][:, lo], sid(256.0), T["lv%d" % b][:, hs(h)], True, False, HW)] * (kh == 0) +
-               ([(T[cb][:, lo], blk(T.ba, SHARED.index(who)), tx[:, mine(h)], False, False, HW)] if kh == 0 and "a" in who else []) +
-               [(T[cb][:, lo], (T.ne if who[kh] == "a" else T.ee)[:, 16 - k:144 - k], slot(mn, k), False, k == 15, HW) for k in held(kh)],
-               both("mn", kh) + ["ee", "ne", ("ba", who), ("tx", t, h), ("lv", b, h), ("sid", 256.0)], [cb + "lo", cb + "hi"], cb, "c")
+            if who[kh] == "f":
+                fold_min(t, h, kh)
+        for kh in sorted(range(4), key=lambda kh: who[kh] in "fF"):
+            if who[kh] == "v":
+                tt(block(mn, kh), block(xc, kh), T.xb[:], A.min, BL, 1, keys(kh) + ["xb0", "xb1"], [("mn", h, kh)], ["xb0", "xb1"], "min")
+            turn[2] += 1
+            mm([(T[cb][:, lo], sid(256.0), T["lv%d" % b][:, hs(h)], True, False, HW)] * (turn[2] % 4 == 1) +
+               [(T[cb][:, lo], T.ee[:, 16 - k:144 - k], slot(mn, k), False, turn[2] % 4 == 0 and k >= 12, HW) for k in held(kh)],
+               [("mn", h, kh), "ee", ("lv", b, h), ("sid", 256.0)], [cb + "lo", cb + "hi"], cb, "c")
         act(T.ck[:, hs(h)], T[cb][:, lo], F.Identity, HW, [cb + "lo", "tb"], [("ck", h)], [cb], bias=T.tb[:], name="ck")
         act(T.nq[:, hs(h)], T[cb][:, lo], F.Relu, HW, [cb + "lo", "thq"], [("nq", h)], [cb], scale=-1.0, bias=T.thf[:, 0:1], name="nq")
 
     def span(q0, q1):
         h, w = q0 // 2, 512 * (q1 - q0)
-        return h, lambda buf, kh: buf[:, kh * BL + 512 * (q0 % 2):kh * BL + 512 * (q0 % 2) + w], w, lambda kh: [("pu", q, kh) for q in range(q0, q1)]
+        return h, lambda buf, kh: buf[:, kh * BL + 512 * (q0 % 2):kh * BL + 512 * (q0 % 2) + w], w, lambda kh: [("pu", q0 and 1 + q0 % 2, kh)]
 
     def gather_u(t, q0, q1):
         h, piece, w, keys = span(q0, q1)
-        n, pu, how = 2 * (t % 2) + h, T["pu%d" % h], finish()[here[0]][0]
+        n, how = 2 * (t % 2) + h, finish()[here[0]]
         wr, first = T["wr%d" % n], h * HW + 32 * (q0 % 2)
         for kh in range(4):
             src = T["tu%d" % t][:].indirect(T["off%d" % t][:, first + 64 * kh:first + 64 * kh + w // 16])
-            rk = four("tu", t) + [("arr", "u", t), ("off", t, h)]
+            rk = four("tu", t) + [("arr", "u", t), ("off", t, h)] + ["flush"] * (how == "T")
             out = product(q0, kh, how)
             if CFG["gu"].get(here[0], "vvvv")[kh] == "v":
                 tt(out, src, piece(wr, kh), A.mult, w, GC, rk + [("wr", n, kh)], keys(kh), name="gu")
             else:
                 turn[1] += 1
                 uc = T["uc%d" % (turn[1] % 2)][:, 0:w]
-                act(uc, src, F.Identity, w, rk, [("uc", turn[1] % 2)], cyc=GC, bias=1.0, name="gu")
+                act(uc, src, F.Identity, w, rk, [("uc", turn[1] % 2)], cyc=GC, bias=LIFT[t], name="gu")
                 dve(w, 1, lambda kh=kh, uc=uc, out=out: ve.tensor_tensor_scan(out, uc, piece(wr, kh), 0.0, A.max, A.mult),
-                    [("uc", turn[1] % 2), ("wr", n, kh)], keys(kh), name="um")
-            if kh + 1 == REMOTE.get(how):
-                fold(t, q0, q1, kh + 1)
+                    [("uc", turn[1] % 2), ("wr", n, kh), "flush"], keys(kh), name="um")
+        if how == "F":
+            fold(t, q0, q1, 4)
 
     def product(q, kh, how):
-        at = 2 * BL * (q % 2)
-        if how == "P":
-            return T["pu%d" % (q // 2)][:, at + BL * (kh // 2) + kh % 2:at + BL * (kh // 2 + 1):2]
-        return T["pu%d" % (q // 2)][:, at + 512 * kh:at + 512 * (kh + 1)]
+        if how == "F":
+            return T.pf[:, 512 * kh:512 * (kh + 1)]
+        a = RUN * (2 * (kh // 2) + q % 2)
+        return T.pt[:, a + kh % 2:a + RUN:3]
 
     def fold(t, q0, q1, n):
         h, piece, w, keys = span(q0, q1)
@@ -763,7 +947,7 @@ def build(g, core, T, topo, PRM):
         srcs, rk, fm = [product(q0, kh, "F") for kh in range(n)], [x for kh in range(n) for x in keys(kh)], topo.mask(core, to)
         wk = [("fo", q) for q in range(q0, q1)]
         i = node("g", 600.0, lambda: g.remote_dma_fused([RemoteDMATransfer(dst_ids=[DstId(rid=topo.addr(to)[0], pnc=topo.addr(to)[1])], dma_engine_mask=fm,
-                                                                           remote_sem=T.sem["fh%d" % k], srcs=srcs, dsts=[there], alu_op=1)],
+                                                                           remote_sem=T.sem["d%d" % k], srcs=srcs, dsts=[there], alu_op=1)],
                                                         local_sem=T.sem["fl%d" % k]),
                  rk + wk, wk, ["turnf"], lat=PRM["lat"] / 2, kind="f", name="fold")
         nodes[i]["sem"] = (T.sem["fl%d" % k], bin(fm).count("1"))
@@ -776,29 +960,27 @@ def build(g, core, T, topo, PRM):
         h, piece, w, keys = span(q0, q1)
         name = "%dU%d%d" % (t, q0, q1)
         last, fin, n, lifted = t == STEPS - 1, finish()[name], w // 4, CFG["gu"].get(name, "vvvv")
-        bank = "u" + CFG["ubank"][q0]
+        bank = "u" + CFG["ubank"].split()[t][q0]
+        out_again = blk(T.bl, LIFTS.index((LIFT[t], lifted))) if (LIFT[t], lifted) in LIFTS else T.bo[:]
         up, s, os_ = T[bank][:, 0:n], slice(q0 * QW, q1 * QW), slice(own + q0 * QW, own + q1 * QW)
-        left, made = LEFT[fin[0]], [("tu", t + 1, q) for q in range(q0, q1)]
-        for kh, who in zip(left, fin[1:]):
-            pu, at, rk, run = T["pu%d" % h], 2 * BL * (q0 % 2) + 512 * kh, keys(kh), 4
-            if kh < 0:
-                pu, at, rk = T["fo%d" % h], 512 * (q0 % 2), [("fo", q) for q in range(q0, q1)]
-            if fin[0] == "P":
-                rk, run = keys(kh) + keys(kh + 1), 8
-            if who == "s":
-                turn[0] += 1
-                sc, m = T["sc%d" % (turn[0] % 2)], n * run
-                dve(m, 1, lambda sc=sc, m=m, run=run, x=pu[:, at:at + m]: ve.tensor_tensor_scan(sc[:, 0:m], T.msk[:, 0:BL:8 // run], x, 0.0, A.mult, A.add),
-                    rk + ["msk"], [("sc", turn[0] % 2)], name="scan")
-                terms, key = [sc[:, run - 1:m:run]], [("sc", turn[0] % 2)]
-            else:
-                terms, key = [pu[:, at + kl:at + w:4] for kl in range(4)], rk
-            mm([(up, T.ik[:], T["tu%d" % t][:, os_], True, False, 4 * n), (up, sid(128.0), T["tx%d" % t][:, os_], False, False, n)] * (kh == left[0]) +
-               [(up, T.bo[:], T["nw%d" % (t % 2)][:, s], False, False, n)] * (kh == left[0] and "a" in lifted) +
-               [(up, T.ni1[:], x, False, kh == left[-1] and i == len(terms) - 1, 4 * n) for i, x in enumerate(terms)],
-               key + four("tu", t) + [("tx", t, h), "ik", "ni1", ("sid", 128.0), ("nw", t % 2, h), "bo"],
-               [bank + "lo", bank + "hi"], bank, "arg")
-        nu = T.uo[:, s] if last else T["tu%d" % (t + 1)][:, os_]
+        made = [("tu", t + 1, q) for q in range(q0, q1)]
+        mm([(up, T.ik[:], T["tu%d" % t][:, os_], True, False, 4 * n), (up, sid(128.0), T["tx%d" % t][:, os_], False, False, n)] +
+           [(up, out_again, T["nw%d" % (t % 2)][:, s], False, False, n)] * ("a" in lifted),
+           four("tu", t) + [("tx", t, h), "ik", ("sid", 128.0), ("nw", t % 2, h), "bo", ("bl", LIFT[t], lifted)], [bank + "lo", bank + "hi"], bank, "own")
+        if fin == "F":
+            terms, key = [T.fo[:, kl:w:4] for kl in range(4)], [("fo", q0)]
+        else:
+            turn[0] += 1
+            sc, a, key = T["sc%d" % (turn[0] % 2)], RUN * (q0 % 2), both("sc", turn[0] % 2)
+            for i in range(2):
+                p = slice(i * RUN // 2, (i + 1) * RUN // 2)
+                dve(RUN // 2, 1, lambda p=p: ve.tensor_tensor_scan(sc[:, p], T.pt[:, a + p.start:a + p.stop], T.pt[:, 2 * RUN + a + p.start:2 * RUN + a + p.stop],
+                                                                   0.0, A.add, A.add),
+                    [x for k in range(4) for x in keys(k)] + ["flush"], key[i:i + 1], name="scan")
+            terms = [sc[:, 10:RUN:12]]
+        mm([(up, T.ni1[:], x, False, i == len(terms) - 1, 4 * n) for i, x in enumerate(terms)], key + ["ni1"], [bank + "lo", bank + "hi"], bank, "arg")
+        nu = spare("tu1", 1, s) if last else T["tu%d" % (t + 1)][:, os_]
+        here[1] = [("arr", "u", 1)] * last
         act(nu, up, F.Tanh, n, [bank + "lo"], made, [bank], scale=2.0 ** -11, bias=-0.5, name="tanh")
         if last:
             dma("sp", [(T.yu[:, s], nu)], n // 2, made, [])
@@ -807,9 +989,10 @@ def build(g, core, T, topo, PRM):
     def slots(t, h):
         b, n, last = t % 2, 1 - t % 2, t == STEPS - 1
         s = hs(h)
-        lv, bb, ww, ga = [(T["%s%d" % (x, i)][:, s], (x, i, h)) for x, i in (("lv", b), ("bb", b), ("ww", b), ("ga", t))]
+        lv, bb, ww, ga = [(T["%s%d" % (x, i)][:, s], (x, i, h)) for x, i in (("lv", b), ("bb", b), ("ww", b * (not short)), ("ga", t))]
         nq, on, sg = (T.nq[:, s], ("nq", h)), (one, "ones"), T["sg%d" % h]
-        nx = T.xo[:, s] if last else T["tx%d" % (t + 1)][:, own + h * HW:own + (h + 1) * HW]
+        nx = spare("tx1", 1, s) if last else T["tx%d" % (t + 1)][:, own + h * HW:own + (h + 1) * HW]
+        ever = [(T["ga%d" % i][:, s], ("ga", i, h)) for i in range(t)]
         for q in range(4):
             bank = pair(h)[q % 2]
             mm([(T[bank][:, sl], blk(T.sh, 1 + 2 * q + i), T.ck[:, s], True, True, HW) for i, sl in enumerate((lo, hi))],
@@ -828,35 +1011,40 @@ def build(g, core, T, topo, PRM):
         if not last:
             ways = [(T["q%d" % t], ("q", t, h), tag, m0), lapse]
         else:
-            ever = [(T["ga%d" % i][:, s], ("ga", i, h)) for i in range(2)]
             ways = [(T.q0, ("q", 0, h), tag + [(BIG / 2,) + x for x in ever] + [(BIG,) + on], m0),
                     (T.q1, ("q", 1, h), tag + [(-BIG / 2,) + x for x in ever], m0), lapse]
         cur = (T["cc%d" % b][:, s], ("cc", b, h))
         for i, (name, key, terms, bank) in enumerate(ways):
             if short and not last and i == 1:
-                lin(T[m0][:, lo], [(-4.0, T.wcp[:, s], ("wcp", h)), (-BIG / 2,) + ga, (BIG / 2,) + on], HW, [m0 + "lo"], m0, "m")
+                lin(T[m0][:, lo], [(-4.0, T.wcp[:, s], ("wcp", h))] + [(-32.0,) + x for x in ever + [on] * t + [ga]], HW, [m0 + "lo"], m0, "m")
                 tt(T["nw%d" % n][:, s], T.na[:, s], T[m0][:, lo], A.min, HW, 1, [("na", h), m0 + "lo"], [("nw", n, h)], [m0], "w")
-            lin(T[bank][:, hi], terms, HW, [bank + "hi"], bank, "N", [(T.inn[:], name[:, s], 1)], ["inn", key])
+            lin(T[bank][:, hi], terms, HW, [bank + "hi"], bank, "N", [(sid(-1.0), name[:, s], 1)], [("sid", -1.0), key])
             out = (T["r%d" % (1 + i % 2)][:, s], ("r%d" % (1 + i % 2), h))
             tt(out[0], cur[0], T[bank][:, hi], A.min, HW, 1, [cur[1], bank + "hi"], [out[1]], [bank], "r")
             cur = out
-        nc = T.co[:, s] if last else T["cc%d" % n][:, s]
+        nc = spare("tu1", 2, s) if last else T["cc%d" % n][:, s]
+        here[1] = [("arr", "u", 1)] * last
         act(nc, cur[0], F.Abs, HW, [cur[1]], [("cc", n, h)], name="abs")
         lin(T[m0][:, lo], [(1.0,) + bb, (-1.5,) + ga, (-4.0,) + lv, (-4.0,) + nq], HW, [m0 + "lo"], m0, "t")
-        lin(T[m1][:, lo], [(1.0,) + ww, (2.0,) + ga], HW, [m1 + "lo"], m1, "W")
-        nb, nw = T["bb%d" % n][:, s], T["ww%d" % n][:, s]
+        if last or not short:
+            lin(T[m1][:, lo], [(1.0,) + ww] + [(2.0,) + x for x in ever * short + [ga]], HW, [m1 + "lo"], m1, "W")
+        nb, nw = T["bb%d" % n][:, s], T["nw1" if last else "ww%d" % (n * (not short))][:, s]
         act(nb, T[m0][:, lo], F.Relu, HW, [m0 + "lo"], [("bb", n, h)], [m0], bias=1.5, name="b")
-        if not last:
+        if not last and not short:
             ts(nw, T[m1][:, lo], 2.0, 15.0, A.add, A.min, HW, 1, [m1 + "lo"], [("ww", n, h)], [m1], "W")
         if last:
-            act(nw, T[m1][:, lo], F.Relu, HW, [m1 + "lo"], [("ww", n, h)], [m1], scale=-1.0, bias=13.0, name="W")
-            lin(T[m1][:, hi], [(-1.0, nw, ("ww", n, h)), (-16.0, nb, ("bb", n, h))], HW, [m1 + "hi"], m1, "yw")
-            act(T.wo[:, s], T[m1][:, hi], F.Identity, HW, [m1 + "hi"], [("wo", h)], [m1], bias=63.0, name="yw")
-            dma("sp", [(T.yw[:, s], T.wo[:, s])], 128, [("wo", h)], [])
+            act(nw, T[m1][:, lo], F.Relu, HW, [m1 + "lo"], [("nw", 1, h)], [m1], scale=-1.0, bias=9.0 if short else 13.0, name="W")
+            lin(T[m1][:, hi], [(-1.0, nw, ("nw", 1, h)), (-16.0, nb, ("bb", n, h))], HW, [m1 + "hi"], m1, "yw")
+            here[1] = [("arr", "u", 1)]
+            act(spare("tu1", 3, s), T[m1][:, hi], F.Identity, HW, [m1 + "hi"], [("wo", h)], [m1], bias=63.0, name="yw")
+            dma("sp", [(T.yw[:, s], spare("tu1", 3, s))], 128, [("wo", h)], [])
             dma("sp", [(T.yc[:, s], nc)], 128, [("cc", n, h)], [])
             return
         offsets(T["cc%d" % n], ("cc", n, h), T["off%d" % (t + 1)], ("off", t + 1, h), h)
-        ts(T["lv%d" % n][:, s], nb, 1.0, None, A.min, None, HW, .5, [("bb", n, h)], [("lv", n, h)], name="lv")
+        if CFG["live"][2 * t + h] == "v":
+            ts(T["lv%d" % n][:, s], nb, 1.0, None, A.min, None, HW, .5, [("bb", n, h)], [("lv", n, h)], name="lv")
+        else:
+            act(T["lv%d" % n][:, s], nb, F.Sign, HW, [("bb", n, h)], [("lv", n, h)], name="lv")
         if not short:
             weights(n, h)
 
@@ -872,7 +1060,7 @@ def build(g, core, T, topo, PRM):
         elif what == "U":
             gather_u(t, j, int(part[3]))
         else:
-            {"w": spread_weights, "X": gather_x, "c": matches, "s": slots, "j": jump, "q": jumped, "a": other_weights, "y": under}[what](t, j)
+            {"w": spread_weights, "X": gather_x, "c": matches, "s": slots, "j": jump, "q": jumped, "a": other_weights}[what](t, j)
     return nodes, ncalls, neng
 
 
@@ -915,7 +1103,10 @@ def emit(g, T, nodes, order, ncalls, neng):
     for i in order:
         x = nodes[i]
         if x["kind"] == "a":
-            sem[i] = (T.sem["a%s%d" % x["fn"]], ncalls[x["fn"]] * (1 if x["fn"][0] == "fo" else neng * (NR - 1)))
+            if len(x["fn"]) == 3:
+                sem[i] = (T.sem["a" + x["fn"][0] + x["fn"][1]], x["fn"][2])
+            else:
+                sem[i] = (T.sem["a%s%d" % x["fn"]], ncalls[x["fn"]] * (1 if x["fn"][0] == "fo" else neng * (NR - 1)))
             continue
         if not real(x):
             continue
@@ -952,5 +1143,9 @@ def rank_program(g, core, T, topo):
                 hand_on(g, core, rank, T, topo)
             if folded() and mirror_of(c, T, topo) == core:
                 hand_back(g, core, c, T, topo)
+            if minned() and mirror_of(c, T, topo, 1) == core:
+                hand_min(g, core, c, T, topo)
+            if "H" in CFG["spread"] and core in spreaders(c, T, topo):
+                hand_spread(g, core, c, spreaders(c, T, topo).index(core), T, topo)
         return
     emit(g, T, *plan(g, core, T, topo))

import math
from concourse.bass import DstId, RemoteDMATransfer
from concourse.mybir import AluOpType, ActivationFunctionType, AxisListType

A = AluOpType
F = ActivationFunctionType
V, NR, STEPS = 512, 4, 3
HW = 256
BL = 4 * HW
QW = 128
RUN = 12 * QW
BIG = 4096.0
LIFT = (8.0, 1.0, 1.0)
CFG = {
    "min": "vvvv vvvv fffv vvvv ffff vvvv", "xs": "ggg", "spread": "ll Hl Hl", "wrap": "vvvv", "live": "aavv", "abank": "ua ub ua ub",
    "xm": "22 211 22 211 22 211", "ids": (-1.0, BIG, 3.0, -4.0),
    "gx": "aaaa aaaa aaaa aaaa aaaa aaaa",
    "gu": {"2U23": "aaaa", "2U34": "aaaa"},
    "jump": "avvv avav aaaa aaaa",
    "split": {"gx": 2, "jg": 1},
    "pieces": "X02 x24 u01 U12 U23 u34",
    "order": "0w0 0w1 0j0 0q0 0j1 0q1 0X0 0c0 0x0 0X1 0x1 0c1 0s0 0U01 0U12 0u12 0U23 0U34 1w0 0s1 0u23 0u01 0u34 1w1 1j0 1j1 "
             "1X0 1c0 1x0 1X1 1x1 1c1 1q0 1q1 1s0 1U01 1U12 1u12 1U23 1U34 2w0 1s1 1u23 1u01 1u34 2w1 "
             "2X0 2c0 2x0 2X1 2x1 2c1 2U01 2U12 2u12 2U23 2U34 2s0 2s1 2u23 2u01 2u34",
    "ubank": "abbb abbb abbb", "qbank": "ua ub xb0 xb1",
    "ages": "aa", "copies": 2, "reads": 2, "behind": (), "kept": ("gu", "gx"),
    "loads": "xsj pawu", "cuts": (192, 512), "first": "xrd",
    "due": {"X": (0, 3), "x": (0, 3), "c": (0, 3), "w": (-28, -25), "s": (0, 3), "U": (0, 1, 2, 3), "u": (0, 3, 6, 9), "j": (0, 3), "q": (0, 3),
            "a": (20, 23), "y": (0, 0)},
    "yield": {"gx": 30, "jg": 52, "xm": 40, "min": 41, "gu": 50, "scan": 45, "relu": 29, "um": 53},
    "early": {"load": -100, "list": -85, "const": 0, "init0": -47, "init1": -45, "0w0": -44, "0w1": -43},
    "period": 28.0, "seed": 3, "starts": 2, "rounds": 500, "temp": 300.0, "swaps": 130000, "heat": 180.0, "cool": 0.7,
}
PRM = {"cy": 0.88, "pe": 0.44, "gc": 1.56, "link": 13.0, "lat": 2500.0, "sync": 100.0, "fx": 40.0, "dr": 3.0, "dl": 2000.0, "fl": 2000.0, "share": 0.4,
       "fr": 1.0, "short": 2.0, "long": 0.9, "cross": 1.5}
NH = 4
SPREAD = [{"cy": 1.0, "gc": 1.5, "pe": 0.55}, {"cy": 0.83, "gc": 1.1, "lat": 2000.0, "sync": 70.0, "pe": 0.42},
          {"cy": 1.2, "gc": 2.05, "pe": 0.65}, {"cy": 0.9, "gc": 1.3, "dr": 3.5, "lat": 3000.0, "link": 18.0, "share": 0.5}]
WEIGHT = [2, 2, 2, 2]
SCALE = [1.20, 1.01, 1.60, 1.21]
FLUSH = 1.5 * 2.0 ** 40

bf, f32, f16, i32, u16 = "bfloat16", "float32", "float16", "int32", "uint16"
ND = f16
SCRATCH = {}


def _buf(name, cols, dt, where="sbuf"):
    SCRATCH[name] = (where, [128, cols], dt)


SCALES = [1.0, -1.0, 256.0, 128.0, 2.0, 3.0, -4.0, -1.5, -16.0, BIG, -2 * BIG, BIG / 2, -BIG / 2, 1.5 * BIG]
SHORT = " 0a0 " in CFG["order"]
SCALES += [-1024.0] * ("a" in CFG["wrap"]) + [-32.0] * SHORT
for _t in range(STEPS):
    _buf("tx%d" % _t, NR * V, bf)
    _buf("tu%d" % _t, NR * V, f32)
    _buf("off%d" % _t, V, u16)
    _buf("ga%d" % _t, V, bf)
for _j in range(2):
    _buf("xc%d" % _j, 4 * BL, bf)
    _buf("wp%d" % _j, HW, bf)
    _buf("wr%d" % _j, 4 * BL, bf)
    _buf("wr%d" % (2 + _j), 4 * BL, bf)
    _buf("sc%d" % _j, RUN, f32)
    _buf("sg%d" % _j, 8 * HW, bf)
    _buf("mn%d" % _j, 4 * BL, bf)
    _buf("jb%d" % _j, 4 * BL, bf)
    if CFG["gu"]:
        _buf("uc%d" % _j, BL // 2, f32)
    if "f" in "".join(CFG["min"].split()[_j::2]):
        _buf("xs%d" % _j, BL, bf)
    for _n in ("bb", "lv", "nw") + ("ww",) * (_j == 0 or not SHORT):
        _buf("%s%d" % (_n, _j), V, bf)
    _buf("cc%d" % _j, V, ND)
    _buf("q%d" % _j, V, ND)
for _n, _c, _d in [
        ("px", 4 * BL, f16), ("jt", NR * V, bf), ("si", V, i32), ("pi", V, i32), ("ab", V, bf), ("ti", 4, i32),
        ("sf", V, ND), ("r1", V, ND), ("r2", V, ND), ("md", V, bf), ("yy", V, bf),
        ("ck", V, f16), ("nq", V, bf), ("ss", V, bf), ("ones", HW, bf), ("pf", 2 * BL, f32), ("fo", 512, f32), ("thf", 4, f32),
        ("ci", 144, bf), ("cm", 128, bf), ("cb", 128, bf), ("ia", 16, i32), ("ib", 16, i32), ("ic", 16, i32), ("fa", 16, f32),
        ("ks", 16, f32), ("mk16", 4, f32), ("tb", 1, f32), ("col", 16, f32), ("m4", 4, f32), ("k12", 1, f32), ("k4", 4, f32),
        ("bo", 128, bf), ("ee", 144, bf), ("dg", 512, bf), ("sh", 2048, bf), ("n32", 128, bf), ("nm", 128, bf), ("nil", HW, bf), ("lc", 4, f32), ("bl", 256, bf),
        ("kd", 128, bf), ("ni1", 128, f32), ("ik", 128, f32), ("pw", 4 * 144, ND),
        ("gm", 4 * 144, bf), ("sid", 128 * len(SCALES), bf)] + \
        [("gn", 4 * 144, bf)] * ("H" in CFG["spread"]) + [("e2", V, bf), ("wcp", V, bf), ("na", V, bf)] * SHORT:
    _buf(_n, _c, _d)
for _j in range(2 * STEPS):
    if "".join(CFG["spread"].split())[_j] == "H":
        SCRATCH["we%d" % _j] = ("dram", [128, HW], bf)
    else:
        SCRATCH["wd%d" % _j] = ("dram", [8, CFG["copies"], 4 * BL], bf)
_buf("pt", 4 * RUN, f32)
_buf("xb", BL, f32, "psum")
for _n in ("ua", "ub", "m0", "m1", "m2", "m3"):
    _buf(_n, 512, f32, "psum")

ENG = ("g", "pe", "dve", "act", "sp")
NDMA = 64
SEMAPHORES = ["q_" + e for e in ENG] + ["d%d" % i for i in range(NDMA)] + ["sent"] + \
             ["%s%d" % (k, i) for k in ("fl", "afo") for i in range(12)] + ["ax%d" % t for t in range(STEPS)] + ["au%d" % t for t in range(STEPS)] + \
             ["%s%d%d" % (k, h, j) for k in ("ml", "am") for h in range(2) for j in range(4)] + ["wl0", "wl1", "aw0", "aw1"]
KEPT = {}


def dispatch(nodes, after, count, pr):
    left, ready = list(count), [0.0] * len(nodes)
    pend, free = {x["eng"]: [] for x in nodes}, {x["eng"]: 0.0 for x in nodes}
    for i, x in enumerate(nodes):
        if left[i] == 0:
            pend[x["eng"]].append(i)
    order = []
    while len(order) < len(nodes):
        t, e = min((max(free[e], min(ready[i] for i in l)), e) for e, l in pend.items() if l)
        i = max((j for j in pend[e] if ready[j] <= t), key=lambda j: pr[j] if e in ENG else -ready[j])
        pend[e].remove(i)
        free[e] = t + nodes[i]["cost"]
        order.append(i)
        for j, gap in after[i]:
            ready[j] = max(ready[j], t + gap)
            left[j] -= 1
            if left[j] == 0:
                pend[nodes[j]["eng"]].append(j)
    return order


def span_of(nodes, order, sync):
    free, end = {}, [0.0] * len(nodes)
    for i in order:
        x = nodes[i]
        st = max([free.get(x["eng"], 0.0)] + [end[d] + sync for d in x["hard"]])
        free[x["eng"]] = st + x["cost"]
        end[i] = st + x["cost"] + x["lat"]
    return max(end)


def replay(nodes, order, sync):
    after, left, last = [[] for _ in nodes], [0] * len(nodes), {}
    for i in order:
        x = nodes[i]
        before = x["soft"] if x["eng"] not in ENG else [last[x["eng"]]] if x["eng"] in last else []
        for d, hard in [(d, True) for d in x["hard"]] + [(d, False) for d in before]:
            after[d].append((i, hard))
            left[i] += 1
        last[x["eng"]] = i
    ready, start, free, out, end = [0.0] * len(nodes), [0.0] * len(nodes), {}, [], 0.0
    pend = [(0.0, i) for i in range(len(nodes)) if not left[i]]
    while pend:
        t, i = first = min(pend)
        pend.remove(first)
        x = nodes[i]
        start[i] = st = max(t, free.get(x["eng"], 0.0))
        free[x["eng"]] = st + x["cost"]
        out.append(i)
        end = max(end, st + x["cost"] + x["lat"])
        for j, hard in after[i]:
            ready[j] = max(ready[j], st + x["cost"] + (x["lat"] + sync if hard else 0.0))
            left[j] -= 1
            if not left[j]:
                pend.append((ready[j], j))
    return end, out, start


def order_nodes(sets):
    nodes, sync = sets[0]
    after, count, parts, kinds, pr = [[] for _ in nodes], [0] * len(nodes), {}, {}, []
    for i, x in enumerate(nodes):
        for d in sorted(x["hard"] | x["soft"]):
            after[d].append((i, nodes[d]["cost"] + (nodes[d]["lat"] + sync if d in x["hard"] else 0.0)))
            count[i] += 1
        p = x["part"]
        if p not in ("const", "load"):
            parts.setdefault(p, []).append(i)
            if x["eng"] in ("dve", "act", "pe"):
                kinds.setdefault(x["name"], []).append(i)
        due = CFG["early"][p] if p in CFG["early"] else int(p[0]) * CFG["period"] + CFG["due"][p[1]][int(p[2])]
        pr.append(-1000.0 * (due + CFG["yield"].get(x["name"], 0.0)) - i)
    parts, kinds, z = list(parts.values()), list(kinds.values()), [CFG["seed"]]
    fixed = [i for i in range(len(nodes) - 1, -1, -1) if nodes[i]["part"] == "const"]

    def rnd():
        z[0] = (z[0] * 1103515245 + 12345) % 2147483648
        return (z[0] + 0.5) / 2147483648

    def judge(pr):
        for i in fixed:
            pr[i] = max([pr[j] for j, _gap in after[i]], default=0.0) + 1.0
        order = dispatch(nodes, after, count, pr)
        return sum(w * span_of(o, order, sy) / s for w, s, (o, sy) in zip(WEIGHT, SCALE, sets)) / sum(WEIGHT), order
    def start(pr):
        best = cur = judge(pr)
        for it in range(CFG["rounds"]):
            new = list(pr)
            for _ in range((1, 1, 2)[int(3 * rnd())]):
                d = (-8, -5, -3, -2, -1, 1, 2, 3, 5, 8)[int(10 * rnd())] * 1000.0
                groups = parts if rnd() < 0.6 else kinds
                for i in groups[int(len(groups) * rnd())]:
                    new[i] += d
            got = judge(new)
            if got[0] < cur[0] - CFG["temp"] * (1 - it / CFG["rounds"]) * math.log(rnd()):
                cur, pr = got, new
                if got[0] < best[0]:
                    best = got
        return polish(sets, best[1], rnd, CFG["swaps"] // 6, CFG["heat"])
    got = sorted(start(list(pr)) for _ in range(CFG["starts"]))
    KEPT["starts"] = [round(x[0]) for x in got]
    return polish(sets, got[0][2], rnd, CFG["swaps"], CFG["heat"] * CFG["cool"])


def polish(sets, order, rnd, swaps, heat):
    nodes = sets[0][0]
    n, anc, hard = len(nodes), [], []
    for x in nodes:
        keep, cover = [], 0
        for d in sorted(x["hard"], reverse=True):
            if not cover >> d & 1:
                keep.append(d)
            cover |= anc[d] | 1 << d
        anc.append(cover)
        hard.append(keep)
    names = sorted({x["eng"] for x in nodes})
    eng = [names.index(x["eng"]) for x in nodes]
    queue = [names[e] in ENG for e in eng]
    pre = [x["hard"] | x["soft"] for x in nodes]
    post, succ = [set() for _ in nodes], [[] for _ in nodes]
    for i in range(n):
        for d in pre[i]:
            post[d].add(i)
        for d in hard[i]:
            succ[d].append(i)
    tabs = [([x["cost"] for x in o], [x["lat"] + sy for x in o]) for o, sy in sets]
    every = range(len(tabs))
    share = [w / sum(WEIGHT) / scale for w, scale in zip(WEIGHT, SCALE)]
    order, pos, ahead, behind = list(order), [0] * n, [n] * (n + 1), [n] * (n + 1)

    def link(lo, part, first, final):
        order[lo:lo + len(part)] = part
        last = dict(first)
        for p, i in enumerate(part, lo):
            pos[i], ahead[i] = p, last[eng[i]]
            behind[ahead[i]] = last[eng[i]] = i
        for e, x in final.items():
            behind[last[e]], ahead[x] = x, last[e]

    def heads(k, lo, end, gone):
        cost, lat = tabs[k]
        for i in order[lo:]:
            st = gone[ahead[i]]
            for d in hard[i]:
                if end[d] > st:
                    st = end[d]
            gone[i] = st = st + cost[i]
            end[i] = st + lat[i]

    def tails(k, hi, tail):
        cost, lat = tabs[k]
        for i in order[hi::-1]:
            q = 0.0
            for d in succ[i]:
                if tail[d] > q:
                    q = tail[d]
            q += lat[i]
            if tail[behind[i]] > q:
                q = tail[behind[i]]
            tail[i] = q + cost[i]

    def chain(k):
        end, gone, pairs = ends[k], gones[k], []
        i = end.index(span[k])
        while i is not None:
            d = max(hard[i], key=lambda d: end[d], default=None)
            p = ahead[i]
            if p != n and (d is None or gone[p] >= end[d]):
                if queue[i] or (hard[p] and d is not None and end[d] <= max(end[x] for x in hard[p])):
                    pairs.append((p, i))
                d = p
            i = d
        return pairs

    ends, gones, tls = [[[0.0] * (n + 1) for _ in every] for _ in range(3)]
    best = (1e18, None, None)
    for it in range(swaps + 1):
        if it % 1000 == 0 or it == swaps:
            got = [replay(o, order, sy) for o, sy in sets]
            v = sum(s * x[0] for s, x in zip(share, got))
            if v < best[0]:
                best = (v, got[0][2], got[0][1])
            if it == swaps:
                return best
            none = {e: n for e in set(eng)}
            link(0, got[int(len(tabs) * rnd())][1], none, none)
            for k in every:
                heads(k, 0, ends[k], gones[k])
                tails(k, n - 1, tls[k])
            span = [max(e) for e in ends]
            cur, pairs = sum(s * v for s, v in zip(share, span)), None
        if pairs is None or rnd() < 0.05:
            pairs = chain(int(len(tabs) * rnd()))
        (a, b), back = pairs[int(len(pairs) * rnd())], rnd() < 0.5
        for _ in range((0, 0, 0, 1, 1, 2, 3, 5)[int(8 * rnd())] * queue[a]):
            if back and ahead[a] != n:
                a = ahead[a]
            if not back and behind[b] != n:
                b = behind[b]
        ia, ib = pos[a], pos[b]
        old = order[ia:ib + 1]
        mover, stop, rel = (b, a, pre) if back else (a, b, post)
        need, engs, tied = [mover], set(), set(rel[mover])
        for x in (old[-2::-1] if back else old[1:]):
            if x in tied or eng[x] in engs:
                need.append(x)
                engs.add(eng[x])
                tied |= rel[x]
        if need[-1] == stop:
            continue
        moved = set(need)
        rest = [x for x in old if x not in moved]
        new = need[::-1] + rest if back else rest + need
        first, final = {eng[x]: ahead[x] for x in reversed(old)}, {eng[x]: behind[x] for x in old}
        bar, v = cur - heat * (1 - it / swaps) * math.log(rnd()), 0.0
        for k in every:
            (cost, lat), end, tail, gone = tabs[k], ends[k], tls[k], gones[k]
            free, now, est, on = {e: gone[p] for e, p in first.items()}, {}, 0.0, False
            for i in new:
                st = free[eng[i]]
                for d in hard[i]:
                    y = now[d] if d in now else end[d]
                    if y > st:
                        st = y
                free[eng[i]] = st = st + cost[i]
                now[i] = st = st + lat[i]
                if st > est:
                    est = st
                for d in succ[i]:
                    if pos[d] > ib and st + tail[d] > est:
                        est = st + tail[d]
                on = on or gone[i] - cost[i] + tail[i] >= span[k] - 1e-6
            for e, x in final.items():
                if free[e] + tail[x] > est:
                    est = free[e] + tail[x]
            v += share[k] * (est if on or est > span[k] else span[k])
        if v >= bar:
            continue
        link(ia, new, first, final)
        e2, g2 = [list(e) for e in ends], [list(e) for e in gones]
        for k in every:
            heads(k, ia, e2[k], g2[k])
        s2 = [max(e) for e in e2]
        v = sum(s * x for s, x in zip(share, s2))
        if v < bar:
            cur, ends, gones, span, pairs = v, e2, g2, s2, None
            for k in every:
                tails(k, ib, tls[k])
        else:
            link(ia, old, first, final)


def plan(g, core, T, topo):
    nodes, ncalls, neng = build(g, core, T, topo, PRM)
    if "order" not in KEPT:
        _end, KEPT["st"], KEPT["order"] = order_nodes([(build(g, core, T, topo, dict(PRM, **m))[0], dict(PRM, **m)["sync"]) for m in SPREAD])
    for x, s in zip(nodes, KEPT["st"]):
        x["st"] = s
    return nodes, KEPT["order"], ncalls, neng


def relayed():
    out = [("u", 0, CFG["cuts"][0], CFG["cuts"][1])] + [("u", 0, CFG["cuts"][1], V)] * ("R" in CFG["first"])
    for part in CFG["order"].split():
        for k in CFG["pieces"].split():
            q0, q1 = (int(part[2]), int(part[3])) if len(part) == 4 else (2 * int(part[2]), 2 * int(part[2]) + 2)
            if k[0].isupper() and part[1] == k[0].lower() and q0 < int(k[2]) <= q1 and int(part[0]) < STEPS - 1:
                out.append((part[1], int(part[0]) + 1, int(k[1]) * QW, int(k[2]) * QW))
    return out


def finish():
    return {p: "FTTT"[int(p[2])] for p in CFG["order"].split() if p[1] == "U"}


def folded():
    return [(int(p[0]), int(p[2]), int(p[3]), 4) for p, how in finish().items() if how == "F"]


def helper_of(core, T, topo):
    return [c for c in topo.cores_of(core) if topo.die(c) != topo.die(core) and T.rank_of(c) is None
            and all(topo.may_write(c, p) for p in T.cores)][0]


def mirror_of(core, T, topo, which=0):
    return [c for c in topo.cores_of(core) if topo.die(c) == topo.die(core) and T.rank_of(c) is None and topo.addr(c)[2] != topo.addr(core)[2]][which]


def spreaders(core, T, topo):
    taken = [helper_of(core, T, topo), mirror_of(core, T, topo), mirror_of(core, T, topo, 1)]
    free = [c for c in topo.cores_of(core) if T.rank_of(c) is None and c not in taken]
    return sorted(free, key=lambda c: topo.addr(c)[2] == topo.addr(core)[2])[:NH]


def minned():
    out = []
    for part in CFG["order"].split():
        if part[1] == "c":
            t, h, run = int(part[0]), int(part[2]), []
            for kh, who in enumerate(CFG["min"].split()[2 * t + h]):
                run += [kh] * (who in "fF")
                if who == "f":
                    out.append((t, h, kh, run))
                    run = []
    return out


def min_place(T, t, h, k0, k1, rows=slice(0, 128)):
    return T[("wr0", "wr1", "wr2", "wr3", "xc0", "xc1")[2 * t + h]][rows, k0 * BL:k1 * BL]


def hand_min(g, core, home, T, topo):
    mask = topo.mask(core, home)
    for k, (t, h, last, blocks) in enumerate(minned()):
        g.wait_ge(T.sem["d%d" % k], bin(topo.mask(home, core)).count("1"))
        g.remote_dma(T["mn%d" % h][:, blocks[0] * BL:(last + 1) * BL], min_place(T, t, h, blocks[0], last + 1), T.sem["am%d%d" % (h, last)], T.sem.sent,
                     topo.addr(home)[1], topo.addr(home)[0], mask)
    g.wait_ge(T.sem.sent, bin(mask).count("1") * len(minned()))


def hand_spread(g, core, home, j, T, topo):
    mask, k, rows = topo.mask(core, home), 4 // NH, 128 // NH
    jobs = [(int(p[0]), int(p[2])) for p in CFG["order"].split() if p[1] == "w" and CFG["spread"].split()[int(p[0])][int(p[2])] == "H"]
    for t, h in jobs:
        here, laid = min_place(T, t, h, j * k, (j + 1) * k), T.sem["d%d" % (8 + 2 * t + h)]
        for i, q in enumerate((g.sync, g.scalar)):
            q.wait_ge(T.sem["d%d" % (2 * t + h)], bin(topo.mask(home, core)).count("1"))
            for trial in range(8 * i, 8 * i + 8):
                q.dma_start(min_place(T, t, h, j * k, (j + 1) * k, slice(trial, 128, 16)), T["we%d" % (2 * t + h)][j * rows:(j + 1) * rows, :]).then_inc(laid, 16)
        g.wait_ge(laid, 16 * 16)
        g.remote_dma(T["wr%d" % (2 * (t % 2) + h)][:, j * k * BL:(j + 1) * k * BL], here, T.sem["aw%d" % h], T.sem.sent,
                     topo.addr(home)[1], topo.addr(home)[0], mask)
    g.wait_ge(T.sem.sent, bin(mask).count("1") * len(jobs))


def fold_sides(T, t, q0, q1):
    return T.pf[:, 512 * t:512 * (t + 1)], T.fo[:]


def hand_back(g, core, home, T, topo):
    mask = topo.mask(core, home)
    for k, (t, q0, q1, _n) in enumerate(folded()):
        there, back = fold_sides(T, t, q0, q1)
        g.wait_ge(T.sem["d%d" % k], bin(topo.mask(home, core)).count("1"))
        g.remote_dma(back, there, T.sem["afo%d" % k], T.sem.sent, topo.addr(home)[1], topo.addr(home)[0], mask)
    g.wait_ge(T.sem.sent, bin(mask).count("1") * len(folded()))


def way_out(src, rank, T, topo):
    peers = [T.cores[(rank + d) % NR] for d in range(1, NR)]
    mask = topo.mask(src, peers[0])
    for p in peers:
        mask &= topo.mask(src, p)
    return mask, [DstId(rid=topo.addr(p)[0], pnc=topo.addr(p)[1]) for p in peers]


def hand_on(g, core, rank, T, topo):
    mask, ids = way_out(core, rank, T, topo)
    neng = bin(mask).count("1")
    for k, (kind, t, c0, c1) in enumerate(relayed()):
        ap = T["t%s%d" % (kind, t)][:, rank * V + c0:rank * V + c1]
        g.wait_ge(T.sem["d%d" % k], neng)
        g.remote_dma_fused([RemoteDMATransfer(dst_ids=ids, dma_engine_mask=mask, remote_sem=T.sem["a%s%d" % (kind, t)], srcs=[ap], dsts=[ap] * len(ids))],
                           local_sem=T.sem.sent)
    g.wait_ge(T.sem.sent, neng * len(relayed()))


def build(g, core, T, topo, PRM):
    rank = T.rank_of(core)
    CY, PEC, GC = PRM["cy"], PRM["pe"], PRM["gc"]
    nodes, here = [], ["load", []]
    lastw, readers, bankt = {}, {}, {}
    ve, ac, pe = g.vector, g.scalar, g.tensor

    def node(eng, cost, fn, r=(), w=(), banks=(), lat=0.0, kind="c", name="", of=None):
        i = len(nodes)
        hard, soft = set(), set()

        def dep(d, raw):
            if raw or nodes[d]["eng"] != eng:
                hard.add(d)
            else:
                soft.add(d)
        for k in r:
            if k in lastw:
                dep(lastw[k], True)
        for k in w:
            if k in lastw:
                dep(lastw[k], eng != "pe")
            for d in readers.get(k, ()):
                dep(d, True)
        for k in here[1]:
            for d in readers.get(k, ()):
                dep(d, True)
        here[1] = []
        if name == "jg" and eng == "act" and here[0] in CFG["behind"]:
            soft.add(bankt[("gx", eng)][eng])
        for b in list(banks) + [(name, eng)] * (name in CFG["kept"]):
            for d in bankt.get(b, {}).values():
                dep(d, False)
            bankt.setdefault(b, {})[eng] = i
        for k in r:
            readers.setdefault(k, []).append(i)
        for k in w:
            lastw[k] = i
            readers[k] = []
        nodes.append({"eng": eng, "cost": cost, "lat": lat, "fn": fn, "hard": hard, "soft": soft - hard, "kind": kind, "name": name,
                      "of": i if of is None else of, "part": here[0]})
        return i

    def join(k):
        first, part = len(nodes) - k, nodes[len(nodes) - k:]
        del nodes[first + 1:]
        nodes[first] = dict(part[0], cost=sum(x["cost"] for x in part), fn=lambda: [x["fn"]() for x in part][-1],
                            hard=set().union(*[x["hard"] for x in part]), soft={d for x in part for d in x["soft"] if d < first})
        assert max(nodes[first]["hard"], default=-1) < first
        for key, i in lastw.items():
            lastw[key] = min(i, first)
        for key, l in readers.items():
            readers[key] = [min(i, first) for i in l]

    def dve(n, cyc, fn, r, w, banks=(), name=""):
        node("dve", PRM["fx"] + max(64, n * cyc) * CY, fn, r, w, banks, name=name)

    def act(out, in_, func, n, r, w, banks=(), cyc=1.0, name="", **kw):
        node("act", PRM["fx"] + 15 + max(64, n * cyc) * CY, lambda: ac.activation(out, in_, func, **kw), r, w, banks, name=name)

    def tt(out, a, b, op, n, cyc, r, w, banks=(), name=""):
        dve(n, cyc, lambda: ve.tensor_tensor(out, a, b, op), r, w, banks, name)

    def ts(out, a, s1, s2, op0, op1, n, cyc, r, w, banks=(), name=""):
        if op1 is None:
            dve(n, cyc, lambda: ve.tensor_scalar(out, a, s1, None, op0), r, w, banks, name)
        else:
            dve(n, cyc, lambda: ve.tensor_scalar(out, a, s1, s2, op0, op1), r, w, banks, name)

    def cp(out, a, n, cyc, r, w, banks=(), name=""):
        dve(n, cyc, lambda: ve.tensor_copy(out, a), r, w, banks, name)

    def mm(items, r, w, bank, name=""):
        def fn():
            last = None
            for o, l, x, s0, s1, _c in items:
                last = pe.matmul(o, l, x, s0, s1)
            return last
        node("pe", 30 + sum(max(64, it[5]) * PEC for it in items), fn, r, w, (bank,), lat=100.0, name=name)

    def acc(out, terms, n, r, w, bank, name=""):
        mm([(out, l, x, i == 0, i == len(terms) - 1, n * c) for i, (l, x, c) in enumerate(terms)], r, w, bank, name)

    def sid(s):
        k = SCALES.index(s)
        return T.sid[:, 128 * k:128 * (k + 1)]

    def lin(out, terms, n, w, bank, name="", more=(), mk=()):
        acc(out, list(more) + [(sid(s), x, 1) for s, x, _k in terms], n,
            list(mk) + [k for _s, _x, k in terms] + [("sid", s) for s, _x, _k in terms], w, bank, name)

    def dma(q, pairs, kb, r, w, name="", add=False):
        eng = {"sp": g.sync, "act": g.scalar, "g": g}[q]
        kw = {"accum_op": A.add} if add else {}
        i = node(q, (1000.0 if q == "g" else 100.0) * len(pairs), lambda: [eng.dma_start(o, x, **kw) for o, x in pairs], r, w, ["fifo" + q] * (here[0] == "load"),
                 lat=PRM["dl"] / 2 + PRM["fl"] * add, kind="d", name=name)
        node("dma", kb * PRM["dr"], None, list(r) + list(w), list(w) + [("dma", i)], ["fifo"] * (here[0] == "load"), lat=PRM["dl"] / 2, kind="l", name=name, of=i)
        nodes[-1]["hard"].add(i)

    def blk(t, k):
        return t[:, 128 * k:128 * (k + 1)]

    own = rank * V
    mask, ids = way_out(core, rank, T, topo)
    neng = bin(mask).count("1")
    aid = helper_of(core, T, topo)
    near = topo.mask(core, aid) & ~mask
    assert bin(near).count("1") == neng and bin(way_out(aid, rank, T, topo)[0]).count("1") == neng
    ncalls = {}

    def send(kind, t, c0, c1):
        unit = HW if kind == "x" else QW
        kb, keys = (c1 - c0) // (4 if kind == "x" else 2), [("t" + kind, t, j) for j in range(c0 // unit, (c1 - 1) // unit + 1)]
        ap = T["t%s%d" % (kind, t)][:, own + c0:own + c1]
        sem = T.sem["a%s%d" % (kind, t)]
        ncalls[(kind, t)] = ncalls.get((kind, t), 0) + 1
        if (kind, t, c0, c1) in relayed():
            hs_ = T.sem["d%d" % relayed().index((kind, t, c0, c1))]
            node("g", 600.0, lambda: g.remote_dma(ap, ap, hs_, T.sem.sent, topo.addr(aid)[1], topo.addr(aid)[0], near),
                 keys, [("wire", kind, t, c0), "turn"], ["fifog"] * (t == 0), kind="r", name="relay")
            node("dma", 300.0 + kb * 2 * PRM["dr"], None, [("wire", kind, t, c0)], [("hop", kind, t, c0)], ["fifo"] * (t == 0), lat=PRM["lat"] + 600.0, kind="l")
            node("link2", 500.0 + kb * 3 * PRM["link"], None, [("hop", kind, t, c0)], [("land", kind, t, c0)], ["turn2"], lat=PRM["lat"], kind="l")
            return ("land", kind, t, c0)

        def fn():
            g.remote_dma_fused([RemoteDMATransfer(dst_ids=ids, dma_engine_mask=mask, remote_sem=sem, srcs=[ap], dsts=[ap] * len(ids))],
                               local_sem=T.sem.sent)
        node("g", 600.0, fn, keys, [("wire", kind, t, c0)], ["fifog"] * (t == 0), kind="r", name="send")
        node("dma", PRM["share"] * kb * 3 * PRM["link"], None, [("wire", kind, t, c0)], [("hop", kind, t, c0)], ["fifo"] * (t == 0), kind="l")
        node("link", 500.0 + (1 - PRM["share"]) * kb * 3 * PRM["link"], None, [("hop", kind, t, c0)], [("land", kind, t, c0)], lat=PRM["lat"], kind="l")
        return ("land", kind, t, c0)

    def sends(kind, t, q0, q1):
        return [send(kind, t, int(k[1]) * QW, int(k[2]) * QW) for k in CFG["pieces"].split() if k[0].lower() == kind and q0 < int(k[2]) <= q1]

    def arrive(kind, t, lands):
        node("arr", 0.0, (kind, t), lands, [("arr", kind, t)], kind="a")

    both = lambda *n: [n + (0,), n + (1,)]
    four = lambda *n: [n + (j,) for j in range(4)]
    loads = {"x": ([(T.tx0[:, own:own + V], T.x0[:])], 128, both("tx", 0)), "u": ([(T.tu0[:, own:own + V], T.u0[:])], 256, four("tu", 0)),
             "s": ([(T.si[:], T.s0[:])], 256, ["si"]), "p": ([(T.pi[:], T.p0[:])], 256, ["pi"]), "a": ([(T.ab[:], T.ag[:])], 128, ["ab"]),
             "w": ([(T.ww0[:], T.w0[:])], 128, both("ww", 0)), "j": ([(T.jt[:], T.ax[:]), (T.ti[:, 0:2], T.th[:])], 512, ["jt", "ti"])}
    soon, late = CFG["loads"].split()
    for k in soon:
        dma("act" if k.isupper() else "sp", loads[k.lower()][0], loads[k.lower()][1], [], loads[k.lower()][2], k)
    cuts = CFG["cuts"]
    first = {"x": lambda: send("x", 0, 0, V), "d": lambda: send("u", 0, 0, cuts[0]), "r": lambda: send("u", 0, cuts[0], cuts[1]),
             "R": lambda: send("u", 0, cuts[1], V)}
    landed = {k: first[k]() for k in CFG["first"] if k == "x" or "u" not in late}
    for k in late.strip("-"):
        dma("sp", loads[k][0], loads[k][1], loads[soon[-1].lower()][2], loads[k][2], k)
    landed.update({k: first[k]() for k in CFG["first"] if k not in landed})
    arrive("x", 0, [landed.pop("x")])
    arrive("u", 0, list(landed.values()))

    def iota(out, pat, base, cm, n, key, small=True):
        if small:
            node("g", 130 + 2 * n * CY, lambda: g.iota(out, pat, base, cm, allow_small_or_imprecise_dtypes=True), [], [key])
        else:
            node("g", 130 + 2 * n * CY, lambda: g.iota(out, pat, base, cm), [], [key])
    here[0] = "const"
    short = SHORT
    iota(T.ia[:], [[-1, 16]], 16, 1, 16, "ia", False)
    iota(T.ci[:], [[1, 144]], 0, 0, 144, "ci")
    iota(T.cm[:], [[0, 8], [1, 16]], 0, 0, 128, "cm")
    iota(T.cb[:], [[16, 8], [0, 16]], 16, 0, 128, "cb")
    ts(T.ib[:], T.ia[:], 15, None, A.bitwise_and, None, 16, 1, ["ia"], ["ib"])
    ts(T.ic[:], T.ia[:], 240, None, A.bitwise_and, None, 16, 1, ["ia"], ["ic"])
    cp(T.fa[:], T.ib[:], 16, 1, ["ib"], ["fa"])
    cp(T.col[:], T.ic[:], 16, 1, ["ic"], ["col"])
    p16, pb16 = T.fa[:, 0:1], T.col[:, 0:1]
    ts(T.ks[:], T.fa[:], pb16, -16.0, A.add, A.add, 16, 1, ["fa", "col"], ["ks"])
    ts(T.mk16[:], T.fa[:, 0:16:4], 3.5, 16.0, A.is_lt, A.mult, 4, 1, ["fa"], ["mk16"])
    act(T.tb[:], p16, F.Identity, 1, ["fa"], ["tb"], scale=-1.0 / 16, bias=15.0 / 16 - 384.0)
    ts(T.ic[:, 0:4], T.ib[:, 0:4], 3, None, A.bitwise_and, None, 4, 1, ["ib", "col"], ["ic"])
    ts(T.m4[:], T.ic[:, 0:4], 0.0, None, A.is_equal, None, 4, 1, ["ic"], ["m4"])
    ts(T.ic[:, 4:5], T.ib[:, 0:1], 2, None, A.arith_shift_right, None, 1, 1, ["ib", "col"], ["id"])
    ts(T.k12[:], T.ic[:, 4:5], pb16, -4.0, A.add, A.add, 1, 1, ["id", "col"], ["k12"])
    ts(T.bo[:], T.cb[:], pb16, None, A.is_equal, None, 128, .5, ["cb", "col"], ["bo"], name="bo")
    ts(T.ee[:], T.ci[:], pb16, None, A.is_equal, None, 144, .5, ["ci", "col"], ["ee"], name="ee")
    sent = [("wire", "u", 0, c) for c in (0,) + cuts] + [("wire", "x", 0, 0)]
    cI = T.ci[:, 0:128]
    k0 = T.ks[:, 0:1]
    ts(sid(1.0), cI, k0, None, A.is_equal, None, 128, .5, ["ci", "ks"], [("sid", 1.0)], name="sid")
    dve(HW, .5, lambda: ve.memset(T.nil[:], 0.0), [], ["nil"], name="nil")
    for out, s, key in [(sid(s), s, ("sid", s)) for s in SCALES[1:]] + [(T.ni1[:], -1.0, "ni1"), (T.ik[:], 1024.0, "ik")]:
        if s in CFG["ids"] and key != "ni1":
            act(out, sid(1.0), F.Identity, 128, [("sid", 1.0)], [key], scale=s, name="id")
        else:
            node("g", 170 + 256 * CY, lambda out=out, s=s: g.affine_select(out, T.nil[:, 0:128], [[-1, 128]], A.not_equal, s, 0, 1), ["nil"] + sent[-1:], [key], name="id")
    act(T.kd[:], sid(1.0), F.Identity, 128, [("sid", 1.0), "fa"], ["kd"], scale=p16, name="id")
    for kh in range(4):
        ts(T.pw[:, 144 * kh:144 * (kh + 1)], T.ci[:], T.k12[:], T.m4[:, kh:kh + 1], A.is_equal, A.mult, 144, .5, ["ci", "k12", "m4"], [("pw", kh)], name="pw")
    join(4)
    ts(T.nm[:], T.cm[:], p16, None, A.is_equal, None, 128, .5, ["cm", "fa"], ["nm"], name="n32")
    node("g", 170 + 256 * CY, lambda: g.affine_select(T.n32[:], T.nm[:], [[-1, 128]], A.not_equal, 33.0, 0, 1), ["nm"] + sent, ["n32"], name="n32")
    if "l" in CFG["spread"]:
        ts(T.k4[:, 0:1], T.ic[:, 0:1], 4.0, -13.0, A.mult, A.add, 1, 1, ["ic"], ["k4a"])
        act(T.k4[:, 1:2], T.k4[:, 0:1], F.Identity, 1, ["k4a", "col"], ["k4"], bias=pb16)
    if "H" in CFG["spread"]:
        k = 4 // NH
        ts(T.ic[:, 8:9], T.ib[:, 0:1], k - 1, None, A.bitwise_and, None, 1, 1, ["ib", "col"], ["ie"])
        ts(T.k4[:, 2:3], T.ic[:, 0:1], 32.0, 3.0 - 4 * k, A.mult, A.add, 1, 1, ["ic"], ["k4b"])
        act(T.k4[:, 3:4], pb16, F.Identity, 1, ["k4b", "col"], ["k4c"], scale=k / 4, bias=T.k4[:, 2:3])
        ts(T.k4[:, 2:3], T.ic[:, 8:9], -28.0, T.k4[:, 3:4], A.mult, A.add, 1, 1, ["ie", "k4c"], ["k4b"])
    for kl in range(4):
        act(blk(T.dg, kl), sid(1.0), F.Identity, 128, [("sid", 1.0), "mk16"], [("dg", kl)], scale=T.mk16[:, kl:kl + 1], name="dg")
    join(4)
    for how, gm, at, key in (("l", "gm", 1, "k4"), ("H", "gn", 2, "k4b")):
        if how in CFG["spread"]:
            for kl in range(4):
                ts(T[gm][:, 144 * kl:144 * (kl + 1)], T.ci[:], T.k4[:, at:at + 1], T.mk16[:, kl:kl + 1], A.is_equal, A.mult, 144, .5,
                   ["ci", key, "mk16"], [(gm, kl)], name="gm")
            join(4)
    LIFTS = sorted({(LIFT[int(p[0])], who) for p, who in CFG["gu"].items()} - {(1.0, "aaaa")})
    for i, (lift, who) in enumerate(LIFTS):
        assert who in ("aaaa", "vvaa", "aavv")
        ts(T.lc[:, i:i + 1], T.ic[:, 0:1], {"aaaa": -1.0}.get(who, 1.5), lift, A.is_lt if who == "aavv" else A.is_gt, A.mult, 1, 1, ["ic"], [("lc", i)])
        act(blk(T.bl, i), T.bo[:], F.Identity, 128, ["bo", ("lc", i)], [("bl", lift, who)], scale=T.lc[:, i:i + 1], name="id")
    for s in range(1, 16):
        ts(blk(T.sh, s), cI, T.ks[:, s:s + 1], None, A.is_equal, None, 128, .5, ["ci", "ks"], [("sh", s)], name="sh")
        if s % 3 == 0:
            join(3)
    sh = T.sh[:, 128:2048]
    node("g", 170 + 2 * 1920 * CY, lambda: g.affine_select(sh, sh, [[0, 15], [-1, 128]], A.not_equal, -1.0, 0, 1),
         [("sh", s) for s in range(1, 16)] + sent, ["sh"], name="sh")
    for i, sign in enumerate((1.0, -1.0)):
        node("g", 130 + 2 * BL * CY, lambda i=i: g.iota(T.pt[:, 2 * RUN * i + 2:2 * RUN * (i + 1):3], [[0, BL]], 0, 0, allow_small_or_imprecise_dtypes=True),
             sent, [("nought", i)], name="nought")
    for i, sign in enumerate((1.0, -1.0)):
        dve(HW, 1, lambda i=i, sign=sign: ve.memset(T.pt[:, 2 * RUN * i + 11:2 * RUN * (i + 1):12], sign * FLUSH), both("nought"), ["flush"][:i], name="flush")
    join(2)
    node("act", PRM["fx"] + 15 + HW * CY + 1300.0, lambda: ac.activation(T.ones[:], T.nil[:], F.Tanh, bias=20.0), ["nil"], ["ones"], name="ones")
    cp(T.thf[:, 0:1], T.ti[:, 0:1], 1, 1, ["ti"], ["thq"], name="th")
    ts(T.thf[:, 1:2], T.ti[:, 1:2], -1.0, 0.5, A.mult, A.add, 1, 1, ["ti"], ["thb"], name="th")

    hs = lambda h: slice(h * HW, (h + 1) * HW)
    mine = lambda h: slice(own + h * HW, own + (h + 1) * HW)
    lo, hi = slice(0, HW), slice(HW, 2 * HW)
    one = T.ones[:]
    block = lambda buf, kh: buf[:, kh * BL:(kh + 1) * BL]
    slot = lambda buf, k: buf[:, k % 4 * BL + k // 4:(k % 4 + 1) * BL:4]
    held = lambda kh: range(kh, 16, 4)
    pair = lambda h: ("m%d" % (2 * h), "m%d" % (2 * h + 1))
    turn = [0, 0, 0]

    spare = lambda table, j, s: T[table][:, (own + j * V) % (NR * V) + s.start:(own + j * V) % (NR * V) + s.stop]

    def lent(bank):
        if bank[0] == "x":
            return T.xb[:, 512 * int(bank[2]):512 * int(bank[2]) + HW], bank, [bank]
        return T[bank][:, hi], bank, [bank + "lo", bank + "hi"]

    def weights(b, h):
        s, m1 = hs(h), pair(h)[1]
        lin(T[m1][:, lo], [(-1.0, T["bb%d" % b][:, s], ("bb", b, h)), (3.0, T["lv%d" % b][:, s], ("lv", b, h)), (-4.0, one, "ones")], HW, [m1 + "lo"], m1, "m")
        tt(T["nw%d" % b][:, s], T["ww%d" % b][:, s], T[m1][:, lo], A.mult, HW, 1, [("ww", b, h), m1 + "lo"], [("nw", b, h)], [m1], "w")

    def other_weights(t, h):
        b, s, (ps, bank, bk) = t % 2, hs(h), lent(CFG["abank"].split()[2 * t + h])
        ts(T.e2[:, s], T["bb%d" % b][:, s], 1.5, None, A.is_gt, None, HW, .5, [("bb", b, h)], [("e2", h)], name="e2")
        if t == 0:
            ts(T.wcp[:, s], T.ww0[:, s], -4.0, 7.0, A.add, A.min, HW, .5, [("ww", 0, h)], [("wcp", h)], name="wcp")
        lin(ps, [(-1.0, T["bb%d" % b][:, s], ("bb", b, h)), (3.0, T.e2[:, s], ("e2", h)), (1.0, T["lv%d" % b][:, s], ("lv", b, h)), (-4.0, one, "ones")],
            HW, bk, bank, "m")
        tt(T.na[:, s], T.ww0[:, s], ps, A.mult, HW, 1, [("ww", 0, h)] + bk, [("na", h)], [bank], "na")

    def offsets(names, key, off, offkey, h):
        m0 = pair(h)[0]
        mm([(T[m0][:, HW + 64 * kh:HW + 64 * (kh + 1)], T.pw[:, 144 * kh + 12 - 4 * vl:144 * kh + 140 - 4 * vl],
             names[:, h * HW + vl:(h + 1) * HW:4], vl == 0, vl == 3, 64) for kh in range(4) for vl in range(4)],
           [key] + four("pw"), [m0 + "hi"], m0, "perm")
        cp(off[:, hs(h)], T[m0][:, hi], HW, 1, [m0 + "hi"], [offkey], [m0], "off")

    def gather(who, buf, table, off, h, kh, rk, wk, name):
        n = CFG["split"][name]
        for i in range(n):
            w = BL // n
            out, at = buf[:, kh * BL + i * w:kh * BL + (i + 1) * w], h * HW + 64 * kh + i * w // 16
            src = table[:].indirect(off[:, at:at + w // 16])
            if who == "v":
                cp(out, src, w, GC, rk, wk[i::n], name=name)
            else:
                act(out, src, F.Copy, w, rk, wk[i::n], cyc=GC, name=name)

    def jumps(t, h):
        return T["jb%d" % h], lambda kh: both("jb", h, kh)

    def jump(t, h):
        (off, offkey), (jb, keys) = (T.off1, ("off", 1, h)) if t else (T.off2, ("off", 2, h)), jumps(t, h)
        for kh in range(4):
            gather(CFG["jump"].split()[2 * t + h][kh], jb, T.jt, off, h, kh, ["jt", offkey], keys(kh), "jg")
        dma("sp", [(jb[kh:128:4, 0:BL], jb[kh:128:4, kh * BL:(kh + 1) * BL]) for kh in range(1, 4)], 192,
            [k for kh in range(1, 4) for k in keys(kh)], keys(0), "jdma")

    def jumped(t, h):
        base, basekey = (T.cc1, ("cc", 1, h)) if t else (T.sf, "sf")
        s, (ps, bank, bk) = hs(h), lent(CFG["qbank"].split()[2 * t + h])
        rest, rk = [(sid(1.0), base[:, s], 1), (T.kd[:], one, 1)], ["kd", "ones", ("sid", 1.0), basekey]
        jb, keys = jumps(t, h)
        rest, rk = rest + [(blk(T.dg, kl), slot(jb, 4 * kl), 1) for kl in range(4)], rk + keys(0) + four("dg")
        acc(ps, rest, HW, rk, bk, bank, "jd")
        if CFG["wrap"][2 * t + h] == "v":
            ts(T.md[:, s], ps, float(NR * V), -float(NR * V), A.is_ge, A.mult, HW, 1, bk, [("md", h)], [bank], "j1")
            tt(T["q%d" % t][:, s], T.md[:, s], ps, A.add, HW, 1, [("md", h)] + bk, [("q", t, h)], [bank], "j2")
        else:
            act(T.md[:, s], ps, F.Sign, HW, bk, [("md", h)], [bank], bias=0.5 - NR * V, name="j1")
            acc(ps, rest + [(sid(-1024.0), T.md[:, s], 1)], HW, rk + [("md", h), ("sid", -1024.0)], bk, bank, "jd")
            act(T["q%d" % t][:, s], ps, F.Identity, HW, bk, [("q", t, h)], [bank], bias=-1024.0, name="j2")

    here[0] = "list"
    cp(T.sf[:], T.si[:], V, 1, ["si"], ["sf"])
    for h in range(2):
        offsets(T.sf, "sf", T.off2, ("off", 2, h), h)
    here[0] = "init0"
    if CFG["ages"][0] == "v":
        ts(T.bb0[:], T.ab[:], -1.0, 3.0, A.mult, A.add, V, .5, ["ab"], both("bb", 0))
    else:
        act(T.bb0[:], T.ab[:], F.Identity, V, ["ab"], both("bb", 0), scale=-1.0, bias=3.0)
    if CFG["ages"][1] == "v":
        ts(T.lv0[:], T.ab[:], 2.5, None, A.is_lt, None, V, .5, ["ab"], both("lv", 0))
    else:
        act(T.lv0[:], T.ab[:], F.Sign, V, ["ab"], both("lv", 0), scale=-1.0, bias=3.0)
    for h in range(2):
        here[0] = "init%d" % h
        s, m0 = hs(h), pair(h)[0]
        lin(T[m0][:, lo], [(BIG, T.lv0[:, s], ("lv", 0, h)), (-1.0, T.sf[:, s], "sf")], HW, [m0 + "lo"], m0, "N")
        tt(T.r1[:, s], T.pi[:, s], T[m0][:, lo], A.min, HW, 1, ["pi", m0 + "lo"], [("r1", h)], [m0], "r")
        act(T.cc0[:, s], T.r1[:, s], F.Abs, HW, [("r1", h)], [("cc", 0, h)], name="abs")
        offsets(T.cc0, ("cc", 0, h), T.off0, ("off", 0, h), h)
        weights(0, h)

    def spread_weights(t, h):
        n, c, nw = 2 * (t % 2) + h, CFG["copies"], T["nw%d" % (t % 2)]
        wr, wp = T["wr%d" % n], T["wp%d" % h]
        bank, gm = pair(h)[1], "gn" if CFG["spread"].split()[t][h] == "H" else "gm"
        mm([(T[bank][:, kl:HW:4], T[gm][:, 144 * kl + 3 - vq:144 * kl + 131 - vq], nw[:, h * HW + 64 * vq:h * HW + 64 * (vq + 1)], vq == 0, vq == 3, 64)
            for kl in range(4) for vq in range(4)], [("nw", t % 2, h)] + four(gm), [bank + "lo", bank + "hi"], bank, "wrep")
        act(wp[:], T[bank][:, lo], F.Identity, HW, [bank + "lo"], [("wp", h)], [bank], scale=1.0 / 16, name="wc")
        if CFG["spread"].split()[t][h] == "H":
            to, k = spreaders(core, T, topo), 4 // NH
            wm = topo.mask(core, to[0])
            ids_ = [DstId(rid=topo.addr(c)[0], pnc=topo.addr(c)[1]) for c in to]
            i = node("g", 600.0, lambda: g.remote_dma_fused([RemoteDMATransfer(dst_ids=ids_, dma_engine_mask=wm, remote_sem=T.sem["d%d" % (2 * t + h)],
                                                                               srcs=[wp[:]], dsts=[T["we%d" % (2 * t + h)][:]] * NH)], local_sem=T.sem["wl%d" % h]),
                     [("wp", h)] + four("wr", n), four("wr", n), ["turnw"], lat=PRM["lat"] / 2, kind="f", name="wsend")
            ncalls["wl%d" % h] = ncalls.get("wl%d" % h, 0) + bin(wm).count("1")
            nodes[i]["sem"] = (T.sem["wl%d" % h], ncalls["wl%d" % h])
            node("dma", 64 * NH * PRM["short"] * PRM["dr"], None, [("wp", h)] + four("wr", n), [("ww", t, h)], kind="l", name="wsend", of=i, lat=PRM["lat"] / 2)
            node("dmaw", 800.0 + 256 * k * PRM["dr"], None, [("ww", t, h)], [("wx", t, h)], kind="l", name="wrep", lat=PRM["dl"])
            node("dmaw", 600.0 + 256 * k * PRM["dr"] * PRM["cross"], None, [("wx", t, h)], [("wy", t, h)], kind="l", name="wback", lat=PRM["lat"])
            ncalls["aw%d" % h] = ncalls.get("aw%d" % h, 0) + sum(bin(topo.mask(c, core)).count("1") for c in to)
            node("arr", 0.0, ("w", str(h), ncalls["aw%d" % h]), [("wy", t, h)], four("wr", n), kind="a")
            return
        wd = T["wd%d" % (2 * t + h)]
        dma("sp", [(wd[:, i, :], wp[:]) for i in range(c)], 64 * c * PRM["short"], [("wp", h)], [("wd", t, h)], "wout")
        for i in range(CFG["reads"]):
            k = 4 // CFG["reads"]
            s = slice(i * k * BL, (i + 1) * k * BL)
            dma("sp", [(wr[q:128:16 // c, s], wd[:, :, s]) for q in range(16 // c)], 256 * k * PRM["long"], [("wd", t, h)], four("wr", n)[i * k:(i + 1) * k], "wdma")

    def gathered(t, h):
        return T["xc%d" % h], lambda kh: both("xc", h, kh), 0.5

    def gather_x(t, h):
        xc, keys, _c = gathered(t, h)
        table, rk = T["tx%d" % t], both("tx", t) + [("arr", "x", t)]
        for kh in range(4):
            gather(CFG["gx"].split()[2 * t + h][kh], xc, table, T["off%d" % t], h, kh, rk + [("off", t, h)], keys(kh), "gx")

    def new_x(t, h):
        n, last, hb = 2 * (t % 2) + h, t == STEPS - 1, pair(h)[1]
        (xc, keys, cyc), px, wr = gathered(t, h), T.px, T["wr%d" % n]
        k0 = 0
        for run in map(int, CFG["xm"].split()[2 * t + h]):
            s, ks = slice(k0 * BL, (k0 + run) * BL), range(k0, k0 + run)
            dve(run * BL, cyc, lambda s=s: ve.tensor_tensor_scan(px[:, s], xc[:, s], wr[:, s], 0.0, A.max, A.mult),
                [x for kh in ks for x in keys(kh) + [("wr", n, kh)]], [("px", kh) for kh in ks], name="xm")
            for kh in ks:
                mm([(T[hb][:, hi], sid(-1.0), slot(px, k), k == 0, k == 15, HW) for k in held(kh)],
                   [("px", kh), ("sid", -1.0)], [hb + "lo", hb + "hi"], hb, "h")
            k0 += run
        act(T.yy[:, hs(h)], T[hb][:, hi], F.Identity, HW, [hb + "hi"], [("yy", h)], [hb], scale=1.0 / 256, bias=160.0 - 255.0 / 512, name="y")
        nx = spare("tx1", 1, hs(h)) if last else T["tx%d" % (t + 1)][:, mine(h)]
        here[1] = [("arr", "x", 1)] * last
        ts(nx, T.yy[:, hs(h)], -160.0, 15.0, A.add, A.min, HW, .5, [("yy", h)], [("tx", t + 1, h)], name="X")
        if last:
            dma("g", [(T.yx[:, hs(h)], nx)], 128, [("tx", t + 1, h)], [])
        return [] if last else sends("x", t + 1, 2 * h, 2 * h + 2)

    def fold_min(t, h, last):
        k = [m[:3] for m in minned()].index((t, h, last))
        blocks, to = minned()[k][3], mirror_of(core, T, topo, 1)
        xc, keys, _c = gathered(t, h)
        eng = topo.engines(core, to)
        share = len(eng) // len(blocks)
        masks = [sum(1 << e for e in eng[i * share:(i + 1) * share]) for i in range(len(blocks))]
        rk, wk = [x for kh in blocks for x in keys(kh)] + four("xs", h), [("mn", h, kh) for kh in blocks]
        s = "%d%d" % (h, last)
        dst = [DstId(rid=topo.addr(to)[0], pnc=topo.addr(to)[1])]
        i = node("g", 600.0, lambda: g.remote_dma_fused(
            [RemoteDMATransfer(dst_ids=dst, dma_engine_mask=m, remote_sem=T.sem["d%d" % k], srcs=[block(xc, kh), T["xs%d" % h][:]],
                               dsts=[min_place(T, t, h, kh, kh + 1)], alu_op=3) for m, kh in zip(masks, blocks)], local_sem=T.sem["ml" + s]),
            rk + wk, wk, ["turnm"], lat=PRM["lat"] / 2, kind="f", name="fmin")
        ncalls["ml" + s] = ncalls.get("ml" + s, 0) + len(eng)
        nodes[i]["sem"] = (T.sem["ml" + s], ncalls["ml" + s])
        node("dma", len(blocks) * 512 * PRM["dr"] * PRM["fr"], None, rk + wk, [("mw", k)], kind="l", name="fmin", of=i, lat=PRM["lat"] / 2)
        node("dma3", 600.0 + len(blocks) * 256 * PRM["dr"], None, [("mw", k)], [("mb", k)], kind="l", name="back", lat=PRM["lat"])
        ncalls["am" + s] = ncalls.get("am" + s, 0) + bin(topo.mask(to, core)).count("1")
        node("arr", 0.0, ("m", s, ncalls["am" + s]), [("mb", k)], wk, kind="a")

    def matches(t, h):
        b, (xc, keys, _c), tx, cb = t % 2, gathered(t, h), T["tx%d" % t], pair(h)[0]
        who = CFG["min"].split()[2 * t + h]
        spread_x = lambda i, start: [(T.xb[:, 512 * i + m:512 * (i + 1):4], sid(1.0), tx[:, own + h * HW + i * QW:own + h * HW + (i + 1) * QW],
                                      start and m == 0, m == 3, QW) for m in range(4)]
        mn, xs = T["mn%d" % h], "f" in who and T["xs%d" % h]
        for i in range(2 * ("v" in who)):
            mm(spread_x(i, True), [("tx", t, h), ("sid", 1.0)], ["xb%d" % i], "xb%d" % i, "xrep")
        if "f" in who.lower():
            for kl in range(4):
                if CFG["xs"][t] == "g":
                    node("g", 170 + 2 * HW * CY, lambda kl=kl: g.affine_select(xs[:, kl:BL:4], tx[:, mine(h)], [[0, HW]], A.is_ge, 0.0, 0, 0),
                         [("tx", t, h)], [("xs", h, kl)], name="xs")
                elif CFG["xs"][t] == "v":
                    cp(xs[:, kl:BL:4], tx[:, mine(h)], HW, .5, [("tx", t, h)], [("xs", h, kl)], name="xs")
                else:
                    act(xs[:, kl:BL:4], tx[:, mine(h)], F.Copy, HW, [("tx", t, h)], [("xs", h, kl)], name="xs")
        for kh in range(4):
            if who[kh] == "f":
                fold_min(t, h, kh)
        for kh in sorted(range(4), key=lambda kh: who[kh] in "fF"):
            if who[kh] == "v":
                tt(block(mn, kh), block(xc, kh), T.xb[:], A.min, BL, 1, keys(kh) + ["xb0", "xb1"], [("mn", h, kh)], ["xb0", "xb1"], "min")
            turn[2] += 1
            mm([(T[cb][:, lo], sid(256.0), T["lv%d" % b][:, hs(h)], True, False, HW)] * (turn[2] % 4 == 1) +
               [(T[cb][:, lo], T.ee[:, 16 - k:144 - k], slot(mn, k), False, turn[2] % 4 == 0 and k >= 12, HW) for k in held(kh)],
               [("mn", h, kh), "ee", ("lv", b, h), ("sid", 256.0)], [cb + "lo", cb + "hi"], cb, "c")
        act(T.ck[:, hs(h)], T[cb][:, lo], F.Identity, HW, [cb + "lo", "tb"], [("ck", h)], [cb], bias=T.tb[:], name="ck")
        act(T.nq[:, hs(h)], T[cb][:, lo], F.Relu, HW, [cb + "lo", "thq"], [("nq", h)], [cb], scale=-1.0, bias=T.thf[:, 0:1], name="nq")

    def span(q0, q1):
        h, w = q0 // 2, 512 * (q1 - q0)
        return h, lambda buf, kh: buf[:, kh * BL + 512 * (q0 % 2):kh * BL + 512 * (q0 % 2) + w], w, lambda kh: [("pu", q0 and 1 + q0 % 2, kh)]

    def gather_u(t, q0, q1):
        h, piece, w, keys = span(q0, q1)
        n, how = 2 * (t % 2) + h, finish()[here[0]]
        wr, first = T["wr%d" % n], h * HW + 32 * (q0 % 2)
        for kh in range(4):
            src = T["tu%d" % t][:].indirect(T["off%d" % t][:, first + 64 * kh:first + 64 * kh + w // 16])
            rk = four("tu", t) + [("arr", "u", t), ("off", t, h)] + ["flush"] * (how == "T")
            out = product(q0, kh, how)
            if CFG["gu"].get(here[0], "vvvv")[kh] == "v":
                tt(out, src, piece(wr, kh), A.mult, w, GC, rk + [("wr", n, kh)], keys(kh), name="gu")
            else:
                turn[1] += 1
                uc = T["uc%d" % (turn[1] % 2)][:, 0:w]
                act(uc, src, F.Identity, w, rk, [("uc", turn[1] % 2)], cyc=GC, bias=LIFT[t], name="gu")
                dve(w, 1, lambda kh=kh, uc=uc, out=out: ve.tensor_tensor_scan(out, uc, piece(wr, kh), 0.0, A.max, A.mult),
                    [("uc", turn[1] % 2), ("wr", n, kh), "flush"], keys(kh), name="um")
        if how == "F":
            fold(t, q0, q1, 4)

    def product(q, kh, how):
        if how == "F":
            return T.pf[:, 512 * kh:512 * (kh + 1)]
        a = RUN * (2 * (kh // 2) + q % 2)
        return T.pt[:, a + kh % 2:a + RUN:3]

    def fold(t, q0, q1, n):
        h, piece, w, keys = span(q0, q1)
        k, there, to = folded().index((t, q0, q1, n)), fold_sides(T, t, q0, q1)[0], mirror_of(core, T, topo)
        srcs, rk, fm = [product(q0, kh, "F") for kh in range(n)], [x for kh in range(n) for x in keys(kh)], topo.mask(core, to)
        wk = [("fo", q) for q in range(q0, q1)]
        i = node("g", 600.0, lambda: g.remote_dma_fused([RemoteDMATransfer(dst_ids=[DstId(rid=topo.addr(to)[0], pnc=topo.addr(to)[1])], dma_engine_mask=fm,
                                                                           remote_sem=T.sem["d%d" % k], srcs=srcs, dsts=[there], alu_op=1)],
                                                        local_sem=T.sem["fl%d" % k]),
                 rk + wk, wk, ["turnf"], lat=PRM["lat"] / 2, kind="f", name="fold")
        nodes[i]["sem"] = (T.sem["fl%d" % k], bin(fm).count("1"))
        node("dma", n * w / 2 * PRM["dr"] * PRM["fr"], None, rk + wk, [("fw", k)], kind="l", name="fold", of=i, lat=PRM["lat"] / 2)
        node("dma2", 600.0 + w / 2 * PRM["dr"], None, [("fw", k)], [("fb", k)], kind="l", name="back", lat=PRM["lat"])
        node("arr", 0.0, ("fo", k), [("fb", k)], wk, kind="a")
        ncalls[("fo", k)] = bin(topo.mask(to, core)).count("1")

    def new_u(t, q0, q1):
        h, piece, w, keys = span(q0, q1)
        name = "%dU%d%d" % (t, q0, q1)
        last, fin, n, lifted = t == STEPS - 1, finish()[name], w // 4, CFG["gu"].get(name, "vvvv")
        bank = "u" + CFG["ubank"].split()[t][q0]
        out_again = blk(T.bl, LIFTS.index((LIFT[t], lifted))) if (LIFT[t], lifted) in LIFTS else T.bo[:]
        up, s, os_ = T[bank][:, 0:n], slice(q0 * QW, q1 * QW), slice(own + q0 * QW, own + q1 * QW)
        made = [("tu", t + 1, q) for q in range(q0, q1)]
        mm([(up, T.ik[:], T["tu%d" % t][:, os_], True, False, 4 * n), (up, sid(128.0), T["tx%d" % t][:, os_], False, False, n)] +
           [(up, out_again, T["nw%d" % (t % 2)][:, s], False, False, n)] * ("a" in lifted),
           four("tu", t) + [("tx", t, h), "ik", ("sid", 128.0), ("nw", t % 2, h), "bo", ("bl", LIFT[t], lifted)], [bank + "lo", bank + "hi"], bank, "own")
        if fin == "F":
            terms, key = [T.fo[:, kl:w:4] for kl in range(4)], [("fo", q0)]
        else:
            turn[0] += 1
            sc, a, key = T["sc%d" % (turn[0] % 2)], RUN * (q0 % 2), both("sc", turn[0] % 2)
            for i in range(2):
                p = slice(i * RUN // 2, (i + 1) * RUN // 2)
                dve(RUN // 2, 1, lambda p=p: ve.tensor_tensor_scan(sc[:, p], T.pt[:, a + p.start:a + p.stop], T.pt[:, 2 * RUN + a + p.start:2 * RUN + a + p.stop],
                                                                   0.0, A.add, A.add),
                    [x for k in range(4) for x in keys(k)] + ["flush"], key[i:i + 1], name="scan")
            terms = [sc[:, 10:RUN:12]]
        mm([(up, T.ni1[:], x, False, i == len(terms) - 1, 4 * n) for i, x in enumerate(terms)], key + ["ni1"], [bank + "lo", bank + "hi"], bank, "arg")
        nu = spare("tu1", 1, s) if last else T["tu%d" % (t + 1)][:, os_]
        here[1] = [("arr", "u", 1)] * last
        act(nu, up, F.Tanh, n, [bank + "lo"], made, [bank], scale=2.0 ** -11, bias=-0.5, name="tanh")
        if last:
            dma("sp", [(T.yu[:, s], nu)], n // 2, made, [])
        return [] if last else sends("u", t + 1, q0, q1)

    def slots(t, h):
        b, n, last = t % 2, 1 - t % 2, t == STEPS - 1
        s = hs(h)
        lv, bb, ww, ga = [(T["%s%d" % (x, i)][:, s], (x, i, h)) for x, i in (("lv", b), ("bb", b), ("ww", b * (not short)), ("ga", t))]
        nq, on, sg = (T.nq[:, s], ("nq", h)), (one, "ones"), T["sg%d" % h]
        nx = spare("tx1", 1, s) if last else T["tx%d" % (t + 1)][:, own + h * HW:own + (h + 1) * HW]
        ever = [(T["ga%d" % i][:, s], ("ga", i, h)) for i in range(t)]
        for q in range(4):
            bank = pair(h)[q % 2]
            mm([(T[bank][:, sl], blk(T.sh, 1 + 2 * q + i), T.ck[:, s], True, True, HW) for i, sl in enumerate((lo, hi))],
               [("ck", h), "sh"], [bank + "lo", bank + "hi"], bank, "diff")
            act(sg[:, 2 * q * HW:(2 * q + 2) * HW], T[bank][:], F.Sign, 2 * HW, [bank + "lo", bank + "hi"],
                [("sg", h, 2 * q + 1), ("sg", h, 2 * q + 2)], [bank], name="sgn")
        m0, m1 = pair(h)
        acc(T[m0][:, hi], [(T.bo[:], nx, 1)], HW, [("tx", t + 1, h), "bo"], [m0 + "hi"], m0, "E")
        act(T.ss[:, s], T[m0][:, hi], F.Sign, HW, [m0 + "hi", "thb"], [("ss", h)], [m0], bias=T.thf[:, 1:2], name="ss")
        lin(T[m1][:, lo], [(128.0,) + lv, (-1.0, sg[:, 7 * HW:8 * HW], ("sg", h, 8))], HW, [m1 + "lo"], m1, "V",
            [(blk(T.sh, 16 - sn), sg[:, (sn - 1) * HW:sn * HW], 1) for sn in range(1, 8)] + [(T.n32[:], T.ss[:, s], 1)],
            [("sg", h, sn) for sn in range(1, 8)] + [("ss", h), "sh", "n32"])
        act(ga[0], T[m1][:, lo], F.Sign, HW, [m1 + "lo"], [ga[1]], [m1], bias=-168.0, name="ga")
        tag = [(BIG,) + lv, (BIG,) + nq]
        lapse = (T.sf, "sf", [(BIG,) + bb, (-2 * BIG,) + lv, (BIG / 2,) + ga, (1.5 * BIG,) + on], m1)
        if not last:
            ways = [(T["q%d" % t], ("q", t, h), tag, m0), lapse]
        else:
            ways = [(T.q0, ("q", 0, h), tag + [(BIG / 2,) + x for x in ever] + [(BIG,) + on], m0),
                    (T.q1, ("q", 1, h), tag + [(-BIG / 2,) + x for x in ever], m0), lapse]
        cur = (T["cc%d" % b][:, s], ("cc", b, h))
        for i, (name, key, terms, bank) in enumerate(ways):
            if short and not last and i == 1:
                lin(T[m0][:, lo], [(-4.0, T.wcp[:, s], ("wcp", h))] + [(-32.0,) + x for x in ever + [on] * t + [ga]], HW, [m0 + "lo"], m0, "m")
                tt(T["nw%d" % n][:, s], T.na[:, s], T[m0][:, lo], A.min, HW, 1, [("na", h), m0 + "lo"], [("nw", n, h)], [m0], "w")
            lin(T[bank][:, hi], terms, HW, [bank + "hi"], bank, "N", [(sid(-1.0), name[:, s], 1)], [("sid", -1.0), key])
            out = (T["r%d" % (1 + i % 2)][:, s], ("r%d" % (1 + i % 2), h))
            tt(out[0], cur[0], T[bank][:, hi], A.min, HW, 1, [cur[1], bank + "hi"], [out[1]], [bank], "r")
            cur = out
        nc = spare("tu1", 2, s) if last else T["cc%d" % n][:, s]
        here[1] = [("arr", "u", 1)] * last
        act(nc, cur[0], F.Abs, HW, [cur[1]], [("cc", n, h)], name="abs")
        lin(T[m0][:, lo], [(1.0,) + bb, (-1.5,) + ga, (-4.0,) + lv, (-4.0,) + nq], HW, [m0 + "lo"], m0, "t")
        if last or not short:
            lin(T[m1][:, lo], [(1.0,) + ww] + [(2.0,) + x for x in ever * short + [ga]], HW, [m1 + "lo"], m1, "W")
        nb, nw = T["bb%d" % n][:, s], T["nw1" if last else "ww%d" % (n * (not short))][:, s]
        act(nb, T[m0][:, lo], F.Relu, HW, [m0 + "lo"], [("bb", n, h)], [m0], bias=1.5, name="b")
        if not last and not short:
            ts(nw, T[m1][:, lo], 2.0, 15.0, A.add, A.min, HW, 1, [m1 + "lo"], [("ww", n, h)], [m1], "W")
        if last:
            act(nw, T[m1][:, lo], F.Relu, HW, [m1 + "lo"], [("nw", 1, h)], [m1], scale=-1.0, bias=9.0 if short else 13.0, name="W")
            lin(T[m1][:, hi], [(-1.0, nw, ("nw", 1, h)), (-16.0, nb, ("bb", n, h))], HW, [m1 + "hi"], m1, "yw")
            here[1] = [("arr", "u", 1)]
            act(spare("tu1", 3, s), T[m1][:, hi], F.Identity, HW, [m1 + "hi"], [("wo", h)], [m1], bias=63.0, name="yw")
            dma("sp", [(T.yw[:, s], spare("tu1", 3, s))], 128, [("wo", h)], [])
            dma("sp", [(T.yc[:, s], nc)], 128, [("cc", n, h)], [])
            return
        offsets(T["cc%d" % n], ("cc", n, h), T["off%d" % (t + 1)], ("off", t + 1, h), h)
        if CFG["live"][2 * t + h] == "v":
            ts(T["lv%d" % n][:, s], nb, 1.0, None, A.min, None, HW, .5, [("bb", n, h)], [("lv", n, h)], name="lv")
        else:
            act(T["lv%d" % n][:, s], nb, F.Sign, HW, [("bb", n, h)], [("lv", n, h)], name="lv")
        if not short:
            weights(n, h)

    lands = {}
    for part in CFG["order"].split():
        t, what, j = int(part[0]), part[1], int(part[2])
        here[0] = part
        if what in "xu":
            ld = lands.setdefault((what, t), [])
            ld += new_x(t, j) if what == "x" else new_u(t, j, int(part[3]))
            if len(ld) == CFG["pieces"].lower().count(what):
                arrive(what, t + 1, ld)
        elif what == "U":
            gather_u(t, j, int(part[3]))
        else:
            {"w": spread_weights, "X": gather_x, "c": matches, "s": slots, "j": jump, "q": jumped, "a": other_weights}[what](t, j)
    return nodes, ncalls, neng


def emit(g, T, nodes, order, ncalls, neng):
    Q = {"g": g, "pe": g.tensor, "dve": g.vector, "act": g.scalar, "sp": g.sync}
    real = lambda x: x["kind"] in "cdrf"
    pos, clock, cnt = {}, {e: {} for e in Q}, {e: 0 for e in Q}
    done, waits, need = {}, {}, set()
    for i in order:
        x = nodes[i]
        if x["kind"] == "a":
            done[i] = {("a",) + x["fn"]: 1}
            pos[i] = (("a",) + x["fn"], 1)
            continue
        if not real(x):
            continue
        ck = clock[x["eng"]]
        ws = []
        for d in sorted({nodes[d]["of"] for d in x["hard"]}, key=lambda d: (-nodes[d]["st"], d)):
            if nodes[d]["kind"] == "r":
                continue
            k, v = pos[d]
            if ck.get(k, 0) >= v:
                continue
            ws.append(d)
            need.add(d)
            for kk, vv in done[d].items():
                if ck.get(kk, 0) < vv:
                    ck[kk] = vv
        waits[i] = ws
        if x["kind"] == "c":
            cnt[x["eng"]] += 1
            pos[i] = (x["eng"], cnt[x["eng"]])
        else:
            pos[i] = (("d", i), 1)
        done[i] = dict(ck)
        done[i][pos[i][0]] = pos[i][1]
    sem, val, nd, nsent = {}, {e: 0 for e in Q}, 0, 0
    tail = []
    for i in order:
        x = nodes[i]
        if x["kind"] == "a":
            if len(x["fn"]) == 3:
                sem[i] = (T.sem["a" + x["fn"][0] + x["fn"][1]], x["fn"][2])
            else:
                sem[i] = (T.sem["a%s%d" % x["fn"]], ncalls[x["fn"]] * (1 if x["fn"][0] == "fo" else neng * (NR - 1)))
            continue
        if not real(x):
            continue
        q = Q[x["eng"]]
        for d in waits[i]:
            q.wait_ge(sem[d][0], sem[d][1])
        ins = x["fn"]()
        if x["kind"] == "r":
            nsent += neng
        elif x["kind"] == "f":
            sem[i] = x["sem"]
            if i not in need:
                tail.append((q, sem[i]))
        elif x["kind"] == "d":
            sem[i] = (T.sem["d%d" % nd], 16 * len(ins))
            nd += 1
            for one in ins:
                one.then_inc(sem[i][0], 16)
            if i not in need:
                tail.append((q, sem[i]))
        elif i in need:
            val[x["eng"]] += 1
            sem[i] = (T.sem["q_" + x["eng"]], val[x["eng"]])
            ins.then_inc(sem[i][0], 1)
    g.wait_ge(T.sem.sent, nsent)
    for q, s in tail:
        q.wait_ge(s[0], s[1])


def rank_program(g, core, T, topo):
    if T.rank_of(core) is None:
        for rank, c in enumerate(T.cores):
            if helper_of(c, T, topo) == core:
                hand_on(g, core, rank, T, topo)
            if folded() and mirror_of(c, T, topo) == core:
                hand_back(g, core, c, T, topo)
            if minned() and mirror_of(c, T, topo, 1) == core:
                hand_min(g, core, c, T, topo)
            if "H" in CFG["spread"] and core in spreaders(c, T, topo):
                hand_spread(g, core, c, spreaders(c, T, topo).index(core), T, topo)
        return
    emit(g, T, *plan(g, core, T, topo))
